import numpy as np, ml_dtypes
CORES = [6,15,38,47]
N = 4
BF = ml_dtypes.bfloat16
W, V, L, S, T, E = 4096, 1024, 256, 16, 6, 1
def parts(rng):
    x = (64 * rng.random((N, 8, 16, W)) * (0.5 + 0.5 * rng.random((N, 8, 1, W)))).astype(np.int64)
    im = (64 * rng.random((N, 8, 16, V)) * (0.25 + 0.75 * rng.random((N, 8, 1, V)))).astype(np.int64)
    z = (64 * rng.random((N, 8, 16, 2, L)) * (0.5 + 0.5 * rng.random((N, 8, 1, 2, L)))).astype(np.int64)
    b = rng.integers(0, W, (N, 8, 16, V)); q = np.minimum((8 * rng.random((N, 8, 16, V)) ** 0.6).astype(np.int64), 7)
    return x, im, b, q, z, rng.integers(1, 4096, (N, 8, 16))
def pack(x, im, b, q, z, w):
    return {"geno": x.reshape(N, 128, W).astype(np.float32).astype(BF), "immun": im.reshape(N, 128, V).astype(np.float32).astype(BF),
            "bank": (b + W * q).reshape(N, 128, V).astype(np.int32), "bites": z.reshape(N, 128, 2 * L).astype(np.float32).astype(BF), "wt": w.reshape(N, 128, 1).astype(np.int32)}
def first(z, w):
    u = np.sum(w[:, :, :, None] * z[:, :, :, 0], axis=2) & 4095
    return ((u * u >> 5) + 37 * u) & (V - 1)
def setup_inputs(rng):
    return pack(*parts(rng))
def setup_inputs_corners(rng):
    x, im, b, q, z, w = parts(rng); w[:, :, 0] = 4095; w[:, :, 1] = 2048
    kind = rng.integers(0, 4, (N, 8, 1, V)); im = np.where(kind == 0, 0, np.where(kind == 1, 63, im))
    mode = rng.integers(0, 7, (N, 8, 1, V)); pos = np.argsort(rng.random((N, 8, 16, V)), axis=2); near = E - 1 + rng.integers(0, 3, q.shape)
    q = np.where(mode == 5, q[:, :, :1], q); q = np.where(mode == 4, near, q); q = np.where(mode == 3, 7 * (pos < 2), q)
    q = np.where(mode == 2, 7 * (pos < 1), q); q = np.where(mode == 1, 0, q); q = np.where(mode == 0, 7, q)
    edge = rng.integers(0, 4, (N, 8, 1, V)); b = np.where(edge == 0, (W - 1) * rng.integers(0, 2, b.shape), b); b = np.where(edge == 1, b[:, :, :1], b)
    z[:, :, :, 0, 4:L - 1] = np.maximum(z[:, :, :, 0, 4:L - 1], 1)
    z[:, :, :, :, 0] = 0; z[:, :, :, :, 1] = 63; z[:, :, :, :, 2] = 0; z[:, :, 1, :, 2] = 1; z[:, :, :, :, L - 1] = 0; z[:, :, 0, :, L - 1] = 1
    v = first(z, w); n = L // 2; m = L // 8
    for a in range(N):
        for g in range(8):
            lanes = (4 + rng.permutation(L - 5))[:n]; zz = z[a, g, :, 0][:, lanes]
            po = np.argsort(rng.random((16, n)), axis=0); cnt = 8 + np.arange(n) % 3
            im[a, g][:, v[a, g, lanes]] = zz - (po < cnt)
            own = lanes[:m]; k = rng.integers(0, 16, m); h = v[a, g, own]
            b[a, g, k, h] = S * own; q[a, g, k, h] = 7
            x[a, g][:, S * own] = np.where(zz[:, :m] < 32, 63, 0)
    return pack(x, im, b, q, z, w)
def setup_inputs_crowd(rng):
    x, im, b, q, z, w = parts(rng); w = np.repeat(rng.integers(1, 4096, (N, 8, 1)), 16, axis=2)
    for a in range(N):
        for g in range(8):
            for c in range(2):
                n = int(rng.choice(np.array([1, 2, 5, 17, 30])))
                if g == a % 8 and c == 0: n = 1
                if g == (a + 3) % 8 and c == 0: continue
                base = z[a, g, :, c, :n].copy()[:, rng.integers(0, n, L)]
                z[a, g, :, c] = np.take_along_axis(base, np.argsort(rng.random((16, L)), axis=0), 0)
        g = (a + 3) % 8; w[a, g] = rng.integers(1, 4096, 16); w[a, g, 0] = 1; w[a, g, 15] = 64
        u = rng.permutation(4096); u = u[np.unique(((u * u >> 5) + 37 * u) & (V - 1), return_index=True)[1]]
        need = (rng.permutation(u)[:L] - np.sum(w[a, g, 1:15, None] * z[a, g, 1:15, 0], axis=0)) & 4095
        z[a, g, 0, 0] = need & 63; z[a, g, 15, 0] = need >> 6
    return pack(x, im, b, q, z, w)
def setup_inputs_ends(rng):
    def rec(n):
        k = rng.integers(0, 3, (N, 8, 1, n)); return 63 * np.where(k == 2, rng.integers(0, 2, (N, 8, 16, n)), k)
    x = rec(W); im = rec(V); z = rec(2 * L).reshape(N, 8, 16, 2, L); w = np.where(rng.integers(0, 2, (N, 8, 16)) == 1, 4095, 1); w[N - 1, 7] = 4095
    x[:, 1::2, :, W - 1] = 0; x[:, ::2, :, W - 1] = 63 * rng.integers(0, 2, (N, 4, 16))
    nz = rng.integers(0, 8, (8, 1, L)) * rng.integers(0, 2, (8, 1, L)); nz[:, :, 0] = 0; nz[:, :, L - 1] = 0
    nz[0, 0, ::2] = 0; nz[0, 0, 1] = 1; nz[0, 0, L - 1] = 0
    z[N - 1, :, :, 0] = 63 * (np.argsort(rng.random((8, 16, L)), axis=1) >= nz)
    z[1, :, :, 0] = 63 * (np.argsort(rng.random((8, 16, L)), axis=1) >= rng.integers(0, 8, (8, 1, L)))
    v = first(z, w); r = np.arange(16)[None, None, :, None]; mode = rng.integers(0, 5, (N, 8, 1, V))
    fl = (mode == 0) | ((mode == 1) & (r >= 14)) | ((mode == 2) & ((r == 0) | (r == 15))) | ((mode == 4) & (rng.random((N, 8, 16, V)) < 0.5))
    anyb = (rng.random((N, 8, 1, V)) < 0.5) & fl
    for g in range(8):
        for a in (1, N - 1):
            h = v[a, g]; fl[a, g, 14:][:, h] = True; anyb[a, g][:, h] = False; im[a, g][:, h] = 0
        im[0, g][:, v[0, g]] = 63
    im[N - 1, 0][:, v[N - 1, 0, 1]] = 63
    woke = 16 * L - 2 * int(np.sum(v[N - 1, 0] == v[N - 1, 0, 1])); assert woke > 15 * L and woke & (V - 1) != 0
    b = np.where(fl, np.where(anyb, rng.integers(0, W, fl.shape), W - 1), 0); q = 7 * fl
    for g, ks in ((1, (2, 5, 9)), (3, (0, 1, 15)), (5, (13, 14, 15))):
        h = v[N - 1, g, 0]; x[N - 1, g, :, W - 2] = 0; x[N - 1, g, rng.integers(0, 16), W - 2] = 1
        b[N - 1, g, :, h] = 0; q[N - 1, g, :, h] = 0
        for k, c in zip(ks, (W - 2, W - 2, W - 1)):
            b[N - 1, g, k, h] = c; q[N - 1, g, k, h] = 7
    return pack(x, im, b, q, z, w)
def setup_inputs_spread(rng):
    x, im, b, q, z, w = parts(rng)
    def pw(*s): return rng.random(s) ** np.exp2(rng.integers(-2, 4, s[:2] + (1,) + s[3:]))
    x = np.minimum((64 * pw(N, 8, 16, W)).astype(np.int64), 63); im = np.minimum((64 * pw(N, 8, 16, V)).astype(np.int64), 63)
    z = np.minimum((64 * pw(N, 8, 16, 2, L)).astype(np.int64), 63); b = np.minimum((W * pw(N, 8, 16, V)).astype(np.int64), W - 1)
    q = np.minimum((8 * rng.random((N, 8, 16, V)) ** np.exp2(rng.integers(-2, 2, (N, 8, 1, V)))).astype(np.int64), 7)
    w = np.minimum(np.exp2(12 * rng.random((N, 8, 16))).astype(np.int64), 4095)
    return pack(x, im, b, q, z, np.maximum(w, 1))
def setup_inputs_ties(rng):
    lv = rng.integers(0, 3, (N, 8, 1, W)); x = lv + rng.integers(0, 3, (N, 8, 16, W)); im = rng.integers(0, 3, (N, 8, 16, V))
    z = rng.integers(0, 3, (N, 8, 1, 2, L)) + rng.integers(0, 3, (N, 8, 16, 2, L)); w = rng.integers(1, 4096, (N, 8, 16)); b = rng.integers(0, W, (N, 8, 16, V))
    q = np.where(rng.random((N, 8, 16, V)) < 0.5, rng.integers(0, 8, (N, 8, 1, V)), rng.integers(4, 8, (N, 8, 1, V)))
    x[:, ::2, :, W // 2:] = x[:, ::2, :, :W // 2]; b[:, :, 8:, ::2] = b[:, :, :8, ::2]
    z[:, :, :, 0, ::4] = np.take_along_axis(x, rng.integers(0, W, (N, 8, 1, L // 4)), 3)
    x[:, 1::2] += 59; im[:, 1::2] += 59; z[:, 1::2] += 59
    r = np.arange(16)[:, None]; x[:, 2] = (r + np.arange(W)) % 3; z[:, 2, :, 0] = (r + np.arange(L)) % 3; im[:, 2] = 0
    same = ((4, 0, [15]), (6, L // 2, [2, 15]), (7, L - 1, [15])); cz = rng.integers(0, W, (N, 8))
    for a in range(N):
        for g, j, ks in same:
            e = 59 * (g % 2) + rng.integers(1, 3, 16); z[a, g, :, 0, j] = e; x[a, g, :, cz[a, g]] = e
    v = first(z, w)
    for a in range(N):
        for j in range(3):
            h = v[a, 2, j]; q[a, 2, :, h] = 0; q[a, 2, 3, h] = 7; q[a, 2, 12, h] = 7
            b[a, 2, 3, h] = 3 * rng.integers(0, W // 3) + (j + 1) % 3; b[a, 2, 12, h] = 3 * rng.integers(0, W // 3) + (j + 2) % 3
        for g, j, ks in same:
            h = v[a, g, j]; im[a, g, :, h] = 0; q[a, g, :, h] = 0; b[a, g, 15, h] = cz[a, g]
            for k in ks: q[a, g, k, h] = 7
    return pack(x, im, b, q, z, w)
def check_inputs(d):
    bad = []
    for k, lo, hi in (("geno", 0, 63), ("immun", 0, 63), ("bank", 0, 8 * W - 1), ("bites", 0, 63), ("wt", 1, 4095)):
        a = np.asarray(d[k]).astype(np.float64)
        if not np.all((a >= lo) & (a <= hi)): bad.append("range of " + k)
        elif np.any(a != np.floor(a)): bad.append("whole numbers of " + k)
    return bad
def beats(a, c):
    return (np.sum(a > c, axis=2) >= 9).astype(np.int64)
def reference(geno, immun, bank, bites, wt):
    X = geno.astype(np.float32).astype(np.int64).reshape(N, 8, 16, W); im = immun.astype(np.float32).astype(np.int64).reshape(N, 8, 16, V)
    bk = bank.astype(np.int64).reshape(N, 8, 16, V); z = bites.astype(np.float32).astype(np.int64).reshape(N, 8, 16, 2, L); w = wt.astype(np.int64).reshape(N, 8, 16, 1)
    todo = [z[:, :, :, 0], np.roll(z[:, :, :, 1], 1, axis=0)]
    A = np.zeros(N, np.int64); row = np.arange(16)[None, None, :, None]; lane = np.arange(L)[None, None, None, :]
    for t in range(T):
        s = todo[t]
        u = np.sum(w * s, axis=2) & 4095; v = ((u * u >> 5) + 37 * u + A[:, None, None]) & (V - 1)
        e = np.take_along_axis(bk, v[:, :, None, :], 3); b = e & (W - 1); q = e // W
        iv = np.take_along_axis(im, v[:, :, None, :], 3)
        c = np.take_along_axis(X, b.reshape(N, 8, 1, 16 * L), 3).reshape(N, 8, 16, 16, L)
        D = np.sum(np.abs(c - s[:, :, :, None, :]), axis=2)
        sick = np.sum(s > iv, axis=2) >= 9
        key = np.where((q >= t + E) & sick[:, :, None, :], D * 16 + 15 - row, -1)
        k1 = np.argmax(key, axis=2); h1 = (np.max(key, axis=2) >= 0).astype(np.int64)
        key = np.where(row == k1[:, :, None, :], -1, key)
        k2 = np.argmax(key, axis=2); h2 = (np.max(key, axis=2) >= 0).astype(np.int64)
        a1 = np.take_along_axis(c, k1[:, :, None, None, :], 3)[:, :, :, 0]; a2 = np.take_along_axis(c, k2[:, :, None, None, :], 3)[:, :, :, 0]
        n0 = h1 * beats(a1, s) + h2 * beats(a2, s); n1 = beats(s, a1) + h2 * beats(a2, a1); n2 = beats(s, a2) + beats(a1, a2)
        o = np.argsort(np.stack([n0 * 4, np.where(h1 == 1, n1 * 4 + 1, 97), np.where(h2 == 1, n2 * 4 + 2, 98)]), axis=0)
        st = np.stack([s, a1, a2]); second = np.where(h1 == 1, o[1], 0)
        f = np.take_along_axis(st, o[0][None, :, :, None, :], 0)[0]; m = np.take_along_axis(st, second[None, :, :, None, :], 0)[0]
        todo.append(np.roll(np.where((u[:, :, None, :] >> (row & 7)) & 1 == 1, f, m), 2, axis=0))
        wake = ((row == k1[:, :, None, :]) & (h1[:, :, None, :] == 1)) | ((row == k2[:, :, None, :]) & (h2[:, :, None, :] == 1))
        q = np.where(wake, 0, q); slot = np.argmin(q * 16 + row, axis=2)
        e = np.where(row == slot[:, :, None, :], S * lane + t + W * (8 + t), b + W * q); iv = np.maximum(iv - 1, f)
        for a in range(N):
            for g in range(8):
                hv, fi = np.unique(v[a, g], return_index=True)
                bk[a, g][:, hv] = e[a, g][:, fi]; im[a, g][:, hv] = iv[a, g][:, fi]
        X[:, :, :, t::S] = s
        A = np.sum(h1 + h2, axis=(1, 2))
    return {"ybank": bk.reshape(N, 128, V).astype(np.float32), "yimm": im.reshape(N, 128, V).astype(np.float32).astype(BF), "ygeno": X.reshape(N, 128, W).astype(np.float32).astype(BF)}

@@ -1,0 +1,667 @@
+from concourse.mybir import dt, AluOpType, AxisListType, ActivationFunctionType
+
+OP = AluOpType
+AF = ActivationFunctionType
+BIG = 1048576.0
+STEPS = 6
+TILES = {
+    "bt": (256, "bfloat16", 1), "geno_s": (4096, "bfloat16", 1), "bk": (1024, "int32", 1), "im0": (1024, "bfloat16", 1),
+    "wti": (1, "int32", 1), "btab": (1280, "float32", 1), "qtab": (1280, "float32", 1), "itab": (1280, "float32", 1),
+    "cb": (256, "bfloat16", 4),
+    "CZ": (6416, "bfloat16", 6), "mx": (4096, "bfloat16", 2),
+    "bki": (1024, "int32", 1), "qki": (1024, "int32", 1),
+    "yb": (1024, "float32", 1), "yi": (1024, "bfloat16", 1),
+    "pI": (8, "int32", 1), "pM": (8, "int32", 1), "pG": (8, "int32", 1), "pf": (32, "float32", 1), "wf": (16, "float32", 1), "wi2": (16, "int32", 1),
+    "ic": (256, "float32", 1), "icg": (128, "float32", 1), "ir": (256, "float32", 1),
+    "I": (128, "bfloat16", 1), "nI": (128, "bfloat16", 1), "IB": (128, "bfloat16", 1), "I16": (128, "bfloat16", 1), "Is": (128, "bfloat16", 1),
+    "row16": (256, "bfloat16", 1), "nD": (128, "bfloat16", 2), "nIt": (128, "bfloat16", 6), "lc": (16, "float32", 1),
+    "Gf": (128, "bfloat16", 1), "Gs": (128, "float32", 1), "SC": (128, "float32", 1), "wSh": (128, "bfloat16", 1), "wSl": (128, "bfloat16", 1),
+    "Gm": (16, "bfloat16", 1), "Gmf": (8, "float32", 1), "G64": (16, "bfloat16", 1), "G32": (16, "bfloat16", 1),
+    "EB": (144, "bfloat16", 1), "wE": (144, "float16", 1), "ww": (32, "float32", 1), "RB": (240, "bfloat16", 1),
+    "C16": (256, "bfloat16", 1), "ones": (128, "bfloat16", 1), "kidx": (256, "int32", 1),
+    "bci": (16, "int32", 1), "bc": (16, "uint16", 1), "lnO": (16, "float32", 1), "lnD": (16, "float32", 1), "LR": (2048, "float16", 1), "Mk": (256, "bfloat16", 1), "m1": (256, "bfloat16", 1), "C48": (48, "float32", 1),
+    "ln32": (32, "float32", 1), "ls32": (32, "float32", 1), "tp32": (32, "float32", 1), "ba32": (32, "float32", 1), "sp32": (32, "float32", 1),
+    "ui": (16, "int32", 2), "u": (16, "int32", 2), "sq": (16, "int32", 2), "sh": (16, "int32", 2), "u37": (16, "int32", 2), "base": (16, "int32", 2),
+    "vb": (16, "int32", 2), "vh": (16, "float16", 2), "bb": (16, "float32", 2), "cs": (16, "float32", 2), "ri": (16, "int32", 2), "fr": (16, "float32", 2),
+    "junk": (256, "bfloat16", 8), "c1": (16, "float32", 2), "c2": (16, "float32", 2),
+    "bti": (256, "int32", 2), "bit": (256, "int32", 2),
+    "vA": (16, "int32", 2), "v": (16, "int32", 2), "vl": (16, "uint16", 2), "dup": (16, "float32", 2), "dv": (16, "float32", 2), "dw": (16, "float32", 2),
+    "wo": (16, "float32", 2), "wl": (16, "uint16", 2),
+    "boff": (256, "uint16", 2), "bg": (256, "float32", 2), "ns": (256, "float32", 1), "qg": (256, "bfloat16", 2), "im1": (256, "float32", 2),
+    "fl": (256, "bfloat16", 2), "gt": (256, "bfloat16", 2), "qks": (128, "float32", 2), "q1": (128, "float32", 2), "q2": (64, "float32", 2), "q3": (32, "float32", 2),
+    "m0": (16, "float32", 2), "n1": (32, "float32", 2), "nsB": (32, "float32", 2), "sk": (16, "float32", 2), "ac": (16, "bfloat16", 2), "A": (8, "float32", 2),
+    "keys": (256, "float32", 2), "h1": (128, "float32", 1), "l1": (128, "float32", 1), "h2": (64, "float32", 1), "mn2": (64, "float32", 1), "ml2": (64, "float32", 1), "l2": (64, "float32", 1),
+    "h3": (32, "float32", 1), "mn3": (32, "float32", 1), "ml3": (32, "float32", 1), "l3": (32, "float32", 1), "mn4": (16, "float32", 1), "ml4": (16, "float32", 1),
+    "HL": (32, "float32", 2), "flg": (32, "float32", 2), "HI": (32, "int32", 2), "HA": (32, "int32", 2), "KM": (32, "float32", 2), "thr": (16, "float32", 2),
+    "kx": (16, "float32", 2), "sm": (16, "float32", 2), "si": (16, "int32", 2), "sl": (16, "int32", 2), "awsl": (512, "bfloat16", 2),
+    "tb": (256, "float32", 1), "t1": (256, "float32", 1), "t2": (256, "float32", 1),
+    "Y": (256, "bfloat16", 2), "mz": (32, "float32", 1), "tm": (32, "float32", 1), "bm": (32, "float32", 1), "of": (32, "float32", 1), "al": (32, "uint16", 2),
+    "SG": (1536, "bfloat16", 1), "TH": (96, "float32", 1), "KK": (48, "float32", 1), "KL": (48, "float32", 1), "mna": (16, "float32", 1), "mxa": (16, "float32", 1), "tta": (16, "float32", 1),
+    "FM": (32, "float32", 1), "FI": (32, "int32", 1), "FA": (32, "int32", 1), "fml": (32, "uint16", 2), "fmb": (512, "bfloat16", 1), "ff": (256, "float32", 1), "tX": (256, "bfloat16", 1),
+}
+BYTES = {"float32": 4, "int32": 4, "bfloat16": 2, "uint16": 2, "float16": 2}
+PLACE = {}
+_size = {d: 0 for d in BYTES}
+for _n, (_w, _d, _c) in TILES.items():
+    _p = (_w + 15) // 16 * 16
+    PLACE[_n] = (_size[_d], _p)
+    _size[_d] += _p * _c
+BUF = {"float32": "bigf", "int32": "bigi", "bfloat16": "bigb", "uint16": "bigu", "float16": "bigh"}
+SCRATCH = {BUF[_d]: ("sbuf", [128, _size[_d]], _d) for _d in BYTES}
+for _k in range(8):
+    SCRATCH["P%d" % _k] = ("psum", [128, 512], "float32")
+LOADS = ["bites", "next", "wt", "bank", "immun", "geno"]
+STORES = ["sg", "sb0", "sb1", "si0", "si1"]
+SEMAPHORES = ["qv", "qs", "qp", "qg", "rl"] + ["arr%d" % t for t in range(1, STEPS)] + ["ld_" + n for n in LOADS] + ["st_" + n for n in STORES]
+
+
+BIAS = {'C48': -8, 'CZ': 2, 'G64': 14, 'Gm': 9, 'Gs': 10, 'I': 20, 'KK': -9, 'LR': -1, 'P1fl': 3, 'P2fl': 8, 'P2ones': -14, 'P3I': -1, 'P4awsl': -1,
+        'P4qtab': 3, 'P6I': 2, 'P6nI': -7, 'SC': 6, 'ac': 12, 'al': -3, 'ba32': -6, 'base': 3, 'bb': 5, 'bci': 17, 'bk': -13, 'btab': 3, 'bti': -4,
+        'c1': 4, 'cs': -12, 'flg': 13, 'geno_s': -27, 'ic': -10, 'im0': 3, 'ir': -2, 'itab': -1, 'keys': 11, 'kidx': -3, 'lnD': -6, 'lnO': 2,
+        'ls32': 7, 'm0': -1, 'm1': 3, 'ml4': -4, 'mn4': -6, 'n1': 11, 'nI': -11, 'ns': 1, 'of': -4, 'outsb1': 1, 'outsi1': 6, 'pG': 3, 'qki': -8,
+        'qtab': -5, 'sh': 1, 'sk': 3, 'sm': -1, 'sp32': 9, 't1': 8, 'thr': -6, 'tp32': -1, 'v': 31, 'vh': 4, 'vl': 19, 'wi2': 1, 'wo': -4, 'wti': -7}
+COST = {"us": 0.00083 * 1.25, "ps": 0.00071 * 1.25, "gather": 1.56, "scatter": 3.8, "wake": 0.08, "link": 4.0}
+LOOK = 0.3
+VG = {t: 512 for t in range(STEPS)}
+
+
+def list_schedule(n, que, cost, succ, need, prio):
+    need = list(need)
+    when = [0.0] * n
+    free, ready, nxt = {}, {}, {}
+    order = []
+    for i in range(n):
+        if need[i] == 0:
+            ready.setdefault(que[i], []).append(i)
+    dirty = set(ready)
+    end = 0.0
+    while len(order) < n:
+        for q in dirty:
+            lst = ready.get(q)
+            if not lst:
+                nxt.pop(q, None)
+                continue
+            f = free.get(q, 0.0)
+            st = max(f, min(when[i] for i in lst))
+            c = -1
+            for i in lst:
+                if when[i] <= st + 1e-9 and (c < 0 or prio[i] > prio[c]):
+                    c = i
+            if cost[c] > LOOK:
+                lim = st + min(LOOK, 0.5 * cost[c])
+                b = c
+                for i in lst:
+                    if when[i] <= lim and prio[i] > prio[b]:
+                        b = i
+                c = b
+            nxt[q] = (max(st, when[c]), c)
+        q = min(nxt, key=lambda x: nxt[x][0])
+        st, c = nxt[q]
+        ready[q].remove(c)
+        order.append(c)
+        free[q] = st + cost[c] if q != "n" else 0.0
+        end = max(end, st + cost[c])
+        dirty = {q}
+        for i, l in succ[c]:
+            need[i] -= 1
+            if st + l > when[i]:
+                when[i] = st + l
+            if need[i] == 0:
+                ready.setdefault(que[i], []).append(i)
+                dirty.add(que[i])
+    return order, end
+
+
+def best_order(n, que, cost, succ, prio, rounds=2):
+    need = [0] * n
+    for j in range(n):
+        for i, l in succ[j]:
+            need[i] += 1
+    back = [[] for _ in range(n)]
+    for j in range(n):
+        for i, l in succ[j]:
+            back[i].append((j, max(0.0, cost[i] + l - cost[j])))
+    bneed = [len(x) for x in succ]
+
+    def starts(order, follow):
+        at, when, free = [0.0] * n, [0.0] * n, {}
+        for i in order:
+            st = when[i]
+            if que[i] != "n":
+                st = max(st, free.get(que[i], 0.0))
+                free[que[i]] = st + cost[i]
+            at[i] = st
+            for k, l in follow[i]:
+                if st + l > when[k]:
+                    when[k] = st + l
+        return at
+    best = None
+    for k in range(rounds):
+        order, end = list_schedule(n, que, cost, succ, need, prio)
+        if best is None or end < best[1]:
+            best = (order, end)
+        if k + 1 < rounds:
+            at = starts(order, succ)
+            rev = list_schedule(n, que, cost, back, bneed, [at[i] + cost[i] for i in range(n)])[0]
+            at = starts(rev, back)
+            prio = [at[i] + cost[i] for i in range(n)]
+    return best
+
+
+def rank_program(g, core, T, topo):
+    rank = T.rank_of(core)
+    if rank is None:
+        return
+    n_ranks = len(T.cores)
+    ops = []
+    last = {}
+    edges = []
+    US, PS = COST["us"], COST["ps"]
+
+    def t_(name, a=0, b=None, c=0, step=1):
+        w, d, copies = TILES[name]
+        if b is None:
+            b = w
+        off, p = PLACE[name]
+        off += p * (c % copies)
+        ap = T[BUF[d]][:, off + a:off + b:step] if step != 1 else T[BUF[d]][:, off + a:off + b]
+        return {"ap": ap, "rg": [(BUF[d], off + a, off + b)], "n": (b - a + step - 1) // step, "by": BYTES[d], "ps": False, "ind": False}
+
+    def p_(k, a, b, step=1, grp=None):
+        ap = T["P%d" % k][:, a:b:step] if step != 1 else T["P%d" % k][:, a:b]
+        return {"ap": ap, "rg": [("P%d" % k, 0, 512)], "n": (b - a + step - 1) // step, "by": 4, "ps": True, "ind": False, "grp": grp}
+
+    def ind(win, off):
+        return {"ap": win["ap"].indirect(off["ap"]), "rg": win["rg"] + off["rg"], "win": win["rg"], "off": off["rg"], "n": 16 * off["n"], "by": win["by"], "ps": False, "ind": True}
+
+    starts = {d: sorted((PLACE[x][0], x) for x in TILES if TILES[x][1] == d) for d in BUF}
+    dtype_of = {BUF[d]: d for d in BUF}
+
+    def name_of(region):
+        if region[0] not in dtype_of:
+            return region[0]
+        return [x for o, x in starts[dtype_of[region[0]]] if o <= region[1]][-1]
+
+    def add(q, cost, emit, R, W, sem, inc, grp=None, role=None, extra=()):
+        i = len(ops)
+        ed = {}
+        acc = [(r, False) for r in R] + [(r, True) for r in W]
+        for (buf, a, b), wr in acc:
+            ps = buf.startswith("P") and len(buf) == 2
+            for (a2, b2, j, wr2, q2, grp2, role2) in last.get(buf, []):
+                if a2 >= b or b2 <= a or j == i:
+                    continue
+                if ps:
+                    if q2 == q:
+                        if q == "p" and not (grp is not None and grp == grp2 and role == "mid" and role2 == "mid"):
+                            ed.setdefault(j, 0)
+                    else:
+                        ed[j] = 1
+                elif wr or wr2:
+                    ed[j] = 1
+        for j in extra:
+            ed[j] = 1
+        for (buf, a, b), wr in acc:
+            ps = buf.startswith("P") and len(buf) == 2
+            lst = last.setdefault(buf, [])
+            if wr and not ps:
+                lst[:] = [x for x in lst if not (x[0] >= a and x[1] <= b and x[2] != i)]
+            lst.append((a, b, i, wr, q, grp, role))
+            if ps and len(lst) > 200:
+                del lst[:80]
+        tag = name_of(W[0]) if W else q
+        if tag[0] == "P" and R:
+            tag += name_of(R[0])
+        ops.append({"q": q, "cost": cost, "emit": emit, "sem": sem, "inc": inc, "tag": tag})
+        edges.append(ed)
+        return i
+
+    def rgs(*xs):
+        out = []
+        for x in xs:
+            if isinstance(x, dict):
+                out += x["rg"]
+        return out
+
+    def raw(x):
+        return x["ap"] if isinstance(x, dict) else x
+
+    def vcost(n, mode, xs):
+        if any(x["ind"] for x in xs[1:]):
+            return 0.05 + n * COST["gather"] * US
+        if xs[0]["ind"]:
+            return 0.05 + n * COST["scatter"] * US
+        if mode == "tt":
+            c = n * (1 if any(x["ps"] for x in xs) else 2)
+        else:
+            c = n * (0.5 if all(x["by"] == 2 for x in xs) else 1)
+        return max(64, c) * US
+
+    def outrg(out):
+        return (out["off"], out["win"]) if out["ind"] else ([], out["rg"])
+
+    def tt(out, a, b, op):
+        r, w = outrg(out)
+        n = out["n"]
+        return add("v", vcost(n, "tt", [out, a, b]), lambda: g.vector.tensor_tensor(raw(out), raw(a), raw(b), op), rgs(a, b) + r, w, "qv", 1)
+
+    def ts(out, a, s1, s2, o1, o2=None):
+        r, w = outrg(out)
+        f = (lambda: g.vector.tensor_scalar(raw(out), raw(a), raw(s1), raw(s2), o1)) if o2 is None else (lambda: g.vector.tensor_scalar(raw(out), raw(a), raw(s1), raw(s2), o1, o2))
+        return add("v", vcost(out["n"], "ts", [out, a]), f, rgs(a, s1, s2) + r, w, "qv", 1)
+
+    def cp(out, a):
+        r, w = outrg(out)
+        return add("v", vcost(out["n"], "ts", [out, a]), lambda: g.vector.tensor_copy(raw(out), raw(a)), rgs(a) + r, w, "qv", 1)
+
+    def ms(out, val):
+        return add("v", max(64, out["n"]) * US, lambda: g.vector.memset(raw(out), val), [], out["rg"], "qv", 1)
+
+    def red(out, a):
+        return add("v", 64 * US, lambda: g.vector.tensor_reduce(raw(out), raw(a), AxisListType.X, OP.add), rgs(a), out["rg"], "qv", 1)
+
+    def act(out, a, fn, bias=0.0, scale=1.0, acc=None):
+        c = 0.065 + a["n"] * COST["gather"] * US if a["ind"] else max(64, a["n"]) * US
+        w = out["rg"] + (acc["rg"] if acc else [])
+        if acc:
+            c += 0.02
+            f = lambda: g.scalar.activation(raw(out), raw(a), fn, bias=raw(bias), scale=scale, accum_out=raw(acc))
+        elif isinstance(bias, float) and bias == 0.0:
+            f = (lambda: g.scalar.activation(raw(out), raw(a), fn, scale=raw(scale))) if scale != 1.0 else (lambda: g.scalar.activation(raw(out), raw(a), fn))
+        else:
+            f = lambda: g.scalar.activation(raw(out), raw(a), fn, bias=raw(bias), scale=scale)
+        return add("s", c, f, rgs(a, bias, scale), w, "qs", 1)
+
+    def mm(out, lhsT, rhs, start, stop, grp=None, role=None, f32=False):
+        c = max(64, rhs["n"]) * PS * (4 if f32 else 1)
+        return add("p", c, lambda: g.tensor.matmul(raw(out), raw(lhsT), raw(rhs), start, stop), rgs(lhsT, rhs), out["rg"], "qp", 1, grp=grp, role=role)
+
+    def iota(out, pattern, base=0, cm=0):
+        small = out["flt"] if "flt" in out else False
+        def f():
+            if small:
+                return g.iota(raw(out), pattern, base, cm, allow_small_or_imprecise_dtypes=True)
+            return g.iota(raw(out), pattern, base, cm)
+        return add("g", 0.13 + 2 * out["n"] * US, f, [], out["rg"], "qg", 1)
+
+    def keep(out, a):
+        return add("g", 0.17 + 2 * out["n"] * US, lambda: g.affine_select(raw(out), raw(a), [[0, out["n"]]], OP.is_ge, 0.0, 0, 0), rgs(a), out["rg"], "qg", 1)
+
+    def flt(x):
+        x["flt"] = True
+        return x
+
+    def load(name, out, q="y"):
+        eng = g.sync if q == "y" else g.scalar
+        src = T.bites[:, 0:256] if name == "bites" else T.bites[:, 256:512] if name == "next" else T[name][:]
+        return add(q, 0.1, lambda: eng.dma_start(raw(out), src), [], out["rg"], "ld_" + name, 16)
+
+    def store(tag, dst, src, q="y"):
+        eng = g.sync if q == "y" else g.scalar
+        return add(q, 0.1, lambda: eng.dma_start(dst, raw(src)), src["rg"], [("out" + tag, 0, 1)], "st_" + tag, 16)
+
+    lag = {}
+
+    for name, dst, tm in (("bites", t_("CZ", 4112, 4368, 0), 2.6), ("wt", t_("wti"), 2.5), ("bank", t_("bk"), 4.5), ("immun", t_("im0"), 5.0), ("next", t_("bt"), 4.0), ("geno", t_("geno_s"), 7.0)):
+        i = load(name, dst, "s" if name in ("wt", "immun", "next") else "y")
+        lag[i] = tm
+
+    def send(src, t, dst_rank):
+        dst = T.cores[dst_rank]
+        rid, pid, _se = topo.addr(dst)
+        m = topo.mask(core, dst)
+        eng = len(topo.engines(core, dst))
+        out = t_("CZ", 4112, 4368, t)
+        def f():
+            return g.remote_dma(raw(out), raw(src), T.sem["arr%d" % t], T.sem.rl, pid, rid, m)
+        i = add("g", 0.3, f, src["rg"], [], None, 0)
+        ops[i]["remote"] = eng
+        lag[i] = 0.3
+        j = add("n", 0.0, None, [], out["rg"], "arr%d" % t, eng)
+        ops[j]["proxy"] = i
+        lag[j] = 0.0
+        return i
+
+    iota(t_("pI", 0, 1), [[0, 1]], 0, 1)
+    iota(flt(t_("ic", 0, 128)), [[1, 128]])
+    iota(flt(t_("icg")), [[1, 8], [0, 16]])
+    iota(flt(t_("ir")), [[0, 16], [1, 16]])
+    iota(t_("bci"), [[1, 16]])
+    iota(t_("kidx"), [[0, 16], [1, 16]])
+    iota(flt(t_("lnO")), [[16, 16]])
+    iota(flt(t_("ln32")), [[16, 8], [0, 2], [128, 2]])
+    iota(flt(t_("ls32")), [[0, 8], [1, 2], [0, 2]])
+    send(t_("bt"), 1, (rank + 1) % n_ranks)
+    ts(t_("pM", 0, 1), t_("pI", 0, 1), 15, None, OP.bitwise_and)
+    ts(t_("pG", 0, 1), t_("pI", 0, 1), 4, None, OP.arith_shift_right)
+    P, PM, PG = t_("pf", 0, 1), t_("pf", 8, 9), t_("pf", 16, 17)
+    cp(P, t_("pI", 0, 1))
+    cp(PM, t_("pM", 0, 1))
+    cp(PG, t_("pG", 0, 1))
+    ts(t_("Gmf"), t_("ic", 0, 8), PG, None, OP.is_equal)
+    ms(t_("EB"), 0.0)
+    cp(t_("EB", 15, 128, step=16), t_("Gmf"))
+    ts(t_("wi2", 0, 1), t_("wti"), 4032, None, OP.bitwise_and)
+    ts(t_("wi2", 8, 9), t_("wti"), 63, None, OP.bitwise_and)
+    WH, WL = t_("wf", 0, 1), t_("wf", 8, 9)
+    cp(WH, t_("wi2", 0, 1))
+    cp(WL, t_("wi2", 8, 9))
+    WF, WG, WS = t_("ww", 0, 1), t_("ww", 8, 9), t_("ww", 16, 17)
+    cp(WF, t_("wti"))
+    ts(WG, WF, 2047.5, -4096.0, OP.is_gt, OP.mult)
+    tt(WS, WF, WG, OP.add)
+    ts(t_("wE"), t_("EB"), WS, None, OP.mult)
+    ts(t_("lnO"), t_("lnO"), PM, None, OP.add)
+    ts(t_("lnD"), t_("lnO"), 1024.0, None, OP.add)
+    cp(t_("bc"), t_("bci"))
+    ts(t_("Gf"), t_("icg"), PG, None, OP.is_equal)
+    ts(t_("I"), t_("ic", 0, 128), P, None, OP.is_equal)
+    ts(t_("bki"), t_("bk"), 4095, None, OP.bitwise_and)
+    cp(t_("btab", 0, 1024), t_("bki"))
+    ts(t_("qki"), t_("bk"), 12, None, OP.arith_shift_right)
+    cp(t_("qtab", 0, 1024), t_("qki"))
+    act(t_("itab", 0, 1024), t_("im0"), AF.Copy)
+    cp(t_("Gm", 0, 8), t_("Gmf"))
+    ts(t_("G64", 0, 8), t_("Gmf"), 1024.0, None, OP.mult)
+    ts(t_("G32", 0, 8), t_("Gmf"), -512.0, None, OP.mult)
+    ts(t_("nI"), t_("I"), -1.0, None, OP.mult)
+    ts(t_("IB"), t_("I"), BIG, None, OP.mult)
+    ts(t_("I16"), t_("I"), -16.0, None, OP.mult)
+    ts(t_("Is"), t_("I"), 1.0 / 128, None, OP.mult)
+    ts(t_("C16"), t_("ir"), -1.0, 256.0, OP.mult, OP.add)
+    ms(t_("ones"), 1.0)
+    ms(t_("RB"), 0.0)
+    ts(t_("RB", 112, 128), t_("ir", 0, 16), PM, None, OP.is_equal)
+    for r in range(16):
+        ts(t_("LR", 128 * r, 128 * r + 128), t_("Gf"), t_("RB", 112 + r, 113 + r), None, OP.mult)
+    iota(flt(t_("row16")), [[16, 256]])
+    for h in range(2):
+        ts(t_("lc", 8 * h, 8 * h + 1), P, -16.0, -2048.0 * h, OP.mult, OP.add)
+        ts(t_("nD", c=h), t_("I"), t_("lc", 8 * h, 8 * h + 1), None, OP.mult)
+    for t in range(1, STEPS):
+        ts(t_("nIt", c=t), t_("I"), float(-t), None, OP.mult)
+    ts(t_("Mk"), t_("ir"), PM, 2048.0, OP.is_ge, OP.mult)
+    for c in range(2):
+        ms(t_("c1", 0, 1, c), 0.0)
+    ms(t_("m1"), -1.0)
+    for c in range(STEPS):
+        ms(t_("CZ", 4096, 4112, c), 0.0)
+    for s in range(8):
+        ms(t_("SC", s, 128, step=8), float(1 << (7 - s)))
+    tt(t_("Gs"), t_("Gf"), t_("SC"), OP.mult)
+    ts(t_("wSh"), t_("Gs"), WH, None, OP.mult)
+    ts(t_("wSl"), t_("Gs"), WL, None, OP.mult)
+    ts(t_("ln32"), t_("ln32"), PM, None, OP.add)
+    ts(t_("ba32"), t_("ln32"), 16.0, 256.0, OP.mult, OP.add)
+    ts(t_("tp32"), t_("ln32"), 16.0, None, OP.add)
+    tt(t_("tp32"), t_("tp32"), t_("ls32"), OP.mult)
+    ts(t_("sp32"), t_("ln32"), -15.0, 3856.0, OP.mult, OP.add)
+    tt(t_("sp32"), t_("sp32"), t_("tp32"), OP.subtract)
+    for k in range(3):
+        ts(t_("C48", 16 * k, 16 * k + 16), t_("lnO"), 256.0 * k, None, OP.add)
+
+    def zt(t, a=0, b=256, step=1):
+        return t_("CZ", 4112 + a, 4112 + b, t, step)
+
+    def early(t):
+        z = zt(t)
+        for r in range(16):
+            mm(p_(2, 320, 336), t_("wE", 15 - r, 143 - r), zt(t, r, 256, 16), r == 0, r == 15)
+        cp(t_("ui", c=t), p_(2, 320, 336))
+        ts(t_("u", c=t), t_("ui", c=t), 4095, None, OP.bitwise_and)
+        tt(t_("sq", c=t), t_("u", c=t), t_("u", c=t), OP.mult)
+        ts(t_("u37", c=t), t_("u", c=t), 37.0, None, OP.mult)
+        ts(t_("sh", c=t), t_("sq", c=t), 5, None, OP.arith_shift_right)
+        tt(t_("base", c=t), t_("sh", c=t), t_("u37", c=t), OP.add)
+        ts(t_("vb", c=t), t_("base", c=t), 1023, None, OP.bitwise_and)
+        cp(t_("vh", c=t), t_("vb", c=t))
+        for b in (256, 0):
+            if b == 0:
+                mm(p_(3, 0, 256), t_("I"), t_("Mk"), True, False)
+            for r in range(16):
+                mm(p_(3, b + r, b + 256, 16), t_("LR", 128 * r, 128 * r + 128), t_("vh", c=t), b == 256, b == 256 or r == 15)
+        ts(t_("bb", c=t), t_("vb", c=t), -32.0, -5.7, OP.mult, OP.add)
+        for j in range(15, -1, -1):
+            if j:
+                act(t_("junk", 0, 16 * j, 2 * j), p_(3, 256, 256 + 16 * j), AF.Sigmoid, bias=t_("bb", j, j + 1, t), scale=32.0, acc=t_("c1", j, j + 1, t))
+            act(t_("junk", 0, 16, 2 * j + 1), p_(3, 16 * j, 16 * j + 16), AF.Sigmoid, bias=t_("bb", j, j + 1, t), scale=32.0, acc=t_("c2", j, j + 1, t))
+        tt(t_("cs", c=t), t_("c1", c=t), t_("c2", c=t), OP.add)
+        ts(t_("ri", c=t), t_("cs", c=t), -0.45, None, OP.add)
+        tt(t_("fr", c=t), t_("cs", c=t), t_("ri", c=t), OP.subtract)
+        ts(t_("dup", c=t), t_("fr", c=t), 0.0017, None, OP.is_gt)
+
+    def step(t):
+        if t == 0:
+            early(0)
+        z = zt(t)
+        mm(p_(0, 0, 256), t_("I"), z, True, True)
+        mm(p_(0, 256, 512), t_("I"), z, True, False)
+        mm(p_(0, 256, 512), t_("I"), t_("m1"), False, True)
+        if t:
+            ts(t_("vA", c=t), t_("base", c=t), t_("A", 0, 1, t - 1), None, OP.add)
+            ts(t_("v", c=t), t_("vA", c=t), 1023, None, OP.bitwise_and)
+        else:
+            ts(t_("v", c=t), t_("base", c=t), 1023, None, OP.bitwise_and)
+        cp(t_("vl", c=t), t_("v", c=t))
+        vl, wl = t_("vl", c=t), t_("wl", c=t)
+        cp(t_("boff", c=t), ind(t_("btab" if t else "bki", 0, 1024), vl))
+        tt(t_("dv", c=t), t_("lnD"), t_("v", c=t), OP.subtract)
+        tt(t_("dw", c=t), t_("dv", c=t), t_("dup", c=t), OP.mult)
+        tt(t_("wo", c=t), t_("v", c=t), t_("dw", c=t), OP.add)
+        cp(wl, t_("wo", c=t))
+        for c in range(4):
+            e = VG.get(t, 0) // 16 if c == 3 else 0
+            act(t_("CZ", 1024 * c, 1024 * c + 1024 - 16 * e, t), ind(t_("geno_s"), t_("boff", 64 * c, 64 * c + 64 - e, t)), AF.Copy)
+            if e:
+                cp(t_("CZ", 4096 - 16 * e, 4096, t), ind(t_("geno_s"), t_("boff", 256 - e, 256, t)))
+        keep(t_("geno_s", t, 4096, step=16), z)
+        if t == STEPS - 1:
+            store("sg", T.ygeno[:], t_("geno_s"))
+        act(t_("bg", c=t), ind(t_("btab", 0, 1024), vl), AF.Copy)
+        act(t_("qg", c=t), ind(t_("qtab", 0, 1024), vl), AF.Copy)
+        act(t_("im1", c=t), ind(t_("itab", 0, 1024), vl), AF.Identity, bias=-1.0)
+        act(t_("fl", c=t), t_("qg", c=t), AF.Sigmoid, bias=-200.0 * t - 100.0, scale=200.0)
+        tt(t_("gt", c=t), t_("im1", c=t), p_(0, 256, 512), OP.is_lt)
+        gk = ("key", t)
+        mm(p_(1, 0, 256), t_("I"), t_("C16"), True, False, gk, "first")
+        mm(p_(2, 0, 256), t_("I"), t_("C16"), True, False)
+        for h in range(2):
+            mm(p_(2, 128 * h, 128 * h + 128), t_("qg", 128 * h, 128 * h + 128, t), t_("I16"), False, h == 1)
+        for h in range(2):
+            mm(p_(2, 256 + 8 * h, 264 + 8 * h), t_("fl", 128 * h, 128 * h + 128, t), t_("Gm", 0, 8), True, True)
+        for h in range(4):
+            mm(p_(2, 272 + 8 * h, 280 + 8 * h), t_("gt", 128 * (h % 2), 128 * (h % 2) + 128, t), t_("Gm", 0, 8), True, True)
+        act(t_("qks", c=t), p_(2, 1, 256, 2), AF.Copy)
+        ts(t_("n1", c=t), p_(2, 272, 304), 9.0, 4194304.0, OP.is_lt, OP.mult)
+        ts(t_("nsB", c=t), t_("n1", c=t), BIG, None, OP.max)
+        if t + 1 < STEPS:
+            ts(t_("sk", c=t), p_(2, 272, 288), 9.0, 2.0, OP.is_ge, OP.mult)
+            tt(t_("ac", c=t), t_("sk", c=t), p_(2, 256, 272), OP.min)
+            mm(p_(2, 304, 320), t_("ones"), t_("ac", c=t), True, True)
+            red(t_("A", 0, 1, t), p_(2, 304, 320))
+        tt(t_("q1", c=t), p_(2, 0, 256, 2), t_("qks", c=t), OP.max)
+        tt(t_("q2", c=t), t_("q1", 0, 128, t, 2), t_("q1", 1, 128, t, 2), OP.max)
+        tt(t_("q3", c=t), t_("q2", 0, 64, t, 2), t_("q2", 1, 64, t, 2), OP.max)
+        tt(t_("m0", c=t), t_("q3", 0, 32, t, 2), t_("q3", 1, 32, t, 2), OP.max)
+        if t + 1 < STEPS:
+            early(t + 1)
+        for h in range(2):
+            mm(p_(1, 128 * h, 128 * h + 128), t_("fl", 128 * h, 128 * h + 128, t), t_("IB"), False, False, gk, "mid")
+            for k in range(16):
+                mm(p_(1, 128 * h + k, 128 * h + 128, 16), t_("CZ", 2048 * h + k, 2048 * h + 2048, t, 16), t_("G32", 0, 8), False, False, gk, "mid")
+            for k in range(16):
+                if h == 0:
+                    tt(t_("mx", 128 * k, 128 * k + 128, t), t_("CZ", k, 2048, t, 16), p_(0, 0, 128), OP.max)
+                else:
+                    for e in range(2):
+                        o = 2048 + 128 * k + 64 * e
+                        tt(t_("mx", o, o + 64, t), t_("CZ", 2048 + 1024 * e + k, 3072 + 1024 * e, t, 16), p_(0, 128 + 64 * e, 192 + 64 * e), OP.max)
+            for k in range(16):
+                o = 2048 * h + 128 * k
+                end = h == 1 and k == 15
+                mm(p_(1, 128 * h + k, 128 * h + 128, 16), t_("mx", o, o + 128, t), t_("G64", 0, 8), False, end, gk, "last" if end else "mid")
+        act(t_("keys", c=t), p_(1, 0, 256), AF.Copy)
+        ko = t_("keys", 1, 256, t, 2)
+        tt(t_("h1"), p_(1, 0, 256, 2), ko, OP.max)
+        tt(t_("l1"), p_(1, 0, 256, 2), ko, OP.min)
+        for a, b, n in (("1", "2", 128), ("2", "3", 64), ("3", "4", 32)):
+            he, ho, le, lo = t_("h" + a, 0, n, step=2), t_("h" + a, 1, n, step=2), t_("l" + a, 0, n, step=2), t_("l" + a, 1, n, step=2)
+            tt(t_("HL", 0, 16, t) if b == "4" else t_("h" + b), he, ho, OP.max)
+            tt(t_("mn" + b), he, ho, OP.min)
+            tt(t_("ml" + b), le, lo, OP.max)
+            tt(t_("HL", 16, 32, t) if b == "4" else t_("l" + b), t_("mn" + b), t_("ml" + b), OP.max)
+        HL = t_("HL", c=t)
+        cp(t_("HI", c=t), HL)
+        tt(t_("flg", c=t), HL, t_("nsB", c=t), OP.is_ge)
+        ts(t_("HA", c=t), t_("HI", c=t), 511, None, OP.bitwise_and)
+        tt(t_("thr", c=t), t_("HL", 16, 32, t), t_("nsB", 0, 16, t), OP.max)
+        tt(t_("KM", c=t), t_("HA", c=t), t_("flg", c=t), OP.mult)
+        tt(t_("kx", c=t), t_("KM", 0, 16, t), t_("KM", 16, 32, t), OP.max)
+        tt(t_("sm", c=t), t_("kx", c=t), t_("m0", c=t), OP.max)
+        ts(t_("si", c=t), t_("sm", c=t), -1.0, 256.0, OP.mult, OP.add)
+        ts(t_("sl", c=t), t_("si", c=t), 15, None, OP.bitwise_and)
+        tt(t_("awsl", 256, 512, t), ind(t_("sl", c=t), t_("bc")), t_("kidx"), OP.not_equal)
+        tt(t_("awsl", 0, 256, t), ind(t_("thr", c=t), t_("bc")), t_("keys", c=t), OP.is_gt)
+        for x in (2, 3, 0, 1):
+            mm(p_(4, 128 * x, 128 * x + 128), t_("awsl", 128 * x, 128 * x + 128, t), t_("I"), True, True)
+        mm(p_(1, 256, 512), t_("I"), t_("row16"), True, False)
+        for h in range(2):
+            w = t_("awsl", 256 + 128 * h, 384 + 128 * h, t)
+            if t:
+                mm(p_(1, 256 + 128 * h, 384 + 128 * h), w, t_("nIt", c=t), False, False)
+            mm(p_(1, 256 + 128 * h, 384 + 128 * h), w, t_("nD", c=h), False, h == 1)
+        act(t_("ns"), p_(1, 256, 512), AF.Identity, bias=float(t))
+        tt(t_("tb"), p_(4, 256, 512), t_("bg", c=t), OP.mult)
+        tt(ind(t_("btab"), wl), t_("tb"), t_("ns"), OP.add)
+        tt(t_("t1"), p_(4, 0, 256), t_("qg", c=t), OP.mult)
+        act(t_("t2"), p_(4, 256, 512), AF.Identity, bias=float(8 + t), scale=-float(8 + t))
+        tt(ind(t_("qtab"), wl), t_("t1"), t_("t2"), OP.max)
+        for j in range(8):
+            act(t_("Y", 32 * j, 32 * j + 32, t), t_("KM", c=t), AF.Copy, scale=t_("Gmf", j, j + 1))
+        for k in range(8):
+            mm(p_(5, 0, 32), t_("RB", 112 - 16 * k, 240 - 16 * k), t_("Y", k, 256, t, 8), k == 0, k == 7)
+        ts(t_("mz"), p_(5, 0, 32), 0.0, None, OP.is_equal)
+        tt(t_("bm"), t_("ba32"), p_(5, 0, 32), OP.subtract)
+        tt(t_("tm"), t_("mz"), t_("sp32"), OP.mult)
+        tt(t_("of"), t_("tm"), t_("bm"), OP.add)
+        for x in range(4):
+            cp(t_("al", 8 * x, 8 * x + 8, t), t_("of", x, 32, 0, 4))
+        act(t_("CZ", 4368, 4880, t), ind(t_("CZ", 0, 4368, t), t_("al", c=t)), AF.Copy)
+        a12, a1, a2 = t_("CZ", 4368, 4880, t), t_("CZ", 4368, 4624, t), t_("CZ", 4624, 4880, t)
+        for k in (768, 1536):
+            keep(t_("CZ", 4112 + k, 4368 + k, t), z)
+            keep(t_("CZ", 4368 + k, 4880 + k, t), a12)
+        mm(p_(6, 0, 512), t_("nI"), a12, True, False)
+        mm(p_(6, 0, 256), t_("I"), z, False, False)
+        mm(p_(6, 256, 512), t_("I"), z, False, True)
+        mm(p_(7, 0, 256), t_("I"), a1, True, False)
+        mm(p_(7, 0, 256), t_("nI"), a2, False, True)
+        act(t_("SG", 0, 512), p_(6, 0, 512), AF.Sign, bias=-0.5, scale=-1.0)
+        act(t_("SG", 512, 1024), p_(6, 0, 512), AF.Sign, bias=-0.5)
+        if t + 1 < STEPS:
+            act(t_("SG", 1024, 1280), p_(7, 0, 256), AF.Sign, bias=-0.5, scale=-1.0)
+            act(t_("SG", 1280, 1536), p_(7, 0, 256), AF.Sign, bias=-0.5)
+        else:
+            ts(t_("SG", 1024, 1280), p_(7, 0, 256), 0.0, -0.5, OP.is_lt, OP.add)
+            ts(t_("SG", 1280, 1536), p_(7, 0, 256), 0.0, -0.5, OP.is_gt, OP.add)
+        for r in range(16):
+            mm(p_(5, 64, 160), t_("EB", 15 - r, 143 - r), t_("SG", r, 1536, 0, 16), r == 0, r == 15)
+        ts(t_("TH"), p_(5, 64, 160), 1.0, 768.0, OP.is_ge, OP.mult)
+        tt(t_("KK", 0, 16), t_("TH", 0, 16), t_("TH", 16, 32), OP.add)
+        tt(t_("KK", 16, 48), t_("TH", 32, 64), t_("TH", 64, 96), OP.add)
+        tt(t_("KL"), t_("KK"), t_("C48"), OP.add)
+        k0, k1, k2 = t_("KL", 0, 16), t_("KL", 16, 32), t_("KL", 32, 48)
+        tt(t_("mna"), k0, k1, OP.min)
+        tt(t_("mxa"), k0, k1, OP.max)
+        tt(t_("FM", 0, 16), t_("mna"), k2, OP.min)
+        tt(t_("tta"), t_("mxa"), k2, OP.min)
+        tt(t_("FM", 16, 32), t_("mna"), t_("tta"), OP.max)
+        cp(t_("fml", c=t), t_("FM"))
+        win = t_("CZ", 4112, 6416, t)
+        if t + 2 < STEPS:
+            f, m = t_("fmb", 0, 256), t_("fmb", 256, 512)
+            act(t_("fmb"), ind(win, t_("fml", c=t)), AF.Copy)
+            act(t_("ff"), f, AF.Copy)
+            mm(p_(6, 0, 256), t_("I"), f, True, False)
+            mm(p_(6, 0, 256), t_("nI"), m, False, True)
+            mm(p_(7, 256, 512), t_("wSh"), z, True, False)
+            mm(p_(7, 256, 512), t_("wSl"), z, False, True)
+            cp(t_("bti", c=t), p_(7, 256, 512))
+            ts(t_("bit", c=t), t_("bti", c=t), 128, None, OP.bitwise_and)
+            tt(t_("tX"), p_(6, 0, 256), t_("bit", c=t), OP.mult)
+            mm(p_(6, 256, 512), t_("I"), m, True, False)
+            mm(p_(6, 256, 512), t_("Is"), t_("tX"), False, True)
+            act(t_("cb", c=t), p_(6, 256, 512), AF.Copy)
+            send(t_("cb", c=t), t + 2, (rank + 2) % n_ranks)
+        else:
+            act(t_("ff"), ind(win, t_("fml", 0, 16, t)), AF.Copy)
+        tt(ind(t_("itab"), wl), t_("im1", c=t), t_("ff"), OP.max)
+
+    for t in range(STEPS):
+        step(t)
+    act(t_("yi", 0, 512), t_("itab", 0, 512), AF.Copy)
+    cp(t_("yi", 512, 1024), t_("itab", 512, 1024))
+    for k in range(2):
+        store("si%d" % k, T.yimm[:, 512 * k:512 * k + 512], t_("yi", 512 * k, 512 * k + 512))
+    for k, b in ((0, 4), (1, 1)):
+        act(p_(b, 0, 512), t_("qtab", 512 * k, 512 * k + 512), AF.Copy, scale=4096.0)
+        tt(t_("yb", 512 * k, 512 * k + 512), t_("btab", 512 * k, 512 * k + 512), p_(b, 0, 512), OP.add)
+        store("sb%d" % k, T.ybank[:, 512 * k:512 * k + 512], t_("yb", 512 * k, 512 * k + 512))
+
+    n = len(ops)
+    for i in range(n):
+        if "proxy" in ops[i]:
+            edges[i][ops[i]["proxy"]] = 0
+    succ = [[] for _ in range(n)]
+    for i in range(n):
+        for j, w in edges[i].items():
+            l = lag.get(j, ops[j]["cost"]) + (COST["wake"] if w else 0.0)
+            if "proxy" in ops[i]:
+                l = COST["link"]
+            succ[j].append((i, l))
+    prio = [0.0] * n
+    for j in range(n - 1, -1, -1):
+        prio[j] = max([lag.get(j, ops[j]["cost"])] + [l + prio[i] for i, l in succ[j]])
+    order = best_order(n, [o["q"] for o in ops], [o["cost"] for o in ops], succ, [prio[i] + BIAS.get(ops[i]["tag"], 0.0) for i in range(n)], 3)[0]
+
+    eng = {"v": g.vector, "s": g.scalar, "p": g.tensor, "g": g, "y": g.sync}
+    total = {}
+    at = [None] * n
+    know = {q: {} for q in eng}
+    snap = [None] * n
+    for i in order:
+        o = ops[i]
+        q = o["q"]
+        if q == "n":
+            at[i] = (o["sem"], o["inc"])
+            snap[i] = {o["sem"]: o["inc"]}
+            total[o["sem"]] = o["inc"]
+            continue
+        k = know[q]
+        want = {}
+        for j, w in edges[i].items():
+            if w and at[j] is not None:
+                s, v = at[j]
+                if k.get(s, 0) < v and want.get(s, (0, 0))[0] < v:
+                    want[s] = (v, j)
+        for s in list(want):
+            v, j = want[s]
+            if any(s2 != s and snap[j2].get(s, 0) >= v for s2, (v2, j2) in want.items()):
+                del want[s]
+        for s, (v, j) in want.items():
+            eng[q].wait_ge(T.sem[s], v)
+            for s2, v2 in snap[j].items():
+                if k.get(s2, 0) < v2:
+                    k[s2] = v2
+        ins = o["emit"]()
+        if o["sem"] is not None:
+            total[o["sem"]] = total.get(o["sem"], 0) + o["inc"]
+            ins.then_inc(T.sem[o["sem"]], o["inc"])
+            at[i] = (o["sem"], total[o["sem"]])
+            snap[i] = dict(k)
+            snap[i][o["sem"]] = total[o["sem"]]
+        if "remote" in o:
+            total["rl"] = total.get("rl", 0) + o["remote"]
+    for s in sorted(total):
+        if know["g"].get(s, 0) < total[s]:
+            g.wait_ge(T.sem[s], total[s])

@@ -1,43 +1,39 @@
+import math
 from concourse.mybir import dt, AluOpType, AxisListType, ActivationFunctionType
+from concourse.bass import DstId, RemoteDMATransfer
 
 OP = AluOpType
 AF = ActivationFunctionType
-BIG = 1048576.0
+BIG = 65536.0
+WN, WO = 32768.0, 8192.0
 STEPS = 6
+LOG = 1024 + 256 * STEPS
 TILES = {
-    "bt": (256, "bfloat16", 1), "geno_s": (4096, "bfloat16", 1), "bk": (1024, "int32", 1), "im0": (1024, "bfloat16", 1),
-    "wti": (1, "int32", 1), "btab": (1280, "float32", 1), "qtab": (1280, "float32", 1), "itab": (1280, "float32", 1),
-    "cb": (256, "bfloat16", 4),
-    "CZ": (6416, "bfloat16", 6), "mx": (4096, "bfloat16", 2),
-    "bki": (1024, "int32", 1), "qki": (1024, "int32", 1),
-    "yb": (1024, "float32", 1), "yi": (1024, "bfloat16", 1),
-    "pI": (8, "int32", 1), "pM": (8, "int32", 1), "pG": (8, "int32", 1), "pf": (32, "float32", 1), "wf": (16, "float32", 1), "wi2": (16, "int32", 1),
-    "ic": (256, "float32", 1), "icg": (128, "float32", 1), "ir": (256, "float32", 1),
-    "I": (128, "bfloat16", 1), "nI": (128, "bfloat16", 1), "IB": (128, "bfloat16", 1), "I16": (128, "bfloat16", 1), "Is": (128, "bfloat16", 1),
-    "row16": (256, "bfloat16", 1), "nD": (128, "bfloat16", 2), "nIt": (128, "bfloat16", 6), "lc": (16, "float32", 1),
-    "Gf": (128, "bfloat16", 1), "Gs": (128, "float32", 1), "SC": (128, "float32", 1), "wSh": (128, "bfloat16", 1), "wSl": (128, "bfloat16", 1),
-    "Gm": (16, "bfloat16", 1), "Gmf": (8, "float32", 1), "G64": (16, "bfloat16", 1), "G32": (16, "bfloat16", 1),
-    "EB": (144, "bfloat16", 1), "wE": (144, "float16", 1), "ww": (32, "float32", 1), "RB": (240, "bfloat16", 1),
-    "C16": (256, "bfloat16", 1), "ones": (128, "bfloat16", 1), "kidx": (256, "int32", 1),
-    "bci": (16, "int32", 1), "bc": (16, "uint16", 1), "lnO": (16, "float32", 1), "lnD": (16, "float32", 1), "LR": (2048, "float16", 1), "Mk": (256, "bfloat16", 1), "m1": (256, "bfloat16", 1), "C48": (48, "float32", 1),
-    "ln32": (32, "float32", 1), "ls32": (32, "float32", 1), "tp32": (32, "float32", 1), "ba32": (32, "float32", 1), "sp32": (32, "float32", 1),
-    "ui": (16, "int32", 2), "u": (16, "int32", 2), "sq": (16, "int32", 2), "sh": (16, "int32", 2), "u37": (16, "int32", 2), "base": (16, "int32", 2),
-    "vb": (16, "int32", 2), "vh": (16, "float16", 2), "bb": (16, "float32", 2), "cs": (16, "float32", 2), "ri": (16, "int32", 2), "fr": (16, "float32", 2),
-    "junk": (256, "bfloat16", 8), "c1": (16, "float32", 2), "c2": (16, "float32", 2),
-    "bti": (256, "int32", 2), "bit": (256, "int32", 2),
-    "vA": (16, "int32", 2), "v": (16, "int32", 2), "vl": (16, "uint16", 2), "dup": (16, "float32", 2), "dv": (16, "float32", 2), "dw": (16, "float32", 2),
-    "wo": (16, "float32", 2), "wl": (16, "uint16", 2),
-    "boff": (256, "uint16", 2), "bg": (256, "float32", 2), "ns": (256, "float32", 1), "qg": (256, "bfloat16", 2), "im1": (256, "float32", 2),
-    "fl": (256, "bfloat16", 2), "gt": (256, "bfloat16", 2), "qks": (128, "float32", 2), "q1": (128, "float32", 2), "q2": (64, "float32", 2), "q3": (32, "float32", 2),
-    "m0": (16, "float32", 2), "n1": (32, "float32", 2), "nsB": (32, "float32", 2), "sk": (16, "float32", 2), "ac": (16, "bfloat16", 2), "A": (8, "float32", 2),
-    "keys": (256, "float32", 2), "h1": (128, "float32", 1), "l1": (128, "float32", 1), "h2": (64, "float32", 1), "mn2": (64, "float32", 1), "ml2": (64, "float32", 1), "l2": (64, "float32", 1),
-    "h3": (32, "float32", 1), "mn3": (32, "float32", 1), "ml3": (32, "float32", 1), "l3": (32, "float32", 1), "mn4": (16, "float32", 1), "ml4": (16, "float32", 1),
-    "HL": (32, "float32", 2), "flg": (32, "float32", 2), "HI": (32, "int32", 2), "HA": (32, "int32", 2), "KM": (32, "float32", 2), "thr": (16, "float32", 2),
-    "kx": (16, "float32", 2), "sm": (16, "float32", 2), "si": (16, "int32", 2), "sl": (16, "int32", 2), "awsl": (512, "bfloat16", 2),
-    "tb": (256, "float32", 1), "t1": (256, "float32", 1), "t2": (256, "float32", 1),
-    "Y": (256, "bfloat16", 2), "mz": (32, "float32", 1), "tm": (32, "float32", 1), "bm": (32, "float32", 1), "of": (32, "float32", 1), "al": (32, "uint16", 2),
-    "SG": (1536, "bfloat16", 1), "TH": (96, "float32", 1), "KK": (48, "float32", 1), "KL": (48, "float32", 1), "mna": (16, "float32", 1), "mxa": (16, "float32", 1), "tta": (16, "float32", 1),
-    "FM": (32, "float32", 1), "FI": (32, "int32", 1), "FA": (32, "int32", 1), "fml": (32, "uint16", 2), "fmb": (512, "bfloat16", 1), "ff": (256, "float32", 1), "tX": (256, "bfloat16", 1),
+    "z": (256, "bfloat16", 6), "bt": (256, "bfloat16", 1), "geno_s": (4096, "bfloat16", 1), "bk": (1024, "int32", 1), "wti": (1, "int32", 1),
+    "blog": (LOG, "float32", 1), "qlog": (LOG, "bfloat16", 1), "ilog": (LOG, "bfloat16", 1), "ptab": (1040, "float32", 1), "psrc": (256, "float32", 5),
+    "EW": (144, "bfloat16", 1), "ptb": (1040, "bfloat16", 1), "psb": (256, "bfloat16", 1), "hb": (16, "float32", 2), "rn": (48, "float32", 1), "thr": (48, "float32", 1), "dd": (48, "float32", 1),
+    "W": (8192, "bfloat16", 2), "bki": (1024, "int32", 1), "q192": (1024, "bfloat16", 1),
+    "X2": (4112, "bfloat16", 1), "T1": (289, "bfloat16", 1), "T2": (32, "bfloat16", 6), "Bt": (1024, "bfloat16", 1),
+    "q4": (1024, "float32", 1), "yb": (1024, "float32", 1), "yi": (1024, "bfloat16", 1), "plF": (64, "uint16", 1),
+    "pI": (1, "int32", 1), "pM": (1, "int32", 1), "pG": (1, "int32", 1), "p8": (1, "int32", 1), "col": (1, "float32", 16),
+    "ic": (256, "float32", 1), "icb": (256, "bfloat16", 1), "icg": (128, "float32", 1), "lnO": (16, "float32", 1), "nr": (256, "bfloat16", 1),
+    "I": (128, "bfloat16", 1), "nI": (128, "bfloat16", 1), "I16": (128, "bfloat16", 1), "IB": (136, "bfloat16", 1), "XG": (128, "float16", 1),
+    "Gmf": (8, "float32", 1), "Gm": (8, "bfloat16", 1), "nGm": (8, "bfloat16", 1), "G64": (8, "bfloat16", 1), "G32": (8, "bfloat16", 1),
+    "EB": (144, "bfloat16", 1), "wE": (144, "float16", 1), "RB": (240, "bfloat16", 1), "LR": (2048, "float16", 1),
+    "eq": (16, "float32", 1), "le": (16, "float32", 1), "ne": (16, "float32", 1), "hic": (16, "float32", 1),
+    "C16": (256, "bfloat16", 1), "C17": (136, "bfloat16", 1), "d16": (256, "bfloat16", 1), "d17": (136, "bfloat16", 1),
+    "ones": (128, "bfloat16", 1), "c16": (16, "bfloat16", 1), "m1": (256, "bfloat16", 1), "ba": (80, "bfloat16", 1), "ordc": (32, "float32", 1),
+    "k1": (289, "bfloat16", 1), "k2": (289, "bfloat16", 1), "pw": (8, "float32", 1), "p8e": (8, "float32", 2), "p8f": (1, "float32", 1), "xi": (256, "int32", 1), "xj": (256, "int32", 1),
+    "ui": (16, "int32", 2), "UV": (32, "int32", 2), "s": (16, "float32", 2), "sq": (16, "float32", 2), "VV": (32, "int32", 2), "vl": (32, "uint16", 3),
+    "vh": (16, "float16", 2), "G": (256, "bfloat16", 1), "pl": (16, "uint16", 2), "wt1": (16, "float32", 1), "wl": (32, "uint16", 2),
+    "boff": (256, "uint16", 2), "bs": (256, "float32", 2), "qg": (256, "bfloat16", 2), "im1": (256, "bfloat16", 2), "nfl": (256, "bfloat16", 2), "gt": (256, "bfloat16", 2),
+    "qs": (256, "float32", 2), "nsB": (32, "float32", 2), "sk": (16, "float32", 2), "ac": (18, "bfloat16", 2), "A": (1, "float32", 2),
+    "s12": (544, "float32", 1), "m": (272, "float32", 1), "HI": (32, "int32", 1), "HA": (32, "int32", 1), "nf": (32, "float32", 1), "nfS": (32, "float32", 1),
+    "KM": (80, "bfloat16", 2), "kx": (16, "float32", 1), "sm": (16, "int32", 1), "sl": (16, "int32", 1), "ca": (16, "float32", 1), "cb": (16, "float32", 1),
+    "ol": (80, "uint16", 2), "kb": (48, "float32", 2), "pen": (16, "float32", 1), "ybk": (256, "float32", 1), "q1": (256, "bfloat16", 1),
+    "a12": (512, "bfloat16", 1), "SG": (768, "bfloat16", 1), "E": (256, "bfloat16", 1), "KK": (48, "float32", 1), "KL": (48, "float32", 1),
+    "mna": (16, "float32", 1), "mxa": (16, "float32", 1), "tta": (16, "float32", 1), "FM": (32, "int32", 1), "FA": (32, "int32", 1), "fml": (32, "uint16", 2),
+    "Bm": (256, "bfloat16", 2), "cx": (512, "bfloat16", 4),
 }
 BYTES = {"float32": 4, "int32": 4, "bfloat16": 2, "uint16": 2, "float16": 2}
 PLACE = {}
@@ -50,19 +46,23 @@ BUF = {"float32": "bigf", "int32": "bigi", "bfloat16": "bigb", "uint16": "bigu",
 SCRATCH = {BUF[_d]: ("sbuf", [128, _size[_d]], _d) for _d in BYTES}
 for _k in range(8):
     SCRATCH["P%d" % _k] = ("psum", [128, 512], "float32")
+for _k in range(2):
+    SCRATCH["Yc%d" % _k] = ("sbuf", [128, 10, 64], "bfloat16")
+SCRATCH["TH3"] = ("sbuf", [128, 6, 16], "float32")
 LOADS = ["bites", "next", "wt", "bank", "immun", "geno"]
 STORES = ["sg", "sb0", "sb1", "si0", "si1"]
 SEMAPHORES = ["qv", "qs", "qp", "qg", "rl"] + ["arr%d" % t for t in range(1, STEPS)] + ["ld_" + n for n in LOADS] + ["st_" + n for n in STORES]
 
 
-BIAS = {'C48': -8, 'CZ': 2, 'G64': 14, 'Gm': 9, 'Gs': 10, 'I': 20, 'KK': -9, 'LR': -1, 'P1fl': 3, 'P2fl': 8, 'P2ones': -14, 'P3I': -1, 'P4awsl': -1,
-        'P4qtab': 3, 'P6I': 2, 'P6nI': -7, 'SC': 6, 'ac': 12, 'al': -3, 'ba32': -6, 'base': 3, 'bb': 5, 'bci': 17, 'bk': -13, 'btab': 3, 'bti': -4,
-        'c1': 4, 'cs': -12, 'flg': 13, 'geno_s': -27, 'ic': -10, 'im0': 3, 'ir': -2, 'itab': -1, 'keys': 11, 'kidx': -3, 'lnD': -6, 'lnO': 2,
-        'ls32': 7, 'm0': -1, 'm1': 3, 'ml4': -4, 'mn4': -6, 'n1': 11, 'nI': -11, 'ns': 1, 'of': -4, 'outsb1': 1, 'outsi1': 6, 'pG': 3, 'qki': -8,
-        'qtab': -5, 'sh': 1, 'sk': 3, 'sm': -1, 'sp32': 9, 't1': 8, 'thr': -6, 'tp32': -1, 'v': 31, 'vh': 4, 'vl': 19, 'wi2': 1, 'wo': -4, 'wti': -7}
-COST = {"us": 0.00083 * 1.25, "ps": 0.00071 * 1.25, "gather": 1.56, "scatter": 3.8, "wake": 0.08, "link": 4.0}
+BIAS = {'pP2ones': -4, 'pP3LR': 4, 'pP4EW': 1, 'pP5I': 7, 'pP7EB': -1, 'pP7I': -5, 'pre.gnr': 8, 'pre.gpI': 6, 'pre.sX2': 8, 'pre.sba': -31, 'pre.skb': -2, 'pre.snI': 5, 'pre.spsb': 50, 'pre.spsrc': 32, 'pre.vEB': 2, 'pre.vGmf': 19, 'pre.vT2': 41, 'pre.vac': 20, 'pre.vcol': 26, 'pre.vcol3': 6, 'pre.vcol4': 20, 'pre.vcol5': 6, 'pre.vcol6': 10, 'pre.vcol7': 11, 'pre.veq': 4, 'pre.vicg': -7, 'pre.vne': 11, 'pre.vp8': 3, 'pre.vp8e': 12, 'pre.vp8f': 26, 'pre.vpM': 4, 'pre.vq192': -8, 'pre.vwt1': 4, 'sSG': -9, 'sW': 3, 'sptab': -15, 'sqg': 5, 'vA': 11, 'vKK': -17, 'vVV': -6, 'vYc0': 3, 'vkb': -7, 'vkb2': -4, 'vkx': 2, 'vnsB': 10, 'vol': 7, 'vpl': -1, 'vvh': 5, 'vcx': 12, 'vsk': 13, 'pP3wE': -2, 'pP1I': 4, 'pre.sptab': 4, 'vE': 3, 'vsq': 6, 'vybk': 2, 'pre.vpw': 25, 'vmna': -1}
+COST = {"us": 0.00083 * 1.25, "ps": 0.00071 * 1.25, "gather": 1.56, "scatter": 3.8, "wake": 0.08, "link": 5.5}
 LOOK = 0.3
-VG = {t: 512 for t in range(STEPS)}
+VG = [512, 256, 256, 256, 256, 512]
+PARTS = [[("s", 0, 64), ("s", 64, 128), ("s", 128, 192), ("s", 192, 256 - v // 16)] + ([("v", 256 - v // 16, 256)] if v else []) for v in VG]
+NFL = "v"
+ON_S = ()
+XS = 12
+YV = 4
 
 
 def list_schedule(n, que, cost, succ, need, prio):
@@ -156,6 +156,7 @@ def rank_program(g, core, T, topo):
     ops = []
     last = {}
     edges = []
+    part = {"name": "pre.", "runs": {}, "last": None}
     US, PS = COST["us"], COST["ps"]
 
     def t_(name, a=0, b=None, c=0, step=1):
@@ -167,9 +168,16 @@ def rank_program(g, core, T, topo):
         ap = T[BUF[d]][:, off + a:off + b:step] if step != 1 else T[BUF[d]][:, off + a:off + b]
         return {"ap": ap, "rg": [(BUF[d], off + a, off + b)], "n": (b - a + step - 1) // step, "by": BYTES[d], "ps": False, "ind": False}
 
-    def p_(k, a, b, step=1, grp=None):
+    def p_(k, a, b, step=1):
         ap = T["P%d" % k][:, a:b:step] if step != 1 else T["P%d" % k][:, a:b]
-        return {"ap": ap, "rg": [("P%d" % k, 0, 512)], "n": (b - a + step - 1) // step, "by": 4, "ps": True, "ind": False, "grp": grp}
+        return {"ap": ap, "rg": [("P%d" % k, 0, 512)], "n": (b - a + step - 1) // step, "by": 4, "ps": True, "ind": False}
+
+    def y_(t, a, b, step, rg):
+        name = "Yc%d" % (t % 2)
+        return {"ap": T[name][:, :, a:b:step], "rg": [(name,) + rg], "n": 80, "by": 2, "ps": False, "ind": False}
+
+    def th_(a, b, step=1):
+        return {"ap": T.TH3[:, a:b:step, :], "rg": [("TH3", a, b)], "n": 48, "by": 4, "ps": False, "ind": False}
 
     def ind(win, off):
         return {"ap": win["ap"].indirect(off["ap"]), "rg": win["rg"] + off["rg"], "win": win["rg"], "off": off["rg"], "n": 16 * off["n"], "by": win["by"], "ps": False, "ind": True}
@@ -182,7 +190,7 @@ def rank_program(g, core, T, topo):
             return region[0]
         return [x for o, x in starts[dtype_of[region[0]]] if o <= region[1]][-1]
 
-    def add(q, cost, emit, R, W, sem, inc, grp=None, role=None, extra=()):
+    def add(q, cost, emit, R, W, sem, inc, grp=None, role=None):
         i = len(ops)
         ed = {}
         acc = [(r, False) for r in R] + [(r, True) for r in W]
@@ -197,22 +205,25 @@ def rank_program(g, core, T, topo):
                             ed.setdefault(j, 0)
                     else:
                         ed[j] = 1
-                elif wr or wr2:
+                elif (wr or wr2) and not (wr and wr2 and grp is not None and grp == grp2):
                     ed[j] = 1
-        for j in extra:
-            ed[j] = 1
         for (buf, a, b), wr in acc:
             ps = buf.startswith("P") and len(buf) == 2
             lst = last.setdefault(buf, [])
             if wr and not ps:
-                lst[:] = [x for x in lst if not (x[0] >= a and x[1] <= b and x[2] != i)]
+                lst[:] = [x for x in lst if not (x[0] >= a and x[1] <= b and x[2] != i and not (grp is not None and x[5] == grp))]
             lst.append((a, b, i, wr, q, grp, role))
             if ps and len(lst) > 200:
                 del lst[:80]
         tag = name_of(W[0]) if W else q
         if tag[0] == "P" and R:
             tag += name_of(R[0])
-        ops.append({"q": q, "cost": cost, "emit": emit, "sem": sem, "inc": inc, "tag": tag})
+        k = q + tag.replace("Yc1", "Yc0")
+        if k != part["last"]:
+            part["runs"][k] = part["runs"].get(k, 0) + 1
+        part["last"] = k
+        run = 1 if k in ("vW", "pP1W") else part["runs"][k]
+        ops.append({"q": q, "cost": cost, "emit": emit, "sem": sem, "inc": inc, "tag": tag, "name": part["name"] + k + (str(run) if run > 1 else "")})
         edges.append(ed)
         return i
 
@@ -241,372 +252,385 @@ def rank_program(g, core, T, topo):
         return (out["off"], out["win"]) if out["ind"] else ([], out["rg"])
 
     def tt(out, a, b, op):
-        r, w = outrg(out)
-        n = out["n"]
-        return add("v", vcost(n, "tt", [out, a, b]), lambda: g.vector.tensor_tensor(raw(out), raw(a), raw(b), op), rgs(a, b) + r, w, "qv", 1)
+        return add("v", vcost(out["n"], "tt", [out, a, b]), lambda: g.vector.tensor_tensor(raw(out), raw(a), raw(b), op), rgs(a, b), out["rg"], "qv", 1)
 
-    def ts(out, a, s1, s2, o1, o2=None):
-        r, w = outrg(out)
+    def ts(out, a, s1, s2, o1, o2=None, grp=None):
         f = (lambda: g.vector.tensor_scalar(raw(out), raw(a), raw(s1), raw(s2), o1)) if o2 is None else (lambda: g.vector.tensor_scalar(raw(out), raw(a), raw(s1), raw(s2), o1, o2))
-        return add("v", vcost(out["n"], "ts", [out, a]), f, rgs(a, s1, s2) + r, w, "qv", 1)
+        return add("v", vcost(out["n"], "ts", [out, a]), f, rgs(a, s1, s2), out["rg"], "qv", 1, grp=grp)
 
     def cp(out, a):
         r, w = outrg(out)
         return add("v", vcost(out["n"], "ts", [out, a]), lambda: g.vector.tensor_copy(raw(out), raw(a)), rgs(a) + r, w, "qv", 1)
 
     def ms(out, val):
-        return add("v", max(64, out["n"]) * US, lambda: g.vector.memset(raw(out), val), [], out["rg"], "qv", 1)
+        return add("v", vcost(out["n"], "ts", [out]), lambda: g.vector.memset(raw(out), val), [], out["rg"], "qv", 1)
 
     def red(out, a):
         return add("v", 64 * US, lambda: g.vector.tensor_reduce(raw(out), raw(a), AxisListType.X, OP.add), rgs(a), out["rg"], "qv", 1)
 
-    def act(out, a, fn, bias=0.0, scale=1.0, acc=None):
+    def runmax(out, reset, a):
+        return add("v", vcost(out["n"], "ts", [out, a]), lambda: g.vector.tensor_tensor_scan(raw(out), raw(reset), raw(a), 0.0, OP.add, OP.max), rgs(reset, a), out["rg"], "qv", 1)
+
+    def act(out, a, fn, bias=0.0, scale=1.0, grp=None):
         c = 0.065 + a["n"] * COST["gather"] * US if a["ind"] else max(64, a["n"]) * US
-        w = out["rg"] + (acc["rg"] if acc else [])
-        if acc:
-            c += 0.02
-            f = lambda: g.scalar.activation(raw(out), raw(a), fn, bias=raw(bias), scale=scale, accum_out=raw(acc))
-        elif isinstance(bias, float) and bias == 0.0:
+        if out["ind"]:
+            return add("s", 0.065 + a["n"] * COST["scatter"] * US, lambda: g.scalar.activation(raw(out), raw(a), fn), rgs(a) + out["off"], out["win"], "qs", 1)
+        if isinstance(bias, float) and bias == 0.0:
             f = (lambda: g.scalar.activation(raw(out), raw(a), fn, scale=raw(scale))) if scale != 1.0 else (lambda: g.scalar.activation(raw(out), raw(a), fn))
         else:
-            f = lambda: g.scalar.activation(raw(out), raw(a), fn, bias=raw(bias), scale=scale)
-        return add("s", c, f, rgs(a, bias, scale), w, "qs", 1)
+            f = lambda: g.scalar.activation(raw(out), raw(a), fn, bias=raw(bias), scale=raw(scale))
+        return add("s", c, f, rgs(a, bias, scale), out["rg"], "qs", 1, grp=grp)
 
-    def mm(out, lhsT, rhs, start, stop, grp=None, role=None, f32=False):
-        c = max(64, rhs["n"]) * PS * (4 if f32 else 1)
+    def lin(name, a, scale, bias):
+        if name in ON_S:
+            return act(t_(name), a, AF.Identity, bias=bias, scale=scale)
+        return ts(t_(name), a, scale, bias, OP.mult, OP.add)
+
+    def mm(out, lhsT, rhs, start, stop, grp=None, role=None):
+        c = max(64, rhs["n"]) * PS * (4 if rhs["by"] == 4 else 1)
         return add("p", c, lambda: g.tensor.matmul(raw(out), raw(lhsT), raw(rhs), start, stop), rgs(lhsT, rhs), out["rg"], "qp", 1, grp=grp, role=role)
 
-    def iota(out, pattern, base=0, cm=0):
-        small = out["flt"] if "flt" in out else False
+    def iota(out, pattern, base=0, cm=0, whole=False):
         def f():
-            if small:
-                return g.iota(raw(out), pattern, base, cm, allow_small_or_imprecise_dtypes=True)
-            return g.iota(raw(out), pattern, base, cm)
+            if whole:
+                return g.iota(raw(out), pattern, base, cm)
+            return g.iota(raw(out), pattern, base, cm, allow_small_or_imprecise_dtypes=True)
         return add("g", 0.13 + 2 * out["n"] * US, f, [], out["rg"], "qg", 1)
+
+    def fill(out, val):
+        return iota(out, [[0, out["n"]]], val)
 
     def keep(out, a):
         return add("g", 0.17 + 2 * out["n"] * US, lambda: g.affine_select(raw(out), raw(a), [[0, out["n"]]], OP.is_ge, 0.0, 0, 0), rgs(a), out["rg"], "qg", 1)
-
-    def flt(x):
-        x["flt"] = True
-        return x
 
     def load(name, out, q="y"):
         eng = g.sync if q == "y" else g.scalar
         src = T.bites[:, 0:256] if name == "bites" else T.bites[:, 256:512] if name == "next" else T[name][:]
         return add(q, 0.1, lambda: eng.dma_start(raw(out), src), [], out["rg"], "ld_" + name, 16)
 
-    def store(tag, dst, src, q="y"):
-        eng = g.sync if q == "y" else g.scalar
-        return add(q, 0.1, lambda: eng.dma_start(dst, raw(src)), src["rg"], [("out" + tag, 0, 1)], "st_" + tag, 16)
-
     lag = {}
 
-    for name, dst, tm in (("bites", t_("CZ", 4112, 4368, 0), 2.6), ("wt", t_("wti"), 2.5), ("bank", t_("bk"), 4.5), ("immun", t_("im0"), 5.0), ("next", t_("bt"), 4.0), ("geno", t_("geno_s"), 7.0)):
-        i = load(name, dst, "s" if name in ("wt", "immun", "next") else "y")
-        lag[i] = tm
+    def store(tag, dst, src, q="y"):
+        eng = g.sync if q == "y" else g.scalar
+        i = add(q, 0.1, lambda: eng.dma_start(dst, raw(src)), src["rg"], [("out" + tag, 0, 1)], "st_" + tag, 16)
+        lag[i] = 2.0 + src["n"] * src["by"] * 0.0005
 
-    def send(src, t, dst_rank):
+    for name, dst, tm in (("bites", t_("z"), 2.6), ("wt", t_("wti"), 2.5), ("bank", t_("bk"), 4.5), ("next", t_("bt"), 4.0), ("geno", t_("geno_s"), 7.0), ("immun", t_("ilog", 0, 1024), 7.0)):
+        lag[load(name, dst, "s" if name in ("wt", "immun", "next") else "y")] = tm
+
+    def send(srcs, t, dst_rank):
         dst = T.cores[dst_rank]
         rid, pid, _se = topo.addr(dst)
         m = topo.mask(core, dst)
         eng = len(topo.engines(core, dst))
-        out = t_("CZ", 4112, 4368, t)
+        out = t_("z", c=t)
+        sem = T.sem["arr%d" % t]
         def f():
-            return g.remote_dma(raw(out), raw(src), T.sem["arr%d" % t], T.sem.rl, pid, rid, m)
-        i = add("g", 0.3, f, src["rg"], [], None, 0)
+            if len(srcs) == 1:
+                return g.remote_dma(raw(out), raw(srcs[0]), sem, T.sem.rl, pid, rid, m)
+            tr = RemoteDMATransfer(dst_ids=[DstId(rid=rid, pnc=pid)], dma_engine_mask=m, remote_sem=sem, srcs=[raw(x) for x in srcs], dsts=[raw(out)], alu_op=2)
+            return g.remote_dma_fused([tr], local_sem=T.sem.rl)
+        i = add("g", 0.3, f, rgs(*srcs), [], None, 0)
         ops[i]["remote"] = eng
-        lag[i] = 0.3
         j = add("n", 0.0, None, [], out["rg"], "arr%d" % t, eng)
         ops[j]["proxy"] = i
-        lag[j] = 0.0
-        return i
 
-    iota(t_("pI", 0, 1), [[0, 1]], 0, 1)
-    iota(flt(t_("ic", 0, 128)), [[1, 128]])
-    iota(flt(t_("icg")), [[1, 8], [0, 16]])
-    iota(flt(t_("ir")), [[0, 16], [1, 16]])
-    iota(t_("bci"), [[1, 16]])
-    iota(t_("kidx"), [[0, 16], [1, 16]])
-    iota(flt(t_("lnO")), [[16, 16]])
-    iota(flt(t_("ln32")), [[16, 8], [0, 2], [128, 2]])
-    iota(flt(t_("ls32")), [[0, 8], [1, 2], [0, 2]])
-    send(t_("bt"), 1, (rank + 1) % n_ranks)
-    ts(t_("pM", 0, 1), t_("pI", 0, 1), 15, None, OP.bitwise_and)
-    ts(t_("pG", 0, 1), t_("pI", 0, 1), 4, None, OP.arith_shift_right)
-    P, PM, PG = t_("pf", 0, 1), t_("pf", 8, 9), t_("pf", 16, 17)
-    cp(P, t_("pI", 0, 1))
-    cp(PM, t_("pM", 0, 1))
-    cp(PG, t_("pG", 0, 1))
-    ts(t_("Gmf"), t_("ic", 0, 8), PG, None, OP.is_equal)
+    P, PM, PG, P8, WF, WG, WS, CI, PK, PK0, JK, PW, L1, L2, H1, W1 = [t_("col", c=k) for k in range(16)]
+    ic = lambda n: t_("ic", 0, n)
+    iota(t_("pI"), [[0, 1]], 0, 1, True)
+    iota(t_("ic"), [[1, 256]])
+    iota(t_("icg"), [[1, 8], [0, 16]])
+    send([t_("bt")], 1, (rank + 1) % n_ranks)
+    iota(t_("C16"), [[0, 16], [-1, 16]], 16)
+    iota(t_("C17"), [[0, 8], [-1, 17]], 17)
+    iota(t_("lnO"), [[16, 16]])
+    iota(t_("nr"), [[-16, 256]])
+    iota(t_("k1"), [[1, 17], [0, 17]])
+    iota(t_("k2"), [[0, 17], [1, 17]])
+    ts(t_("pM"), t_("pI"), 15, None, OP.bitwise_and)
+    ts(t_("pG"), t_("pI"), 4, None, OP.arith_shift_right)
+    ts(t_("p8"), t_("pI"), 7, None, OP.bitwise_and)
+    cp(P, t_("pI"))
+    cp(PM, t_("pM"))
+    cp(PG, t_("pG"))
+    ts(P8, t_("p8"), -1.0, 7.0, OP.mult, OP.add)
+    cp(t_("p8f"), t_("p8"))
+    ts(t_("Gmf"), ic(8), PG, None, OP.is_equal)
     ms(t_("EB"), 0.0)
     cp(t_("EB", 15, 128, step=16), t_("Gmf"))
-    ts(t_("wi2", 0, 1), t_("wti"), 4032, None, OP.bitwise_and)
-    ts(t_("wi2", 8, 9), t_("wti"), 63, None, OP.bitwise_and)
-    WH, WL = t_("wf", 0, 1), t_("wf", 8, 9)
-    cp(WH, t_("wi2", 0, 1))
-    cp(WL, t_("wi2", 8, 9))
-    WF, WG, WS = t_("ww", 0, 1), t_("ww", 8, 9), t_("ww", 16, 17)
     cp(WF, t_("wti"))
     ts(WG, WF, 2047.5, -4096.0, OP.is_gt, OP.mult)
     tt(WS, WF, WG, OP.add)
     ts(t_("wE"), t_("EB"), WS, None, OP.mult)
-    ts(t_("lnO"), t_("lnO"), PM, None, OP.add)
-    ts(t_("lnD"), t_("lnO"), 1024.0, None, OP.add)
-    cp(t_("bc"), t_("bci"))
-    ts(t_("Gf"), t_("icg"), PG, None, OP.is_equal)
-    ts(t_("I"), t_("ic", 0, 128), P, None, OP.is_equal)
+    ts(t_("I"), ic(128), P, None, OP.is_equal)
     ts(t_("bki"), t_("bk"), 4095, None, OP.bitwise_and)
-    cp(t_("btab", 0, 1024), t_("bki"))
-    ts(t_("qki"), t_("bk"), 12, None, OP.arith_shift_right)
-    cp(t_("qtab", 0, 1024), t_("qki"))
-    act(t_("itab", 0, 1024), t_("im0"), AF.Copy)
-    cp(t_("Gm", 0, 8), t_("Gmf"))
-    ts(t_("G64", 0, 8), t_("Gmf"), 1024.0, None, OP.mult)
-    ts(t_("G32", 0, 8), t_("Gmf"), -512.0, None, OP.mult)
-    ts(t_("nI"), t_("I"), -1.0, None, OP.mult)
-    ts(t_("IB"), t_("I"), BIG, None, OP.mult)
-    ts(t_("I16"), t_("I"), -16.0, None, OP.mult)
-    ts(t_("Is"), t_("I"), 1.0 / 128, None, OP.mult)
-    ts(t_("C16"), t_("ir"), -1.0, 256.0, OP.mult, OP.add)
-    ms(t_("ones"), 1.0)
-    ms(t_("RB"), 0.0)
-    ts(t_("RB", 112, 128), t_("ir", 0, 16), PM, None, OP.is_equal)
-    for r in range(16):
-        ts(t_("LR", 128 * r, 128 * r + 128), t_("Gf"), t_("RB", 112 + r, 113 + r), None, OP.mult)
-    iota(flt(t_("row16")), [[16, 256]])
-    for h in range(2):
-        ts(t_("lc", 8 * h, 8 * h + 1), P, -16.0, -2048.0 * h, OP.mult, OP.add)
-        ts(t_("nD", c=h), t_("I"), t_("lc", 8 * h, 8 * h + 1), None, OP.mult)
-    for t in range(1, STEPS):
-        ts(t_("nIt", c=t), t_("I"), float(-t), None, OP.mult)
-    ts(t_("Mk"), t_("ir"), PM, 2048.0, OP.is_ge, OP.mult)
+    cp(t_("blog", 0, 1024), t_("bki"))
+    ts(t_("q192"), t_("bk"), 1.0 / 4096, 191.5 + 1.0 / 8192, OP.mult, OP.add)
+    act(t_("qlog", 0, 1024), t_("q192"), AF.Identity, bias=-192.0)
+    for name, f in (("Gm", 1.0), ("nGm", -1.0), ("G64", 64.0), ("G32", -32.0)):
+        act(t_(name), t_("Gmf"), AF.Copy, scale=f)
+    act(t_("nI"), t_("I"), AF.Copy, scale=-1.0)
+    act(t_("I16"), t_("I"), AF.Copy, scale=-16.0)
+    ts(CI, P, PG, 1.0, OP.add, OP.add)
+    ts(t_("IB"), ic(136), CI, -BIG, OP.is_equal, OP.mult)
+    fill(t_("C17", 0, 136, step=17), 0)
+    fill(t_("d16"), 0)
+    fill(t_("d16", 0, 256, step=16), -4096)
+    fill(t_("d17"), 0)
+    fill(t_("d17", 0, 136, step=17), -1048576)
+    fill(t_("m", 0, 272, step=136), 0)
+    fill(t_("ones"), 1)
+    fill(t_("c16"), 16)
     for c in range(2):
-        ms(t_("c1", 0, 1, c), 0.0)
-    ms(t_("m1"), -1.0)
-    for c in range(STEPS):
-        ms(t_("CZ", 4096, 4112, c), 0.0)
-    for s in range(8):
-        ms(t_("SC", s, 128, step=8), float(1 << (7 - s)))
-    tt(t_("Gs"), t_("Gf"), t_("SC"), OP.mult)
-    ts(t_("wSh"), t_("Gs"), WH, None, OP.mult)
-    ts(t_("wSl"), t_("Gs"), WL, None, OP.mult)
-    ts(t_("ln32"), t_("ln32"), PM, None, OP.add)
-    ts(t_("ba32"), t_("ln32"), 16.0, 256.0, OP.mult, OP.add)
-    ts(t_("tp32"), t_("ln32"), 16.0, None, OP.add)
-    tt(t_("tp32"), t_("tp32"), t_("ls32"), OP.mult)
-    ts(t_("sp32"), t_("ln32"), -15.0, 3856.0, OP.mult, OP.add)
-    tt(t_("sp32"), t_("sp32"), t_("tp32"), OP.subtract)
+        ms(t_("ac", 16, 17, c), 304.0 / 128)
+        ms(t_("ac", 17, 18, c), 7.59375 / 128)
+    ts(t_("eq"), ic(16), PM, None, OP.is_equal)
+    ts(t_("le"), ic(16), PM, None, OP.is_ge)
+    ts(t_("ne"), ic(16), PM, 16384.0, OP.not_equal, OP.mult)
+    fill(t_("RB"), 0)
+    ts(t_("RB", 112, 128), t_("eq"), -1.0, None, OP.mult)
+    ts(t_("icg"), t_("icg"), PG, None, OP.is_equal)
+    ts(t_("XG"), t_("I"), -2.0, None, OP.mult)
+    tt(t_("XG"), t_("XG"), t_("icg"), OP.add)
+    for r in range(16):
+        ts(t_("LR", 128 * r, 128 * r + 128), t_("XG"), t_("eq", r, r + 1), t_("le", r, r + 1), OP.min, OP.mult)
+    ts(JK, PM, 1024.0, None, OP.add)
+    ts(t_("lnO"), t_("lnO"), PM, 16.0, OP.add, OP.mult)
     for k in range(3):
-        ts(t_("C48", 16 * k, 16 * k + 16), t_("lnO"), 256.0 * k, None, OP.add)
+        act(t_("ba", 16 * k, 16 * k + 16), t_("lnO"), AF.Identity, bias=16.0)
+    iota(t_("ba", 48, 80), [[128, 2], [0, 16]], 16)
+    iota(t_("ordc"), [[int(WO), 2], [0, 16]], int(WO))
+    for c in range(2):
+        act(t_("kb", 0, 16, c), t_("lnO"), AF.Identity, bias=4096.0)
+    fill(t_("X2", 0, 1), 0)
+    for k in range(16):
+        if k < XS:
+            act(t_("X2", k or 16, 4097, step=16), t_("nr"), AF.Identity, bias=t_("ne", k, k + 1), grp="X2")
+        else:
+            ts(t_("X2", k or 16, 4097, step=16), t_("nr"), t_("ne", k, k + 1), None, OP.add, grp="X2")
+    ts(PK0, PM, 0.0, 16.0, OP.is_equal, OP.mult)
+    tt(PK, PM, PK0, OP.add)
+    for t in range(STEPS):
+        ts(t_("T2", c=t), ic(32), PK, 8.0 + t, OP.is_equal, OP.mult)
+    ts(t_("k1"), t_("k1"), PM, 64.0, OP.not_equal, OP.mult)
+    ts(t_("k2"), t_("k2"), PM, 64.0, OP.not_equal, OP.mult)
+    tt(t_("T1"), t_("k1"), t_("k2"), OP.min)
+    ms(t_("pw", 0, 1), 1.0)
+    for k in (1, 2, 4):
+        ts(t_("pw", k, 2 * k), t_("pw", 0, k), float(2 ** k), None, OP.mult)
+    ts(t_("p8e"), ic(8), P8, None, OP.is_equal)
+    tt(t_("p8e"), t_("p8e"), t_("pw"), OP.mult)
+    red(PW, t_("p8e"))
+    ts(t_("xi"), t_("ic"), PW, None, OP.mult)
+    ts(t_("xj"), t_("xi"), 128, None, OP.bitwise_and)
+    ts(t_("Bt", 0, 256), t_("xj"), 0.5, None, OP.mult)
+    for k in range(1, 4):
+        keep(t_("Bt", 256 * k, 256 * k + 256), t_("Bt", 0, 256))
+    ts(L1, PM, 8.0, 1.0 / 64, OP.is_lt, OP.mult)
+    ts(L2, L1, 200.0, None, OP.mult)
+    ts(H1, L1, -1.0, 1.0 / 64, OP.mult, OP.add)
+    ts(t_("hb"), t_("Bt", 0, 16), H1, None, OP.mult)
+    ts(t_("hb", c=1), t_("hb"), 200.0, -100.0, OP.mult, OP.add)
+    for k in range(4):
+        act(t_("ptab", 256 * k, 256 * k + 256), t_("Bt", 0, 256), AF.Identity, bias=t_("hb", k, k + 1), scale=L1)
+    for t in range(STEPS - 1):
+        act(t_("psrc", c=t), t_("Bt", 0, 256), AF.Identity, bias=t_("hb", 4 + t, 5 + t, 1), scale=L2)
+    act(t_("psb"), t_("Bt", 0, 256), AF.Identity, bias=t_("hb", 3 + STEPS, 4 + STEPS), scale=L1)
+    ts(t_("p8e", c=1), ic(8), t_("p8f"), None, OP.is_equal)
+    tt(t_("p8e", c=1), t_("p8e", c=1), t_("pw"), OP.mult)
+    red(W1, t_("p8e", c=1))
+    ts(H1, H1, 255.0 * 64, 1.0, OP.mult, OP.add)
+    ts(t_("EW"), t_("EB"), W1, H1, OP.mult, OP.mult)
 
-    def zt(t, a=0, b=256, step=1):
-        return t_("CZ", 4112 + a, 4112 + b, t, step)
-
-    def early(t):
-        z = zt(t)
+    def to_list(out, src, a, b, wts="EB"):
         for r in range(16):
-            mm(p_(2, 320, 336), t_("wE", 15 - r, 143 - r), zt(t, r, 256, 16), r == 0, r == 15)
-        cp(t_("ui", c=t), p_(2, 320, 336))
-        ts(t_("u", c=t), t_("ui", c=t), 4095, None, OP.bitwise_and)
-        tt(t_("sq", c=t), t_("u", c=t), t_("u", c=t), OP.mult)
-        ts(t_("u37", c=t), t_("u", c=t), 37.0, None, OP.mult)
-        ts(t_("sh", c=t), t_("sq", c=t), 5, None, OP.arith_shift_right)
-        tt(t_("base", c=t), t_("sh", c=t), t_("u37", c=t), OP.add)
-        ts(t_("vb", c=t), t_("base", c=t), 1023, None, OP.bitwise_and)
-        cp(t_("vh", c=t), t_("vb", c=t))
-        for b in (256, 0):
-            if b == 0:
-                mm(p_(3, 0, 256), t_("I"), t_("Mk"), True, False)
-            for r in range(16):
-                mm(p_(3, b + r, b + 256, 16), t_("LR", 128 * r, 128 * r + 128), t_("vh", c=t), b == 256, b == 256 or r == 15)
-        ts(t_("bb", c=t), t_("vb", c=t), -32.0, -5.7, OP.mult, OP.add)
-        for j in range(15, -1, -1):
-            if j:
-                act(t_("junk", 0, 16 * j, 2 * j), p_(3, 256, 256 + 16 * j), AF.Sigmoid, bias=t_("bb", j, j + 1, t), scale=32.0, acc=t_("c1", j, j + 1, t))
-            act(t_("junk", 0, 16, 2 * j + 1), p_(3, 16 * j, 16 * j + 16), AF.Sigmoid, bias=t_("bb", j, j + 1, t), scale=32.0, acc=t_("c2", j, j + 1, t))
-        tt(t_("cs", c=t), t_("c1", c=t), t_("c2", c=t), OP.add)
-        ts(t_("ri", c=t), t_("cs", c=t), -0.45, None, OP.add)
-        tt(t_("fr", c=t), t_("cs", c=t), t_("ri", c=t), OP.subtract)
-        ts(t_("dup", c=t), t_("fr", c=t), 0.0017, None, OP.is_gt)
+            mm(out, t_(wts, 15 - r, 143 - r), t_(src, a + r, b, 0, 16), r == 0, r == 15)
+
+    def host(t):
+        for r in range(16):
+            mm(p_(3, 256, 272), t_("wE", 15 - r, 143 - r), t_("z", r, 256, t, 16), r == 0, r == 15)
+        u = t_("UV", 16, 32, t)
+        cp(t_("ui", c=t), p_(3, 256, 272))
+        ts(u, t_("ui", c=t), 4095, None, OP.bitwise_and)
+        ts(t_("s", c=t), u, 592.0, None, OP.add)
+        tt(t_("sq", c=t), t_("s", c=t), t_("s", c=t), OP.mult)
+        ts(t_("UV", 0, 16, t), t_("sq", c=t), 1.0 / 32, t_("A", c=t - 1) if t else 311.59375, OP.mult, OP.add)
+        ts(t_("VV", c=t), t_("UV", c=t), 1023, None, OP.bitwise_and)
+        cp(t_("vl", c=t), t_("VV", c=t))
+        if t:
+            act(t_("G"), ind(t_("ptab", 0, 1024), t_("vl", 0, 16, t)), AF.Copy)
+            to_list(p_(4, 0, 16), "G", 0, 256, "EW")
+            cp(t_("pl", c=t), p_(4, 0, 16))
+        ts(t_("vh", c=t), t_("VV", 0, 16, t), 1.0, None, OP.add)
+        for r in range(16):
+            mm(p_(3, r, 256, 16), t_("LR", 128 * r, 128 * r + 128), t_("vh", c=t), True, True)
+        ts(t_("E"), p_(3, 0, 256), 0.0, 4096.0, OP.is_equal, OP.mult)
+        to_list(p_(3, 272, 288), "E", 0, 256)
+        tt(t_("wt1"), t_("VV", 0, 16, t), p_(3, 272, 288), OP.add)
+        ts(t_("wl", 0, 32, t, 2), t_("wt1"), JK, None, OP.min)
 
     def step(t):
-        if t == 0:
-            early(0)
-        z = zt(t)
+        z = t_("z", c=t)
+        n = 1024 + 256 * t
+        pl = t_("pl", c=t) if t else t_("vl", 0, 16, t)
+        W = lambda a, b, s=1: t_("W", a, b, t, s)
         mm(p_(0, 0, 256), t_("I"), z, True, True)
-        mm(p_(0, 256, 512), t_("I"), z, True, False)
-        mm(p_(0, 256, 512), t_("I"), t_("m1"), False, True)
-        if t:
-            ts(t_("vA", c=t), t_("base", c=t), t_("A", 0, 1, t - 1), None, OP.add)
-            ts(t_("v", c=t), t_("vA", c=t), 1023, None, OP.bitwise_and)
-        else:
-            ts(t_("v", c=t), t_("base", c=t), 1023, None, OP.bitwise_and)
-        cp(t_("vl", c=t), t_("v", c=t))
-        vl, wl = t_("vl", c=t), t_("wl", c=t)
-        cp(t_("boff", c=t), ind(t_("btab" if t else "bki", 0, 1024), vl))
-        tt(t_("dv", c=t), t_("lnD"), t_("v", c=t), OP.subtract)
-        tt(t_("dw", c=t), t_("dv", c=t), t_("dup", c=t), OP.mult)
-        tt(t_("wo", c=t), t_("v", c=t), t_("dw", c=t), OP.add)
-        cp(wl, t_("wo", c=t))
-        for c in range(4):
-            e = VG.get(t, 0) // 16 if c == 3 else 0
-            act(t_("CZ", 1024 * c, 1024 * c + 1024 - 16 * e, t), ind(t_("geno_s"), t_("boff", 64 * c, 64 * c + 64 - e, t)), AF.Copy)
-            if e:
-                cp(t_("CZ", 4096 - 16 * e, 4096, t), ind(t_("geno_s"), t_("boff", 256 - e, 256, t)))
+        for h in range(2):
+            cp(t_("boff", 128 * h, 128 * h + 128, t), ind(t_("blog", 0, n) if t else t_("bki"), t_("pl" if t else "vl", 8 * h, 8 * h + 8, t)))
+        for q, a, b in PARTS[t]:
+            if q == "s":
+                act(W(16 * a, 16 * b), ind(t_("geno_s"), t_("boff", a, b, t)), AF.Copy)
+            else:
+                cp(W(16 * a, 16 * b), ind(t_("geno_s"), t_("boff", a, b, t)))
         keep(t_("geno_s", t, 4096, step=16), z)
         if t == STEPS - 1:
             store("sg", T.ygeno[:], t_("geno_s"))
-        act(t_("bg", c=t), ind(t_("btab", 0, 1024), vl), AF.Copy)
-        act(t_("qg", c=t), ind(t_("qtab", 0, 1024), vl), AF.Copy)
-        act(t_("im1", c=t), ind(t_("itab", 0, 1024), vl), AF.Identity, bias=-1.0)
-        act(t_("fl", c=t), t_("qg", c=t), AF.Sigmoid, bias=-200.0 * t - 100.0, scale=200.0)
-        tt(t_("gt", c=t), t_("im1", c=t), p_(0, 256, 512), OP.is_lt)
-        gk = ("key", t)
-        mm(p_(1, 0, 256), t_("I"), t_("C16"), True, False, gk, "first")
+        qg, nfl, gt, im1 = t_("qg", c=t), lambda h: t_("nfl", 128 * h, 128 * h + 128, t), lambda h: t_("gt", 128 * h, 128 * h + 128, t), t_("im1", c=t)
+        act(t_("bs", c=t), ind(t_("blog", 0, n), pl), AF.Identity, bias=float(t))
+        act(qg, ind(t_("qlog", 0, n), pl), AF.Copy)
+        act(im1, ind(t_("ilog", 0, n), pl), AF.Identity, bias=-1.0)
+        if NFL == "v":
+            ts(t_("nfl", c=t), qg, t + 0.5, None, OP.is_lt)
+        else:
+            act(t_("nfl", c=t), qg, AF.Sigmoid, bias=200.0 * t + 100.0, scale=-200.0)
+        mm(p_(4, 256, 512), t_("I"), z, True, False)
+        mm(p_(4, 256, 512), t_("nI"), im1, False, True)
+        act(t_("gt", c=t), p_(4, 256, 512), AF.Sign, bias=-1.5)
         mm(p_(2, 0, 256), t_("I"), t_("C16"), True, False)
         for h in range(2):
             mm(p_(2, 128 * h, 128 * h + 128), t_("qg", 128 * h, 128 * h + 128, t), t_("I16"), False, h == 1)
-        for h in range(2):
-            mm(p_(2, 256 + 8 * h, 264 + 8 * h), t_("fl", 128 * h, 128 * h + 128, t), t_("Gm", 0, 8), True, True)
+        runmax(t_("qs", c=t), t_("d16"), p_(2, 0, 256))
+        if t + 1 < STEPS:
+            mm(p_(2, 256, 272), t_("I"), t_("c16"), True, False)
+            for h in range(2):
+                mm(p_(2, 256 + 8 * h, 264 + 8 * h), nfl(h), t_("nGm"), False, h == 1)
         for h in range(4):
-            mm(p_(2, 272 + 8 * h, 280 + 8 * h), t_("gt", 128 * (h % 2), 128 * (h % 2) + 128, t), t_("Gm", 0, 8), True, True)
-        act(t_("qks", c=t), p_(2, 1, 256, 2), AF.Copy)
-        ts(t_("n1", c=t), p_(2, 272, 304), 9.0, 4194304.0, OP.is_lt, OP.mult)
-        ts(t_("nsB", c=t), t_("n1", c=t), BIG, None, OP.max)
+            mm(p_(2, 272 + 8 * h, 280 + 8 * h), gt(h % 2), t_("Gm"), True, True)
         if t + 1 < STEPS:
-            ts(t_("sk", c=t), p_(2, 272, 288), 9.0, 2.0, OP.is_ge, OP.mult)
-            tt(t_("ac", c=t), t_("sk", c=t), p_(2, 256, 272), OP.min)
-            mm(p_(2, 304, 320), t_("ones"), t_("ac", c=t), True, True)
-            red(t_("A", 0, 1, t), p_(2, 304, 320))
-        tt(t_("q1", c=t), p_(2, 0, 256, 2), t_("qks", c=t), OP.max)
-        tt(t_("q2", c=t), t_("q1", 0, 128, t, 2), t_("q1", 1, 128, t, 2), OP.max)
-        tt(t_("q3", c=t), t_("q2", 0, 64, t, 2), t_("q2", 1, 64, t, 2), OP.max)
-        tt(t_("m0", c=t), t_("q3", 0, 32, t, 2), t_("q3", 1, 32, t, 2), OP.max)
+            ts(t_("sk", c=t), p_(2, 272, 288), 1.0, 2.0, OP.is_ge, OP.mult)
+            tt(t_("ac", 0, 16, t), t_("sk", c=t), p_(2, 256, 272), OP.min)
+        ts(t_("nsB", c=t), p_(2, 272, 304), 1.0, 4194304.0, OP.is_lt, OP.mult)
         if t + 1 < STEPS:
-            early(t + 1)
+            mm(p_(2, 304, 322), t_("ones"), t_("ac", c=t), True, True)
+            red(t_("A", c=t), p_(2, 304, 322))
+        if t + 1 < STEPS:
+            for j in range(15, -1, -1):
+                act(ind(t_("ptab"), t_("wl", 2 * j, 2 * j + 1, t)), t_("psrc", 16 * j, 16 * j + 16, t), AF.Sigmoid)
+            host(t + 1)
+        else:
+            act(t_("ptb", 0, 1024), t_("ptab", 0, 1024), AF.Copy)
+            for j in range(15, -1, -1):
+                cp(ind(t_("ptb"), t_("wl", 2 * j, 2 * j + 1, t)), t_("psb", 16 * j, 16 * j + 16))
+            to_list(p_(4, 64, 128), "ptb", 0, 1024, "EW")
+            cp(t_("plF"), p_(4, 64, 128))
         for h in range(2):
-            mm(p_(1, 128 * h, 128 * h + 128), t_("fl", 128 * h, 128 * h + 128, t), t_("IB"), False, False, gk, "mid")
+            gk, kb = ("key", t, h), (1, 6)[h]
+            mm(p_(kb, 0, 136), t_("I"), t_("C17"), True, False, gk, "first")
+            mm(p_(kb, 0, 136), nfl(h), t_("IB"), False, False, gk, "mid")
             for k in range(16):
-                mm(p_(1, 128 * h + k, 128 * h + 128, 16), t_("CZ", 2048 * h + k, 2048 * h + 2048, t, 16), t_("G32", 0, 8), False, False, gk, "mid")
+                mm(p_(kb, 1 + k, 136, 17), W(2048 * h + k, 2048 * h + 2048, 16), t_("G32"), False, False, gk, "mid")
             for k in range(16):
+                o = 4096 + 2048 * h + 128 * k
                 if h == 0:
-                    tt(t_("mx", 128 * k, 128 * k + 128, t), t_("CZ", k, 2048, t, 16), p_(0, 0, 128), OP.max)
+                    tt(W(o, o + 128), W(k, 2048, 16), p_(0, 0, 128), OP.max)
                 else:
                     for e in range(2):
-                        o = 2048 + 128 * k + 64 * e
-                        tt(t_("mx", o, o + 64, t), t_("CZ", 2048 + 1024 * e + k, 3072 + 1024 * e, t, 16), p_(0, 128 + 64 * e, 192 + 64 * e), OP.max)
+                        tt(W(o + 64 * e, o + 64 * e + 64), W(2048 + 1024 * e + k, 3072 + 1024 * e, 16), p_(0, 128 + 64 * e, 192 + 64 * e), OP.max)
             for k in range(16):
-                o = 2048 * h + 128 * k
-                end = h == 1 and k == 15
-                mm(p_(1, 128 * h + k, 128 * h + 128, 16), t_("mx", o, o + 128, t), t_("G64", 0, 8), False, end, gk, "last" if end else "mid")
-        act(t_("keys", c=t), p_(1, 0, 256), AF.Copy)
-        ko = t_("keys", 1, 256, t, 2)
-        tt(t_("h1"), p_(1, 0, 256, 2), ko, OP.max)
-        tt(t_("l1"), p_(1, 0, 256, 2), ko, OP.min)
-        for a, b, n in (("1", "2", 128), ("2", "3", 64), ("3", "4", 32)):
-            he, ho, le, lo = t_("h" + a, 0, n, step=2), t_("h" + a, 1, n, step=2), t_("l" + a, 0, n, step=2), t_("l" + a, 1, n, step=2)
-            tt(t_("HL", 0, 16, t) if b == "4" else t_("h" + b), he, ho, OP.max)
-            tt(t_("mn" + b), he, ho, OP.min)
-            tt(t_("ml" + b), le, lo, OP.max)
-            tt(t_("HL", 16, 32, t) if b == "4" else t_("l" + b), t_("mn" + b), t_("ml" + b), OP.max)
-        HL = t_("HL", c=t)
-        cp(t_("HI", c=t), HL)
-        tt(t_("flg", c=t), HL, t_("nsB", c=t), OP.is_ge)
-        ts(t_("HA", c=t), t_("HI", c=t), 511, None, OP.bitwise_and)
-        tt(t_("thr", c=t), t_("HL", 16, 32, t), t_("nsB", 0, 16, t), OP.max)
-        tt(t_("KM", c=t), t_("HA", c=t), t_("flg", c=t), OP.mult)
-        tt(t_("kx", c=t), t_("KM", 0, 16, t), t_("KM", 16, 32, t), OP.max)
-        tt(t_("sm", c=t), t_("kx", c=t), t_("m0", c=t), OP.max)
-        ts(t_("si", c=t), t_("sm", c=t), -1.0, 256.0, OP.mult, OP.add)
-        ts(t_("sl", c=t), t_("si", c=t), 15, None, OP.bitwise_and)
-        tt(t_("awsl", 256, 512, t), ind(t_("sl", c=t), t_("bc")), t_("kidx"), OP.not_equal)
-        tt(t_("awsl", 0, 256, t), ind(t_("thr", c=t), t_("bc")), t_("keys", c=t), OP.is_gt)
-        for x in (2, 3, 0, 1):
-            mm(p_(4, 128 * x, 128 * x + 128), t_("awsl", 128 * x, 128 * x + 128, t), t_("I"), True, True)
-        mm(p_(1, 256, 512), t_("I"), t_("row16"), True, False)
-        for h in range(2):
-            w = t_("awsl", 256 + 128 * h, 384 + 128 * h, t)
-            if t:
-                mm(p_(1, 256 + 128 * h, 384 + 128 * h), w, t_("nIt", c=t), False, False)
-            mm(p_(1, 256 + 128 * h, 384 + 128 * h), w, t_("nD", c=h), False, h == 1)
-        act(t_("ns"), p_(1, 256, 512), AF.Identity, bias=float(t))
-        tt(t_("tb"), p_(4, 256, 512), t_("bg", c=t), OP.mult)
-        tt(ind(t_("btab"), wl), t_("tb"), t_("ns"), OP.add)
-        tt(t_("t1"), p_(4, 0, 256), t_("qg", c=t), OP.mult)
-        act(t_("t2"), p_(4, 256, 512), AF.Identity, bias=float(8 + t), scale=-float(8 + t))
-        tt(ind(t_("qtab"), wl), t_("t1"), t_("t2"), OP.max)
-        for j in range(8):
-            act(t_("Y", 32 * j, 32 * j + 32, t), t_("KM", c=t), AF.Copy, scale=t_("Gmf", j, j + 1))
+                o = 4096 + 2048 * h + 128 * k
+                mm(p_(kb, 1 + k, 136, 17), W(o, o + 128), t_("G64"), False, k == 15, gk, "last" if k == 15 else "mid")
+            keep(W(4096 + 2048 * h, 6144 + 2048 * h, 16), t_("z", 128 * h, 128 * h + 128, t))
+            o = 136 * h
+            runmax(t_("s12", o, o + 136), t_("d17"), p_(kb, 0, 136))
+            tt(t_("m", o + 1, o + 136), t_("s12", o, o + 135), p_(kb, 1, 136), OP.min)
+            runmax(t_("s12", 272 + o, 408 + o), t_("d17"), t_("m", o, o + 136))
+        HL = t_("s12", 16, 544, 0, 17)
+        KM = lambda a, b: t_("KM", a, b, t)
+        cp(t_("HI"), HL)
+        tt(t_("nf"), HL, t_("nsB", c=t), OP.is_le)
+        ts(t_("HA"), t_("HI"), 31, None, OP.bitwise_and)
+        lin("nfS", t_("nf"), -4096.0, 16.0)
+        tt(KM(0, 32), t_("HA"), t_("nfS"), OP.min)
+        tt(t_("kx"), KM(0, 16), KM(16, 32), OP.max)
+        tt(t_("sm"), t_("kx"), t_("qs", 15, 256, t, 16), OP.max)
+        ts(t_("sl"), t_("sm"), 15, None, OP.bitwise_and)
+        cp(KM(32, 48), t_("sl"))
+        cp(KM(48, 64), t_("sl"))
+        if "ca" in ON_S:
+            act(t_("ca"), KM(0, 16), AF.Relu, scale=17.0)
+        else:
+            ts(t_("ca"), KM(0, 16), 0.0, 17.0, OP.max, OP.mult)
+        ts(t_("cb"), KM(16, 32), 0.0, -144.0, OP.max, OP.add)
+        tt(KM(64, 80), t_("ca"), t_("cb"), OP.add)
+        for x in range(8):
+            if x < YV:
+                ts(y_(t, x, 64, 8, (0, 64)), KM(0, 80), t_("Gmf", x, x + 1), None, OP.mult, grp=("Y", t))
+            else:
+                act(y_(t, x, 64, 8, (0, 64)), KM(0, 80), AF.Copy, scale=t_("Gmf", x, x + 1), grp=("Y", t))
+        mm(p_(5, 0, 80), t_("I"), t_("ba"), True, False)
         for k in range(8):
-            mm(p_(5, 0, 32), t_("RB", 112 - 16 * k, 240 - 16 * k), t_("Y", k, 256, t, 8), k == 0, k == 7)
-        ts(t_("mz"), p_(5, 0, 32), 0.0, None, OP.is_equal)
-        tt(t_("bm"), t_("ba32"), p_(5, 0, 32), OP.subtract)
-        tt(t_("tm"), t_("mz"), t_("sp32"), OP.mult)
-        tt(t_("of"), t_("tm"), t_("bm"), OP.add)
-        for x in range(4):
-            cp(t_("al", 8 * x, 8 * x + 8, t), t_("of", x, 32, 0, 4))
-        act(t_("CZ", 4368, 4880, t), ind(t_("CZ", 0, 4368, t), t_("al", c=t)), AF.Copy)
-        a12, a1, a2 = t_("CZ", 4368, 4880, t), t_("CZ", 4368, 4624, t), t_("CZ", 4624, 4880, t)
-        for k in (768, 1536):
-            keep(t_("CZ", 4112 + k, 4368 + k, t), z)
-            keep(t_("CZ", 4368 + k, 4880 + k, t), a12)
-        mm(p_(6, 0, 512), t_("nI"), a12, True, False)
-        mm(p_(6, 0, 256), t_("I"), z, False, False)
-        mm(p_(6, 256, 512), t_("I"), z, False, True)
-        mm(p_(7, 0, 256), t_("I"), a1, True, False)
-        mm(p_(7, 0, 256), t_("nI"), a2, False, True)
-        act(t_("SG", 0, 512), p_(6, 0, 512), AF.Sign, bias=-0.5, scale=-1.0)
-        act(t_("SG", 512, 1024), p_(6, 0, 512), AF.Sign, bias=-0.5)
-        if t + 1 < STEPS:
-            act(t_("SG", 1024, 1280), p_(7, 0, 256), AF.Sign, bias=-0.5, scale=-1.0)
-            act(t_("SG", 1280, 1536), p_(7, 0, 256), AF.Sign, bias=-0.5)
-        else:
-            ts(t_("SG", 1024, 1280), p_(7, 0, 256), 0.0, -0.5, OP.is_lt, OP.add)
-            ts(t_("SG", 1280, 1536), p_(7, 0, 256), 0.0, -0.5, OP.is_gt, OP.add)
-        for r in range(16):
-            mm(p_(5, 64, 160), t_("EB", 15 - r, 143 - r), t_("SG", r, 1536, 0, 16), r == 0, r == 15)
-        ts(t_("TH"), p_(5, 64, 160), 1.0, 768.0, OP.is_ge, OP.mult)
-        tt(t_("KK", 0, 16), t_("TH", 0, 16), t_("TH", 16, 32), OP.add)
-        tt(t_("KK", 16, 48), t_("TH", 32, 64), t_("TH", 64, 96), OP.add)
-        tt(t_("KL"), t_("KK"), t_("C48"), OP.add)
+            mm(p_(5, 0, 80), t_("RB", 112 - 16 * k, 240 - 16 * k), y_(t, 8 * k, 8 * k + 8, 1, (0, 64)), False, k == 7)
+        ol = lambda k, m=1: t_("ol", 16 * k, 16 * (k + m), t)
+        cp(ol(0, 5), p_(5, 0, 80))
+        tt(t_("kb", 16, 48, t), t_("ordc"), p_(5, 0, 32), OP.add)
+        ts(t_("pen"), p_(5, 16, 32), 4096.0, 3 * WN, OP.is_ge, OP.mult)
+        tt(t_("kb", 32, 48, t), t_("kb", 32, 48, t), t_("pen"), OP.add)
+        tt(t_("ybk"), ind(t_("X2", 0, 4097), ol(2)), t_("bs", c=t), OP.min)
+        act(t_("blog", n, n + 256), t_("ybk"), AF.Abs, bias=float(-t))
+        tt(t_("q1"), ind(t_("T1"), ol(4)), qg, OP.min)
+        tt(t_("qlog", n, n + 256), ind(t_("T2", c=t), ol(3)), t_("q1"), OP.max)
+        win = W(0, 8192)
+        d1, d2 = t_("a12", 0, 256), t_("a12", 256, 512)
+        tt(d1, ind(win, ol(0)), z, OP.subtract)
+        tt(d2, ind(win, ol(1)), z, OP.subtract)
+        mm(p_(7, 0, 256), t_("I"), d1, True, False)
+        mm(p_(7, 0, 256), t_("nI"), d2, False, True)
+        for k, d in enumerate((d1, d2)):
+            act(t_("SG", 256 * k, 256 * k + 256), d, AF.Sigmoid, bias=-math.log(31.0), scale=-40.0)
+        act(t_("SG", 512, 768), p_(7, 0, 256), AF.Sigmoid, bias=-math.log(31.0), scale=40.0)
+        to_list(p_(7, 256, 304), "SG", 0, 768)
+        cnt = p_(7, 256, 304)
+        ts(t_("rn"), cnt, 12582912.0, 12582912.0, OP.add, OP.subtract)
+        ts(th_(3, 6), cnt, 9.0, WN, OP.is_ge, OP.mult)
+        lin("thr", t_("rn"), 31.0 / 32, 7.5 / 32)
+        tt(t_("dd"), t_("thr"), cnt, OP.subtract)
+        ts(th_(0, 3), t_("dd"), 0.0, WN, OP.is_ge, OP.mult)
+        tt(t_("KK"), th_(0, 6, 2), th_(1, 6, 2), OP.add)
+        tt(t_("KL"), t_("KK"), t_("kb", c=t), OP.add)
         k0, k1, k2 = t_("KL", 0, 16), t_("KL", 16, 32), t_("KL", 32, 48)
+        cross = t + 2 < STEPS
         tt(t_("mna"), k0, k1, OP.min)
-        tt(t_("mxa"), k0, k1, OP.max)
         tt(t_("FM", 0, 16), t_("mna"), k2, OP.min)
-        tt(t_("tta"), t_("mxa"), k2, OP.min)
-        tt(t_("FM", 16, 32), t_("mna"), t_("tta"), OP.max)
-        cp(t_("fml", c=t), t_("FM"))
-        win = t_("CZ", 4112, 6416, t)
-        if t + 2 < STEPS:
-            f, m = t_("fmb", 0, 256), t_("fmb", 256, 512)
-            act(t_("fmb"), ind(win, t_("fml", c=t)), AF.Copy)
-            act(t_("ff"), f, AF.Copy)
-            mm(p_(6, 0, 256), t_("I"), f, True, False)
-            mm(p_(6, 0, 256), t_("nI"), m, False, True)
-            mm(p_(7, 256, 512), t_("wSh"), z, True, False)
-            mm(p_(7, 256, 512), t_("wSl"), z, False, True)
-            cp(t_("bti", c=t), p_(7, 256, 512))
-            ts(t_("bit", c=t), t_("bti", c=t), 128, None, OP.bitwise_and)
-            tt(t_("tX"), p_(6, 0, 256), t_("bit", c=t), OP.mult)
-            mm(p_(6, 256, 512), t_("I"), m, True, False)
-            mm(p_(6, 256, 512), t_("Is"), t_("tX"), False, True)
-            act(t_("cb", c=t), p_(6, 256, 512), AF.Copy)
-            send(t_("cb", c=t), t + 2, (rank + 2) % n_ranks)
-        else:
-            act(t_("ff"), ind(win, t_("fml", 0, 16, t)), AF.Copy)
-        tt(ind(t_("itab"), wl), t_("im1", c=t), t_("ff"), OP.max)
+        if cross:
+            tt(t_("mxa"), k0, k1, OP.max)
+            tt(t_("tta"), t_("mxa"), k2, OP.min)
+            tt(t_("FM", 16, 32), t_("mna"), t_("tta"), OP.max)
+        w = 32 if cross else 16
+        ts(t_("FA", 0, w), t_("FM", 0, w), 8191, None, OP.bitwise_and)
+        cp(t_("fml", 0, w, t), t_("FA", 0, w))
+        f, m = ind(win, t_("fml", 0, 16, t)), ind(win, t_("fml", 16, 32, t))
+        tt(t_("ilog", n, n + 256), f, im1, OP.max)
+        if cross:
+            act(t_("Bm", c=t), ind(t_("Bt"), t_("vl", 16, 32, t)), AF.Copy)
+            tt(t_("cx", 0, 256, t), f, t_("Bm", c=t), OP.min)
+            tt(t_("cx", 256, 512, t), m, t_("Bm", c=t), OP.subtract)
+            send([t_("cx", 0, 256, t), t_("cx", 256, 512, t)], t + 2, (rank + 2) % n_ranks)
 
+    host(0)
     for t in range(STEPS):
+        part.update(name="", runs={}, last=None)
         step(t)
-    act(t_("yi", 0, 512), t_("itab", 0, 512), AF.Copy)
-    cp(t_("yi", 512, 1024), t_("itab", 512, 1024))
+    part.update(name="end.", runs={}, last=None)
     for k in range(2):
-        store("si%d" % k, T.yimm[:, 512 * k:512 * k + 512], t_("yi", 512 * k, 512 * k + 512))
-    for k, b in ((0, 4), (1, 1)):
-        act(p_(b, 0, 512), t_("qtab", 512 * k, 512 * k + 512), AF.Copy, scale=4096.0)
-        tt(t_("yb", 512 * k, 512 * k + 512), t_("btab", 512 * k, 512 * k + 512), p_(b, 0, 512), OP.add)
-        store("sb%d" % k, T.ybank[:, 512 * k:512 * k + 512], t_("yb", 512 * k, 512 * k + 512))
+        a, b, lst = 512 * k, 512 * k + 512, t_("plF", 32 * k, 32 * k + 32)
+        act(t_("q4", a, b), ind(t_("qlog"), lst), AF.Copy, scale=4096.0)
+        tt(t_("yb", a, b), ind(t_("blog"), lst), t_("q4", a, b), OP.add)
+        store("sb%d" % k, T.ybank[:, a:b], t_("yb", a, b))
+        if k:
+            cp(t_("yi", a, b), ind(t_("ilog"), lst))
+        else:
+            act(t_("yi", a, b), ind(t_("ilog"), lst), AF.Copy)
+        store("si%d" % k, T.yimm[:, a:b], t_("yi", a, b), "s" if k == 0 else "y")
 
     n = len(ops)
     for i in range(n):
@@ -622,7 +646,7 @@ def rank_program(g, core, T, topo):
     prio = [0.0] * n
     for j in range(n - 1, -1, -1):
         prio[j] = max([lag.get(j, ops[j]["cost"])] + [l + prio[i] for i, l in succ[j]])
-    order = best_order(n, [o["q"] for o in ops], [o["cost"] for o in ops], succ, [prio[i] + BIAS.get(ops[i]["tag"], 0.0) for i in range(n)], 3)[0]
+    order = list_schedule(n, [o["q"] for o in ops], [o["cost"] for o in ops], succ, [len(e) for e in edges], [prio[i] + BIAS.get(ops[i]["name"], 0.0) for i in range(n)])[0]
 
     eng = {"v": g.vector, "s": g.scalar, "p": g.tensor, "g": g, "y": g.sync}
     total = {}

@@ -10,16 +10,16 @@ STEPS = 6
 LOG = 1024 + 256 * STEPS
 TILES = {
     "z": (256, "bfloat16", 6), "bt": (256, "bfloat16", 1), "geno_s": (4096, "bfloat16", 1), "bk": (1024, "int32", 1), "wti": (1, "int32", 1),
-    "blog": (LOG, "float32", 1), "qlog": (LOG, "bfloat16", 1), "ilog": (LOG, "bfloat16", 1), "ptab": (1040, "float32", 1), "psrc": (256, "float32", 5),
+    "blog": (LOG, "float32", 1), "qlog": (LOG, "bfloat16", 1), "ilog": (LOG, "bfloat16", 1), "ptab": (1040, "float32", 1), "psrc": (256, "float32", 6),
     "EW": (144, "bfloat16", 1), "ptb": (1040, "bfloat16", 1), "psb": (256, "bfloat16", 1), "hb": (16, "float32", 2), "rn": (48, "float32", 1), "thr": (48, "float32", 1), "dd": (48, "float32", 1),
-    "W": (8192, "bfloat16", 2), "bki": (1024, "int32", 1), "q192": (1024, "bfloat16", 1),
+    "W": (8192, "bfloat16", 2), "Iq": (128, "bfloat16", 1), "q192": (1024, "bfloat16", 1),
     "X2": (4112, "bfloat16", 1), "T1": (289, "bfloat16", 1), "T2": (32, "bfloat16", 6), "Bt": (1024, "bfloat16", 1),
     "q4": (1024, "float32", 1), "yb": (1024, "float32", 1), "yi": (1024, "bfloat16", 1), "plF": (64, "uint16", 1),
     "pI": (1, "int32", 1), "pM": (1, "int32", 1), "pG": (1, "int32", 1), "p8": (1, "int32", 1), "col": (1, "float32", 16),
     "ic": (256, "float32", 1), "icb": (256, "bfloat16", 1), "icg": (128, "float32", 1), "lnO": (16, "float32", 1), "nr": (256, "bfloat16", 1),
-    "I": (128, "bfloat16", 1), "nI": (128, "bfloat16", 1), "I16": (128, "bfloat16", 1), "IB": (136, "bfloat16", 1), "XG": (128, "float16", 1),
+    "I": (128, "bfloat16", 1), "nI": (128, "bfloat16", 1), "I16": (128, "bfloat16", 1), "IB": (136, "bfloat16", 1), "XG": (128, "bfloat16", 1),
     "Gmf": (8, "float32", 1), "Gm": (8, "bfloat16", 1), "nGm": (8, "bfloat16", 1), "G64": (8, "bfloat16", 1), "G32": (8, "bfloat16", 1),
-    "EB": (144, "bfloat16", 1), "wE": (144, "float16", 1), "RB": (240, "bfloat16", 1), "LR": (2048, "float16", 1),
+    "EB": (144, "bfloat16", 1), "wE": (144, "float16", 1), "RB": (240, "bfloat16", 1), "LR": (2048, "bfloat16", 1),
     "eq": (16, "float32", 1), "le": (16, "float32", 1), "ne": (16, "float32", 1), "hic": (16, "float32", 1),
     "C16": (256, "bfloat16", 1), "C17": (136, "bfloat16", 1), "d16": (256, "bfloat16", 1), "d17": (136, "bfloat16", 1),
     "ones": (128, "bfloat16", 1), "c16": (16, "bfloat16", 1), "m1": (256, "bfloat16", 1), "ba": (80, "bfloat16", 1), "ordc": (32, "float32", 1),
@@ -50,19 +50,37 @@ for _k in range(2):
     SCRATCH["Yc%d" % _k] = ("sbuf", [128, 10, 64], "bfloat16")
 SCRATCH["TH3"] = ("sbuf", [128, 6, 16], "float32")
 LOADS = ["bites", "next", "wt", "bank", "immun", "geno"]
-STORES = ["sg", "sb0", "sb1", "si0", "si1"]
+STORES = ["sg", "sb0", "sb1", "sb2", "sb3", "si0", "si1"]
 SEMAPHORES = ["qv", "qs", "qp", "qg", "rl"] + ["arr%d" % t for t in range(1, STEPS)] + ["ld_" + n for n in LOADS] + ["st_" + n for n in STORES]
 
 
-BIAS = {'pP2ones': -4, 'pP3LR': 4, 'pP4EW': 1, 'pP5I': 7, 'pP7EB': -1, 'pP7I': -5, 'pre.gnr': 8, 'pre.gpI': 6, 'pre.sX2': 8, 'pre.sba': -31, 'pre.skb': -2, 'pre.snI': 5, 'pre.spsb': 50, 'pre.spsrc': 32, 'pre.vEB': 2, 'pre.vGmf': 19, 'pre.vT2': 41, 'pre.vac': 20, 'pre.vcol': 26, 'pre.vcol3': 6, 'pre.vcol4': 20, 'pre.vcol5': 6, 'pre.vcol6': 10, 'pre.vcol7': 11, 'pre.veq': 4, 'pre.vicg': -7, 'pre.vne': 11, 'pre.vp8': 3, 'pre.vp8e': 12, 'pre.vp8f': 26, 'pre.vpM': 4, 'pre.vq192': -8, 'pre.vwt1': 4, 'sSG': -9, 'sW': 3, 'sptab': -15, 'sqg': 5, 'vA': 11, 'vKK': -17, 'vVV': -6, 'vYc0': 3, 'vkb': -7, 'vkb2': -4, 'vkx': 2, 'vnsB': 10, 'vol': 7, 'vpl': -1, 'vvh': 5, 'vcx': 12, 'vsk': 13, 'pP3wE': -2, 'pP1I': 4, 'pre.sptab': 4, 'vE': 3, 'vsq': 6, 'vybk': 2, 'pre.vpw': 25, 'vmna': -1}
 COST = {"us": 0.00083 * 1.25, "ps": 0.00071 * 1.25, "gather": 1.56, "scatter": 3.8, "wake": 0.08, "link": 5.5}
 LOOK = 0.3
-VG = [512, 256, 256, 256, 256, 512]
+PERIOD = 14.3
+TAIL = 9.5
+FIRM = True
+DUE = {'pP6W2': -5.8, 'pre.sX2': -19.3, 'pre.spsrc': -0.5, 'pre.vE': -6.1, 'pre.vRB': -12.2, 'pre.vT2': -7.5, 'sBm': 0.3, 'sSG2': 0.5, 'sbs': -4.1, 'sptab': -1.2, 'vboff': -6.8, 'vqs': -6.1, 'vsq': -2.3, 'vybk': -0.2, 'pre.vEW': -0.9, 'pre.vpM': -29.1, 'vE': 5.6, 'vpen': 0.3, 'pre.vhb': -21.3, 'sqg': -13.1, 'pre.pP1Iq': -14.7, 'pre.vEB': -23.1, 'pre.vX2': -5.0, 'vplF': 3.7}
+VG = [768, 256, 256, 256, 256, 640]
 PARTS = [[("s", 0, 64), ("s", 64, 128), ("s", 128, 192), ("s", 192, 256 - v // 16)] + ([("v", 256 - v // 16, 256)] if v else []) for v in VG]
 NFL = "v"
+SCV = ()
+YI = "ssvs"
+A2 = "s"
+LAST = "v"
 ON_S = ()
-XS = 12
+XS = 7
 YV = 4
+
+
+def urgency(ops, succ, lag, due):
+    at = [0.0] * len(ops)
+    for j in range(len(ops) - 1, -1, -1):
+        o = ops[j]
+        at[j] = min([PERIOD * (STEPS - 1) + TAIL - lag.get(j, o["cost"])] + [at[i] - l for i, l in succ[j]])
+        if o["name"] in due:
+            named = PERIOD * o["step"] + due[o["name"]] + 1e-4 * j
+            at[j] = min(at[j], named) if FIRM or o["step"] == STEPS - 1 else named
+    return [-x for x in at]
 
 
 def list_schedule(n, que, cost, succ, need, prio):
@@ -156,7 +174,7 @@ def rank_program(g, core, T, topo):
     ops = []
     last = {}
     edges = []
-    part = {"name": "pre.", "runs": {}, "last": None}
+    part = {"name": "pre.", "runs": {}, "last": None, "step": 0}
     US, PS = COST["us"], COST["ps"]
 
     def t_(name, a=0, b=None, c=0, step=1):
@@ -222,8 +240,8 @@ def rank_program(g, core, T, topo):
         if k != part["last"]:
             part["runs"][k] = part["runs"].get(k, 0) + 1
         part["last"] = k
-        run = 1 if k in ("vW", "pP1W") else part["runs"][k]
-        ops.append({"q": q, "cost": cost, "emit": emit, "sem": sem, "inc": inc, "tag": tag, "name": part["name"] + k + (str(run) if run > 1 else "")})
+        run = 1 if k in ("vW", "pP1W", "vptab", "sptab") else part["runs"][k]
+        ops.append({"q": q, "cost": cost, "emit": emit, "sem": sem, "inc": inc, "step": part["step"], "name": part["name"] + k + (str(run) if run > 1 else "")})
         edges.append(ed)
         return i
 
@@ -256,7 +274,8 @@ def rank_program(g, core, T, topo):
 
     def ts(out, a, s1, s2, o1, o2=None, grp=None):
         f = (lambda: g.vector.tensor_scalar(raw(out), raw(a), raw(s1), raw(s2), o1)) if o2 is None else (lambda: g.vector.tensor_scalar(raw(out), raw(a), raw(s1), raw(s2), o1, o2))
-        return add("v", vcost(out["n"], "ts", [out, a]), f, rgs(a, s1, s2), out["rg"], "qv", 1, grp=grp)
+        r, w = outrg(out)
+        return add("v", vcost(out["n"], "ts", [out, a]), f, rgs(a, s1, s2) + r, w, "qv", 1, grp=grp)
 
     def cp(out, a):
         r, w = outrg(out)
@@ -300,8 +319,11 @@ def rank_program(g, core, T, topo):
     def fill(out, val):
         return iota(out, [[0, out["n"]]], val)
 
+    def select(out, a, pattern, op, other, base, cm):
+        return add("g", 0.17 + 2 * out["n"] * US, lambda: g.affine_select(raw(out), raw(a), pattern, op, other, base, cm), rgs(a), out["rg"], "qg", 1)
+
     def keep(out, a):
-        return add("g", 0.17 + 2 * out["n"] * US, lambda: g.affine_select(raw(out), raw(a), [[0, out["n"]]], OP.is_ge, 0.0, 0, 0), rgs(a), out["rg"], "qg", 1)
+        return select(out, a, [[0, out["n"]]], OP.is_ge, 0.0, 0, 0)
 
     def load(name, out, q="y"):
         eng = g.sync if q == "y" else g.scalar
@@ -315,8 +337,14 @@ def rank_program(g, core, T, topo):
         i = add(q, 0.1, lambda: eng.dma_start(dst, raw(src)), src["rg"], [("out" + tag, 0, 1)], "st_" + tag, 16)
         lag[i] = 2.0 + src["n"] * src["by"] * 0.0005
 
-    for name, dst, tm in (("bites", t_("z"), 2.6), ("wt", t_("wti"), 2.5), ("bank", t_("bk"), 4.5), ("next", t_("bt"), 4.0), ("geno", t_("geno_s"), 7.0), ("immun", t_("ilog", 0, 1024), 7.0)):
-        lag[load(name, dst, "s" if name in ("wt", "immun", "next") else "y")] = tm
+    prev = None
+    for name, dst, tm in (("wt", t_("wti"), 2.5), ("bites", t_("z"), 2.6), ("bank", t_("bk"), 4.2), ("geno", t_("geno_s"), 6.8), ("next", t_("bt"), 7.0), ("immun", t_("ilog", 0, 1024), 7.6)):
+        i = load(name, dst, "s" if name == "wt" else "y")
+        if name != "wt":
+            if prev is not None:
+                edges[i][prev] = 0
+            prev = i
+        lag[i] = tm
 
     def send(srcs, t, dst_rank):
         dst = T.cores[dst_rank]
@@ -339,7 +367,7 @@ def rank_program(g, core, T, topo):
     ic = lambda n: t_("ic", 0, n)
     iota(t_("pI"), [[0, 1]], 0, 1, True)
     iota(t_("ic"), [[1, 256]])
-    iota(t_("icg"), [[1, 8], [0, 16]])
+    fill(t_("ones"), 1)
     send([t_("bt")], 1, (rank + 1) % n_ranks)
     iota(t_("C16"), [[0, 16], [-1, 16]], 16)
     iota(t_("C17"), [[0, 8], [-1, 17]], 17)
@@ -362,12 +390,20 @@ def rank_program(g, core, T, topo):
     ts(WG, WF, 2047.5, -4096.0, OP.is_gt, OP.mult)
     tt(WS, WF, WG, OP.add)
     ts(t_("wE"), t_("EB"), WS, None, OP.mult)
-    ts(t_("I"), ic(128), P, None, OP.is_equal)
-    ts(t_("bki"), t_("bk"), 4095, None, OP.bitwise_and)
-    cp(t_("blog", 0, 1024), t_("bki"))
-    ts(t_("q192"), t_("bk"), 1.0 / 4096, 191.5 + 1.0 / 8192, OP.mult, OP.add)
-    act(t_("qlog", 0, 1024), t_("q192"), AF.Identity, bias=-192.0)
-    for name, f in (("Gm", 1.0), ("nGm", -1.0), ("G64", 64.0), ("G32", -32.0)):
+    select(t_("I"), t_("ones"), [[-1, 128]], OP.is_equal, 0.0, 0, 1)
+    quarters = [(a, a + 256) for a in range(0, 1024, 256)]
+    act(t_("Iq"), t_("I"), AF.Copy, scale=-4096.0)
+    for a, b in quarters:
+        ts(t_("q192", a, b), t_("bk", a, b), 1.0 / 4096, 191.5 + 1.0 / 8192, OP.mult, OP.add)
+    for a, b in quarters:
+        act(t_("qlog", a, b), t_("q192", a, b), AF.Identity, bias=-192.0)
+    for k, (a, b) in enumerate(quarters):
+        mm(p_((5, 7, 1, 6)[k], 0, 256), t_("Iq"), t_("qlog", a, b), True, True)
+    for k, (a, b) in enumerate(quarters):
+        tt(t_("blog", a, b), t_("bk", a, b), p_((5, 7, 1, 6)[k], 0, 256), OP.add)
+    i = act(t_("Gm"), t_("Gmf"), AF.Sigmoid, bias=-100.0, scale=200.0)
+    ops[i]["cost"] += 1.6
+    for name, f in (("nGm", -1.0), ("G64", 64.0), ("G32", -32.0)):
         act(t_(name), t_("Gmf"), AF.Copy, scale=f)
     act(t_("nI"), t_("I"), AF.Copy, scale=-1.0)
     act(t_("I16"), t_("I"), AF.Copy, scale=-16.0)
@@ -379,7 +415,6 @@ def rank_program(g, core, T, topo):
     fill(t_("d17"), 0)
     fill(t_("d17", 0, 136, step=17), -1048576)
     fill(t_("m", 0, 272, step=136), 0)
-    fill(t_("ones"), 1)
     fill(t_("c16"), 16)
     for c in range(2):
         ms(t_("ac", 16, 17, c), 304.0 / 128)
@@ -389,9 +424,9 @@ def rank_program(g, core, T, topo):
     ts(t_("ne"), ic(16), PM, 16384.0, OP.not_equal, OP.mult)
     fill(t_("RB"), 0)
     ts(t_("RB", 112, 128), t_("eq"), -1.0, None, OP.mult)
-    ts(t_("icg"), t_("icg"), PG, None, OP.is_equal)
-    ts(t_("XG"), t_("I"), -2.0, None, OP.mult)
-    tt(t_("XG"), t_("XG"), t_("icg"), OP.add)
+    select(t_("XG"), t_("ones"), [[-16, 8], [0, 16]], OP.is_ge, 0.0, 0, 1)
+    select(t_("XG"), t_("XG"), [[16, 8], [0, 16]], OP.is_ge, 0.0, 15, -1)
+    select(t_("XG"), t_("XG"), [[-1, 128]], OP.not_equal, -1.0, 0, 1)
     for r in range(16):
         ts(t_("LR", 128 * r, 128 * r + 128), t_("XG"), t_("eq", r, r + 1), t_("le", r, r + 1), OP.min, OP.mult)
     ts(JK, PM, 1024.0, None, OP.add)
@@ -433,18 +468,19 @@ def rank_program(g, core, T, topo):
     ts(t_("hb", c=1), t_("hb"), 200.0, -100.0, OP.mult, OP.add)
     for k in range(4):
         act(t_("ptab", 256 * k, 256 * k + 256), t_("Bt", 0, 256), AF.Identity, bias=t_("hb", k, k + 1), scale=L1)
-    for t in range(STEPS - 1):
+    for t in range(STEPS - (LAST == "v")):
         act(t_("psrc", c=t), t_("Bt", 0, 256), AF.Identity, bias=t_("hb", 4 + t, 5 + t, 1), scale=L2)
-    act(t_("psb"), t_("Bt", 0, 256), AF.Identity, bias=t_("hb", 3 + STEPS, 4 + STEPS), scale=L1)
+    if LAST == "v":
+        act(t_("psb"), t_("Bt", 0, 256), AF.Identity, bias=t_("hb", 3 + STEPS, 4 + STEPS), scale=L1)
     ts(t_("p8e", c=1), ic(8), t_("p8f"), None, OP.is_equal)
     tt(t_("p8e", c=1), t_("p8e", c=1), t_("pw"), OP.mult)
     red(W1, t_("p8e", c=1))
     ts(H1, H1, 255.0 * 64, 1.0, OP.mult, OP.add)
     ts(t_("EW"), t_("EB"), W1, H1, OP.mult, OP.mult)
 
-    def to_list(out, src, a, b, wts="EB"):
+    def to_list(out, src, a, b, wts="EB", first=True):
         for r in range(16):
-            mm(out, t_(wts, 15 - r, 143 - r), t_(src, a + r, b, 0, 16), r == 0, r == 15)
+            mm(out, t_(wts, 15 - r, 143 - r), t_(src, a + r, b, 0, 16), first and r == 0, r == 15)
 
     def host(t):
         for r in range(16):
@@ -465,9 +501,9 @@ def rank_program(g, core, T, topo):
         for r in range(16):
             mm(p_(3, r, 256, 16), t_("LR", 128 * r, 128 * r + 128), t_("vh", c=t), True, True)
         ts(t_("E"), p_(3, 0, 256), 0.0, 4096.0, OP.is_equal, OP.mult)
-        to_list(p_(3, 272, 288), "E", 0, 256)
-        tt(t_("wt1"), t_("VV", 0, 16, t), p_(3, 272, 288), OP.add)
-        ts(t_("wl", 0, 32, t, 2), t_("wt1"), JK, None, OP.min)
+        mm(p_(3, 272, 288), t_("I"), t_("vh", c=t), True, False)
+        to_list(p_(3, 272, 288), "E", 0, 256, first=False)
+        ts(t_("wl", 0, 32, t, 2), p_(3, 272, 288), -1.0, JK, OP.add, OP.min)
 
     def step(t):
         z = t_("z", c=t)
@@ -476,7 +512,7 @@ def rank_program(g, core, T, topo):
         W = lambda a, b, s=1: t_("W", a, b, t, s)
         mm(p_(0, 0, 256), t_("I"), z, True, True)
         for h in range(2):
-            cp(t_("boff", 128 * h, 128 * h + 128, t), ind(t_("blog", 0, n) if t else t_("bki"), t_("pl" if t else "vl", 8 * h, 8 * h + 8, t)))
+            cp(t_("boff", 128 * h, 128 * h + 128, t), ind(t_("blog", 0, n), t_("pl" if t else "vl", 8 * h, 8 * h + 8, t)))
         for q, a, b in PARTS[t]:
             if q == "s":
                 act(W(16 * a, 16 * b), ind(t_("geno_s"), t_("boff", a, b, t)), AF.Copy)
@@ -515,12 +551,21 @@ def rank_program(g, core, T, topo):
             red(t_("A", c=t), p_(2, 304, 322))
         if t + 1 < STEPS:
             for j in range(15, -1, -1):
-                act(ind(t_("ptab"), t_("wl", 2 * j, 2 * j + 1, t)), t_("psrc", 16 * j, 16 * j + 16, t), AF.Sigmoid)
+                to, src = ind(t_("ptab"), t_("wl", 2 * j, 2 * j + 1, t)), t_("psrc", 16 * j, 16 * j + 16, t)
+                if j in SCV:
+                    ts(to, src, 0.005, 0.5, OP.mult, OP.add)
+                else:
+                    act(to, src, AF.Sigmoid)
             host(t + 1)
         else:
-            act(t_("ptb", 0, 1024), t_("ptab", 0, 1024), AF.Copy)
-            for j in range(15, -1, -1):
-                cp(ind(t_("ptb"), t_("wl", 2 * j, 2 * j + 1, t)), t_("psb", 16 * j, 16 * j + 16))
+            if LAST == "v":
+                keep(t_("ptb", 0, 1024), t_("ptab", 0, 1024))
+                for j in range(15, -1, -1):
+                    cp(ind(t_("ptb"), t_("wl", 2 * j, 2 * j + 1, t)), t_("psb", 16 * j, 16 * j + 16))
+            else:
+                for j in range(15, -1, -1):
+                    act(ind(t_("ptab"), t_("wl", 2 * j, 2 * j + 1, t)), t_("psrc", 16 * j, 16 * j + 16, t), AF.Sigmoid)
+                keep(t_("ptb", 0, 1024), t_("ptab", 0, 1024))
             to_list(p_(4, 64, 128), "ptb", 0, 1024, "EW")
             cp(t_("plF"), p_(4, 64, 128))
         for h in range(2):
@@ -529,13 +574,10 @@ def rank_program(g, core, T, topo):
             mm(p_(kb, 0, 136), nfl(h), t_("IB"), False, False, gk, "mid")
             for k in range(16):
                 mm(p_(kb, 1 + k, 136, 17), W(2048 * h + k, 2048 * h + 2048, 16), t_("G32"), False, False, gk, "mid")
-            for k in range(16):
-                o = 4096 + 2048 * h + 128 * k
-                if h == 0:
-                    tt(W(o, o + 128), W(k, 2048, 16), p_(0, 0, 128), OP.max)
-                else:
-                    for e in range(2):
-                        tt(W(o + 64 * e, o + 64 * e + 64), W(2048 + 1024 * e + k, 3072 + 1024 * e, 16), p_(0, 128 + 64 * e, 192 + 64 * e), OP.max)
+            for e in range(2):
+                for k in range(16):
+                    o, a = 4096 + 2048 * h + 128 * k + 64 * e, 128 * h + 64 * e
+                    tt(W(o, o + 64), W(16 * a + k, 16 * a + 1024, 16), p_(0, a, a + 64), OP.max)
             for k in range(16):
                 o = 4096 + 2048 * h + 128 * k
                 mm(p_(kb, 1 + k, 136, 17), W(o, o + 128), t_("G64"), False, k == 15, gk, "last" if k == 15 else "mid")
@@ -582,18 +624,27 @@ def rank_program(g, core, T, topo):
         win = W(0, 8192)
         d1, d2 = t_("a12", 0, 256), t_("a12", 256, 512)
         tt(d1, ind(win, ol(0)), z, OP.subtract)
-        tt(d2, ind(win, ol(1)), z, OP.subtract)
-        mm(p_(7, 0, 256), t_("I"), d1, True, False)
-        mm(p_(7, 0, 256), t_("nI"), d2, False, True)
-        for k, d in enumerate((d1, d2)):
-            act(t_("SG", 256 * k, 256 * k + 256), d, AF.Sigmoid, bias=-math.log(31.0), scale=-40.0)
-        act(t_("SG", 512, 768), p_(7, 0, 256), AF.Sigmoid, bias=-math.log(31.0), scale=40.0)
-        to_list(p_(7, 256, 304), "SG", 0, 768)
-        cnt = p_(7, 256, 304)
+        act(t_("SG", 0, 256), d1, AF.Sigmoid, bias=-math.log(31.0), scale=-40.0)
+        if A2 == "v":
+            tt(d2, ind(win, ol(1)), z, OP.subtract)
+            mm(p_(7, 0, 256), t_("I"), d1, True, False)
+            mm(p_(7, 0, 256), t_("nI"), d2, False, True)
+            act(t_("SG", 256, 512), d2, AF.Sigmoid, bias=-math.log(31.0), scale=-40.0)
+            act(t_("SG", 512, 768), p_(7, 0, 256), AF.Sigmoid, bias=-math.log(31.0), scale=40.0)
+        else:
+            act(d2, ind(win, ol(1)), AF.Copy)
+            for k in range(2):
+                mm(p_(7, 256 * k, 256 * k + 256), t_("I"), z, k == 0, False)
+            for k in range(2):
+                mm(p_(7, 256 * k, 256 * k + 256), t_("nI"), d2, False, False)
+            mm(p_(7, 256, 512), t_("I"), d1, False, True)
+            act(t_("SG", 256, 768), p_(7, 0, 512), AF.Sigmoid, bias=-math.log(31.0), scale=40.0)
+        to_list(p_(5, 256, 304), "SG", 0, 768)
+        cnt = p_(5, 256, 304)
         ts(t_("rn"), cnt, 12582912.0, 12582912.0, OP.add, OP.subtract)
         ts(th_(3, 6), cnt, 9.0, WN, OP.is_ge, OP.mult)
-        lin("thr", t_("rn"), 31.0 / 32, 7.5 / 32)
-        tt(t_("dd"), t_("thr"), cnt, OP.subtract)
+        ts(t_("thr"), cnt, 32.0 / 31, -7.5 / 31, OP.mult, OP.add)
+        tt(t_("dd"), t_("rn"), t_("thr"), OP.subtract)
         ts(th_(0, 3), t_("dd"), 0.0, WN, OP.is_ge, OP.mult)
         tt(t_("KK"), th_(0, 6, 2), th_(1, 6, 2), OP.add)
         tt(t_("KL"), t_("KK"), t_("kb", c=t), OP.add)
@@ -618,19 +669,20 @@ def rank_program(g, core, T, topo):
 
     host(0)
     for t in range(STEPS):
-        part.update(name="", runs={}, last=None)
+        part.update(name="", runs={}, last=None, step=t)
         step(t)
     part.update(name="end.", runs={}, last=None)
-    for k in range(2):
-        a, b, lst = 512 * k, 512 * k + 512, t_("plF", 32 * k, 32 * k + 32)
+    for k, (a, b) in enumerate(quarters):
+        lst = t_("plF", a // 16, b // 16)
         act(t_("q4", a, b), ind(t_("qlog"), lst), AF.Copy, scale=4096.0)
         tt(t_("yb", a, b), ind(t_("blog"), lst), t_("q4", a, b), OP.add)
         store("sb%d" % k, T.ybank[:, a:b], t_("yb", a, b))
-        if k:
+        if YI[k] == "v":
             cp(t_("yi", a, b), ind(t_("ilog"), lst))
         else:
             act(t_("yi", a, b), ind(t_("ilog"), lst), AF.Copy)
-        store("si%d" % k, T.yimm[:, a:b], t_("yi", a, b), "s" if k == 0 else "y")
+        if k % 2:
+            store("si%d" % (k // 2), T.yimm[:, a - 256:b], t_("yi", a - 256, b))
 
     n = len(ops)
     for i in range(n):
@@ -639,14 +691,11 @@ def rank_program(g, core, T, topo):
     succ = [[] for _ in range(n)]
     for i in range(n):
         for j, w in edges[i].items():
-            l = lag.get(j, ops[j]["cost"]) + (COST["wake"] if w else 0.0)
+            l = lag.get(j, ops[j]["cost"]) + COST["wake"] if w else ops[j]["cost"]
             if "proxy" in ops[i]:
                 l = COST["link"]
             succ[j].append((i, l))
-    prio = [0.0] * n
-    for j in range(n - 1, -1, -1):
-        prio[j] = max([lag.get(j, ops[j]["cost"])] + [l + prio[i] for i, l in succ[j]])
-    order = list_schedule(n, [o["q"] for o in ops], [o["cost"] for o in ops], succ, [len(e) for e in edges], [prio[i] + BIAS.get(ops[i]["name"], 0.0) for i in range(n)])[0]
+    order = list_schedule(n, [o["q"] for o in ops], [o["cost"] for o in ops], succ, [len(e) for e in edges], urgency(ops, succ, lag, DUE))[0]
 
     eng = {"v": g.vector, "s": g.scalar, "p": g.tensor, "g": g, "y": g.sync}
     total = {}

@@ -4,33 +4,35 @@ from concourse.bass import DstId, RemoteDMATransfer
 
 OP = AluOpType
 AF = ActivationFunctionType
-BIG = 65536.0
+BIG = 131072.0
+Q0 = 192.0
 WN, WO = 32768.0, 8192.0
 STEPS = 6
 LOG = 1024 + 256 * STEPS
 TILES = {
-    "z": (256, "bfloat16", 6), "bt": (256, "bfloat16", 1), "geno_s": (4096, "bfloat16", 1), "bk": (1024, "int32", 1), "wti": (1, "int32", 1),
+    "z": (256, "bfloat16", 7), "bk": (1024, "int32", 1), "wti": (1, "int32", 1),
+    "T1a": (272, "bfloat16", 1), "LR": (2048, "bfloat16", 1), "Bt": (1024, "bfloat16", 1), "C16": (256, "bfloat16", 1), "d16": (256, "bfloat16", 1),
+    "RB": (240, "bfloat16", 1), "T1b": (272, "bfloat16", 1), "X2": (2064, "bfloat16", 1), "geno_s": (4096, "bfloat16", 1), "W": (8192, "bfloat16", 2),
     "blog": (LOG, "float32", 1), "qlog": (LOG, "bfloat16", 1), "ilog": (LOG, "bfloat16", 1), "ptab": (1040, "float32", 1), "psrc": (256, "float32", 6),
     "EW": (144, "bfloat16", 1), "ptb": (1040, "bfloat16", 1), "psb": (256, "bfloat16", 1), "hb": (16, "float32", 2), "rn": (48, "float32", 1), "thr": (48, "float32", 1), "dd": (48, "float32", 1),
-    "W": (8192, "bfloat16", 2), "Iq": (128, "bfloat16", 1), "q192": (1024, "bfloat16", 1),
-    "X2": (4112, "bfloat16", 1), "T1": (289, "bfloat16", 1), "T2": (32, "bfloat16", 6), "Bt": (1024, "bfloat16", 1),
+    "Iq": (128, "bfloat16", 1), "T2": (32, "bfloat16", 6), "cq": (256, "bfloat16", 1),
     "q4": (1024, "float32", 1), "yb": (1024, "float32", 1), "yi": (1024, "bfloat16", 1), "plF": (64, "uint16", 1),
-    "pI": (1, "int32", 1), "pM": (1, "int32", 1), "pG": (1, "int32", 1), "p8": (1, "int32", 1), "col": (1, "float32", 16),
-    "ic": (256, "float32", 1), "icb": (256, "bfloat16", 1), "icg": (128, "float32", 1), "lnO": (16, "float32", 1), "nr": (256, "bfloat16", 1),
-    "I": (128, "bfloat16", 1), "nI": (128, "bfloat16", 1), "I16": (128, "bfloat16", 1), "IB": (136, "bfloat16", 1), "XG": (128, "bfloat16", 1),
-    "Gmf": (8, "float32", 1), "Gm": (8, "bfloat16", 1), "nGm": (8, "bfloat16", 1), "G64": (8, "bfloat16", 1), "G32": (8, "bfloat16", 1),
-    "EB": (144, "bfloat16", 1), "wE": (144, "float16", 1), "RB": (240, "bfloat16", 1), "LR": (2048, "bfloat16", 1),
-    "eq": (16, "float32", 1), "le": (16, "float32", 1), "ne": (16, "float32", 1), "hic": (16, "float32", 1),
-    "C16": (256, "bfloat16", 1), "C17": (136, "bfloat16", 1), "d16": (256, "bfloat16", 1), "d17": (136, "bfloat16", 1),
-    "ones": (128, "bfloat16", 1), "c16": (16, "bfloat16", 1), "m1": (256, "bfloat16", 1), "ba": (80, "bfloat16", 1), "ordc": (32, "float32", 1),
-    "k1": (289, "bfloat16", 1), "k2": (289, "bfloat16", 1), "pw": (8, "float32", 1), "p8e": (8, "float32", 2), "p8f": (1, "float32", 1), "xi": (256, "int32", 1), "xj": (256, "int32", 1),
-    "ui": (16, "int32", 2), "UV": (32, "int32", 2), "s": (16, "float32", 2), "sq": (16, "float32", 2), "VV": (32, "int32", 2), "vl": (32, "uint16", 3),
-    "vh": (16, "float16", 2), "G": (256, "bfloat16", 1), "pl": (16, "uint16", 2), "wt1": (16, "float32", 1), "wl": (32, "uint16", 2),
-    "boff": (256, "uint16", 2), "bs": (256, "float32", 2), "qg": (256, "bfloat16", 2), "im1": (256, "bfloat16", 2), "nfl": (256, "bfloat16", 2), "gt": (256, "bfloat16", 2),
-    "qs": (256, "float32", 2), "nsB": (32, "float32", 2), "sk": (16, "float32", 2), "ac": (18, "bfloat16", 2), "A": (1, "float32", 2),
-    "s12": (544, "float32", 1), "m": (272, "float32", 1), "HI": (32, "int32", 1), "HA": (32, "int32", 1), "nf": (32, "float32", 1), "nfS": (32, "float32", 1),
-    "KM": (80, "bfloat16", 2), "kx": (16, "float32", 1), "sm": (16, "int32", 1), "sl": (16, "int32", 1), "ca": (16, "float32", 1), "cb": (16, "float32", 1),
-    "ol": (80, "uint16", 2), "kb": (48, "float32", 2), "pen": (16, "float32", 1), "ybk": (256, "float32", 1), "q1": (256, "bfloat16", 1),
+    "pI": (1, "int32", 1), "pM": (1, "int32", 1), "pG": (1, "int32", 1), "p8": (1, "int32", 1), "col": (1, "float32", 17),
+    "ic": (256, "float32", 1), "lnO": (16, "float32", 1),
+    "I": (128, "bfloat16", 1), "nI": (128, "bfloat16", 1), "I16": (128, "bfloat16", 1), "I31": (128, "bfloat16", 1), "J": (128, "bfloat16", 1), "IB": (136, "bfloat16", 1), "XG": (128, "bfloat16", 1),
+    "Gmf": (8, "float32", 1), "Gm4": (4, "float32", 1), "GS": (8, "bfloat16", 1), "G64": (8, "bfloat16", 1), "G32": (8, "bfloat16", 1),
+    "EB": (144, "bfloat16", 1), "wE": (144, "float16", 1),
+    "eq": (16, "float32", 1), "le": (16, "float32", 1), "ne": (16, "float32", 1),
+    "C17": (136, "bfloat16", 1), "d17": (136, "bfloat16", 1),
+    "ones": (128, "bfloat16", 1), "ba": (96, "bfloat16", 1), "ordc": (48, "bfloat16", 1),
+    "T1s": (544, "bfloat16", 1), "E16": (128, "bfloat16", 1), "b0": (256, "int32", 1), "pw": (8, "float32", 1), "p8e": (8, "float32", 2), "p8f": (1, "float32", 1), "xi": (256, "int32", 1), "xj": (256, "int32", 1),
+    "ui": (16, "float32", 2), "c05": (16, "bfloat16", 1), "UV": (32, "int32", 2), "s": (16, "float32", 2), "sq": (16, "float32", 2), "VV": (32, "int32", 2), "vl": (32, "uint16", 3),
+    "vh": (16, "float16", 2), "G": (256, "bfloat16", 1), "pl": (16, "uint16", 2), "wl": (32, "uint16", 2),
+    "boff": (256, "uint16", 2), "bs": (256, "float32", 2), "qg": (256, "bfloat16", 2), "im1": (256, "bfloat16", 2), "fl": (256, "bfloat16", 2), "gt": (256, "bfloat16", 2),
+    "qs": (256, "float32", 2), "ac": (34, "bfloat16", 1), "A": (1, "float32", 2),
+    "s12": (576, "float32", 1), "m": (288, "float32", 1), "HI": (32, "int32", 1), "HA": (32, "int32", 1),
+    "KM": (80, "bfloat16", 2), "kx": (16, "float32", 1), "sm": (16, "int32", 1), "sl": (16, "int32", 1), "ca": (16, "float32", 1),
+    "ol": (80, "uint16", 2), "o2": (16, "uint16", 1), "nz": (128, "bfloat16", 1), "pen": (32, "bfloat16", 1), "ybk": (256, "float32", 1), "q1": (256, "bfloat16", 1),
     "a12": (512, "bfloat16", 1), "SG": (768, "bfloat16", 1), "E": (256, "bfloat16", 1), "KK": (48, "float32", 1), "KL": (48, "float32", 1),
     "mna": (16, "float32", 1), "mxa": (16, "float32", 1), "tta": (16, "float32", 1), "FM": (32, "int32", 1), "FA": (32, "int32", 1), "fml": (32, "uint16", 2),
     "Bm": (256, "bfloat16", 2), "cx": (512, "bfloat16", 4),
@@ -45,42 +47,99 @@ for _n, (_w, _d, _c) in TILES.items():
 BUF = {"float32": "bigf", "int32": "bigi", "bfloat16": "bigb", "uint16": "bigu", "float16": "bigh"}
 SCRATCH = {BUF[_d]: ("sbuf", [128, _size[_d]], _d) for _d in BYTES}
 for _k in range(8):
-    SCRATCH["P%d" % _k] = ("psum", [128, 512], "float32")
+    SCRATCH["P%d" % _k] = ("psum", [128, 64, 8] if _k == 5 else [128, 512], "float32")
 for _k in range(2):
-    SCRATCH["Yc%d" % _k] = ("sbuf", [128, 10, 64], "bfloat16")
+    SCRATCH["Yc%d" % _k] = ("sbuf", [128, 10, 32], "bfloat16")
 SCRATCH["TH3"] = ("sbuf", [128, 6, 16], "float32")
-LOADS = ["bites", "next", "wt", "bank", "immun", "geno"]
+LOADS = ["bites", "wt", "bank", "immun", "geno"]
 STORES = ["sg", "sb0", "sb1", "sb2", "sb3", "si0", "si1"]
 SEMAPHORES = ["qv", "qs", "qp", "qg", "rl"] + ["arr%d" % t for t in range(1, STEPS)] + ["ld_" + n for n in LOADS] + ["st_" + n for n in STORES]
 
 
-COST = {"us": 0.00083 * 1.25, "ps": 0.00071 * 1.25, "gather": 1.56, "scatter": 3.8, "wake": 0.08, "link": 5.5}
+COST = {"us": 0.00083 * 1.25, "ps": 0.00071 * 1.25, "gather": 1.56, "scatter": 3.8, "wake": 0.08, "link": 5.5, "issue": 1.0, "dma": 2.5, "add": 0.0013}
 LOOK = 0.3
-PERIOD = 14.3
+PERIOD = 14.46
 TAIL = 9.5
-FIRM = True
-DUE = {'pP6W2': -5.8, 'pre.sX2': -19.3, 'pre.spsrc': -0.5, 'pre.vE': -6.1, 'pre.vRB': -12.2, 'pre.vT2': -7.5, 'sBm': 0.3, 'sSG2': 0.5, 'sbs': -4.1, 'sptab': -1.2, 'vboff': -6.8, 'vqs': -6.1, 'vsq': -2.3, 'vybk': -0.2, 'pre.vEW': -0.9, 'pre.vpM': -29.1, 'vE': 5.6, 'vpen': 0.3, 'pre.vhb': -21.3, 'sqg': -13.1, 'pre.pP1Iq': -14.7, 'pre.vEB': -23.1, 'pre.vX2': -5.0, 'vplF': 3.7}
-VG = [768, 256, 256, 256, 256, 640]
-PARTS = [[("s", 0, 64), ("s", 64, 128), ("s", 128, 192), ("s", 192, 256 - v // 16)] + ([("v", 256 - v // 16, 256)] if v else []) for v in VG]
+RUN = 0.07
+GAP = {'vcx': .01, 'vboff': .01, 'vbs': .01, 'sblog': .01, 'pP7I': .01, 'pP7nI': .01, 'pP0I': .01, 'pP5I2': .01, 'sptab': .21, 'sYc0': .083}
+DUE = {'vboff': -13.249, 'sW.0': -13.05, 'sW.1': -11.625, 'sW.2': -10.731, 'sqg': -9.009, 'sW.3': -8.53, 'sim1': -6.186, 'sW.4': -5.706, 'sgt': -4.813, 'sptab': -4.547, 'sBm': -2.626, 'vW.5': -12.27, 'vfl': -7.453, 'pP2qg': -7.523, 'pP6fl': -7.182, 'pP1fl': -7.054, 'vW.m0': -11.549, 'vW.m1': -10.651, 'vW.m2': -7.32, 'vW.m3': -6.106, 'vW.m4': -5.043, 'vW.m5': -4.247, 'pP1W.c0': -8.886, 'pP1W.m': -6.87, 'pP6W.c1': -5.961, 'pP6W.c2': -4.733, 'pP6W.m': -3.994, 'pP4nI': -5.279, 'pP6gt': -4.307, 'pP1gt': -4.222, 'pP4I': -9.241, 'pP0I': -12.805, 'pP6I': -9.511, 'pP1I': -9.014, 'pP2J': -7.75, 'vs12.0': -3.715, 'vm.0': -3.433, 'vs12.2': -3.152, 'vs12.1': -3.003, 'vm.1': -2.773, 'vs12.3': -2.545, 'vqs': -4.977, 'vbs': -3.566, 'vHI': -2.315, 'vHA': -2.169, 'vkx': -1.884, 'vac': -2.023, 'vKM': -1.738, 'vsm': -1.671, 'vca': -1.538, 'vsl': -1.472, 'vA': -1.406, 'vKM3': -1.339, 'vKM2': -1.273, 'vUV2': -1.14, 'vYc0': -1.06, 'sYc0': -1.06, 'pP5I': -9.383, 'pP5RB': -0.648, 'vol': 0.0, 'pP7I': -8.829, 'pP3wE': -3.086, 'vui': -2.097, 'vUV': -1.95, 'vs': -1.804, 'vsq': -1.605, 'pP2ones': -1.876, 'vVV': -0.927, 'vvl': -0.728, 'vvh': -0.662, 'sG': -0.582, 'gW.0': -3.914, 'gW.1': -3.006, 'ggeno_s': -4.733, 'vybk': 0.163, 'sa12': 0.163, 'va12': 0.627, 'sblog': 0.707, 'vpen': 1.158, 'sSG': 1.172, 'pP7nI': 0.887, 'pP7I2': 1.341, 'sSG2': 2.331, 'vq1': 1.752, 'vqlog': 2.681, 'pP4EW': -0.022, 'vpl': 1.092, 'pP5I2': 1.568, 'pP5EB': 3.045, 'pP3LR': 2.136, 'vE': 3.544, 'pP3I': 3.954, 'pP3EB': 4.011, 'vwl': 8.23, 'vrn': 4.034, 'pP5I31': 4.181, 'vTH3': 4.384, 'vTH32': 4.318, 'vKK': 4.531, 'vKL': 4.71, 'vmxa': 4.857, 'vmna': 4.923, 'vtta': 5.056, 'vFM': 5.122, 'vFM2': 5.202, 'vFA': 5.349, 'vfml': 5.495, 'vcx': 5.641, 'gg': 6.65, 'vilog': 6.57}
+PERIOD = 14.679
+DUE = {'ggeno_s': -4.52, 'gW.0': -4.04, 'gW.1': -2.35, 'gg': 6.45, 'pP0I': -13.52, 'pP6I': -10.63, 'pP1I': -9.95, 'pP5I': -9.5, 'pP4I': -9.06, 'pP1W.c0': -8.87, 'pP7I': -8.56, 'pP2qg': -7.87, 'pP1fl': -7.05, 'pP6fl': -6.56, 'pP2J': -6.54, 'pP1W.m': -6.39, 'pP6W.c1': -5.77, 'pP4nI': -5.54, 'pP6W.c2': -4.89, 'pP6W.m': -4.28, 'pP1gt': -4.25, 'pP6gt': -4.2, 'pP3wE': -2.83, 'pP2ones': -1.91, 'pP5RB': -0.65, 'pP4EW': 0.12, 'pP7nI': 1.03, 'pP7I2': 1.49, 'pP3LR': 1.8, 'pP5I2': 2.17, 'pP5EB': 3.11, 'pP3I': 4.13, 'vthr': 4.23, 'vdd': 4.66, 'pP3EB': 4.34, 'sW.0': -13.89, 'sW.1': -12.04, 'sW.2': -10.77, 'sqg': -9.2, 'sW.3': -8.72, 'sim1': -6.33, 'sW.4': -6.21, 'sgt': -5.57, 'sBm': -4.61, 'sptab': -3.81, 'sYc0': -1.11, 'sG': -0.43, 'sa12': -0.04, 'sblog': 0.71, 'sSG': 1.17, 'sSG2': 2.19, 'vboff': -13.46, 'vW.5': -12.31, 'vW.m0': -11.28, 'vW.m1': -10.17, 'vfl': -8.72, 'vW.m2': -7.61, 'vW.m3': -5.74, 'vqs': -4.71, 'vW.m5': -4.59, 'vW.m4': -4.39, 'vbs': -3.96, 'vm.0': -3.92, 'vKM': -3.63, 'vHI': -2.75, 'vs12.0': -2.73, 'vs12.1': -2.69, 'vHA': -2.6, 'vs12.2': -2.49, 'vs12.3': -2.48, 'vui': -2.44, 'vm.1': -2.31, 'vkx': -1.92, 'vUV': -1.86, 'vsm': -1.72, 'vac': -1.55, 'vca': -1.51, 'vsl': -1.49, 'vs': -1.41, 'vKM3': -1.27, 'vKM2': -1.13, 'vsq': -0.99, 'vA': -0.93, 'vYc0': -0.86, 'vUV2': -0.77, 'vVV': -0.28, 'vvl': -0.12, 'vybk': 0.26, 'vol': 0.5, 'va12': 0.93, 'vpl': 1.02, 'vpen': 1.17, 'vvh': 1.24, 'vq1': 2.05, 'vqlog': 2.63, 'vE': 3.81, 'vmna': 3.99, 'vmxa': 4.09, 'vrn': 4.22, 'vTH3': 4.64, 'vTH32': 4.71, 'vKK': 4.79, 'vKL': 4.92, 'vtta': 5.12, 'vFA': 5.15, 'vFM': 5.22, 'vFM2': 5.29, 'vfml': 5.72, 'vcx': 5.82, 'vilog': 6.88, 'vwl': 8.76}
+ORDER = {
+    'v': 'a12 ybk q1 pen pl boff+*2 qlog W.5+ rn thr TH3 dd TH32 KK M.m0+ KL M.m0+ mxa mna tta FM FM2 M.m0+ FA M.m0+ fml E cx*2 fl+ M.m0+*12 M.m1+*16 ilog M.m2+*11 wl M.m2+*5 M.m3+*12 s12.0+ M.m3+*4 qs+ m.0+ s12.1+ m.1+ s12.2+ s12.3+ HI+ HA+ kx+ KM+ ac+ sm+ ca+ sl+ KM3+ ui+ KM2+ UV+ KM2+ s+ A+ sq+ Yc0+ UV2+ Yc0+*2 VV+ Yc0+ vl+ bs+ vh+ bs+ ol+',
+    's': 'a12 SG blog*2 SG2 W.0+ W.1+ qg+ W.2+ W.3+ W.4+ im1+ ptab+*5 gt+ ptab+ Bm+ ptab+*8 Yc0+*3 ptab+ Yc0+ ptab+ G+',
+    'p': 'P5I2 P3LR*3 P5I2 P5EB*16 P4I+ P2J+ P3LR*13 P2qg+*2 P3I P3EB*16 P1W.c0+*16 P6fl+ P1fl+ P1M.m+*16 P6W.c1+*16 P6W.c2+*16 P4nI+ P6M.m+*16 P5I+*2 P2gt+*4 P3wE+*16 P0I++ P2ones+ P6I++ P1I++ P7I+*2 P5RB+*8 P4EW+*13 P7I2+ P7nI+*2 P4EW+*3',
+    'g': 'g M.0+ geno_s+ M.1+',
+}
+FIRST = {
+    'v': '_J _pM _pG _p8 _pw _EB _col _pw _col*2 _pw _col _p8f _pw _Gmf _eq _ne _p8e _EB _le _p8e _col7 _col6 _col7*2 _xi _p8e2 _xj _p8e2 _col2 _Bt _col2 _col8 _col2 _hb _wE _hb _LR*14 _ui _qlog _UV _LR _s _LR _sq _col3 _UV2 _col4 _VV _qlog _vl _vh b0 _qlog boff b0 _C16 boff _qlog _E W.5 _wl _IB _blog _blog2 M.m0*16 fl M.m1*16 ui _col8 UV _col5 s _lnO sq _col5 M.m2*16 _blog3 _blog4 M.m3*16 s12.0 qs m.0 _ac*2 s12.1 s12.2 m.1 _EW _RB s12.3 _ba HI _T2 HA kx ac KM sm ca sl A KM3 KM2 UV2 KM2 VV Yc0*2 vl Yc0*2 bs*2 vh ol',
+    's': '_wti _ones _X2*16 _G32 _G64 _GS _I16 _nI _Iq _ptab*4 _psrc*5 W.0 W.1 ptab qg ptab W.2 ptab W.3 ptab W.4 ptab im1 ptab _psrc ptab _ba*2 ptab _ba*2 ptab gt ptab*2 Bm ptab _T1a ptab*2 _T1b ptab*2 Yc0*4 G _T2*5',
+    'p': '_P3wE*16 P0I P4I _P3LR*16 P6I P1I P2J _P5J _P5Iq _P3I _P3EB*16 _P7J _P7Iq P1W.c0*16 P2qg*2 _P5J2 _P5Iq2 P1fl P6fl P3wE*4 P1M.m*16 _P7J2 _P7Iq2 P3wE*5 P6W.c1*16 P3wE*2 P6W.c2*16 P3wE*5 P4nI P6M.m*16 _P7E16 P2gt*4 P5I*2 P0I+ _P7E162 P2ones P6I+ P1I+ P7I*2 P5RB*8 P4EW*13 P7I2 P7nI*2 P4EW*3',
+    'g': '_pI _ic _XG*3 _I _XG _g _C17 _C16 _C172 _cq _lnO _RB _d16*2 _d17 _m _d17 _ba _ordc*2 _T1s _E16 _T1s*3 _Bt M.0 _Bt*2 geno_s _X2*2 _pen M.1',
+}
+FINAL = {
+    'v': 'a12 pen ybk q1 pl boff+*2 qlog E W.5+ rn thr TH3 dd TH32 M.m0+ KK KL fl+ mna M.m0+*5 FM M.m0+*2 FA M.m0+*4 fml M.m0+*2 ilog wl M.m0+*2 M.m1+*16 M.m2+*16 M.m3+*12 s12.0+ M.m3+*4 qs+ m.0+ s12.1+ s12.2+ m.1+ s12.3+ bs+ HI+ HA+ kx+ KM+ sm+ ca+ sl+ KM3+ KM2+*2 bs+ Yc0+*4 ol+ a12+ pen+ q1+ qlog+ plF+ ybk+ rn+ thr+ TH3+ dd+ TH32+ ^yb+ KK+ KL+ mna+ FM+ FA+ fml+ ilog+ ^yb2+ ^yb3+ ^yb4+ ^yi+',
+    's': 'a12 SG blog*2 SG2 W.0+ W.1+ qg+ W.2+ W.3+ W.4+ ptab+ im1+ ptab+*7 gt+ ptab+*8 Yc0+*4 ptb+*2 a12+ SG+ SG2+ ^q4+ blog+*2 ^q42+ ^q43+ ^q44+ ^yi+ ^yi2+ ^yi3+',
+    'p': 'P3LR*16 P5I2*2 P5EB*16 P3I P3EB*16 P2J+ P4I+ P2qg+*2 P6fl+ P1fl+ P1W.c0+*16 P1M.m+*16 P6W.c1+*16 P6W.c2+*16 P4nI+ P6M.m+*16 P2gt+*4 P7I+*2 P5I+*2 P5RB+*8 P7I2+ P7nI+*2 P3EW.F+*10 P5I2+*2 P3EW.F+*6 P5EB+*16',
+    'g': 'M.0+ geno_s+ M.1+ ptb+*2',
+}
+ORDER = {
+    'v': 'a12 ybk pen q1 pl boff+*2 qlog W.5+ rn thr dd TH3 TH32 KK KL M.m0+ mxa mna tta FM FM2 M.m0+ FA E fml M.m0+ cx*2 fl+ M.m0+*13 wl M.m1+*16 ilog M.m2+*16 M.m3+*16 s12.0+ qs+ m.0+ s12.1+ s12.2+ m.1+ s12.3+ HI+ HA+ kx+ KM+ ac+ sm+ ca+ sl+ ui+ KM2+*2 s+ KM3+ A+ Yc0+*2 UV+*2 VV+ vl+ bs+*2 vh+ ol+',
+    's': 'a12 SG psrc+ blog*2 SG2 T2+ W.0+ W.1+ qg+ W.2+ W.3+ ptab+ W.4+ ptab+ im1+ ptab+*4 gt+ ptab+*4 Bm+ ptab+*4 sq+ Yc0+*2 ptab+*2 G+',
+    'p': 'P4EW*7 P7I2 P7nI*2 P4EW*7 P5I2*2 P5EB*16 P3LR*16 P2J+ P4I+ P2qg+*2 P3I P3EB*16 P1W.c0+*16 P1fl+ P6fl+ P1M.m+*16 P6W.c1+*16 P6W.c2+*16 P4nI+ P6M.m+*16 P2gt+*4 P5I+ P3J+ P3wE+*16 P2ones+ P0I++ P7I+*2 P5I.o+ P5RB+*16 P1I++ P6I++ P4EW+*2',
+    'g': 'g M.0+ geno_s+ M.1+',
+}
+FIRST = {
+    'v': '_J _pM _pG _p8 _pw _EB _col _pw _col*2 _pw _col _p8f _pw _Gmf _eq _ne _p8e _EB _le _p8e _col7 _col6 _col7*2 _xi _c05*2 _xj _col2 _Bt _col2 _p8e2 _col2 _hb _wE _hb _LR*14 _ui _qlog _s _LR*2 _p8e2 _col3 _UV*2 _qlog _VV _col4 _vl _vh b0 _qlog boff b0 _C16 boff _qlog _E W.5 _wl _IB _blog _blog2 M.m0*16 fl M.m1*8 ui M.m1*2 s M.m1*6 _col8*2 UV _col5 _lnO _col5 M.m2*16 _ba qs M.m3*16 s12.0 _RB _EW m.0 _ac*2 s12.1 s12.2 m.1 bs s12.3 bs HI _T2 HA _Gm4 kx ac KM sm ca sl KM3 KM2*2 A Yc0 UV Yc0 VV vl vh blog blog2 ol',
+    's': '_wti _ones _X2*16 _G32 _G64 _GS _I16 _nI _Iq _sq _ptab*4 _psrc*3 W.0 W.1 qg W.2 W.3 ptab W.4 ptab im1 ptab _ba ptab _ba ptab gt ptab _ba ptab _ba ptab sq ptab _T1a ptab _T1b ptab Bm ptab*2 Yc0 ptab Yc0 ptab T2 ptab G',
+    'p': '_P3J _P3wE*16 P0I P4I _P3LR*16 P6I P1I P2J _P5J _P5Iq _P3I _P3EB*16 _P7J _P7Iq P3J P3wE*16 P1W.c0*16 P2qg*2 P1fl P6fl P1M.m*16 _P7E16 P6W.c1*16 P6W.c2*16 P4nI P6M.m*16 P2gt*4 P5I P1J P1Iq _P7E162 P2ones P6J P6Iq P7I*2 P5I.o P5RB*16 P0I+ P4EW*2 P1I+ P6I+',
+    'g': '_pI _ic _XG*3 _I _XG _g _C17 _C16 _C172 _cq _lnO _d16*2 _T1s _E16 _T1s*3 _d17 _m _d17 _RB _ba _ordc*2 _Bt M.0 _Bt*2 geno_s _X2*2 _pen M.1',
+}
+FINAL = {
+    'v': 'a12 ybk pen q1 pl boff+*2 qlog W.5+ E rn thr TH3 dd M.m0+ TH32 M.m0+ KK M.m0+*2 KL M.m0+ fl+ mna wl M.m0+ FM M.m0+*2 FA M.m0+*2 fml M.m0+*6 ilog M.m1+*16 M.m2+*16 M.m3+*16 s12.0+ qs+ m.0+ s12.1+ s12.2+ m.1+ bs+ s12.3+ bs+ HI+ HA+ kx+ KM+ sm+ ca+ sl+ KM3+ KM2+*2 Yc0+*2 ol+ a12+ pen+ q1+ qlog+ ybk+ plF+ rn+ thr+ TH3+ dd+ TH32+ KK+ KL+ mna+ FM+ FA+ fml+ ilog+ ^yb+ ^yb2+ ^yb3+ ^yb4+',
+    's': 'a12 SG blog*2 SG2 W.0+ W.1+ qg+ W.2+ W.3+ ptab+ W.4+ ptab+ im1+ ptab+*6 gt+ ptab+*8 Yc0+*2 ptb+*3 a12+ SG+ SG2+ blog+*2 ^q4+ ^q42+ ^q43+ ^q44+ ^yi+ ^yi2+ ^yi3+ ^yi4+',
+    'p': 'P4EW*6 P7I2 P7nI*2 P4EW*8 P3LR*8 P5I2*2 P5EB*16 P3LR*8 P2J+ P4I+ P3I P3EB*16 P2qg+*2 P1W.c0+*16 P6fl+ P1fl+ P1M.m+*16 P6W.c1+*16 P6W.c2+*16 P4nI+ P6M.m+*16 P2gt+*4 P7I+*2 P5I+ P5I.o+ P5RB+*16 P3EW.F+*8 P7I2+ P7nI+*2 P5I2+*2 P3EW.F+*8 P5EB+*16',
+    'g': 'M.0+ geno_s+ M.1+ ptb+',
+}
+PARTS = [[("s", 0, 32), ("s", 32, 64), ("s", 64, 128 - v), ("s", 128, 224), ("s", 224, 256), ("v", 128 - v, 128)] for v in (40, 14, 14, 14, 14, 40)]
+PARTS[0] = [("s", 0, 32), ("s", 32, 88), ("s", 128, 192), ("s", 192, 224), ("s", 224, 256), ("v", 88, 128)]
+OFFS = [(0, 64), (64, 256)]
+ADDS = [[]] * STEPS
+ZV = 0
+MAXIMA = [[(0, 64), (64, 128), (128, 192), (192, 256)]] * STEPS
+ZP = [256] * STEPS
+SEMAPHORES += ["ad%d_%d" % (t, e) for t in range(STEPS) for e in range(len(ADDS[t]))]
+SUMS = [(0, 128), (128, 224), (224, 256)]
 NFL = "v"
+BS = "v"
 SCV = ()
-YI = "ssvs"
+YI = "ssss"
 A2 = "s"
-LAST = "v"
+LAST = "s"
 ON_S = ()
-XS = 7
-YV = 4
+PB = 768
+EARLY = 3
+YV = 2
 
 
-def urgency(ops, succ, lag, due):
-    at = [0.0] * len(ops)
-    for j in range(len(ops) - 1, -1, -1):
-        o = ops[j]
-        at[j] = min([PERIOD * (STEPS - 1) + TAIL - lag.get(j, o["cost"])] + [at[i] - l for i, l in succ[j]])
-        if o["name"] in due:
-            named = PERIOD * o["step"] + due[o["name"]] + 1e-4 * j
-            at[j] = min(at[j], named) if FIRM or o["step"] == STEPS - 1 else named
-    return [-x for x in at]
+def timetable(ops, edges, succ, lag):
+    calls = {}
+    for i, o in enumerate(ops):
+        calls.setdefault((o["step"], o["name"]), []).append(i)
+    follow, need = [list(x) for x in succ], [len(e) for e in edges]
+    for q in "vspg":
+        row = []
+        for t, words in [(0, FIRST[q])] + [(t, ORDER[q]) for t in range(STEPS - 2)] + [(STEPS - 2, FINAL[q])]:
+            for word in words.split():
+                name, _, count = word.partition("*")
+                part = {"_": "pre.", "^": "end."}.get(name[0], "")
+                left = calls.get((t + name.count("+"), part + q + name.strip("_^+")), [])
+                row += [left.pop(0) for _ in range(min(int(count or 1), len(left)))]
+        assert len(row) == sum(o["q"] == q for o in ops)
+        for a, b in zip(row, row[1:]):
+            follow[a].append((b, ops[a]["cost"]))
+            need[b] += 1
+    return follow, need, [-i for i in range(len(ops))]
 
 
 def list_schedule(n, que, cost, succ, need, prio):
@@ -174,28 +233,32 @@ def rank_program(g, core, T, topo):
     ops = []
     last = {}
     edges = []
-    part = {"name": "pre.", "runs": {}, "last": None, "step": 0}
+    part = {"name": "pre.", "runs": {}, "last": None, "step": 0, "of": ""}
     US, PS = COST["us"], COST["ps"]
 
-    def t_(name, a=0, b=None, c=0, step=1):
+    def t_(name, a=0, b=None, c=0, step=1, rows=(0, 128)):
         w, d, copies = TILES[name]
         if b is None:
             b = w
         off, p = PLACE[name]
-        off += p * (c % copies)
-        ap = T[BUF[d]][:, off + a:off + b:step] if step != 1 else T[BUF[d]][:, off + a:off + b]
+        off += p * (c + (c > 0) if name == "z" else c % copies)
+        ap = T[BUF[d]][rows[0]:rows[1], off + a:off + b:step] if step != 1 else T[BUF[d]][rows[0]:rows[1], off + a:off + b]
         return {"ap": ap, "rg": [(BUF[d], off + a, off + b)], "n": (b - a + step - 1) // step, "by": BYTES[d], "ps": False, "ind": False}
 
-    def p_(k, a, b, step=1):
-        ap = T["P%d" % k][:, a:b:step] if step != 1 else T["P%d" % k][:, a:b]
+    def p_(k, a, b, step=1, rows=(0, 128)):
+        ap = T.P5[:, a // 8:b // 8, :] if k == 5 else T["P%d" % k][rows[0]:rows[1], a:b:step] if step != 1 else T["P%d" % k][rows[0]:rows[1], a:b]
         return {"ap": ap, "rg": [("P%d" % k, 0, 512)], "n": (b - a + step - 1) // step, "by": 4, "ps": True, "ind": False}
 
-    def y_(t, a, b, step, rg):
+    def y_(t, a, b, step, rows=(0, 128)):
         name = "Yc%d" % (t % 2)
-        return {"ap": T[name][:, :, a:b:step], "rg": [(name,) + rg], "n": 80, "by": 2, "ps": False, "ind": False}
+        return {"ap": T[name][rows[0]:rows[1], :, a:b:step], "rg": [(name, 0, 32)], "n": 10 * len(range(a, b, step)), "by": 2, "ps": False, "ind": False}
 
     def th_(a, b, step=1):
         return {"ap": T.TH3[:, a:b:step, :], "rg": [("TH3", a, b)], "n": 48, "by": 4, "ps": False, "ind": False}
+
+    def m_(t, a, b, k=None):
+        x = t_("W", 4096 + 16 * a, 4096 + 16 * b, t) if k is None else t_("W", 4096 + 16 * a + k, 4096 + 16 * b, t, 16)
+        return dict(x, rg=[("M%d.%d" % (t % 2, r), a, b) for r in (range(16) if k is None else [k])])
 
     def ind(win, off):
         return {"ap": win["ap"].indirect(off["ap"]), "rg": win["rg"] + off["rg"], "win": win["rg"], "off": off["rg"], "n": 16 * off["n"], "by": win["by"], "ps": False, "ind": True}
@@ -205,7 +268,7 @@ def rank_program(g, core, T, topo):
 
     def name_of(region):
         if region[0] not in dtype_of:
-            return region[0]
+            return "M" if region[0][0] == "M" else region[0]
         return [x for o, x in starts[dtype_of[region[0]]] if o <= region[1]][-1]
 
     def add(q, cost, emit, R, W, sem, inc, grp=None, role=None):
@@ -236,11 +299,11 @@ def rank_program(g, core, T, topo):
         tag = name_of(W[0]) if W else q
         if tag[0] == "P" and R:
             tag += name_of(R[0])
-        k = q + tag.replace("Yc1", "Yc0")
+        k = q + tag.replace("Yc1", "Yc0") + part["of"]
         if k != part["last"]:
             part["runs"][k] = part["runs"].get(k, 0) + 1
         part["last"] = k
-        run = 1 if k in ("vW", "pP1W", "vptab", "sptab") else part["runs"][k]
+        run = 1 if part["of"] or k in ("vptab", "sptab") else part["runs"][k]
         ops.append({"q": q, "cost": cost, "emit": emit, "sem": sem, "inc": inc, "step": part["step"], "name": part["name"] + k + (str(run) if run > 1 else "")})
         edges.append(ed)
         return i
@@ -306,7 +369,7 @@ def rank_program(g, core, T, topo):
         return ts(t_(name), a, scale, bias, OP.mult, OP.add)
 
     def mm(out, lhsT, rhs, start, stop, grp=None, role=None):
-        c = max(64, rhs["n"]) * PS * (4 if rhs["by"] == 4 else 1)
+        c = max(min(64, lhsT["n"]), rhs["n"]) * PS * (4 if rhs["by"] == 4 else 1)
         return add("p", c, lambda: g.tensor.matmul(raw(out), raw(lhsT), raw(rhs), start, stop), rgs(lhsT, rhs), out["rg"], "qp", 1, grp=grp, role=role)
 
     def iota(out, pattern, base=0, cm=0, whole=False):
@@ -327,7 +390,7 @@ def rank_program(g, core, T, topo):
 
     def load(name, out, q="y"):
         eng = g.sync if q == "y" else g.scalar
-        src = T.bites[:, 0:256] if name == "bites" else T.bites[:, 256:512] if name == "next" else T[name][:]
+        src = T[name][:]
         return add(q, 0.1, lambda: eng.dma_start(raw(out), src), [], out["rg"], "ld_" + name, 16)
 
     lag = {}
@@ -337,8 +400,12 @@ def rank_program(g, core, T, topo):
         i = add(q, 0.1, lambda: eng.dma_start(dst, raw(src)), src["rg"], [("out" + tag, 0, 1)], "st_" + tag, 16)
         lag[i] = 2.0 + src["n"] * src["by"] * 0.0005
 
+    def adding(tag, out, src):
+        i = add("g", COST["issue"], lambda: g.dma_start(raw(out), raw(src), accum_op=OP.add), src["rg"] + out["rg"], out["rg"], tag, 16)
+        lag[i] = COST["dma"] + src["n"] * COST["add"]
+
     prev = None
-    for name, dst, tm in (("wt", t_("wti"), 2.5), ("bites", t_("z"), 2.6), ("bank", t_("bk"), 4.2), ("geno", t_("geno_s"), 6.8), ("next", t_("bt"), 7.0), ("immun", t_("ilog", 0, 1024), 7.6)):
+    for name, dst, tm in (("wt", t_("wti"), 2.5), ("bites", t_("z", 0, 512), 2.7), ("bank", t_("bk"), 4.35), ("geno", t_("geno_s"), 6.95), ("immun", t_("ilog", 0, 1024), 7.6)):
         i = load(name, dst, "s" if name == "wt" else "y")
         if name != "wt":
             if prev is not None:
@@ -363,22 +430,25 @@ def rank_program(g, core, T, topo):
         j = add("n", 0.0, None, [], out["rg"], "arr%d" % t, eng)
         ops[j]["proxy"] = i
 
-    P, PM, PG, P8, WF, WG, WS, CI, PK, PK0, JK, PW, L1, L2, H1, W1 = [t_("col", c=k) for k in range(16)]
+    P, PM, PG, P8, WF, WG, WS, CI, PK, PK0, JK, PW, L1, L2, H1, W1, PC = [t_("col", c=k) for k in range(17)]
     ic = lambda n: t_("ic", 0, n)
     iota(t_("pI"), [[0, 1]], 0, 1, True)
     iota(t_("ic"), [[1, 256]])
-    fill(t_("ones"), 1)
-    send([t_("bt")], 1, (rank + 1) % n_ranks)
+    ms(t_("J"), 1.0 / 64)
+    ms(t_("c05", rows=(0, 64)), -2048.0)
+    ms(t_("c05", rows=(64, 128)), 0.5)
+    i = act(t_("ones"), t_("J"), AF.Sigmoid, scale=6400.0)
+    ops[i]["cost"] += 1.6
+    send([t_("z", 256, 512)], 1, (rank + 1) % n_ranks)
     iota(t_("C16"), [[0, 16], [-1, 16]], 16)
+    ms(t_("C16", rows=(64, 128)), 16 * Q0 + BIG)
+    fill(t_("cq"), int(2048 * Q0))
     iota(t_("C17"), [[0, 8], [-1, 17]], 17)
     iota(t_("lnO"), [[16, 16]])
-    iota(t_("nr"), [[-16, 256]])
-    iota(t_("k1"), [[1, 17], [0, 17]])
-    iota(t_("k2"), [[0, 17], [1, 17]])
     ts(t_("pM"), t_("pI"), 15, None, OP.bitwise_and)
     ts(t_("pG"), t_("pI"), 4, None, OP.arith_shift_right)
     ts(t_("p8"), t_("pI"), 7, None, OP.bitwise_and)
-    cp(P, t_("pI"))
+    ts(P, t_("pI"), 1.0, None, OP.add)
     cp(PM, t_("pM"))
     cp(PG, t_("pG"))
     ts(P8, t_("p8"), -1.0, 7.0, OP.mult, OP.add)
@@ -392,71 +462,77 @@ def rank_program(g, core, T, topo):
     ts(t_("wE"), t_("EB"), WS, None, OP.mult)
     select(t_("I"), t_("ones"), [[-1, 128]], OP.is_equal, 0.0, 0, 1)
     quarters = [(a, a + 256) for a in range(0, 1024, 256)]
-    act(t_("Iq"), t_("I"), AF.Copy, scale=-4096.0)
+    act(t_("Iq"), t_("I"), AF.Copy, scale=-4096.0 * 256)
     for a, b in quarters:
-        ts(t_("q192", a, b), t_("bk", a, b), 1.0 / 4096, 191.5 + 1.0 / 8192, OP.mult, OP.add)
-    for a, b in quarters:
-        act(t_("qlog", a, b), t_("q192", a, b), AF.Identity, bias=-192.0)
-    for k, (a, b) in enumerate(quarters):
-        mm(p_((5, 7, 1, 6)[k], 0, 256), t_("Iq"), t_("qlog", a, b), True, True)
-    for k, (a, b) in enumerate(quarters):
+        ts(t_("qlog", a, b), t_("bk", a, b), 1.0 / 4096 / 256, (Q0 - 0.5 + 1.0 / 8192) / 256, OP.mult, OP.add)
+
+    def numbers(k):
+        a, b = quarters[k]
+        mm(p_((5, 7, 1, 6)[k], 0, 256), t_("J"), t_("cq"), True, False)
+        mm(p_((5, 7, 1, 6)[k], 0, 256), t_("Iq"), t_("qlog", a, b), False, True)
         tt(t_("blog", a, b), t_("bk", a, b), p_((5, 7, 1, 6)[k], 0, 256), OP.add)
-    i = act(t_("Gm"), t_("Gmf"), AF.Sigmoid, bias=-100.0, scale=200.0)
-    ops[i]["cost"] += 1.6
-    for name, f in (("nGm", -1.0), ("G64", 64.0), ("G32", -32.0)):
+    numbers(0)
+    numbers(1)
+    for name, f in (("GS", BIG), ("G64", 64.0), ("G32", -32.0)):
         act(t_(name), t_("Gmf"), AF.Copy, scale=f)
-    act(t_("nI"), t_("I"), AF.Copy, scale=-1.0)
-    act(t_("I16"), t_("I"), AF.Copy, scale=-16.0)
-    ts(CI, P, PG, 1.0, OP.add, OP.add)
-    ts(t_("IB"), ic(136), CI, -BIG, OP.is_equal, OP.mult)
+    for name, f in (("nI", -1.0), ("I16", -4096.0)):
+        act(t_(name), t_("I"), AF.Copy, scale=f)
+    tt(CI, PG, P, OP.add)
+    ts(t_("IB"), ic(136), CI, BIG, OP.is_equal, OP.mult)
     fill(t_("C17", 0, 136, step=17), 0)
     fill(t_("d16"), 0)
     fill(t_("d16", 0, 256, step=16), -4096)
     fill(t_("d17"), 0)
-    fill(t_("d17", 0, 136, step=17), -1048576)
+    fill(t_("d17", 0, 136, step=17), int(-8 * BIG))
     fill(t_("m", 0, 272, step=136), 0)
-    fill(t_("c16"), 16)
-    for c in range(2):
-        ms(t_("ac", 16, 17, c), 304.0 / 128)
-        ms(t_("ac", 17, 18, c), 7.59375 / 128)
+    ms(t_("ac", 32, 33), 304.0 / 128)
+    ms(t_("ac", 33, 34), 7.59375 / 128)
     ts(t_("eq"), ic(16), PM, None, OP.is_equal)
     ts(t_("le"), ic(16), PM, None, OP.is_ge)
     ts(t_("ne"), ic(16), PM, 16384.0, OP.not_equal, OP.mult)
+    tt(t_("Gm4"), t_("Gmf", 0, 4), t_("Gmf", 4, 8), OP.add)
     fill(t_("RB"), 0)
     ts(t_("RB", 112, 128), t_("eq"), -1.0, None, OP.mult)
-    select(t_("XG"), t_("ones"), [[-16, 8], [0, 16]], OP.is_ge, 0.0, 0, 1)
+    fill(t_("XG"), 1)
+    select(t_("XG"), t_("XG"), [[-16, 8], [0, 16]], OP.is_ge, 0.0, 0, 1)
     select(t_("XG"), t_("XG"), [[16, 8], [0, 16]], OP.is_ge, 0.0, 15, -1)
     select(t_("XG"), t_("XG"), [[-1, 128]], OP.not_equal, -1.0, 0, 1)
     for r in range(16):
         ts(t_("LR", 128 * r, 128 * r + 128), t_("XG"), t_("eq", r, r + 1), t_("le", r, r + 1), OP.min, OP.mult)
     ts(JK, PM, 1024.0, None, OP.add)
     ts(t_("lnO"), t_("lnO"), PM, 16.0, OP.add, OP.mult)
-    for k in range(3):
+    cp(t_("ba", 0, 16), t_("lnO"))
+    for k in (1, 2):
         act(t_("ba", 16 * k, 16 * k + 16), t_("lnO"), AF.Identity, bias=16.0)
-    iota(t_("ba", 48, 80), [[128, 2], [0, 16]], 16)
-    iota(t_("ordc"), [[int(WO), 2], [0, 16]], int(WO))
-    for c in range(2):
-        act(t_("kb", 0, 16, c), t_("lnO"), AF.Identity, bias=4096.0)
+    for h in range(2):
+        act(t_("ba", 48 + 8 * h, 56 + 8 * h), t_("lnO", 0, 8), AF.Identity, bias=16.0)
+    iota(t_("ba", 64, 96), [[4080, 2], [0, 16]], 16)
+    iota(t_("ordc", 0, 32), [[4096, 2], [0, 16]], 4096 - int(WO))
+    fill(t_("ordc", 32, 48), int(WO))
     fill(t_("X2", 0, 1), 0)
+    fill(t_("X2", 2049, 2064), 0)
     for k in range(16):
-        if k < XS:
-            act(t_("X2", k or 16, 4097, step=16), t_("nr"), AF.Identity, bias=t_("ne", k, k + 1), grp="X2")
-        else:
-            ts(t_("X2", k or 16, 4097, step=16), t_("nr"), t_("ne", k, k + 1), None, OP.add, grp="X2")
+        act(t_("X2", k or 16, 2049, step=16), ic(128), AF.Identity, bias=t_("ne", k, k + 1), scale=-16.0, grp="X2")
     ts(PK0, PM, 0.0, 16.0, OP.is_equal, OP.mult)
     tt(PK, PM, PK0, OP.add)
-    for t in range(STEPS):
-        ts(t_("T2", c=t), ic(32), PK, 8.0 + t, OP.is_equal, OP.mult)
-    ts(t_("k1"), t_("k1"), PM, 64.0, OP.not_equal, OP.mult)
-    ts(t_("k2"), t_("k2"), PM, 64.0, OP.not_equal, OP.mult)
-    tt(t_("T1"), t_("k1"), t_("k2"), OP.min)
+    ts(t_("T2", c=0), ic(32), PK, (Q0 + 8) / 256, OP.is_equal, OP.mult)
+    seed = lambda a, b: t_("T1s", a, b, rows=(0, 16))
+    fill(t_("pen", 0, 16), 0)
+    fill(seed(0, 544), 1)
+    select(seed(0, 272), seed(0, 272), [[1, 272]], OP.not_equal, Q0 / 256, -256, 16)
+    for pattern in ([[-1, 16], [0, 16]], [[0, 16], [-1, 16]]):
+        select(seed(273, 529), seed(273, 529), pattern, OP.not_equal, Q0 / 256, 15, -1)
+    select(t_("E16", rows=(0, 16)), t_("ones", rows=(0, 16)), [[0, 8], [-1, 16]], OP.is_equal, 0.0, 0, 1)
+    for k, name in enumerate(("T1a", "T1b")):
+        mm(p_(7, 0, 272), t_("E16", rows=(0, 16)), seed(272 * k, 272 * k + 272), True, True)
+        act(t_(name), p_(7, 0, 272), AF.Copy)
     ms(t_("pw", 0, 1), 1.0)
     for k in (1, 2, 4):
         ts(t_("pw", k, 2 * k), t_("pw", 0, k), float(2 ** k), None, OP.mult)
     ts(t_("p8e"), ic(8), P8, None, OP.is_equal)
     tt(t_("p8e"), t_("p8e"), t_("pw"), OP.mult)
     red(PW, t_("p8e"))
-    ts(t_("xi"), t_("ic"), PW, None, OP.mult)
+    ts(t_("xi"), ic(256), PW, None, OP.mult)
     ts(t_("xj"), t_("xi"), 128, None, OP.bitwise_and)
     ts(t_("Bt", 0, 256), t_("xj"), 0.5, None, OP.mult)
     for k in range(1, 4):
@@ -468,28 +544,27 @@ def rank_program(g, core, T, topo):
     ts(t_("hb", c=1), t_("hb"), 200.0, -100.0, OP.mult, OP.add)
     for k in range(4):
         act(t_("ptab", 256 * k, 256 * k + 256), t_("Bt", 0, 256), AF.Identity, bias=t_("hb", k, k + 1), scale=L1)
-    for t in range(STEPS - (LAST == "v")):
-        act(t_("psrc", c=t), t_("Bt", 0, 256), AF.Identity, bias=t_("hb", 4 + t, 5 + t, 1), scale=L2)
-    if LAST == "v":
-        act(t_("psb"), t_("Bt", 0, 256), AF.Identity, bias=t_("hb", 3 + STEPS, 4 + STEPS), scale=L1)
+    places = lambda t: act(t_("psrc", c=t), t_("Bt", 0, 256), AF.Identity, bias=t_("hb", 4 + t, 5 + t, 1), scale=L2)
+    for t in range(EARLY):
+        places(t)
     ts(t_("p8e", c=1), ic(8), t_("p8f"), None, OP.is_equal)
     tt(t_("p8e", c=1), t_("p8e", c=1), t_("pw"), OP.mult)
     red(W1, t_("p8e", c=1))
     ts(H1, H1, 255.0 * 64, 1.0, OP.mult, OP.add)
     ts(t_("EW"), t_("EB"), W1, H1, OP.mult, OP.mult)
 
-    def to_list(out, src, a, b, wts="EB", first=True):
+    def to_list(out, src, a, b, wts="EB", first=True, close=True):
         for r in range(16):
-            mm(out, t_(wts, 15 - r, 143 - r), t_(src, a + r, b, 0, 16), first and r == 0, r == 15)
+            mm(out, t_(wts, 15 - r, 143 - r), t_(src, a + r, b, 0, 16), first and r == 0, close and r == 15)
 
     def host(t):
+        mm(p_(3, 256, 272), t_("J"), t_("c05"), True, False)
         for r in range(16):
-            mm(p_(3, 256, 272), t_("wE", 15 - r, 143 - r), t_("z", r, 256, t, 16), r == 0, r == 15)
-        u = t_("UV", 16, 32, t)
-        cp(t_("ui", c=t), p_(3, 256, 272))
-        ts(u, t_("ui", c=t), 4095, None, OP.bitwise_and)
-        ts(t_("s", c=t), u, 592.0, None, OP.add)
-        tt(t_("sq", c=t), t_("s", c=t), t_("s", c=t), OP.mult)
+            mm(p_(3, 256, 272), t_("wE", 15 - r, 143 - r), t_("z", r, 256, t, 16), False, r == 15)
+        ts(t_("ui", c=t), p_(3, 256, 272), 1.5 * 2 ** 35, 1.5 * 2 ** 35, OP.add, OP.subtract)
+        tt(t_("s", c=t), p_(3, 256, 272), t_("ui", c=t), OP.subtract)
+        act(t_("sq", c=t), t_("s", c=t), AF.Square, bias=2047.5 + 592)
+        ts(t_("UV", 16, 32, t), t_("s", c=t), 2047.5, None, OP.add)
         ts(t_("UV", 0, 16, t), t_("sq", c=t), 1.0 / 32, t_("A", c=t - 1) if t else 311.59375, OP.mult, OP.add)
         ts(t_("VV", c=t), t_("UV", c=t), 1023, None, OP.bitwise_and)
         cp(t_("vl", c=t), t_("VV", c=t))
@@ -510,45 +585,50 @@ def rank_program(g, core, T, topo):
         n = 1024 + 256 * t
         pl = t_("pl", c=t) if t else t_("vl", 0, 16, t)
         W = lambda a, b, s=1: t_("W", a, b, t, s)
-        mm(p_(0, 0, 256), t_("I"), z, True, True)
-        for h in range(2):
-            cp(t_("boff", 128 * h, 128 * h + 128, t), ind(t_("blog", 0, n), t_("pl" if t else "vl", 8 * h, 8 * h + 8, t)))
-        for q, a, b in PARTS[t]:
+        mm(p_(0, 0, ZP[t]), t_("I"), t_("z", 0, ZP[t], t), True, True)
+        for a, b in MAXIMA[t]:
+            for e in range(2 if b - a <= 32 else 0):
+                mm(p_(0, 256 + e, 256 + 2 * (b - a), 2), t_("I"), t_("z", a, b, t), True, True)
+        for a, b in OFFS:
+            if t:
+                cp(t_("boff", a, b, t), ind(t_("blog", 0, n), t_("pl", a // 16, b // 16, t)))
+            else:
+                ts(t_("b0", a, b), ind(t_("bk"), t_("vl", a // 16, b // 16)), 4095, None, OP.bitwise_and)
+                cp(t_("boff", a, b), t_("b0", a, b))
+                part["runs"].pop("vb0"), part["runs"].pop("vboff")
+        for k, (q, a, b) in enumerate(PARTS[t]):
+            part["of"] = ".%d" % k
             if q == "s":
                 act(W(16 * a, 16 * b), ind(t_("geno_s"), t_("boff", a, b, t)), AF.Copy)
             else:
                 cp(W(16 * a, 16 * b), ind(t_("geno_s"), t_("boff", a, b, t)))
+        part["of"] = ""
         keep(t_("geno_s", t, 4096, step=16), z)
         if t == STEPS - 1:
             store("sg", T.ygeno[:], t_("geno_s"))
-        qg, nfl, gt, im1 = t_("qg", c=t), lambda h: t_("nfl", 128 * h, 128 * h + 128, t), lambda h: t_("gt", 128 * h, 128 * h + 128, t), t_("im1", c=t)
-        act(t_("bs", c=t), ind(t_("blog", 0, n), pl), AF.Identity, bias=float(t))
+        qg, fl, gt, im1 = t_("qg", c=t), lambda h: t_("fl", 128 * h, 128 * h + 128, t), lambda h: t_("gt", 128 * h, 128 * h + 128, t), t_("im1", c=t)
+        for h in range(2):
+            if BS == "v":
+                ts(t_("bs", 128 * h, 128 * h + 128, t), t_("boff", 128 * h, 128 * h + 128, t), float(t + 2048 * h), None, OP.add)
+            else:
+                act(t_("bs", 128 * h, 128 * h + 128, t), ind(t_("blog", 0, n), t_("pl" if t else "vl", 8 * h, 8 * h + 8, t)), AF.Identity, bias=float(t + 2048 * h))
         act(qg, ind(t_("qlog", 0, n), pl), AF.Copy)
         act(im1, ind(t_("ilog", 0, n), pl), AF.Identity, bias=-1.0)
         if NFL == "v":
-            ts(t_("nfl", c=t), qg, t + 0.5, None, OP.is_lt)
+            ts(t_("fl", c=t), qg, (Q0 + t + 0.5) / 256, None, OP.is_gt)
         else:
-            act(t_("nfl", c=t), qg, AF.Sigmoid, bias=200.0 * t + 100.0, scale=-200.0)
+            act(t_("fl", c=t), qg, AF.Sigmoid, bias=-200.0 * (Q0 + t + 0.5), scale=200.0 * 256)
         mm(p_(4, 256, 512), t_("I"), z, True, False)
         mm(p_(4, 256, 512), t_("nI"), im1, False, True)
         act(t_("gt", c=t), p_(4, 256, 512), AF.Sign, bias=-1.5)
-        mm(p_(2, 0, 256), t_("I"), t_("C16"), True, False)
+        mm(p_(2, 0, 256), t_("J"), t_("C16"), True, False)
         for h in range(2):
             mm(p_(2, 128 * h, 128 * h + 128), t_("qg", 128 * h, 128 * h + 128, t), t_("I16"), False, h == 1)
         runmax(t_("qs", c=t), t_("d16"), p_(2, 0, 256))
         if t + 1 < STEPS:
-            mm(p_(2, 256, 272), t_("I"), t_("c16"), True, False)
-            for h in range(2):
-                mm(p_(2, 256 + 8 * h, 264 + 8 * h), nfl(h), t_("nGm"), False, h == 1)
-        for h in range(4):
-            mm(p_(2, 272 + 8 * h, 280 + 8 * h), gt(h % 2), t_("Gm"), True, True)
-        if t + 1 < STEPS:
-            ts(t_("sk", c=t), p_(2, 272, 288), 1.0, 2.0, OP.is_ge, OP.mult)
-            tt(t_("ac", 0, 16, t), t_("sk", c=t), p_(2, 256, 272), OP.min)
-        ts(t_("nsB", c=t), p_(2, 272, 304), 1.0, 4194304.0, OP.is_lt, OP.mult)
-        if t + 1 < STEPS:
-            mm(p_(2, 304, 322), t_("ones"), t_("ac", c=t), True, True)
-            red(t_("A", c=t), p_(2, 304, 322))
+            act(t_("T2", c=t + 1), t_("T2", c=0), AF.Copy, scale=(Q0 + 9 + t) / (Q0 + 8))
+        if t and t + EARLY - 1 < STEPS:
+            places(t + EARLY - 1)
         if t + 1 < STEPS:
             for j in range(15, -1, -1):
                 to, src = ind(t_("ptab"), t_("wl", 2 * j, 2 * j + 1, t)), t_("psrc", 16 * j, 16 * j + 16, t)
@@ -556,7 +636,6 @@ def rank_program(g, core, T, topo):
                     ts(to, src, 0.005, 0.5, OP.mult, OP.add)
                 else:
                     act(to, src, AF.Sigmoid)
-            host(t + 1)
         else:
             if LAST == "v":
                 keep(t_("ptb", 0, 1024), t_("ptab", 0, 1024))
@@ -565,89 +644,130 @@ def rank_program(g, core, T, topo):
             else:
                 for j in range(15, -1, -1):
                     act(ind(t_("ptab"), t_("wl", 2 * j, 2 * j + 1, t)), t_("psrc", 16 * j, 16 * j + 16, t), AF.Sigmoid)
-                keep(t_("ptb", 0, 1024), t_("ptab", 0, 1024))
-            to_list(p_(4, 64, 128), "ptb", 0, 1024, "EW")
-            cp(t_("plF"), p_(4, 64, 128))
+                for a in range(0, 1024, 256):
+                    if a < PB:
+                        act(t_("ptb", a, a + 256), t_("ptab", a, a + 256), AF.Copy)
+                    else:
+                        keep(t_("ptb", a, a + 256), t_("ptab", a, a + 256))
+            part["of"] = ".F"
+            to_list(p_(3, 64, 128), "ptb", 0, 1024, "EW")
+            part["of"] = ""
+            cp(t_("plF"), p_(3, 64, 128))
+        if ADDS[t]:
+            a, b = ADDS[t][0][0], ADDS[t][-1][1]
+            ts(t_("nz", 0, b - a), t_("z", a, b, t), -1.0, None, OP.mult)
+            part["of"] = ".z"
+            for k in range(16):
+                if k < ZV:
+                    cp(m_(t, a, b, k), t_("nz", 0, b - a))
+                else:
+                    keep(m_(t, a, b, k), t_("nz", 0, b - a))
+        for e, (a, b) in enumerate(ADDS[t]):
+            part["of"] = ".a%d" % e
+            adding("ad%d_%d" % (t, e), m_(t, a, b), W(16 * a, 16 * b))
+            ts(m_(t, a, b), m_(t, a, b), 0.0, 32.0, OP.max, OP.add)
+        for e, (a, b) in enumerate(MAXIMA[t]):
+            part["of"] = ".m%d" % e
+            for k in range(16 if b - a > 32 else 0):
+                tt(m_(t, a, b, k), W(16 * a + k, 16 * b, 16), p_(0, a, b), OP.max)
+            for k in range(8 if b - a <= 32 else 0):
+                two = dict(W(4096 + 16 * a + k, 4096 + 16 * b, 8), rg=m_(t, a, b, k)["rg"] + m_(t, a, b, k + 8)["rg"])
+                tt(two, W(16 * a + k, 16 * b, 8), p_(0, 256, 256 + 2 * (b - a)), OP.max)
+        part["of"] = ""
         for h in range(2):
             gk, kb = ("key", t, h), (1, 6)[h]
             mm(p_(kb, 0, 136), t_("I"), t_("C17"), True, False, gk, "first")
-            mm(p_(kb, 0, 136), nfl(h), t_("IB"), False, False, gk, "mid")
-            for k in range(16):
-                mm(p_(kb, 1 + k, 136, 17), W(2048 * h + k, 2048 * h + 2048, 16), t_("G32"), False, False, gk, "mid")
-            for e in range(2):
-                for k in range(16):
-                    o, a = 4096 + 2048 * h + 128 * k + 64 * e, 128 * h + 64 * e
-                    tt(W(o, o + 64), W(16 * a + k, 16 * a + 1024, 16), p_(0, a, a + 64), OP.max)
-            for k in range(16):
-                o = 4096 + 2048 * h + 128 * k
-                mm(p_(kb, 1 + k, 136, 17), W(o, o + 128), t_("G64"), False, k == 15, gk, "last" if k == 15 else "mid")
-            keep(W(4096 + 2048 * h, 6144 + 2048 * h, 16), t_("z", 128 * h, 128 * h + 128, t))
+            mm(p_(kb, 0, 136), fl(h), t_("IB"), False, False, gk, "mid")
+            for c, (a, b) in enumerate(SUMS):
+                part["of"] = ".c%d" % c
+                for k in range(16 if a // 128 == h else 0):
+                    mm(p_(kb, 1 + k, 136, 17, (a % 128, b - 128 * h)), W(16 * a + k, 16 * b, 16), t_("G32"), False, False, gk, "mid")
+            part["of"] = ".m"
+            for k in sorted(range(16), key=lambda k: k % 8 if h else k):
+                mm(p_(kb, 1 + k, 136, 17), m_(t, 128 * h, 128 * h + 128, k), t_("G64"), False, k == 15, gk, "last" if k == 15 else "mid")
+            part["of"] = ".%d" % h
+            keep(m_(t, 128 * h, 128 * h + 128, 0), t_("z", 128 * h, 128 * h + 128, t))
             o = 136 * h
             runmax(t_("s12", o, o + 136), t_("d17"), p_(kb, 0, 136))
             tt(t_("m", o + 1, o + 136), t_("s12", o, o + 135), p_(kb, 1, 136), OP.min)
+            part["of"] = ".%d" % (2 + h)
             runmax(t_("s12", 272 + o, 408 + o), t_("d17"), t_("m", o, o + 136))
-        HL = t_("s12", 16, 544, 0, 17)
+            part["of"] = ""
+        for k in range(2, 4 if t == 0 else 0):
+            numbers(k)
         KM = lambda a, b: t_("KM", a, b, t)
-        cp(t_("HI"), HL)
-        tt(t_("nf"), HL, t_("nsB", c=t), OP.is_le)
-        ts(t_("HA"), t_("HI"), 31, None, OP.bitwise_and)
-        lin("nfS", t_("nf"), -4096.0, 16.0)
-        tt(KM(0, 32), t_("HA"), t_("nfS"), OP.min)
-        tt(t_("kx"), KM(0, 16), KM(16, 32), OP.max)
+        for h in range(4):
+            mm(p_(2, 272 + 8 * h, 280 + 8 * h), gt(h % 2), t_("GS"), True, True)
+        tt(t_("HI"), t_("s12", 16, 544, 0, 17), p_(2, 272, 304), OP.min)
+        ts(t_("HA"), t_("HI"), int(BIG) + 31, None, OP.bitwise_and)
+        ts(KM(0, 32), t_("HA"), -BIG, -4080.0, OP.add, OP.max)
+        if t + 1 < STEPS:
+            ts(t_("ac", 0, 32, t), t_("HA"), BIG, None, OP.is_ge)
+            mm(p_(2, 304, 338), t_("ones"), t_("ac", c=t), True, True)
+            red(t_("A", c=t), p_(2, 304, 338))
+            host(t + 1)
+        tt(t_("kx"), t_("HA", 0, 16), t_("HA", 16, 32), OP.max)
         tt(t_("sm"), t_("kx"), t_("qs", 15, 256, t, 16), OP.max)
         ts(t_("sl"), t_("sm"), 15, None, OP.bitwise_and)
         cp(KM(32, 48), t_("sl"))
         cp(KM(48, 64), t_("sl"))
-        if "ca" in ON_S:
-            act(t_("ca"), KM(0, 16), AF.Relu, scale=17.0)
-        else:
-            ts(t_("ca"), KM(0, 16), 0.0, 17.0, OP.max, OP.mult)
-        ts(t_("cb"), KM(16, 32), 0.0, -144.0, OP.max, OP.add)
-        tt(KM(64, 80), t_("ca"), t_("cb"), OP.add)
-        for x in range(8):
+        lin("ca", KM(0, 16), -16.0, 16.0)
+        tt(KM(64, 80), t_("ca"), KM(16, 32), OP.subtract)
+        for x in range(4):
             if x < YV:
-                ts(y_(t, x, 64, 8, (0, 64)), KM(0, 80), t_("Gmf", x, x + 1), None, OP.mult, grp=("Y", t))
+                ts(y_(t, x, 32, 4), KM(0, 80), t_("Gm4", x, x + 1), None, OP.mult, grp=("Y", t))
             else:
-                act(y_(t, x, 64, 8, (0, 64)), KM(0, 80), AF.Copy, scale=t_("Gmf", x, x + 1), grp=("Y", t))
-        mm(p_(5, 0, 80), t_("I"), t_("ba"), True, False)
-        for k in range(8):
-            mm(p_(5, 0, 80), t_("RB", 112 - 16 * k, 240 - 16 * k), y_(t, 8 * k, 8 * k + 8, 1, (0, 64)), False, k == 7)
+                act(y_(t, x, 32, 4), KM(0, 80), AF.Copy, scale=t_("Gm4", x, x + 1), grp=("Y", t))
+        mm(p_(5, 0, 96), t_("I"), t_("ba"), True, False)
+        part["of"] = ".o"
+        i = mm(p_(5, 0, 48), t_("I"), t_("ordc"), False, False)
+        part["of"] = ""
+        for e in range(2):
+            before = i
+            for k in range(8):
+                a, rows = 112 - 16 * (k % 2), (64 * e, 64 * e + 64)
+                out = dict(p_(5, 16, 56), ap=T.P5[32 * (k // 2):32 * (k // 2) + 32, 2:12, 4 * e:4 * e + 4])
+                i = mm(out, t_("RB", a, a + 32, rows=rows), y_(t, 4 * k, 4 * k + 4, 1, rows), False, e == 1 and k % 2 == 1)
+                edges[i][before] = 1
         ol = lambda k, m=1: t_("ol", 16 * k, 16 * (k + m), t)
-        cp(ol(0, 5), p_(5, 0, 80))
-        tt(t_("kb", 16, 48, t), t_("ordc"), p_(5, 0, 32), OP.add)
-        ts(t_("pen"), p_(5, 16, 32), 4096.0, 3 * WN, OP.is_ge, OP.mult)
-        tt(t_("kb", 32, 48, t), t_("kb", 32, 48, t), t_("pen"), OP.add)
-        tt(t_("ybk"), ind(t_("X2", 0, 4097), ol(2)), t_("bs", c=t), OP.min)
-        act(t_("blog", n, n + 256), t_("ybk"), AF.Abs, bias=float(-t))
-        tt(t_("q1"), ind(t_("T1"), ol(4)), qg, OP.min)
+        cp(ol(0, 5), p_(5, 16, 96))
+        ts(t_("pen", 16, 32), p_(5, 32, 48), WO + 4096, 16.0, OP.is_ge, OP.mult)
+        tt(t_("ybk"), ind(t_("X2", 0, 2049), ol(2)), t_("bs", c=t), OP.min)
+        for h in range(2):
+            act(t_("blog", n + 128 * h, n + 128 * h + 128), t_("ybk", 128 * h, 128 * h + 128), AF.Abs, bias=float(-t - 2048 * h))
+        tt(t_("q1"), ind(t_("T1a", 0, 4096 + 257), ol(4)), qg, OP.min)
         tt(t_("qlog", n, n + 256), ind(t_("T2", c=t), ol(3)), t_("q1"), OP.max)
-        win = W(0, 8192)
+        win = dict(W(0, 8192), rg=W(0, 4096)["rg"] + m_(t, 0, 256)["rg"])
+        win2 = dict(W(-int(WO), 8192), rg=W(-int(WO), 4096)["rg"] + m_(t, 0, 256)["rg"] + (m_(t - 1, 0, 256)["rg"] if t % 2 else []))
         d1, d2 = t_("a12", 0, 256), t_("a12", 256, 512)
         tt(d1, ind(win, ol(0)), z, OP.subtract)
         act(t_("SG", 0, 256), d1, AF.Sigmoid, bias=-math.log(31.0), scale=-40.0)
         if A2 == "v":
-            tt(d2, ind(win, ol(1)), z, OP.subtract)
+            tt(d2, ind(win2, ol(1)), z, OP.subtract)
             mm(p_(7, 0, 256), t_("I"), d1, True, False)
             mm(p_(7, 0, 256), t_("nI"), d2, False, True)
             act(t_("SG", 256, 512), d2, AF.Sigmoid, bias=-math.log(31.0), scale=-40.0)
             act(t_("SG", 512, 768), p_(7, 0, 256), AF.Sigmoid, bias=-math.log(31.0), scale=40.0)
         else:
-            act(d2, ind(win, ol(1)), AF.Copy)
+            act(d2, ind(win2, ol(1)), AF.Copy)
             for k in range(2):
                 mm(p_(7, 256 * k, 256 * k + 256), t_("I"), z, k == 0, False)
+            part["last"] = None
+            mm(p_(7, 256, 512), t_("I"), d1, False, False)
             for k in range(2):
-                mm(p_(7, 256 * k, 256 * k + 256), t_("nI"), d2, False, False)
-            mm(p_(7, 256, 512), t_("I"), d1, False, True)
+                mm(p_(7, 256 * k, 256 * k + 256), t_("nI"), d2, False, k == 1)
             act(t_("SG", 256, 768), p_(7, 0, 512), AF.Sigmoid, bias=-math.log(31.0), scale=40.0)
-        to_list(p_(5, 256, 304), "SG", 0, 768)
         cnt = p_(5, 256, 304)
+        mm(p_(5, 256, 288), t_("I"), t_("pen"), True, False)
+        mm(p_(5, 288, 304), t_("I"), t_("pen", 16, 32), False, False)
+        to_list(cnt, "SG", 0, 768, first=False)
         ts(t_("rn"), cnt, 12582912.0, 12582912.0, OP.add, OP.subtract)
-        ts(th_(3, 6), cnt, 9.0, WN, OP.is_ge, OP.mult)
         ts(t_("thr"), cnt, 32.0 / 31, -7.5 / 31, OP.mult, OP.add)
+        ts(th_(3, 6), cnt, 9.0, WN, OP.is_ge, OP.mult)
         tt(t_("dd"), t_("rn"), t_("thr"), OP.subtract)
         ts(th_(0, 3), t_("dd"), 0.0, WN, OP.is_ge, OP.mult)
         tt(t_("KK"), th_(0, 6, 2), th_(1, 6, 2), OP.add)
-        tt(t_("KL"), t_("KK"), t_("kb", c=t), OP.add)
+        tt(t_("KL"), t_("KK"), p_(5, 0, 48), OP.add)
         k0, k1, k2 = t_("KL", 0, 16), t_("KL", 16, 32), t_("KL", 32, 48)
         cross = t + 2 < STEPS
         tt(t_("mna"), k0, k1, OP.min)
@@ -674,7 +794,7 @@ def rank_program(g, core, T, topo):
     part.update(name="end.", runs={}, last=None)
     for k, (a, b) in enumerate(quarters):
         lst = t_("plF", a // 16, b // 16)
-        act(t_("q4", a, b), ind(t_("qlog"), lst), AF.Copy, scale=4096.0)
+        act(t_("q4", a, b), ind(t_("qlog"), lst), AF.Identity, bias=-4096.0 * Q0, scale=4096.0 * 256)
         tt(t_("yb", a, b), ind(t_("blog"), lst), t_("q4", a, b), OP.add)
         store("sb%d" % k, T.ybank[:, a:b], t_("yb", a, b))
         if YI[k] == "v":
@@ -695,7 +815,7 @@ def rank_program(g, core, T, topo):
             if "proxy" in ops[i]:
                 l = COST["link"]
             succ[j].append((i, l))
-    order = list_schedule(n, [o["q"] for o in ops], [o["cost"] for o in ops], succ, [len(e) for e in edges], urgency(ops, succ, lag, DUE))[0]
+    order = list_schedule(n, [o["q"] for o in ops], [o["cost"] for o in ops], *timetable(ops, edges, succ, lag))[0]
 
     eng = {"v": g.vector, "s": g.scalar, "p": g.tensor, "g": g, "y": g.sync}
     total = {}

@@ -6,36 +6,35 @@ OP = AluOpType
 AF = ActivationFunctionType
 BIG = 131072.0
 Q0 = 192.0
-WN, WO = 32768.0, 8192.0
 STEPS = 6
 LOG = 1024 + 256 * STEPS
 TILES = {
     "z": (256, "bfloat16", 7), "bk": (1024, "int32", 1), "wti": (1, "int32", 1),
-    "T1a": (272, "bfloat16", 1), "LR": (2048, "bfloat16", 1), "Bt": (1024, "bfloat16", 1), "C16": (256, "bfloat16", 1), "d16": (256, "bfloat16", 1),
-    "RB": (240, "bfloat16", 1), "T1b": (272, "bfloat16", 1), "X2": (2064, "bfloat16", 1), "geno_s": (4096, "bfloat16", 1), "W": (8192, "bfloat16", 2),
+    "T1a": (272, "bfloat16", 1), "LR": (1920, "bfloat16", 1), "Bt": (256, "bfloat16", 1), "T3": (1040, "bfloat16", 1), "C16": (256, "bfloat16", 1),
+    "d16": (256, "bfloat16", 1), "ba": (80, "bfloat16", 1), "c05": (16, "bfloat16", 1), "T1b": (272, "bfloat16", 1),
+    "RB": (240, "bfloat16", 1), "X2": (2064, "bfloat16", 1), "geno_s": (4096, "bfloat16", 1), "W": (8192, "bfloat16", 2),
     "blog": (LOG, "float32", 1), "qlog": (LOG, "bfloat16", 1), "ilog": (LOG, "bfloat16", 1), "ptab": (1040, "float32", 1), "psrc": (256, "float32", 6),
-    "EW": (144, "bfloat16", 1), "ptb": (1040, "bfloat16", 1), "psb": (256, "bfloat16", 1), "hb": (16, "float32", 2), "rn": (48, "float32", 1), "thr": (48, "float32", 1), "dd": (48, "float32", 1),
+    "EW": (144, "bfloat16", 1), "ptb": (1024, "bfloat16", 1), "hb": (16, "float32", 2),
     "Iq": (128, "bfloat16", 1), "T2": (32, "bfloat16", 6), "cq": (256, "bfloat16", 1),
     "q4": (1024, "float32", 1), "yb": (1024, "float32", 1), "yi": (1024, "bfloat16", 1), "plF": (64, "uint16", 1),
-    "pI": (1, "int32", 1), "pM": (1, "int32", 1), "pG": (1, "int32", 1), "p8": (1, "int32", 1), "col": (1, "float32", 17),
-    "ic": (256, "float32", 1), "lnO": (16, "float32", 1),
-    "I": (128, "bfloat16", 1), "nI": (128, "bfloat16", 1), "I16": (128, "bfloat16", 1), "I31": (128, "bfloat16", 1), "J": (128, "bfloat16", 1), "IB": (136, "bfloat16", 1), "XG": (128, "bfloat16", 1),
+    "pI": (1, "int32", 1), "pM": (1, "int32", 1), "pG": (1, "int32", 1), "p8": (1, "int32", 1), "col": (1, "float32", 15),
+    "ic": (256, "float32", 1), "lnO": (16, "float32", 1), "lnq": (16, "float32", 1),
+    "I": (128, "bfloat16", 1), "nI": (128, "bfloat16", 1), "I16": (128, "bfloat16", 1), "I9": (128, "bfloat16", 1), "J": (128, "bfloat16", 1),
+    "IB": (136, "bfloat16", 1), "XG": (128, "bfloat16", 1),
     "Gmf": (8, "float32", 1), "Gm4": (4, "float32", 1), "GS": (8, "bfloat16", 1), "G64": (8, "bfloat16", 1), "G32": (8, "bfloat16", 1),
-    "EB": (144, "bfloat16", 1), "wE": (144, "float16", 1),
-    "eq": (16, "float32", 1), "le": (16, "float32", 1), "ne": (16, "float32", 1),
-    "C17": (136, "bfloat16", 1), "d17": (136, "bfloat16", 1),
-    "ones": (128, "bfloat16", 1), "ba": (96, "bfloat16", 1), "ordc": (48, "bfloat16", 1),
-    "T1s": (544, "bfloat16", 1), "E16": (128, "bfloat16", 1), "b0": (256, "int32", 1), "pw": (8, "float32", 1), "p8e": (8, "float32", 2), "p8f": (1, "float32", 1), "xi": (256, "int32", 1), "xj": (256, "int32", 1),
-    "ui": (16, "float32", 2), "c05": (16, "bfloat16", 1), "UV": (32, "int32", 2), "s": (16, "float32", 2), "sq": (16, "float32", 2), "VV": (32, "int32", 2), "vl": (32, "uint16", 3),
-    "vh": (16, "float16", 2), "G": (256, "bfloat16", 1), "pl": (16, "uint16", 2), "wl": (32, "uint16", 2),
+    "EB": (144, "bfloat16", 1), "wE": (144, "float16", 1), "eq": (16, "float32", 1), "ne": (16, "float32", 1),
+    "C17": (136, "bfloat16", 1), "d17": (136, "bfloat16", 1), "ones": (128, "bfloat16", 1),
+    "T1s": (544, "bfloat16", 1), "E16": (128, "bfloat16", 1), "b0": (256, "int32", 1), "pw": (8, "float32", 1), "p8e": (8, "float32", 2),
+    "p8f": (1, "float32", 1), "xi": (256, "int32", 1), "xj": (256, "int32", 1),
+    "ui": (16, "float32", 2), "UV": (32, "int32", 2), "s": (16, "float32", 2), "sq": (16, "float32", 2), "VV": (32, "int32", 2), "vl": (16, "uint16", 3),
+    "vh": (32, "float16", 2), "G": (256, "bfloat16", 1), "pl": (16, "uint16", 2), "wl": (32, "uint16", 2), "E": (256, "bfloat16", 1),
     "boff": (256, "uint16", 2), "bs": (256, "float32", 2), "qg": (256, "bfloat16", 2), "im1": (256, "bfloat16", 2), "fl": (256, "bfloat16", 2), "gt": (256, "bfloat16", 2),
-    "qs": (256, "float32", 2), "ac": (34, "bfloat16", 1), "A": (1, "float32", 2),
-    "s12": (576, "float32", 1), "m": (288, "float32", 1), "HI": (32, "int32", 1), "HA": (32, "int32", 1),
+    "qs": (256, "float32", 2), "ac": (34, "bfloat16", 1), "A": (1, "float32", 2), "s12": (576, "float32", 1), "HI": (32, "int32", 1), "HA": (32, "int32", 1),
     "KM": (80, "bfloat16", 2), "kx": (16, "float32", 1), "sm": (16, "int32", 1), "sl": (16, "int32", 1), "ca": (16, "float32", 1),
-    "ol": (80, "uint16", 2), "o2": (16, "uint16", 1), "nz": (128, "bfloat16", 1), "pen": (32, "bfloat16", 1), "ybk": (256, "float32", 1), "q1": (256, "bfloat16", 1),
-    "a12": (512, "bfloat16", 1), "SG": (768, "bfloat16", 1), "E": (256, "bfloat16", 1), "KK": (48, "float32", 1), "KL": (48, "float32", 1),
-    "mna": (16, "float32", 1), "mxa": (16, "float32", 1), "tta": (16, "float32", 1), "FM": (32, "int32", 1), "FA": (32, "int32", 1), "fml": (32, "uint16", 2),
-    "Bm": (256, "bfloat16", 2), "cx": (512, "bfloat16", 4),
+    "ol": (80, "uint16", 2), "pen": (32, "bfloat16", 1), "ybk": (256, "float32", 1), "q1": (256, "bfloat16", 1),
+    "d12": (512, "bfloat16", 1), "a2": (256, "bfloat16", 1), "SG": (768, "bfloat16", 1), "ti": (48, "int32", 1), "mk": (48, "int32", 1),
+    "nb": (48, "bfloat16", 1), "C": (48, "bfloat16", 1), "R": (32, "float32", 1), "ad": (32, "float32", 1), "K": (32, "float32", 1),
+    "mna": (16, "float32", 1), "mnb": (16, "float32", 1), "fl1": (16, "uint16", 2), "cl": (32, "uint16", 2), "cx": (512, "bfloat16", 4),
 }
 BYTES = {"float32": 4, "int32": 4, "bfloat16": 2, "uint16": 2, "float16": 2}
 PLACE = {}
@@ -50,191 +49,48 @@ for _k in range(8):
     SCRATCH["P%d" % _k] = ("psum", [128, 64, 8] if _k == 5 else [128, 512], "float32")
 for _k in range(2):
     SCRATCH["Yc%d" % _k] = ("sbuf", [128, 10, 32], "bfloat16")
-SCRATCH["TH3"] = ("sbuf", [128, 6, 16], "float32")
+SCRATCH["TH"] = ("sbuf", [128, 6, 16], "bfloat16")
 LOADS = ["bites", "wt", "bank", "immun", "geno"]
-STORES = ["sg", "sb0", "sb1", "sb2", "sb3", "si0", "si1"]
+OUTS = [("yb", 0, 512, "y"), ("yb", 512, 1024, "y"), ("yi", 0, 1024, "s")]
+STORES = ["sg"] + ["so%d" % k for k in range(len(OUTS))]
 SEMAPHORES = ["qv", "qs", "qp", "qg", "rl"] + ["arr%d" % t for t in range(1, STEPS)] + ["ld_" + n for n in LOADS] + ["st_" + n for n in STORES]
 
-
-COST = {"us": 0.00083 * 1.25, "ps": 0.00071 * 1.25, "gather": 1.56, "scatter": 3.8, "wake": 0.08, "link": 5.5, "issue": 1.0, "dma": 2.5, "add": 0.0013}
-LOOK = 0.3
-PERIOD = 14.46
-TAIL = 9.5
-RUN = 0.07
-GAP = {'vcx': .01, 'vboff': .01, 'vbs': .01, 'sblog': .01, 'pP7I': .01, 'pP7nI': .01, 'pP0I': .01, 'pP5I2': .01, 'sptab': .21, 'sYc0': .083}
-DUE = {'vboff': -13.249, 'sW.0': -13.05, 'sW.1': -11.625, 'sW.2': -10.731, 'sqg': -9.009, 'sW.3': -8.53, 'sim1': -6.186, 'sW.4': -5.706, 'sgt': -4.813, 'sptab': -4.547, 'sBm': -2.626, 'vW.5': -12.27, 'vfl': -7.453, 'pP2qg': -7.523, 'pP6fl': -7.182, 'pP1fl': -7.054, 'vW.m0': -11.549, 'vW.m1': -10.651, 'vW.m2': -7.32, 'vW.m3': -6.106, 'vW.m4': -5.043, 'vW.m5': -4.247, 'pP1W.c0': -8.886, 'pP1W.m': -6.87, 'pP6W.c1': -5.961, 'pP6W.c2': -4.733, 'pP6W.m': -3.994, 'pP4nI': -5.279, 'pP6gt': -4.307, 'pP1gt': -4.222, 'pP4I': -9.241, 'pP0I': -12.805, 'pP6I': -9.511, 'pP1I': -9.014, 'pP2J': -7.75, 'vs12.0': -3.715, 'vm.0': -3.433, 'vs12.2': -3.152, 'vs12.1': -3.003, 'vm.1': -2.773, 'vs12.3': -2.545, 'vqs': -4.977, 'vbs': -3.566, 'vHI': -2.315, 'vHA': -2.169, 'vkx': -1.884, 'vac': -2.023, 'vKM': -1.738, 'vsm': -1.671, 'vca': -1.538, 'vsl': -1.472, 'vA': -1.406, 'vKM3': -1.339, 'vKM2': -1.273, 'vUV2': -1.14, 'vYc0': -1.06, 'sYc0': -1.06, 'pP5I': -9.383, 'pP5RB': -0.648, 'vol': 0.0, 'pP7I': -8.829, 'pP3wE': -3.086, 'vui': -2.097, 'vUV': -1.95, 'vs': -1.804, 'vsq': -1.605, 'pP2ones': -1.876, 'vVV': -0.927, 'vvl': -0.728, 'vvh': -0.662, 'sG': -0.582, 'gW.0': -3.914, 'gW.1': -3.006, 'ggeno_s': -4.733, 'vybk': 0.163, 'sa12': 0.163, 'va12': 0.627, 'sblog': 0.707, 'vpen': 1.158, 'sSG': 1.172, 'pP7nI': 0.887, 'pP7I2': 1.341, 'sSG2': 2.331, 'vq1': 1.752, 'vqlog': 2.681, 'pP4EW': -0.022, 'vpl': 1.092, 'pP5I2': 1.568, 'pP5EB': 3.045, 'pP3LR': 2.136, 'vE': 3.544, 'pP3I': 3.954, 'pP3EB': 4.011, 'vwl': 8.23, 'vrn': 4.034, 'pP5I31': 4.181, 'vTH3': 4.384, 'vTH32': 4.318, 'vKK': 4.531, 'vKL': 4.71, 'vmxa': 4.857, 'vmna': 4.923, 'vtta': 5.056, 'vFM': 5.122, 'vFM2': 5.202, 'vFA': 5.349, 'vfml': 5.495, 'vcx': 5.641, 'gg': 6.65, 'vilog': 6.57}
-PERIOD = 14.679
-DUE = {'ggeno_s': -4.52, 'gW.0': -4.04, 'gW.1': -2.35, 'gg': 6.45, 'pP0I': -13.52, 'pP6I': -10.63, 'pP1I': -9.95, 'pP5I': -9.5, 'pP4I': -9.06, 'pP1W.c0': -8.87, 'pP7I': -8.56, 'pP2qg': -7.87, 'pP1fl': -7.05, 'pP6fl': -6.56, 'pP2J': -6.54, 'pP1W.m': -6.39, 'pP6W.c1': -5.77, 'pP4nI': -5.54, 'pP6W.c2': -4.89, 'pP6W.m': -4.28, 'pP1gt': -4.25, 'pP6gt': -4.2, 'pP3wE': -2.83, 'pP2ones': -1.91, 'pP5RB': -0.65, 'pP4EW': 0.12, 'pP7nI': 1.03, 'pP7I2': 1.49, 'pP3LR': 1.8, 'pP5I2': 2.17, 'pP5EB': 3.11, 'pP3I': 4.13, 'vthr': 4.23, 'vdd': 4.66, 'pP3EB': 4.34, 'sW.0': -13.89, 'sW.1': -12.04, 'sW.2': -10.77, 'sqg': -9.2, 'sW.3': -8.72, 'sim1': -6.33, 'sW.4': -6.21, 'sgt': -5.57, 'sBm': -4.61, 'sptab': -3.81, 'sYc0': -1.11, 'sG': -0.43, 'sa12': -0.04, 'sblog': 0.71, 'sSG': 1.17, 'sSG2': 2.19, 'vboff': -13.46, 'vW.5': -12.31, 'vW.m0': -11.28, 'vW.m1': -10.17, 'vfl': -8.72, 'vW.m2': -7.61, 'vW.m3': -5.74, 'vqs': -4.71, 'vW.m5': -4.59, 'vW.m4': -4.39, 'vbs': -3.96, 'vm.0': -3.92, 'vKM': -3.63, 'vHI': -2.75, 'vs12.0': -2.73, 'vs12.1': -2.69, 'vHA': -2.6, 'vs12.2': -2.49, 'vs12.3': -2.48, 'vui': -2.44, 'vm.1': -2.31, 'vkx': -1.92, 'vUV': -1.86, 'vsm': -1.72, 'vac': -1.55, 'vca': -1.51, 'vsl': -1.49, 'vs': -1.41, 'vKM3': -1.27, 'vKM2': -1.13, 'vsq': -0.99, 'vA': -0.93, 'vYc0': -0.86, 'vUV2': -0.77, 'vVV': -0.28, 'vvl': -0.12, 'vybk': 0.26, 'vol': 0.5, 'va12': 0.93, 'vpl': 1.02, 'vpen': 1.17, 'vvh': 1.24, 'vq1': 2.05, 'vqlog': 2.63, 'vE': 3.81, 'vmna': 3.99, 'vmxa': 4.09, 'vrn': 4.22, 'vTH3': 4.64, 'vTH32': 4.71, 'vKK': 4.79, 'vKL': 4.92, 'vtta': 5.12, 'vFA': 5.15, 'vFM': 5.22, 'vFM2': 5.29, 'vfml': 5.72, 'vcx': 5.82, 'vilog': 6.88, 'vwl': 8.76}
-ORDER = {
-    'v': 'a12 ybk q1 pen pl boff+*2 qlog W.5+ rn thr TH3 dd TH32 KK M.m0+ KL M.m0+ mxa mna tta FM FM2 M.m0+ FA M.m0+ fml E cx*2 fl+ M.m0+*12 M.m1+*16 ilog M.m2+*11 wl M.m2+*5 M.m3+*12 s12.0+ M.m3+*4 qs+ m.0+ s12.1+ m.1+ s12.2+ s12.3+ HI+ HA+ kx+ KM+ ac+ sm+ ca+ sl+ KM3+ ui+ KM2+ UV+ KM2+ s+ A+ sq+ Yc0+ UV2+ Yc0+*2 VV+ Yc0+ vl+ bs+ vh+ bs+ ol+',
-    's': 'a12 SG blog*2 SG2 W.0+ W.1+ qg+ W.2+ W.3+ W.4+ im1+ ptab+*5 gt+ ptab+ Bm+ ptab+*8 Yc0+*3 ptab+ Yc0+ ptab+ G+',
-    'p': 'P5I2 P3LR*3 P5I2 P5EB*16 P4I+ P2J+ P3LR*13 P2qg+*2 P3I P3EB*16 P1W.c0+*16 P6fl+ P1fl+ P1M.m+*16 P6W.c1+*16 P6W.c2+*16 P4nI+ P6M.m+*16 P5I+*2 P2gt+*4 P3wE+*16 P0I++ P2ones+ P6I++ P1I++ P7I+*2 P5RB+*8 P4EW+*13 P7I2+ P7nI+*2 P4EW+*3',
-    'g': 'g M.0+ geno_s+ M.1+',
-}
 FIRST = {
-    'v': '_J _pM _pG _p8 _pw _EB _col _pw _col*2 _pw _col _p8f _pw _Gmf _eq _ne _p8e _EB _le _p8e _col7 _col6 _col7*2 _xi _p8e2 _xj _p8e2 _col2 _Bt _col2 _col8 _col2 _hb _wE _hb _LR*14 _ui _qlog _UV _LR _s _LR _sq _col3 _UV2 _col4 _VV _qlog _vl _vh b0 _qlog boff b0 _C16 boff _qlog _E W.5 _wl _IB _blog _blog2 M.m0*16 fl M.m1*16 ui _col8 UV _col5 s _lnO sq _col5 M.m2*16 _blog3 _blog4 M.m3*16 s12.0 qs m.0 _ac*2 s12.1 s12.2 m.1 _EW _RB s12.3 _ba HI _T2 HA kx ac KM sm ca sl A KM3 KM2 UV2 KM2 VV Yc0*2 vl Yc0*2 bs*2 vh ol',
-    's': '_wti _ones _X2*16 _G32 _G64 _GS _I16 _nI _Iq _ptab*4 _psrc*5 W.0 W.1 ptab qg ptab W.2 ptab W.3 ptab W.4 ptab im1 ptab _psrc ptab _ba*2 ptab _ba*2 ptab gt ptab*2 Bm ptab _T1a ptab*2 _T1b ptab*2 Yc0*4 G _T2*5',
-    'p': '_P3wE*16 P0I P4I _P3LR*16 P6I P1I P2J _P5J _P5Iq _P3I _P3EB*16 _P7J _P7Iq P1W.c0*16 P2qg*2 _P5J2 _P5Iq2 P1fl P6fl P3wE*4 P1M.m*16 _P7J2 _P7Iq2 P3wE*5 P6W.c1*16 P3wE*2 P6W.c2*16 P3wE*5 P4nI P6M.m*16 _P7E16 P2gt*4 P5I*2 P0I+ _P7E162 P2ones P6I+ P1I+ P7I*2 P5RB*8 P4EW*13 P7I2 P7nI*2 P4EW*3',
-    'g': '_pI _ic _XG*3 _I _XG _g _C17 _C16 _C172 _cq _lnO _RB _d16*2 _d17 _m _d17 _ba _ordc*2 _T1s _E16 _T1s*3 _Bt M.0 _Bt*2 geno_s _X2*2 _pen M.1',
-}
-FINAL = {
-    'v': 'a12 pen ybk q1 pl boff+*2 qlog E W.5+ rn thr TH3 dd TH32 M.m0+ KK KL fl+ mna M.m0+*5 FM M.m0+*2 FA M.m0+*4 fml M.m0+*2 ilog wl M.m0+*2 M.m1+*16 M.m2+*16 M.m3+*12 s12.0+ M.m3+*4 qs+ m.0+ s12.1+ s12.2+ m.1+ s12.3+ bs+ HI+ HA+ kx+ KM+ sm+ ca+ sl+ KM3+ KM2+*2 bs+ Yc0+*4 ol+ a12+ pen+ q1+ qlog+ plF+ ybk+ rn+ thr+ TH3+ dd+ TH32+ ^yb+ KK+ KL+ mna+ FM+ FA+ fml+ ilog+ ^yb2+ ^yb3+ ^yb4+ ^yi+',
-    's': 'a12 SG blog*2 SG2 W.0+ W.1+ qg+ W.2+ W.3+ W.4+ ptab+ im1+ ptab+*7 gt+ ptab+*8 Yc0+*4 ptb+*2 a12+ SG+ SG2+ ^q4+ blog+*2 ^q42+ ^q43+ ^q44+ ^yi+ ^yi2+ ^yi3+',
-    'p': 'P3LR*16 P5I2*2 P5EB*16 P3I P3EB*16 P2J+ P4I+ P2qg+*2 P6fl+ P1fl+ P1W.c0+*16 P1M.m+*16 P6W.c1+*16 P6W.c2+*16 P4nI+ P6M.m+*16 P2gt+*4 P7I+*2 P5I+*2 P5RB+*8 P7I2+ P7nI+*2 P3EW.F+*10 P5I2+*2 P3EW.F+*6 P5EB+*16',
-    'g': 'M.0+ geno_s+ M.1+ ptb+*2',
+    'v': '_pw*2 _J _pw _col _pM _pG _col*2 _p8 _col6 _EB _Gmf _col4 _ac _ne _pw _P3 _eq _p8f _lnO _c05 _col _col6 _p8e _col3 _EB _p8e _c05 _col2 _col5 _col2*2 _col6 _wE _xi _xj _Bt _ui _p8e2 _s _hb _UV.u _hb _qlog _UV _qlog _VV _qlog _vl _qlog b0 _vh _col4 boff b0 _LR*5 boff _LR*10 W.5 _blog bs fl _ac _IB _blog2 _p8e2 _C16 _E M.m1*6 M.m0*8 _T2 M.m4*2 M.m1*2 _wl _col7 M.m4*2 M.m0*6 M.m1*6 M.m0*2 M.m2*4 M.m1*2 M.m2*8 M.m4*2 M.m3*4 _RB M.m3*2 s12.0 M.m2*4 M.m3*2 M.m4*2 _T3 qs s12.2 s12.1 ui s12.3 _Gm4 HI s HA UV.u kx ac sm KM sl ca KM2*2 KM3 A _col7 Yc0 _EW Yc0 bs blog UV blog2 VV ol vl ybk d12 d122 vh _T3 pl boff+ q1',
+    's': '_wti _ones _X2*8 _ba _nI _ba _G32 _X2*4 _GS _I16 _Iq _sq _ptab _psrc _ptab _ba _G64 _ptab*2 qg W.0 W.1 W.4 W.2 ptab W.3 ptab _ba ptab im1 ptab _T1a ptab gt ptab _I9 ptab _X2*4 ptab*2 sq ptab _T1b ptab Yc0*2 ptab T2 ptab _psrc ptab*3 pen G _lnq blog ad blog SG _psrc',
+    'p': '_P3J _P3wE*16 _P3LR*10 P0I*2 _P5J P0I P6I _P5Iq P1I _P7J P0I*2 P4I _P7Iq _P3LR*5 _P3I _P3I16*5 P1W.c0*4 _P3I16*10 _P5E16 P3J P6W.c2*4 P3wE*4 P6W.c2*4 P1M.m*8 P6fl P3wE*4 P2J P3wE*4 P1M.m*4 P2qg*2 P1W.c0*4 P6W.c2*4 P3wE*4 P1W.c0*4 P6W.c2*4 P1W.c0*4 P1M.m*4 P1fl P6W.c1*4 P6M.m*8 P4nI P6W.c1*12 P6M.m*8 P4gt*2 _P5E162 P4gt*2 P1J P1Iq P6J P7J P0I+ P6Iq P5I P0I+',
+    'g': '_pI _lnO _ic _X2 _cq _d17 _I _C17 _XG _g _XG*2 _d17 _XG _pen _d16 _T1s _C172 _C16 _T1s _E16 _T1s _T3 _d16 _RB _X2 _T1s _ba M.1 geno_s M.0',
 }
 ORDER = {
-    'v': 'a12 ybk pen q1 pl boff+*2 qlog W.5+ rn thr dd TH3 TH32 KK KL M.m0+ mxa mna tta FM FM2 M.m0+ FA E fml M.m0+ cx*2 fl+ M.m0+*13 wl M.m1+*16 ilog M.m2+*16 M.m3+*16 s12.0+ qs+ m.0+ s12.1+ s12.2+ m.1+ s12.3+ HI+ HA+ kx+ KM+ ac+ sm+ ca+ sl+ ui+ KM2+*2 s+ KM3+ A+ Yc0+*2 UV+*2 VV+ vl+ bs+*2 vh+ ol+',
-    's': 'a12 SG psrc+ blog*2 SG2 T2+ W.0+ W.1+ qg+ W.2+ W.3+ ptab+ W.4+ ptab+ im1+ ptab+*4 gt+ ptab+*4 Bm+ ptab+*4 sq+ Yc0+*2 ptab+*2 G+',
-    'p': 'P4EW*7 P7I2 P7nI*2 P4EW*7 P5I2*2 P5EB*16 P3LR*16 P2J+ P4I+ P2qg+*2 P3I P3EB*16 P1W.c0+*16 P1fl+ P6fl+ P1M.m+*16 P6W.c1+*16 P6W.c2+*16 P4nI+ P6M.m+*16 P2gt+*4 P5I+ P3J+ P3wE+*16 P2ones+ P0I++ P7I+*2 P5I.o+ P5RB+*16 P1I++ P6I++ P4EW+*2',
+    'v': 'boff+ qlog ti TH mk E TH.l W.6+ C M.m0+*6 cl M.m0+*2 cx M.m1+*2 K M.m0+*2 M.m1+*2 M.m0+*4 mna M.m1+*6 M.m0+*2 M.m1+*2 mnb M.m1+*2 wl M.m2+*2 fl1 fl+ M.m2+*4 M.m1+*2 M.m2+*4 M.m3+*2 M.m2+*2 ilog M.m3+*2 M.m2+*2 M.m4+*6 M.m3+*2 M.m4+*2 M.m3+*2 M.m2+*2 qs+ s12.0+ s12.1+ s12.2+ s12.3+ HI+ HA+ kx+ KM+ sm+ ca+ sl+ KM3+ KM2+*2 ac+ ui+ Yc0+ s+ Yc0+ bs+ A+ bs+ UV.u+ UV+ VV+ vl+ ol+ vh+ ybk+ d12+ d122+ pl+ boff++ q1+',
+    's': 'SG2 SG3 W.0+ W.1+ W.2+ W.3+ qg+ W.4+ W.5+ ptab+ im1+ ptab+*3 gt+ ptab+ T2+ ptab+*7 Yc0+*2 ptab+ sq+ ptab+*2 psrc+ ptab+ G+ a2+ pen+ blog+*2 ad+ SG+',
+    'p': 'P0I+ P5RB*16 P4I.u P2EW*16 P7I P7nI P1I+ P3LR*5 P5I9.p P3LR*5 P0I+*2 P5I9.p P5EB*16 P3LR*5 P4I.u P2I.g P0I+ P2I.g P2I.l P2nI.l*3 P3I P3I16*5 P6I+ P4I.c*2 P4nI.c P4I.k*2 P4nI.k P3I16*10 P1W.c0+*4 P2J+ P1W.c0+*4 P4I+ P1M.m+*12 P2qg+*2 P1W.c0+*4 P1M.m+*4 P6W.c1+*16 P1W.c0+*4 P1fl+ P6W.c2+*12 P6M.m+*4 P6W.c2+*4 P6M.m+*4 P4nI+ P6fl+ P6M.m+*8 P5I+ P4gt+*2 P3J+ P4gt+*2 P3wE+*16 P7J+ P0I++',
     'g': 'g M.0+ geno_s+ M.1+',
 }
-FIRST = {
-    'v': '_J _pM _pG _p8 _pw _EB _col _pw _col*2 _pw _col _p8f _pw _Gmf _eq _ne _p8e _EB _le _p8e _col7 _col6 _col7*2 _xi _c05*2 _xj _col2 _Bt _col2 _p8e2 _col2 _hb _wE _hb _LR*14 _ui _qlog _s _LR*2 _p8e2 _col3 _UV*2 _qlog _VV _col4 _vl _vh b0 _qlog boff b0 _C16 boff _qlog _E W.5 _wl _IB _blog _blog2 M.m0*16 fl M.m1*8 ui M.m1*2 s M.m1*6 _col8*2 UV _col5 _lnO _col5 M.m2*16 _ba qs M.m3*16 s12.0 _RB _EW m.0 _ac*2 s12.1 s12.2 m.1 bs s12.3 bs HI _T2 HA _Gm4 kx ac KM sm ca sl KM3 KM2*2 A Yc0 UV Yc0 VV vl vh blog blog2 ol',
-    's': '_wti _ones _X2*16 _G32 _G64 _GS _I16 _nI _Iq _sq _ptab*4 _psrc*3 W.0 W.1 qg W.2 W.3 ptab W.4 ptab im1 ptab _ba ptab _ba ptab gt ptab _ba ptab _ba ptab sq ptab _T1a ptab _T1b ptab Bm ptab*2 Yc0 ptab Yc0 ptab T2 ptab G',
-    'p': '_P3J _P3wE*16 P0I P4I _P3LR*16 P6I P1I P2J _P5J _P5Iq _P3I _P3EB*16 _P7J _P7Iq P3J P3wE*16 P1W.c0*16 P2qg*2 P1fl P6fl P1M.m*16 _P7E16 P6W.c1*16 P6W.c2*16 P4nI P6M.m*16 P2gt*4 P5I P1J P1Iq _P7E162 P2ones P6J P6Iq P7I*2 P5I.o P5RB*16 P0I+ P4EW*2 P1I+ P6I+',
-    'g': '_pI _ic _XG*3 _I _XG _g _C17 _C16 _C172 _cq _lnO _d16*2 _T1s _E16 _T1s*3 _d17 _m _d17 _RB _ba _ordc*2 _Bt M.0 _Bt*2 geno_s _X2*2 _pen M.1',
-}
 FINAL = {
-    'v': 'a12 ybk pen q1 pl boff+*2 qlog W.5+ E rn thr TH3 dd M.m0+ TH32 M.m0+ KK M.m0+*2 KL M.m0+ fl+ mna wl M.m0+ FM M.m0+*2 FA M.m0+*2 fml M.m0+*6 ilog M.m1+*16 M.m2+*16 M.m3+*16 s12.0+ qs+ m.0+ s12.1+ s12.2+ m.1+ bs+ s12.3+ bs+ HI+ HA+ kx+ KM+ sm+ ca+ sl+ KM3+ KM2+*2 Yc0+*2 ol+ a12+ pen+ q1+ qlog+ ybk+ plF+ rn+ thr+ TH3+ dd+ TH32+ KK+ KL+ mna+ FM+ FA+ fml+ ilog+ ^yb+ ^yb2+ ^yb3+ ^yb4+',
-    's': 'a12 SG blog*2 SG2 W.0+ W.1+ qg+ W.2+ W.3+ ptab+ W.4+ ptab+ im1+ ptab+*6 gt+ ptab+*8 Yc0+*2 ptb+*3 a12+ SG+ SG2+ blog+*2 ^q4+ ^q42+ ^q43+ ^q44+ ^yi+ ^yi2+ ^yi3+ ^yi4+',
-    'p': 'P4EW*6 P7I2 P7nI*2 P4EW*8 P3LR*8 P5I2*2 P5EB*16 P3LR*8 P2J+ P4I+ P3I P3EB*16 P2qg+*2 P1W.c0+*16 P6fl+ P1fl+ P1M.m+*16 P6W.c1+*16 P6W.c2+*16 P4nI+ P6M.m+*16 P2gt+*4 P7I+*2 P5I+ P5I.o+ P5RB+*16 P3EW.F+*8 P7I2+ P7nI+*2 P5I2+*2 P3EW.F+*8 P5EB+*16',
-    'g': 'M.0+ geno_s+ M.1+ ptb+',
+    'v': 'boff+ qlog W.6+ ti E mk M.m0+*2 TH M.m0+*2 TH.l M.m0+*2 nb M.m1+*2 C M.m1+*2 C M.m1+*2 M.m0+*2 M.m1+*6 R M.m0+*2 M.m1+*2 M.m0+*2 K M.m0+*2 mna M.m0+*2 mnb M.m2+*2 M.m1+*2 fl1 M.m2+*4 ilog M.m2+*2 wl M.m3+*2 fl+ M.m3+*2 M.m2+*4 M.m4+*4 M.m3+*2 M.m2+*2 M.m4+*4 M.m3+*2 M.m2+*2 s12.0+ qs+ s12.1+ s12.2+ s12.3+ HI+ HA+ kx+ KM+ sm+ ca+ sl+ KM3+ KM2+*2 Yc0+*2 ol+ d12+ bs+ q1+ bs+ qlog+ plF+ ybk+ ti+ TH+ mk+ TH.l+ nb+ C+*2 R+ K+ mna+ ^yb2+ mnb+ fl1+ ^yb+ ilog+ ^yb3+ ^yb4+ ^yi+',
+    's': 'SG2 W.1+ W.0+ W.2+ qg+ W.3+ W.4+ W.5+ ptab+ im1+ ptab+*4 gt+ ptab+*9 Yc0+*2 ptab+*2 ptb+*2 a2+ ad+ pen+ SG+ SG2+ ^q42+ ^q4+ blog+*2 ^q43+ ^q44+ ^yi+*3 ^outso2+',
+    'p': 'P5RB*16 P7I.z P4I+ P1I+ P7I.z P2EW*16 P7I P7nI*2 P5I9.p P0I+ P3LR*5 P5I9.p P0I+ P5EB*4 P3LR*5 P5EB*8 P0I+ P5EB*4 P3LR*5 P0I+ P1M.m+*4 P2J+ P3I P7I.z+ P3I16*5 P1W.c0+*4 P3I16*5 P1W.c0+*4 P3I16*5 P6I+ P1M.m+*4 P5I+ P6W.c1+*12 P1M.m+*4 P1W.c0+*4 P1M.m+*4 P6fl+ P6W.c2+*8 P6W.c1+*4 P1W.c0+*4 P6W.c2+*4 P2qg+*2 P6M.m+*4 P4nI+ P6W.c2+*4 P1fl+ P6M.m+*12 P4gt+ P7I.z+ P4gt+*3 P5RB+*16 P7I+ P7nI+*2 P5I9.p+ P3EW.F+*8 P5I9.p+ P3EW.F+*8 P5EB+*16',
+    'g': 'M.0+ M.1+ ptb+*2 geno_s+',
 }
-PARTS = [[("s", 0, 32), ("s", 32, 64), ("s", 64, 128 - v), ("s", 128, 224), ("s", 224, 256), ("v", 128 - v, 128)] for v in (40, 14, 14, 14, 14, 40)]
-PARTS[0] = [("s", 0, 32), ("s", 32, 88), ("s", 128, 192), ("s", 192, 224), ("s", 224, 256), ("v", 88, 128)]
+PARTS = [[("s", 0, 32), ("s", 32, 64), ("s", 64, 128 - v), ("s", 128, 192), ("s", 192, 224), ("s", 224, 256), ("v", 128 - v, 128)] for v in (32, 20, 20, 20, 20, 40)]
+PARTS[0] = [("s", 0, 32), ("s", 32, 96), ("s", 128, 192), ("s", 192, 224), ("s", 224, 256), ("v", 96, 128)]
 OFFS = [(0, 64), (64, 256)]
-ADDS = [[]] * STEPS
-ZV = 0
-MAXIMA = [[(0, 64), (64, 128), (128, 192), (192, 256)]] * STEPS
-ZP = [256] * STEPS
-SEMAPHORES += ["ad%d_%d" % (t, e) for t in range(STEPS) for e in range(len(ADDS[t]))]
+MAXIMA = [(0, 64), (64, 128), (128, 192), (192, 224), (224, 256)]
 SUMS = [(0, 128), (128, 224), (224, 256)]
-NFL = "v"
-BS = "v"
-SCV = ()
-YI = "ssss"
-A2 = "s"
-LAST = "s"
-ON_S = ()
-PB = 768
+YI = "sssv"
+PB = 512
 EARLY = 3
 YV = 2
 
 
-def timetable(ops, edges, succ, lag):
-    calls = {}
-    for i, o in enumerate(ops):
-        calls.setdefault((o["step"], o["name"]), []).append(i)
-    follow, need = [list(x) for x in succ], [len(e) for e in edges]
-    for q in "vspg":
-        row = []
-        for t, words in [(0, FIRST[q])] + [(t, ORDER[q]) for t in range(STEPS - 2)] + [(STEPS - 2, FINAL[q])]:
-            for word in words.split():
-                name, _, count = word.partition("*")
-                part = {"_": "pre.", "^": "end."}.get(name[0], "")
-                left = calls.get((t + name.count("+"), part + q + name.strip("_^+")), [])
-                row += [left.pop(0) for _ in range(min(int(count or 1), len(left)))]
-        assert len(row) == sum(o["q"] == q for o in ops)
-        for a, b in zip(row, row[1:]):
-            follow[a].append((b, ops[a]["cost"]))
-            need[b] += 1
-    return follow, need, [-i for i in range(len(ops))]
-
-
-def list_schedule(n, que, cost, succ, need, prio):
-    need = list(need)
-    when = [0.0] * n
-    free, ready, nxt = {}, {}, {}
-    order = []
-    for i in range(n):
-        if need[i] == 0:
-            ready.setdefault(que[i], []).append(i)
-    dirty = set(ready)
-    end = 0.0
-    while len(order) < n:
-        for q in dirty:
-            lst = ready.get(q)
-            if not lst:
-                nxt.pop(q, None)
-                continue
-            f = free.get(q, 0.0)
-            st = max(f, min(when[i] for i in lst))
-            c = -1
-            for i in lst:
-                if when[i] <= st + 1e-9 and (c < 0 or prio[i] > prio[c]):
-                    c = i
-            if cost[c] > LOOK:
-                lim = st + min(LOOK, 0.5 * cost[c])
-                b = c
-                for i in lst:
-                    if when[i] <= lim and prio[i] > prio[b]:
-                        b = i
-                c = b
-            nxt[q] = (max(st, when[c]), c)
-        q = min(nxt, key=lambda x: nxt[x][0])
-        st, c = nxt[q]
-        ready[q].remove(c)
-        order.append(c)
-        free[q] = st + cost[c] if q != "n" else 0.0
-        end = max(end, st + cost[c])
-        dirty = {q}
-        for i, l in succ[c]:
-            need[i] -= 1
-            if st + l > when[i]:
-                when[i] = st + l
-            if need[i] == 0:
-                ready.setdefault(que[i], []).append(i)
-                dirty.add(que[i])
-    return order, end
-
-
-def best_order(n, que, cost, succ, prio, rounds=2):
-    need = [0] * n
-    for j in range(n):
-        for i, l in succ[j]:
-            need[i] += 1
-    back = [[] for _ in range(n)]
-    for j in range(n):
-        for i, l in succ[j]:
-            back[i].append((j, max(0.0, cost[i] + l - cost[j])))
-    bneed = [len(x) for x in succ]
-
-    def starts(order, follow):
-        at, when, free = [0.0] * n, [0.0] * n, {}
-        for i in order:
-            st = when[i]
-            if que[i] != "n":
-                st = max(st, free.get(que[i], 0.0))
-                free[que[i]] = st + cost[i]
-            at[i] = st
-            for k, l in follow[i]:
-                if st + l > when[k]:
-                    when[k] = st + l
-        return at
-    best = None
-    for k in range(rounds):
-        order, end = list_schedule(n, que, cost, succ, need, prio)
-        if best is None or end < best[1]:
-            best = (order, end)
-        if k + 1 < rounds:
-            at = starts(order, succ)
-            rev = list_schedule(n, que, cost, back, bneed, [at[i] + cost[i] for i in range(n)])[0]
-            at = starts(rev, back)
-            prio = [at[i] + cost[i] for i in range(n)]
-    return best
-
-
-def rank_program(g, core, T, topo):
+def program(g, core, T, topo):
     rank = T.rank_of(core)
-    if rank is None:
-        return
     n_ranks = len(T.cores)
     ops = []
     last = {}
     edges = []
     part = {"name": "pre.", "runs": {}, "last": None, "step": 0, "of": ""}
-    US, PS = COST["us"], COST["ps"]
 
     def t_(name, a=0, b=None, c=0, step=1, rows=(0, 128)):
         w, d, copies = TILES[name]
@@ -243,25 +99,25 @@ def rank_program(g, core, T, topo):
         off, p = PLACE[name]
         off += p * (c + (c > 0) if name == "z" else c % copies)
         ap = T[BUF[d]][rows[0]:rows[1], off + a:off + b:step] if step != 1 else T[BUF[d]][rows[0]:rows[1], off + a:off + b]
-        return {"ap": ap, "rg": [(BUF[d], off + a, off + b)], "n": (b - a + step - 1) // step, "by": BYTES[d], "ps": False, "ind": False}
+        return {"ap": ap, "rg": [(BUF[d], off + a, off + b)], "n": (b - a + step - 1) // step, "ind": False}
 
     def p_(k, a, b, step=1, rows=(0, 128)):
         ap = T.P5[:, a // 8:b // 8, :] if k == 5 else T["P%d" % k][rows[0]:rows[1], a:b:step] if step != 1 else T["P%d" % k][rows[0]:rows[1], a:b]
-        return {"ap": ap, "rg": [("P%d" % k, 0, 512)], "n": (b - a + step - 1) // step, "by": 4, "ps": True, "ind": False}
+        return {"ap": ap, "rg": [("P%d" % k, 0, 512)], "ind": False}
 
     def y_(t, a, b, step, rows=(0, 128)):
         name = "Yc%d" % (t % 2)
-        return {"ap": T[name][rows[0]:rows[1], :, a:b:step], "rg": [(name, 0, 32)], "n": 10 * len(range(a, b, step)), "by": 2, "ps": False, "ind": False}
+        return {"ap": T[name][rows[0]:rows[1], :, a:b:step], "rg": [(name, 0, 32)], "ind": False}
 
     def th_(a, b, step=1):
-        return {"ap": T.TH3[:, a:b:step, :], "rg": [("TH3", a, b)], "n": 48, "by": 4, "ps": False, "ind": False}
+        return {"ap": T.TH[:, a:b:step, :], "rg": [("TH", x, x + 1) for x in range(a, b, step)], "ind": False}
 
     def m_(t, a, b, k=None):
         x = t_("W", 4096 + 16 * a, 4096 + 16 * b, t) if k is None else t_("W", 4096 + 16 * a + k, 4096 + 16 * b, t, 16)
         return dict(x, rg=[("M%d.%d" % (t % 2, r), a, b) for r in (range(16) if k is None else [k])])
 
     def ind(win, off):
-        return {"ap": win["ap"].indirect(off["ap"]), "rg": win["rg"] + off["rg"], "win": win["rg"], "off": off["rg"], "n": 16 * off["n"], "by": win["by"], "ps": False, "ind": True}
+        return {"ap": win["ap"].indirect(off["ap"]), "rg": win["rg"] + off["rg"], "win": win["rg"], "off": off["rg"], "ind": True}
 
     starts = {d: sorted((PLACE[x][0], x) for x in TILES if TILES[x][1] == d) for d in BUF}
     dtype_of = {BUF[d]: d for d in BUF}
@@ -271,31 +127,28 @@ def rank_program(g, core, T, topo):
             return "M" if region[0][0] == "M" else region[0]
         return [x for o, x in starts[dtype_of[region[0]]] if o <= region[1]][-1]
 
-    def add(q, cost, emit, R, W, sem, inc, grp=None, role=None):
+    def add(q, emit, R, W, sem, inc, grp=None, role=None):
         i = len(ops)
         ed = {}
-        acc = [(r, False) for r in R] + [(r, True) for r in W]
-        for (buf, a, b), wr in acc:
-            ps = buf.startswith("P") and len(buf) == 2
-            for (a2, b2, j, wr2, q2, grp2, role2) in last.get(buf, []):
-                if a2 >= b or b2 <= a or j == i:
-                    continue
-                if ps:
-                    if q2 == q:
-                        if q == "p" and not (grp is not None and grp == grp2 and role == "mid" and role2 == "mid"):
-                            ed.setdefault(j, 0)
-                    else:
-                        ed[j] = 1
-                elif (wr or wr2) and not (wr and wr2 and grp is not None and grp == grp2):
+        for (buf, a, b), wr in [(r, False) for r in R] + [(r, True) for r in W]:
+            if buf[0] == "P":
+                runs = last.setdefault(buf, [("", []), ("", [])])
+                if runs[1][0] != q:
+                    runs[:] = [runs[1], (q, [])]
+                for j, grp2, role2 in runs[0][1]:
                     ed[j] = 1
-        for (buf, a, b), wr in acc:
-            ps = buf.startswith("P") and len(buf) == 2
+                for j, grp2, role2 in runs[1][1]:
+                    if q == "p" and j != i and not (grp is not None and grp == grp2 and role == "mid" and role2 == "mid"):
+                        ed.setdefault(j, 0)
+                runs[1][1].append((i, grp, role))
+                continue
             lst = last.setdefault(buf, [])
-            if wr and not ps:
-                lst[:] = [x for x in lst if not (x[0] >= a and x[1] <= b and x[2] != i and not (grp is not None and x[5] == grp))]
-            lst.append((a, b, i, wr, q, grp, role))
-            if ps and len(lst) > 200:
-                del lst[:80]
+            for (a2, b2, j, wr2, grp2) in lst:
+                if a2 < b and a < b2 and j != i and (wr or wr2) and not (wr and wr2 and grp is not None and grp == grp2):
+                    ed[j] = 1
+            if wr:
+                lst[:] = [x for x in lst if not (x[0] >= a and x[1] <= b and x[2] != i and not (grp is not None and x[4] == grp))]
+            lst.append((a, b, i, wr, grp))
         tag = name_of(W[0]) if W else q
         if tag[0] == "P" and R:
             tag += name_of(R[0])
@@ -303,8 +156,8 @@ def rank_program(g, core, T, topo):
         if k != part["last"]:
             part["runs"][k] = part["runs"].get(k, 0) + 1
         part["last"] = k
-        run = 1 if part["of"] or k in ("vptab", "sptab") else part["runs"][k]
-        ops.append({"q": q, "cost": cost, "emit": emit, "sem": sem, "inc": inc, "step": part["step"], "name": part["name"] + k + (str(run) if run > 1 else "")})
+        run = 1 if part["of"] or k == "sptab" else part["runs"][k]
+        ops.append({"q": q, "emit": emit, "sem": sem, "inc": inc, "step": part["step"], "name": part["name"] + k + (str(run) if run > 1 else "")})
         edges.append(ed)
         return i
 
@@ -318,100 +171,64 @@ def rank_program(g, core, T, topo):
     def raw(x):
         return x["ap"] if isinstance(x, dict) else x
 
-    def vcost(n, mode, xs):
-        if any(x["ind"] for x in xs[1:]):
-            return 0.05 + n * COST["gather"] * US
-        if xs[0]["ind"]:
-            return 0.05 + n * COST["scatter"] * US
-        if mode == "tt":
-            c = n * (1 if any(x["ps"] for x in xs) else 2)
-        else:
-            c = n * (0.5 if all(x["by"] == 2 for x in xs) else 1)
-        return max(64, c) * US
-
-    def outrg(out):
-        return (out["off"], out["win"]) if out["ind"] else ([], out["rg"])
-
     def tt(out, a, b, op):
-        return add("v", vcost(out["n"], "tt", [out, a, b]), lambda: g.vector.tensor_tensor(raw(out), raw(a), raw(b), op), rgs(a, b), out["rg"], "qv", 1)
+        return add("v", lambda: g.vector.tensor_tensor(raw(out), raw(a), raw(b), op), rgs(a, b), out["rg"], "qv", 1)
 
     def ts(out, a, s1, s2, o1, o2=None, grp=None):
         f = (lambda: g.vector.tensor_scalar(raw(out), raw(a), raw(s1), raw(s2), o1)) if o2 is None else (lambda: g.vector.tensor_scalar(raw(out), raw(a), raw(s1), raw(s2), o1, o2))
-        r, w = outrg(out)
-        return add("v", vcost(out["n"], "ts", [out, a]), f, rgs(a, s1, s2) + r, w, "qv", 1, grp=grp)
+        return add("v", f, rgs(a, s1, s2), out["rg"], "qv", 1, grp=grp)
 
     def cp(out, a):
-        r, w = outrg(out)
-        return add("v", vcost(out["n"], "ts", [out, a]), lambda: g.vector.tensor_copy(raw(out), raw(a)), rgs(a) + r, w, "qv", 1)
+        return add("v", lambda: g.vector.tensor_copy(raw(out), raw(a)), rgs(a), out["rg"], "qv", 1)
 
     def ms(out, val):
-        return add("v", vcost(out["n"], "ts", [out]), lambda: g.vector.memset(raw(out), val), [], out["rg"], "qv", 1)
+        return add("v", lambda: g.vector.memset(raw(out), val), [], out["rg"], "qv", 1)
 
     def red(out, a):
-        return add("v", 64 * US, lambda: g.vector.tensor_reduce(raw(out), raw(a), AxisListType.X, OP.add), rgs(a), out["rg"], "qv", 1)
+        return add("v", lambda: g.vector.tensor_reduce(raw(out), raw(a), AxisListType.X, OP.add), rgs(a), out["rg"], "qv", 1)
 
-    def runmax(out, reset, a):
-        return add("v", vcost(out["n"], "ts", [out, a]), lambda: g.vector.tensor_tensor_scan(raw(out), raw(reset), raw(a), 0.0, OP.add, OP.max), rgs(reset, a), out["rg"], "qv", 1)
+    def scan(out, a, b, o0, o1):
+        return add("v", lambda: g.vector.tensor_tensor_scan(raw(out), raw(a), raw(b), 0.0, o0, o1), rgs(a, b), out["rg"], "qv", 1)
 
     def act(out, a, fn, bias=0.0, scale=1.0, grp=None):
-        c = 0.065 + a["n"] * COST["gather"] * US if a["ind"] else max(64, a["n"]) * US
         if out["ind"]:
-            return add("s", 0.065 + a["n"] * COST["scatter"] * US, lambda: g.scalar.activation(raw(out), raw(a), fn), rgs(a) + out["off"], out["win"], "qs", 1)
+            return add("s", lambda: g.scalar.activation(raw(out), raw(a), fn), rgs(a) + out["off"], out["win"], "qs", 1)
         if isinstance(bias, float) and bias == 0.0:
             f = (lambda: g.scalar.activation(raw(out), raw(a), fn, scale=raw(scale))) if scale != 1.0 else (lambda: g.scalar.activation(raw(out), raw(a), fn))
         else:
             f = lambda: g.scalar.activation(raw(out), raw(a), fn, bias=raw(bias), scale=raw(scale))
-        return add("s", c, f, rgs(a, bias, scale), out["rg"], "qs", 1, grp=grp)
-
-    def lin(name, a, scale, bias):
-        if name in ON_S:
-            return act(t_(name), a, AF.Identity, bias=bias, scale=scale)
-        return ts(t_(name), a, scale, bias, OP.mult, OP.add)
+        return add("s", f, rgs(a, bias, scale), out["rg"], "qs", 1, grp=grp)
 
     def mm(out, lhsT, rhs, start, stop, grp=None, role=None):
-        c = max(min(64, lhsT["n"]), rhs["n"]) * PS * (4 if rhs["by"] == 4 else 1)
-        return add("p", c, lambda: g.tensor.matmul(raw(out), raw(lhsT), raw(rhs), start, stop), rgs(lhsT, rhs), out["rg"], "qp", 1, grp=grp, role=role)
+        return add("p", lambda: g.tensor.matmul(raw(out), raw(lhsT), raw(rhs), start, stop), rgs(lhsT, rhs), out["rg"], "qp", 1, grp=grp, role=role)
 
     def iota(out, pattern, base=0, cm=0, whole=False):
         def f():
             if whole:
                 return g.iota(raw(out), pattern, base, cm)
             return g.iota(raw(out), pattern, base, cm, allow_small_or_imprecise_dtypes=True)
-        return add("g", 0.13 + 2 * out["n"] * US, f, [], out["rg"], "qg", 1)
+        return add("g", f, [], out["rg"], "qg", 1)
 
     def fill(out, val):
         return iota(out, [[0, out["n"]]], val)
 
     def select(out, a, pattern, op, other, base, cm):
-        return add("g", 0.17 + 2 * out["n"] * US, lambda: g.affine_select(raw(out), raw(a), pattern, op, other, base, cm), rgs(a), out["rg"], "qg", 1)
+        return add("g", lambda: g.affine_select(raw(out), raw(a), pattern, op, other, base, cm), rgs(a), out["rg"], "qg", 1)
 
     def keep(out, a):
         return select(out, a, [[0, out["n"]]], OP.is_ge, 0.0, 0, 0)
 
     def load(name, out, q="y"):
         eng = g.sync if q == "y" else g.scalar
-        src = T[name][:]
-        return add(q, 0.1, lambda: eng.dma_start(raw(out), src), [], out["rg"], "ld_" + name, 16)
-
-    lag = {}
+        return add(q, lambda: eng.dma_start(raw(out), T[name][:]), [], out["rg"], "ld_" + name, 16)
 
     def store(tag, dst, src, q="y"):
         eng = g.sync if q == "y" else g.scalar
-        i = add(q, 0.1, lambda: eng.dma_start(dst, raw(src)), src["rg"], [("out" + tag, 0, 1)], "st_" + tag, 16)
-        lag[i] = 2.0 + src["n"] * src["by"] * 0.0005
+        return add(q, lambda: eng.dma_start(dst, raw(src)), src["rg"], [("out" + tag, 0, 1)], "st_" + tag, 16)
 
-    def adding(tag, out, src):
-        i = add("g", COST["issue"], lambda: g.dma_start(raw(out), raw(src), accum_op=OP.add), src["rg"] + out["rg"], out["rg"], tag, 16)
-        lag[i] = COST["dma"] + src["n"] * COST["add"]
-
-    prev = None
-    for name, dst, tm in (("wt", t_("wti"), 2.5), ("bites", t_("z", 0, 512), 2.7), ("bank", t_("bk"), 4.35), ("geno", t_("geno_s"), 6.95), ("immun", t_("ilog", 0, 1024), 7.6)):
-        i = load(name, dst, "s" if name == "wt" else "y")
-        if name != "wt":
-            if prev is not None:
-                edges[i][prev] = 0
-            prev = i
-        lag[i] = tm
+    load("wt", t_("wti"), "s")
+    for name, dst in (("bites", t_("z", 0, 512)), ("bank", t_("bk")), ("geno", t_("geno_s")), ("immun", t_("ilog", 0, 1024))):
+        load(name, dst)
 
     def send(srcs, t, dst_rank):
         dst = T.cores[dst_rank]
@@ -423,22 +240,21 @@ def rank_program(g, core, T, topo):
         def f():
             if len(srcs) == 1:
                 return g.remote_dma(raw(out), raw(srcs[0]), sem, T.sem.rl, pid, rid, m)
-            tr = RemoteDMATransfer(dst_ids=[DstId(rid=rid, pnc=pid)], dma_engine_mask=m, remote_sem=sem, srcs=[raw(x) for x in srcs], dsts=[raw(out)], alu_op=2)
+            tr = RemoteDMATransfer(dst_ids=[DstId(rid=rid, pnc=pid)], dma_engine_mask=m, remote_sem=sem, srcs=[raw(x) for x in srcs], dsts=[raw(out)], alu_op=1)
             return g.remote_dma_fused([tr], local_sem=T.sem.rl)
-        i = add("g", 0.3, f, rgs(*srcs), [], None, 0)
+        i = add("g", f, rgs(*srcs), [], None, 0)
         ops[i]["remote"] = eng
-        j = add("n", 0.0, None, [], out["rg"], "arr%d" % t, eng)
-        ops[j]["proxy"] = i
+        j = add("n", None, [], out["rg"], "arr%d" % t, eng)
+        edges[j][i] = 0
 
-    P, PM, PG, P8, WF, WG, WS, CI, PK, PK0, JK, PW, L1, L2, H1, W1, PC = [t_("col", c=k) for k in range(17)]
+    P, PM, PG, P8, WF, WG, WS, CI, PK, PK0, PW, L1, L2, H1, W1 = [t_("col", c=k) for k in range(15)]
     ic = lambda n: t_("ic", 0, n)
     iota(t_("pI"), [[0, 1]], 0, 1, True)
     iota(t_("ic"), [[1, 256]])
     ms(t_("J"), 1.0 / 64)
     ms(t_("c05", rows=(0, 64)), -2048.0)
     ms(t_("c05", rows=(64, 128)), 0.5)
-    i = act(t_("ones"), t_("J"), AF.Sigmoid, scale=6400.0)
-    ops[i]["cost"] += 1.6
+    act(t_("ones"), t_("J"), AF.Sigmoid, scale=6400.0)
     send([t_("z", 256, 512)], 1, (rank + 1) % n_ranks)
     iota(t_("C16"), [[0, 16], [-1, 16]], 16)
     ms(t_("C16", rows=(64, 128)), 16 * Q0 + BIG)
@@ -475,7 +291,7 @@ def rank_program(g, core, T, topo):
     numbers(1)
     for name, f in (("GS", BIG), ("G64", 64.0), ("G32", -32.0)):
         act(t_(name), t_("Gmf"), AF.Copy, scale=f)
-    for name, f in (("nI", -1.0), ("I16", -4096.0)):
+    for name, f in (("nI", -1.0), ("I16", -4096.0), ("I9", 9.0)):
         act(t_(name), t_("I"), AF.Copy, scale=f)
     tt(CI, PG, P, OP.add)
     ts(t_("IB"), ic(136), CI, BIG, OP.is_equal, OP.mult)
@@ -484,31 +300,28 @@ def rank_program(g, core, T, topo):
     fill(t_("d16", 0, 256, step=16), -4096)
     fill(t_("d17"), 0)
     fill(t_("d17", 0, 136, step=17), int(-8 * BIG))
-    fill(t_("m", 0, 272, step=136), 0)
-    ms(t_("ac", 32, 33), 304.0 / 128)
-    ms(t_("ac", 33, 34), 7.59375 / 128)
+    ms(t_("ac", 32, 33), 304.0 / 2)
+    ms(t_("ac", 33, 34), 7.59375 / 2)
     ts(t_("eq"), ic(16), PM, None, OP.is_equal)
-    ts(t_("le"), ic(16), PM, None, OP.is_ge)
     ts(t_("ne"), ic(16), PM, 16384.0, OP.not_equal, OP.mult)
     tt(t_("Gm4"), t_("Gmf", 0, 4), t_("Gmf", 4, 8), OP.add)
+    fill(t_("pen", 0, 16), 0)
     fill(t_("RB"), 0)
     ts(t_("RB", 112, 128), t_("eq"), -1.0, None, OP.mult)
     fill(t_("XG"), 1)
     select(t_("XG"), t_("XG"), [[-16, 8], [0, 16]], OP.is_ge, 0.0, 0, 1)
-    select(t_("XG"), t_("XG"), [[16, 8], [0, 16]], OP.is_ge, 0.0, 15, -1)
+    select(t_("XG"), t_("XG"), [[1, 128]], OP.is_gt, 0.0, 0, -1)
     select(t_("XG"), t_("XG"), [[-1, 128]], OP.not_equal, -1.0, 0, 1)
-    for r in range(16):
-        ts(t_("LR", 128 * r, 128 * r + 128), t_("XG"), t_("eq", r, r + 1), t_("le", r, r + 1), OP.min, OP.mult)
-    ts(JK, PM, 1024.0, None, OP.add)
+    for m in range(15):
+        ts(t_("LR", 128 * m, 128 * m + 128), t_("XG"), t_("eq", m, m + 1), None, OP.min)
+    ms(p_(3, 0, 256, 16), 0.0)
     ts(t_("lnO"), t_("lnO"), PM, 16.0, OP.add, OP.mult)
-    cp(t_("ba", 0, 16), t_("lnO"))
-    for k in (1, 2):
+    act(t_("lnq"), t_("lnO"), AF.Copy, scale=1.0 / 4096)
+    for k in range(2):
         act(t_("ba", 16 * k, 16 * k + 16), t_("lnO"), AF.Identity, bias=16.0)
     for h in range(2):
-        act(t_("ba", 48 + 8 * h, 56 + 8 * h), t_("lnO", 0, 8), AF.Identity, bias=16.0)
-    iota(t_("ba", 64, 96), [[4080, 2], [0, 16]], 16)
-    iota(t_("ordc", 0, 32), [[4096, 2], [0, 16]], 4096 - int(WO))
-    fill(t_("ordc", 32, 48), int(WO))
+        act(t_("ba", 32 + 8 * h, 40 + 8 * h), t_("lnO", 0, 8), AF.Identity, bias=16.0)
+    iota(t_("ba", 48, 80), [[4080, 2], [0, 16]], 16)
     fill(t_("X2", 0, 1), 0)
     fill(t_("X2", 2049, 2064), 0)
     for k in range(16):
@@ -517,15 +330,14 @@ def rank_program(g, core, T, topo):
     tt(PK, PM, PK0, OP.add)
     ts(t_("T2", c=0), ic(32), PK, (Q0 + 8) / 256, OP.is_equal, OP.mult)
     seed = lambda a, b: t_("T1s", a, b, rows=(0, 16))
-    fill(t_("pen", 0, 16), 0)
     fill(seed(0, 544), 1)
     select(seed(0, 272), seed(0, 272), [[1, 272]], OP.not_equal, Q0 / 256, -256, 16)
     for pattern in ([[-1, 16], [0, 16]], [[0, 16], [-1, 16]]):
         select(seed(273, 529), seed(273, 529), pattern, OP.not_equal, Q0 / 256, 15, -1)
     select(t_("E16", rows=(0, 16)), t_("ones", rows=(0, 16)), [[0, 8], [-1, 16]], OP.is_equal, 0.0, 0, 1)
     for k, name in enumerate(("T1a", "T1b")):
-        mm(p_(7, 0, 272), t_("E16", rows=(0, 16)), seed(272 * k, 272 * k + 272), True, True)
-        act(t_(name), p_(7, 0, 272), AF.Copy)
+        mm(p_(5, 0, 272), t_("E16", rows=(0, 16)), seed(272 * k, 272 * k + 272), True, True)
+        act(t_(name), p_(5, 0, 272), AF.Copy)
     ms(t_("pw", 0, 1), 1.0)
     for k in (1, 2, 4):
         ts(t_("pw", k, 2 * k), t_("pw", 0, k), float(2 ** k), None, OP.mult)
@@ -534,17 +346,19 @@ def rank_program(g, core, T, topo):
     red(PW, t_("p8e"))
     ts(t_("xi"), ic(256), PW, None, OP.mult)
     ts(t_("xj"), t_("xi"), 128, None, OP.bitwise_and)
-    ts(t_("Bt", 0, 256), t_("xj"), 0.5, None, OP.mult)
-    for k in range(1, 4):
-        keep(t_("Bt", 256 * k, 256 * k + 256), t_("Bt", 0, 256))
+    ts(t_("Bt"), t_("xj"), 0.5, None, OP.mult)
+    fill(t_("T3"), 0)
+    ts(t_("T3", 15, 1039, step=4), t_("Bt"), 1.0 / 64, None, OP.mult)
+    ts(t_("T3", 16, 1040, step=4), t_("Bt"), -1.0 / 64, 1.0, OP.mult, OP.add)
     ts(L1, PM, 8.0, 1.0 / 64, OP.is_lt, OP.mult)
     ts(L2, L1, 200.0, None, OP.mult)
     ts(H1, L1, -1.0, 1.0 / 64, OP.mult, OP.add)
     ts(t_("hb"), t_("Bt", 0, 16), H1, None, OP.mult)
     ts(t_("hb", c=1), t_("hb"), 200.0, -100.0, OP.mult, OP.add)
+    hosts = lambda a=0, b=1024: t_("ptab", 16 + a, 16 + b)
     for k in range(4):
-        act(t_("ptab", 256 * k, 256 * k + 256), t_("Bt", 0, 256), AF.Identity, bias=t_("hb", k, k + 1), scale=L1)
-    places = lambda t: act(t_("psrc", c=t), t_("Bt", 0, 256), AF.Identity, bias=t_("hb", 4 + t, 5 + t, 1), scale=L2)
+        act(hosts(256 * k, 256 * k + 256), t_("Bt"), AF.Identity, bias=t_("hb", k, k + 1), scale=L1)
+    places = lambda t: act(t_("psrc", c=t), t_("Bt"), AF.Identity, bias=t_("hb", 4 + t, 5 + t, 1), scale=L2)
     for t in range(EARLY):
         places(t)
     ts(t_("p8e", c=1), ic(8), t_("p8f"), None, OP.is_equal)
@@ -553,42 +367,49 @@ def rank_program(g, core, T, topo):
     ts(H1, H1, 255.0 * 64, 1.0, OP.mult, OP.add)
     ts(t_("EW"), t_("EB"), W1, H1, OP.mult, OP.mult)
 
-    def to_list(out, src, a, b, wts="EB", first=True, close=True):
+    def to_list(out, src, a, b, wts="EB", first=True):
         for r in range(16):
-            mm(out, t_(wts, 15 - r, 143 - r), t_(src, a + r, b, 0, 16), first and r == 0, close and r == 15)
+            mm(out, t_(wts, 15 - r, 143 - r), t_(src, a + r, b, 0, 16), first and r == 0, r == 15)
 
     def host(t):
+        w = 32 if t + 2 < STEPS else 16
         mm(p_(3, 256, 272), t_("J"), t_("c05"), True, False)
         for r in range(16):
             mm(p_(3, 256, 272), t_("wE", 15 - r, 143 - r), t_("z", r, 256, t, 16), False, r == 15)
         ts(t_("ui", c=t), p_(3, 256, 272), 1.5 * 2 ** 35, 1.5 * 2 ** 35, OP.add, OP.subtract)
         tt(t_("s", c=t), p_(3, 256, 272), t_("ui", c=t), OP.subtract)
         act(t_("sq", c=t), t_("s", c=t), AF.Square, bias=2047.5 + 592)
-        ts(t_("UV", 16, 32, t), t_("s", c=t), 2047.5, None, OP.add)
+        if w > 16:
+            part["of"] = ".u"
+            ts(t_("UV", 16, 32, t), t_("s", c=t), 4.0, 8190.0, OP.mult, OP.add)
+            part["of"] = ""
         ts(t_("UV", 0, 16, t), t_("sq", c=t), 1.0 / 32, t_("A", c=t - 1) if t else 311.59375, OP.mult, OP.add)
-        ts(t_("VV", c=t), t_("UV", c=t), 1023, None, OP.bitwise_and)
-        cp(t_("vl", c=t), t_("VV", c=t))
+        ts(t_("VV", 0, w, t), t_("UV", 0, w, t), 1023, None, OP.bitwise_and)
+        cp(t_("vl", c=t), t_("VV", 0, 16, t))
         if t:
-            act(t_("G"), ind(t_("ptab", 0, 1024), t_("vl", 0, 16, t)), AF.Copy)
-            to_list(p_(4, 0, 16), "G", 0, 256, "EW")
-            cp(t_("pl", c=t), p_(4, 0, 16))
-        ts(t_("vh", c=t), t_("VV", 0, 16, t), 1.0, None, OP.add)
-        for r in range(16):
-            mm(p_(3, r, 256, 16), t_("LR", 128 * r, 128 * r + 128), t_("vh", c=t), True, True)
-        ts(t_("E"), p_(3, 0, 256), 0.0, 4096.0, OP.is_equal, OP.mult)
-        mm(p_(3, 272, 288), t_("I"), t_("vh", c=t), True, False)
-        to_list(p_(3, 272, 288), "E", 0, 256, first=False)
-        ts(t_("wl", 0, 32, t, 2), p_(3, 272, 288), -1.0, JK, OP.add, OP.min)
+            act(t_("G"), ind(hosts(), t_("vl", c=t)), AF.Copy)
+            to_list(p_(2, 256, 272), "G", 0, 256, "EW")
+            cp(t_("pl", c=t), p_(2, 256, 272))
+        ts(t_("vh", 0, w, t), t_("VV", 0, w, t), 16.0, None, OP.add)
+        for m in range(15):
+            mm(p_(3, m + 1, 256, 16), t_("LR", 128 * m, 128 * m + 128), t_("vh", 0, 16, t), True, True)
+        ts(t_("E"), p_(3, 0, 256), 0.0, None, OP.is_equal)
+        mm(p_(3, 272, 288), t_("I"), t_("vh", 0, 16, t), True, False)
+        for m in range(15):
+            mm(p_(3, 272, 288), t_("I16"), t_("E", m + 1, 256, 0, 16), False, m == 14)
+        ts(t_("wl", 0, 32, t, 2), p_(3, 272, 288), PM, None, OP.max)
 
     def step(t):
         z = t_("z", c=t)
         n = 1024 + 256 * t
-        pl = t_("pl", c=t) if t else t_("vl", 0, 16, t)
+        cross = t + 2 < STEPS
+        pl = t_("pl", c=t) if t else t_("vl", c=t)
         W = lambda a, b, s=1: t_("W", a, b, t, s)
-        mm(p_(0, 0, ZP[t]), t_("I"), t_("z", 0, ZP[t], t), True, True)
-        for a, b in MAXIMA[t]:
-            for e in range(2 if b - a <= 32 else 0):
-                mm(p_(0, 256 + e, 256 + 2 * (b - a), 2), t_("I"), t_("z", a, b, t), True, True)
+        mm(p_(0, 0, 256), t_("I"), z, True, True)
+        twice = {x: 256 + 64 * k for k, x in enumerate(x for x in MAXIMA if x[1] - x[0] <= 32)}
+        for (a, b), o in twice.items():
+            for e in range(2):
+                mm(p_(0, o + e, o + 2 * (b - a), 2), t_("I"), t_("z", a, b, t), True, True)
         for a, b in OFFS:
             if t:
                 cp(t_("boff", a, b, t), ind(t_("blog", 0, n), t_("pl", a // 16, b // 16, t)))
@@ -608,120 +429,90 @@ def rank_program(g, core, T, topo):
             store("sg", T.ygeno[:], t_("geno_s"))
         qg, fl, gt, im1 = t_("qg", c=t), lambda h: t_("fl", 128 * h, 128 * h + 128, t), lambda h: t_("gt", 128 * h, 128 * h + 128, t), t_("im1", c=t)
         for h in range(2):
-            if BS == "v":
-                ts(t_("bs", 128 * h, 128 * h + 128, t), t_("boff", 128 * h, 128 * h + 128, t), float(t + 2048 * h), None, OP.add)
-            else:
-                act(t_("bs", 128 * h, 128 * h + 128, t), ind(t_("blog", 0, n), t_("pl" if t else "vl", 8 * h, 8 * h + 8, t)), AF.Identity, bias=float(t + 2048 * h))
+            ts(t_("bs", 128 * h, 128 * h + 128, t), t_("boff", 128 * h, 128 * h + 128, t), float(t + 2048 * h), None, OP.add)
         act(qg, ind(t_("qlog", 0, n), pl), AF.Copy)
         act(im1, ind(t_("ilog", 0, n), pl), AF.Identity, bias=-1.0)
-        if NFL == "v":
-            ts(t_("fl", c=t), qg, (Q0 + t + 0.5) / 256, None, OP.is_gt)
-        else:
-            act(t_("fl", c=t), qg, AF.Sigmoid, bias=-200.0 * (Q0 + t + 0.5), scale=200.0 * 256)
+        ts(t_("fl", c=t), qg, (Q0 + t + 0.5) / 256, None, OP.is_gt)
         mm(p_(4, 256, 512), t_("I"), z, True, False)
         mm(p_(4, 256, 512), t_("nI"), im1, False, True)
         act(t_("gt", c=t), p_(4, 256, 512), AF.Sign, bias=-1.5)
         mm(p_(2, 0, 256), t_("J"), t_("C16"), True, False)
         for h in range(2):
             mm(p_(2, 128 * h, 128 * h + 128), t_("qg", 128 * h, 128 * h + 128, t), t_("I16"), False, h == 1)
-        runmax(t_("qs", c=t), t_("d16"), p_(2, 0, 256))
         if t + 1 < STEPS:
             act(t_("T2", c=t + 1), t_("T2", c=0), AF.Copy, scale=(Q0 + 9 + t) / (Q0 + 8))
         if t and t + EARLY - 1 < STEPS:
             places(t + EARLY - 1)
-        if t + 1 < STEPS:
-            for j in range(15, -1, -1):
-                to, src = ind(t_("ptab"), t_("wl", 2 * j, 2 * j + 1, t)), t_("psrc", 16 * j, 16 * j + 16, t)
-                if j in SCV:
-                    ts(to, src, 0.005, 0.5, OP.mult, OP.add)
+        for j in range(15, -1, -1):
+            act(ind(t_("ptab"), t_("wl", 2 * j, 2 * j + 1, t)), t_("psrc", 16 * j, 16 * j + 16, t), AF.Sigmoid)
+        if t + 1 == STEPS:
+            for a, b in quarters:
+                if a < PB:
+                    act(t_("ptb", a, b), hosts(a, b), AF.Copy)
                 else:
-                    act(to, src, AF.Sigmoid)
-        else:
-            if LAST == "v":
-                keep(t_("ptb", 0, 1024), t_("ptab", 0, 1024))
-                for j in range(15, -1, -1):
-                    cp(ind(t_("ptb"), t_("wl", 2 * j, 2 * j + 1, t)), t_("psb", 16 * j, 16 * j + 16))
-            else:
-                for j in range(15, -1, -1):
-                    act(ind(t_("ptab"), t_("wl", 2 * j, 2 * j + 1, t)), t_("psrc", 16 * j, 16 * j + 16, t), AF.Sigmoid)
-                for a in range(0, 1024, 256):
-                    if a < PB:
-                        act(t_("ptb", a, a + 256), t_("ptab", a, a + 256), AF.Copy)
-                    else:
-                        keep(t_("ptb", a, a + 256), t_("ptab", a, a + 256))
+                    keep(t_("ptb", a, b), hosts(a, b))
             part["of"] = ".F"
             to_list(p_(3, 64, 128), "ptb", 0, 1024, "EW")
             part["of"] = ""
             cp(t_("plF"), p_(3, 64, 128))
-        if ADDS[t]:
-            a, b = ADDS[t][0][0], ADDS[t][-1][1]
-            ts(t_("nz", 0, b - a), t_("z", a, b, t), -1.0, None, OP.mult)
-            part["of"] = ".z"
-            for k in range(16):
-                if k < ZV:
-                    cp(m_(t, a, b, k), t_("nz", 0, b - a))
-                else:
-                    keep(m_(t, a, b, k), t_("nz", 0, b - a))
-        for e, (a, b) in enumerate(ADDS[t]):
-            part["of"] = ".a%d" % e
-            adding("ad%d_%d" % (t, e), m_(t, a, b), W(16 * a, 16 * b))
-            ts(m_(t, a, b), m_(t, a, b), 0.0, 32.0, OP.max, OP.add)
-        for e, (a, b) in enumerate(MAXIMA[t]):
+        for h in range(4):
+            mm(p_(4, 16 + 8 * h, 24 + 8 * h), gt(h % 2), t_("GS"), True, True)
+        scan(t_("qs", c=t), t_("d16"), p_(2, 0, 256), OP.add, OP.max)
+        for e, (a, b) in enumerate(MAXIMA):
             part["of"] = ".m%d" % e
             for k in range(16 if b - a > 32 else 0):
                 tt(m_(t, a, b, k), W(16 * a + k, 16 * b, 16), p_(0, a, b), OP.max)
             for k in range(8 if b - a <= 32 else 0):
                 two = dict(W(4096 + 16 * a + k, 4096 + 16 * b, 8), rg=m_(t, a, b, k)["rg"] + m_(t, a, b, k + 8)["rg"])
-                tt(two, W(16 * a + k, 16 * b, 8), p_(0, 256, 256 + 2 * (b - a)), OP.max)
+                tt(two, W(16 * a + k, 16 * b, 8), p_(0, twice[a, b], twice[a, b] + 2 * (b - a)), OP.max)
         part["of"] = ""
         for h in range(2):
             gk, kb = ("key", t, h), (1, 6)[h]
             mm(p_(kb, 0, 136), t_("I"), t_("C17"), True, False, gk, "first")
-            mm(p_(kb, 0, 136), fl(h), t_("IB"), False, False, gk, "mid")
+            if h:
+                mm(p_(kb, 0, 136), fl(h), t_("IB"), False, False, gk, "mid")
             for c, (a, b) in enumerate(SUMS):
                 part["of"] = ".c%d" % c
                 for k in range(16 if a // 128 == h else 0):
                     mm(p_(kb, 1 + k, 136, 17, (a % 128, b - 128 * h)), W(16 * a + k, 16 * b, 16), t_("G32"), False, False, gk, "mid")
             part["of"] = ".m"
             for k in sorted(range(16), key=lambda k: k % 8 if h else k):
-                mm(p_(kb, 1 + k, 136, 17), m_(t, 128 * h, 128 * h + 128, k), t_("G64"), False, k == 15, gk, "last" if k == 15 else "mid")
+                end = h == 1 and k == 15
+                mm(p_(kb, 1 + k, 136, 17), m_(t, 128 * h, 128 * h + 128, k), t_("G64"), False, end, gk, "last" if end else "mid")
+            part["of"] = ""
+            if not h:
+                mm(p_(kb, 0, 136), fl(h), t_("IB"), False, True, gk, "last")
             part["of"] = ".%d" % h
             keep(m_(t, 128 * h, 128 * h + 128, 0), t_("z", 128 * h, 128 * h + 128, t))
             o = 136 * h
-            runmax(t_("s12", o, o + 136), t_("d17"), p_(kb, 0, 136))
-            tt(t_("m", o + 1, o + 136), t_("s12", o, o + 135), p_(kb, 1, 136), OP.min)
+            scan(t_("s12", o, o + 136), t_("d17"), p_(kb, 0, 136), OP.add, OP.max)
             part["of"] = ".%d" % (2 + h)
-            runmax(t_("s12", 272 + o, 408 + o), t_("d17"), t_("m", o, o + 136))
+            scan(t_("s12", 273 + o, 408 + o), p_(kb, 1, 136), t_("s12", o, o + 135), OP.max, OP.min)
             part["of"] = ""
         for k in range(2, 4 if t == 0 else 0):
             numbers(k)
         KM = lambda a, b: t_("KM", a, b, t)
-        for h in range(4):
-            mm(p_(2, 272 + 8 * h, 280 + 8 * h), gt(h % 2), t_("GS"), True, True)
-        tt(t_("HI"), t_("s12", 16, 544, 0, 17), p_(2, 272, 304), OP.min)
+        tt(t_("HI"), t_("s12", 16, 544, 0, 17), p_(4, 16, 48), OP.min)
         ts(t_("HA"), t_("HI"), int(BIG) + 31, None, OP.bitwise_and)
         ts(KM(0, 32), t_("HA"), -BIG, -4080.0, OP.add, OP.max)
         if t + 1 < STEPS:
-            ts(t_("ac", 0, 32, t), t_("HA"), BIG, None, OP.is_ge)
-            mm(p_(2, 304, 338), t_("ones"), t_("ac", c=t), True, True)
-            red(t_("A", c=t), p_(2, 304, 338))
+            ts(t_("ac", 0, 32), t_("HA"), BIG, 64.0, OP.is_ge, OP.mult)
+            mm(p_(7, 0, 34), t_("J"), t_("ac"), True, True)
+            red(t_("A", c=t), p_(7, 0, 34))
             host(t + 1)
         tt(t_("kx"), t_("HA", 0, 16), t_("HA", 16, 32), OP.max)
         tt(t_("sm"), t_("kx"), t_("qs", 15, 256, t, 16), OP.max)
         ts(t_("sl"), t_("sm"), 15, None, OP.bitwise_and)
         cp(KM(32, 48), t_("sl"))
         cp(KM(48, 64), t_("sl"))
-        lin("ca", KM(0, 16), -16.0, 16.0)
+        ts(t_("ca"), KM(0, 16), -16.0, 16.0, OP.mult, OP.add)
         tt(KM(64, 80), t_("ca"), KM(16, 32), OP.subtract)
         for x in range(4):
             if x < YV:
                 ts(y_(t, x, 32, 4), KM(0, 80), t_("Gm4", x, x + 1), None, OP.mult, grp=("Y", t))
             else:
                 act(y_(t, x, 32, 4), KM(0, 80), AF.Copy, scale=t_("Gm4", x, x + 1), grp=("Y", t))
-        mm(p_(5, 0, 96), t_("I"), t_("ba"), True, False)
-        part["of"] = ".o"
-        i = mm(p_(5, 0, 48), t_("I"), t_("ordc"), False, False)
-        part["of"] = ""
+        i = mm(p_(5, 16, 96), t_("I"), t_("ba"), True, False)
         for e in range(2):
             before = i
             for k in range(8):
@@ -731,61 +522,88 @@ def rank_program(g, core, T, topo):
                 edges[i][before] = 1
         ol = lambda k, m=1: t_("ol", 16 * k, 16 * (k + m), t)
         cp(ol(0, 5), p_(5, 16, 96))
-        ts(t_("pen", 16, 32), p_(5, 32, 48), WO + 4096, 16.0, OP.is_ge, OP.mult)
+        act(t_("pen", 16, 32), p_(5, 32, 48), AF.Sigmoid, bias=-409550.0, scale=100.0)
+        act(t_("ad"), p_(5, 16, 48), AF.Copy, scale=1.0 / 4096)
         tt(t_("ybk"), ind(t_("X2", 0, 2049), ol(2)), t_("bs", c=t), OP.min)
         for h in range(2):
             act(t_("blog", n + 128 * h, n + 128 * h + 128), t_("ybk", 128 * h, 128 * h + 128), AF.Abs, bias=float(-t - 2048 * h))
         tt(t_("q1"), ind(t_("T1a", 0, 4096 + 257), ol(4)), qg, OP.min)
         tt(t_("qlog", n, n + 256), ind(t_("T2", c=t), ol(3)), t_("q1"), OP.max)
         win = dict(W(0, 8192), rg=W(0, 4096)["rg"] + m_(t, 0, 256)["rg"])
-        win2 = dict(W(-int(WO), 8192), rg=W(-int(WO), 4096)["rg"] + m_(t, 0, 256)["rg"] + (m_(t - 1, 0, 256)["rg"] if t % 2 else []))
-        d1, d2 = t_("a12", 0, 256), t_("a12", 256, 512)
-        tt(d1, ind(win, ol(0)), z, OP.subtract)
-        act(t_("SG", 0, 256), d1, AF.Sigmoid, bias=-math.log(31.0), scale=-40.0)
-        if A2 == "v":
-            tt(d2, ind(win2, ol(1)), z, OP.subtract)
-            mm(p_(7, 0, 256), t_("I"), d1, True, False)
-            mm(p_(7, 0, 256), t_("nI"), d2, False, True)
-            act(t_("SG", 256, 512), d2, AF.Sigmoid, bias=-math.log(31.0), scale=-40.0)
+        if cross:
+            for k in range(2):
+                d = t_("d12", 256 * k, 256 * k + 256)
+                tt(d, ind(win, ol(k)), z, OP.subtract)
+                act(t_("SG", 256 * k, 256 * k + 256), d, AF.Sigmoid, bias=-math.log(31.0), scale=-40.0)
+                mm(p_(7, 0, 256), t_(("I", "nI")[k]), d, k == 0, k == 1)
             act(t_("SG", 512, 768), p_(7, 0, 256), AF.Sigmoid, bias=-math.log(31.0), scale=40.0)
         else:
-            act(d2, ind(win2, ol(1)), AF.Copy)
+            d = t_("d12", 0, 256)
+            part["of"] = ".z"
             for k in range(2):
                 mm(p_(7, 256 * k, 256 * k + 256), t_("I"), z, k == 0, False)
-            part["last"] = None
-            mm(p_(7, 256, 512), t_("I"), d1, False, False)
+            part["of"] = ""
+            tt(d, ind(win, ol(0)), z, OP.subtract)
+            act(t_("a2"), ind(win, ol(1)), AF.Copy)
+            act(t_("SG", 0, 256), d, AF.Sigmoid, bias=-math.log(31.0), scale=-40.0)
+            mm(p_(7, 256, 512), t_("I"), d, False, False)
             for k in range(2):
-                mm(p_(7, 256 * k, 256 * k + 256), t_("nI"), d2, False, k == 1)
+                mm(p_(7, 256 * k, 256 * k + 256), t_("nI"), t_("a2"), False, k == 1)
             act(t_("SG", 256, 768), p_(7, 0, 512), AF.Sigmoid, bias=-math.log(31.0), scale=40.0)
         cnt = p_(5, 256, 304)
-        mm(p_(5, 256, 288), t_("I"), t_("pen"), True, False)
-        mm(p_(5, 288, 304), t_("I"), t_("pen", 16, 32), False, False)
+        part["of"] = ".p"
+        mm(p_(5, 256, 288), t_("I9"), t_("pen"), True, False)
+        mm(p_(5, 288, 304), t_("I9"), t_("pen", 16, 32), False, False)
+        part["of"] = ""
         to_list(cnt, "SG", 0, 768, first=False)
-        ts(t_("rn"), cnt, 12582912.0, 12582912.0, OP.add, OP.subtract)
-        ts(t_("thr"), cnt, 32.0 / 31, -7.5 / 31, OP.mult, OP.add)
-        ts(th_(3, 6), cnt, 9.0, WN, OP.is_ge, OP.mult)
-        tt(t_("dd"), t_("rn"), t_("thr"), OP.subtract)
-        ts(th_(0, 3), t_("dd"), 0.0, WN, OP.is_ge, OP.mult)
-        tt(t_("KK"), th_(0, 6, 2), th_(1, 6, 2), OP.add)
-        tt(t_("KL"), t_("KK"), p_(5, 0, 48), OP.add)
-        k0, k1, k2 = t_("KL", 0, 16), t_("KL", 16, 32), t_("KL", 32, 48)
-        cross = t + 2 < STEPS
-        tt(t_("mna"), k0, k1, OP.min)
-        tt(t_("FM", 0, 16), t_("mna"), k2, OP.min)
+        ts(t_("ti"), cnt, 1056.0, None, OP.mult)
+        ts(th_(3, 6), cnt, 8.75, None, OP.is_gt)
+        ts(t_("mk"), t_("ti"), 768, None, OP.bitwise_and)
+        part["of"] = ".l"
+        ts(th_(0, 3), t_("mk"), 0.0, None, OP.is_equal)
+        part["of"] = ""
         if cross:
-            tt(t_("mxa"), k0, k1, OP.max)
-            tt(t_("tta"), t_("mxa"), k2, OP.min)
-            tt(t_("FM", 16, 32), t_("mna"), t_("tta"), OP.max)
-        w = 32 if cross else 16
-        ts(t_("FA", 0, w), t_("FM", 0, w), 8191, None, OP.bitwise_and)
-        cp(t_("fml", 0, w, t), t_("FA", 0, w))
-        f, m = ind(win, t_("fml", 0, 16, t)), ind(win, t_("fml", 16, 32, t))
-        tt(t_("ilog", n, n + 256), f, im1, OP.max)
-        if cross:
-            act(t_("Bm", c=t), ind(t_("Bt"), t_("vl", 16, 32, t)), AF.Copy)
-            tt(t_("cx", 0, 256, t), f, t_("Bm", c=t), OP.min)
-            tt(t_("cx", 256, 512, t), m, t_("Bm", c=t), OP.subtract)
-            send([t_("cx", 0, 256, t), t_("cx", 256, 512, t)], t + 2, (rank + 2) % n_ranks)
+            D = lambda a, b: p_(2, 304 + 16 * a, 304 + 16 * b)
+            code = lambda a, b: p_(4, 64 + 16 * a, 64 + 16 * b)
+            part["of"] = ".u"
+            for k in range(2):
+                mm(code(k, k + 1), t_("I"), t_("vh", 16, 32, t), k == 0, False)
+            part["of"] = ".g"
+            mm(D(0, 3), t_("I"), th_(3, 6), True, False)
+            mm(D(2, 3), t_("I"), th_(4, 5), False, False)
+            part["of"] = ".l"
+            mm(D(0, 2), t_("I"), th_(2, 6, 3), False, False)
+            mm(D(0, 3), t_("nI"), th_(0, 3), False, False)
+            mm(D(0, 1), t_("nI"), th_(1, 2), False, False)
+            mm(D(1, 3), t_("nI"), th_(0, 4, 3), False, True)
+            part["of"] = ""
+            ts(t_("C"), D(0, 3), -0.5, 0.5, OP.is_gt, OP.subtract)
+
+            def ranks(o, first):
+                mm(code(o, o + 2), t_("I"), t_("C", 0, 32), first, False)
+                mm(code(o + 1, o + 2), t_("I"), t_("C", 32, 48), False, False)
+                mm(code(o, o + 1), t_("nI"), t_("C", 32, 48), False, True)
+            part["of"] = ".c"
+            ranks(0, False)
+            part["of"] = ""
+            cp(t_("cl", c=t), code(0, 2))
+            tt(t_("cx", c=t), ind(t_("T3"), t_("cl", c=t)), t_("d12"), OP.mult)
+            send([z, t_("cx", 0, 256, t), t_("cx", 256, 512, t)], t + 2, (rank + 2) % n_ranks)
+            part["of"] = ".k"
+            ranks(2, True)
+            part["of"] = ""
+            less1 = code(2, 4)
+        else:
+            tt(t_("nb"), th_(0, 6, 2), th_(1, 6, 2), OP.add)
+            tt(t_("C", 0, 32), t_("nb", 0, 32), t_("nb", 16, 48), OP.is_le)
+            tt(t_("C", 32, 48), t_("nb", 32, 48), t_("nb", 0, 16), OP.is_lt)
+            tt(t_("R"), t_("C", 0, 32), t_("C", 16, 48), OP.subtract)
+            less1 = t_("R")
+        tt(t_("K"), t_("ad"), less1, OP.add)
+        tt(t_("mna"), t_("lnq"), t_("K", 0, 16), OP.min)
+        tt(t_("mnb"), t_("mna"), t_("K", 16, 32), OP.min)
+        ts(t_("fl1", c=t), t_("mnb"), 4096.0, 4096.0, OP.mult, OP.add)
+        tt(t_("ilog", n, n + 256), ind(win, t_("fl1", c=t)), im1, OP.max)
 
     host(0)
     for t in range(STEPS):
@@ -796,44 +614,57 @@ def rank_program(g, core, T, topo):
         lst = t_("plF", a // 16, b // 16)
         act(t_("q4", a, b), ind(t_("qlog"), lst), AF.Identity, bias=-4096.0 * Q0, scale=4096.0 * 256)
         tt(t_("yb", a, b), ind(t_("blog"), lst), t_("q4", a, b), OP.add)
-        store("sb%d" % k, T.ybank[:, a:b], t_("yb", a, b))
+    for k, (a, b) in enumerate(quarters):
+        lst = t_("plF", a // 16, b // 16)
         if YI[k] == "v":
             cp(t_("yi", a, b), ind(t_("ilog"), lst))
         else:
             act(t_("yi", a, b), ind(t_("ilog"), lst), AF.Copy)
-        if k % 2:
-            store("si%d" % (k // 2), T.yimm[:, a - 256:b], t_("yi", a - 256, b))
+    for k, (name, a, b, q) in enumerate(OUTS):
+        store("so%d" % k, {"yb": T.ybank, "yi": T.yimm}[name][:, a:b], t_(name, a, b), q)
+    return ops, edges
 
-    n = len(ops)
-    for i in range(n):
-        if "proxy" in ops[i]:
-            edges[i][ops[i]["proxy"]] = 0
-    succ = [[] for _ in range(n)]
-    for i in range(n):
-        for j, w in edges[i].items():
-            l = lag.get(j, ops[j]["cost"]) + COST["wake"] if w else ops[j]["cost"]
-            if "proxy" in ops[i]:
-                l = COST["link"]
-            succ[j].append((i, l))
-    order = list_schedule(n, [o["q"] for o in ops], [o["cost"] for o in ops], *timetable(ops, edges, succ, lag))[0]
 
+def queues(ops):
+    calls = {}
+    for i, o in enumerate(ops):
+        calls.setdefault((o["step"], o["name"]), []).append(i)
+    rows = {q: [i for i, o in enumerate(ops) if o["q"] == q] for q in "yn"}
+    for q in "vspg":
+        row = rows[q] = []
+        for t, words in [(0, FIRST[q])] + [(t, ORDER[q]) for t in range(STEPS - 2)] + [(STEPS - 2, FINAL[q])]:
+            for word in words.split():
+                name, _, count = word.partition("*")
+                part = {"_": "pre.", "^": "end."}.get(name[0], "")
+                left = calls.get((t + name.count("+"), part + q + name.strip("_^+")), [])
+                row += [left.pop(0) for _ in range(min(int(count or 1), len(left)))]
+        assert len(row) == sum(o["q"] == q for o in ops)
+    return rows
+
+
+def rank_program(g, core, T, topo):
+    if T.rank_of(core) is None:
+        return
+    ops, edges = program(g, core, T, topo)
+    rows = queues(ops)
     eng = {"v": g.vector, "s": g.scalar, "p": g.tensor, "g": g, "y": g.sync}
     total = {}
-    at = [None] * n
+    at = [None] * len(ops)
     know = {q: {} for q in eng}
-    snap = [None] * n
-    for i in order:
+    snap = [None] * len(ops)
+
+    def issue(i):
         o = ops[i]
         q = o["q"]
         if q == "n":
             at[i] = (o["sem"], o["inc"])
             snap[i] = {o["sem"]: o["inc"]}
             total[o["sem"]] = o["inc"]
-            continue
+            return
         k = know[q]
         want = {}
         for j, w in edges[i].items():
-            if w and at[j] is not None:
+            if w:
                 s, v = at[j]
                 if k.get(s, 0) < v and want.get(s, (0, 0))[0] < v:
                     want[s] = (v, j)
@@ -847,14 +678,25 @@ def rank_program(g, core, T, topo):
                 if k.get(s2, 0) < v2:
                     k[s2] = v2
         ins = o["emit"]()
+        snap[i] = dict(k)
         if o["sem"] is not None:
             total[o["sem"]] = total.get(o["sem"], 0) + o["inc"]
             ins.then_inc(T.sem[o["sem"]], o["inc"])
             at[i] = (o["sem"], total[o["sem"]])
-            snap[i] = dict(k)
             snap[i][o["sem"]] = total[o["sem"]]
         if "remote" in o:
             total["rl"] = total.get("rl", 0) + o["remote"]
+
+    ahead = {q: 0 for q in rows}
+    left = len(ops)
+    while left:
+        before = left
+        for q, row in rows.items():
+            while ahead[q] < len(row) and all(snap[j] is not None for j in edges[row[ahead[q]]]):
+                issue(row[ahead[q]])
+                ahead[q] += 1
+                left -= 1
+        assert left < before
     for s in sorted(total):
         if know["g"].get(s, 0) < total[s]:
             g.wait_ge(T.sem[s], total[s])

@@ -9,27 +9,29 @@ Q0 = 192.0
 STEPS = 6
 LOG = 1024 + 256 * STEPS
 TILES = {
-    "z": (256, "bfloat16", 7), "bk": (1024, "int32", 1), "wti": (1, "int32", 1),
-    "T1a": (272, "bfloat16", 1), "LR": (1920, "bfloat16", 1), "Bt": (256, "bfloat16", 1), "T3": (1040, "bfloat16", 1), "C16": (256, "bfloat16", 1),
-    "d16": (256, "bfloat16", 1), "ba": (80, "bfloat16", 1), "c05": (16, "bfloat16", 1), "T1b": (272, "bfloat16", 1),
-    "RB": (240, "bfloat16", 1), "X2": (2064, "bfloat16", 1), "geno_s": (4096, "bfloat16", 1), "W": (8192, "bfloat16", 2),
-    "blog": (LOG, "float32", 1), "qlog": (LOG, "bfloat16", 1), "ilog": (LOG, "bfloat16", 1), "ptab": (1040, "float32", 1), "psrc": (256, "float32", 6),
+    "LR": (1920, "bfloat16", 1), "z": (256, "bfloat16", 7), "bk": (1024, "int32", 1), "wti": (1, "int32", 1),
+    "T1a": (272, "bfloat16", 1), "T3": (1040, "bfloat16", 1), "Bt": (256, "bfloat16", 1), "RB": (240, "bfloat16", 1), "ba": (80, "bfloat16", 1),
+    "bb": (32, "bfloat16", 1), "nI": (128, "bfloat16", 1), "T1b": (288, "bfloat16", 1),
+    "C16": (256, "bfloat16", 1), "d16": (256, "bfloat16", 1), "c05": (16, "bfloat16", 1), "X2": (2064, "bfloat16", 1),
+    "MX": (512, "bfloat16", 1), "m17": (256, "bfloat16", 1), "nw": (256, "bfloat16", 2), "NB": (144, "bfloat16", 1), "NC": (8, "bfloat16", 1),
+    "HB": (32, "int32", 1), "y": (32, "bfloat16", 1), "KC": (32, "bfloat16", 1), "geno_s": (4096, "bfloat16", 1), "W": (8192, "bfloat16", 2),
+    "blog": (LOG, "float32", 1), "qlog": (LOG, "bfloat16", 1), "ilog": (LOG, "bfloat16", 1), "ptab": (1056, "float32", 1), "psrc": (256, "float32", 6),
     "EW": (144, "bfloat16", 1), "ptb": (1024, "bfloat16", 1), "hb": (16, "float32", 2),
     "Iq": (128, "bfloat16", 1), "T2": (32, "bfloat16", 6), "cq": (256, "bfloat16", 1),
     "q4": (1024, "float32", 1), "yb": (1024, "float32", 1), "yi": (1024, "bfloat16", 1), "plF": (64, "uint16", 1),
-    "pI": (1, "int32", 1), "pM": (1, "int32", 1), "pG": (1, "int32", 1), "p8": (1, "int32", 1), "col": (1, "float32", 15),
+    "pI": (1, "int32", 1), "pM": (1, "int32", 1), "pG": (1, "int32", 1), "p8": (1, "int32", 1), "col": (1, "float32", 17), "FS": (2048, "bfloat16", 1), "XF": (128, "bfloat16", 1), "I16p": (128, "bfloat16", 1),
     "ic": (256, "float32", 1), "lnO": (16, "float32", 1), "lnq": (16, "float32", 1),
-    "I": (128, "bfloat16", 1), "nI": (128, "bfloat16", 1), "I16": (128, "bfloat16", 1), "I9": (128, "bfloat16", 1), "J": (128, "bfloat16", 1),
-    "IB": (136, "bfloat16", 1), "XG": (128, "bfloat16", 1),
-    "Gmf": (8, "float32", 1), "Gm4": (4, "float32", 1), "GS": (8, "bfloat16", 1), "G64": (8, "bfloat16", 1), "G32": (8, "bfloat16", 1),
+    "I": (128, "bfloat16", 1), "I16": (128, "bfloat16", 1), "I9": (128, "bfloat16", 1), "J": (128, "bfloat16", 1),
+    "IB": (144, "bfloat16", 1), "XG": (128, "bfloat16", 1),
+    "Gmf": (8, "float32", 1), "Gm4": (4, "float32", 1), "GS": (16, "bfloat16", 1), "G64": (8, "bfloat16", 1), "G32": (8, "bfloat16", 1), "Gh": (16, "bfloat16", 1), "c8": (32, "bfloat16", 1),
     "EB": (144, "bfloat16", 1), "wE": (144, "float16", 1), "eq": (16, "float32", 1), "ne": (16, "float32", 1),
-    "C17": (136, "bfloat16", 1), "d17": (136, "bfloat16", 1), "ones": (128, "bfloat16", 1),
-    "T1s": (544, "bfloat16", 1), "E16": (128, "bfloat16", 1), "b0": (256, "int32", 1), "pw": (8, "float32", 1), "p8e": (8, "float32", 2),
+    "C17": (144, "bfloat16", 1), "d17": (144, "bfloat16", 1), "ones": (128, "bfloat16", 1),
+    "T1s": (560, "bfloat16", 1), "E16": (128, "bfloat16", 1), "b0": (256, "int32", 1), "pw": (8, "float32", 1), "p8e": (8, "float32", 2),
     "p8f": (1, "float32", 1), "xi": (256, "int32", 1), "xj": (256, "int32", 1),
-    "ui": (16, "float32", 2), "UV": (32, "int32", 2), "s": (16, "float32", 2), "sq": (16, "float32", 2), "VV": (32, "int32", 2), "vl": (16, "uint16", 3),
-    "vh": (32, "float16", 2), "G": (256, "bfloat16", 1), "pl": (16, "uint16", 2), "wl": (32, "uint16", 2), "E": (256, "bfloat16", 1),
+    "ui": (16, "float32", 2), "UV": (32, "int32", 2), "s": (16, "float32", 2), "sq": (16, "float32", 2), "s2": (16, "float32", 1), "X": (32, "float32", 1), "VV": (32, "int32", 2), "vl": (16, "uint16", 3),
+    "vh": (32, "float16", 2), "G": (256, "bfloat16", 1), "pl": (16, "uint16", 2), "wl": (16, "uint16", 2), "E": (384, "bfloat16", 1),
     "boff": (256, "uint16", 2), "bs": (256, "float32", 2), "qg": (256, "bfloat16", 2), "im1": (256, "bfloat16", 2), "fl": (256, "bfloat16", 2), "gt": (256, "bfloat16", 2),
-    "qs": (256, "float32", 2), "ac": (34, "bfloat16", 1), "A": (1, "float32", 2), "s12": (576, "float32", 1), "HI": (32, "int32", 1), "HA": (32, "int32", 1),
+    "qs": (256, "float32", 2), "sk": (32, "float32", 1), "ac": (34, "bfloat16", 1), "A": (1, "float32", 2), "s12": (576, "float32", 1), "HI": (32, "int32", 1), "HA": (32, "int32", 1),
     "KM": (80, "bfloat16", 2), "kx": (16, "float32", 1), "sm": (16, "int32", 1), "sl": (16, "int32", 1), "ca": (16, "float32", 1),
     "ol": (80, "uint16", 2), "pen": (32, "bfloat16", 1), "ybk": (256, "float32", 1), "q1": (256, "bfloat16", 1),
     "d12": (512, "bfloat16", 1), "a2": (256, "bfloat16", 1), "SG": (768, "bfloat16", 1), "ti": (48, "int32", 1), "mk": (48, "int32", 1),
@@ -51,37 +53,45 @@ for _k in range(2):
     SCRATCH["Yc%d" % _k] = ("sbuf", [128, 10, 32], "bfloat16")
 SCRATCH["TH"] = ("sbuf", [128, 6, 16], "bfloat16")
 LOADS = ["bites", "wt", "bank", "immun", "geno"]
-OUTS = [("yb", 0, 512, "y"), ("yb", 512, 1024, "y"), ("yi", 0, 1024, "s")]
+OUTS = [("yb", 0, 512, "y"), ("yb", 512, 1024, "y"), ("yi", 0, 512, "y"), ("yi", 512, 1024, "s")]
 STORES = ["sg"] + ["so%d" % k for k in range(len(OUTS))]
 SEMAPHORES = ["qv", "qs", "qp", "qg", "rl"] + ["arr%d" % t for t in range(1, STEPS)] + ["ld_" + n for n in LOADS] + ["st_" + n for n in STORES]
 
+SHARE = (40, 16, 16, 16, 16, 32)
+PARTS = [[("s", 0, 32), ("s", 32, 64), ("s", 64, 128 - v), ("s", 128, 192), ("s", 192, 224), ("s", 224, 256)] + [("v", 128 - v, 128)] * (v > 0) for v in SHARE]
+OFFS = [(0, 64), (64, 256)]
+MAXIMA = [(0, 32), (32, 64), (64, 128), (128, 192), (192, 224), (224, 256)]
+SUMS = [(0, 128), (128, 224), (224, 256)]
+YI = "svvs"
+PB = 512
+AHEAD = [False, False, False, False, False, False, False]
+OVER = "ssssss"
+CB = 4
+SQUARE = "ssssss"
+PLACES = "ssssss"
+RANKS = "pppppp"
+SECOND = "ssssss"
+NUMBERS = "vvvvvv"
+YV = (2, 2)
+CYCLE, GATHER, SCATTER, WAKE, OWN, LANDS = 0.83e-3, 1.56, 3.8, 0.19, 0.19, 3.0
 FIRST = {
-    'v': '_pw*2 _J _pw _col _pM _pG _col*2 _p8 _col6 _EB _Gmf _col4 _ac _ne _pw _P3 _eq _p8f _lnO _c05 _col _col6 _p8e _col3 _EB _p8e _c05 _col2 _col5 _col2*2 _col6 _wE _xi _xj _Bt _ui _p8e2 _s _hb _UV.u _hb _qlog _UV _qlog _VV _qlog _vl _qlog b0 _vh _col4 boff b0 _LR*5 boff _LR*10 W.5 _blog bs fl _ac _IB _blog2 _p8e2 _C16 _E M.m1*6 M.m0*8 _T2 M.m4*2 M.m1*2 _wl _col7 M.m4*2 M.m0*6 M.m1*6 M.m0*2 M.m2*4 M.m1*2 M.m2*8 M.m4*2 M.m3*4 _RB M.m3*2 s12.0 M.m2*4 M.m3*2 M.m4*2 _T3 qs s12.2 s12.1 ui s12.3 _Gm4 HI s HA UV.u kx ac sm KM sl ca KM2*2 KM3 A _col7 Yc0 _EW Yc0 bs blog UV blog2 VV ol vl ybk d12 d122 vh _T3 pl boff+ q1',
-    's': '_wti _ones _X2*8 _ba _nI _ba _G32 _X2*4 _GS _I16 _Iq _sq _ptab _psrc _ptab _ba _G64 _ptab*2 qg W.0 W.1 W.4 W.2 ptab W.3 ptab _ba ptab im1 ptab _T1a ptab gt ptab _I9 ptab _X2*4 ptab*2 sq ptab _T1b ptab Yc0*2 ptab T2 ptab _psrc ptab*3 pen G _lnq blog ad blog SG _psrc',
-    'p': '_P3J _P3wE*16 _P3LR*10 P0I*2 _P5J P0I P6I _P5Iq P1I _P7J P0I*2 P4I _P7Iq _P3LR*5 _P3I _P3I16*5 P1W.c0*4 _P3I16*10 _P5E16 P3J P6W.c2*4 P3wE*4 P6W.c2*4 P1M.m*8 P6fl P3wE*4 P2J P3wE*4 P1M.m*4 P2qg*2 P1W.c0*4 P6W.c2*4 P3wE*4 P1W.c0*4 P6W.c2*4 P1W.c0*4 P1M.m*4 P1fl P6W.c1*4 P6M.m*8 P4nI P6W.c1*12 P6M.m*8 P4gt*2 _P5E162 P4gt*2 P1J P1Iq P6J P7J P0I+ P6Iq P5I P0I+',
-    'g': '_pI _lnO _ic _X2 _cq _d17 _I _C17 _XG _g _XG*2 _d17 _XG _pen _d16 _T1s _C172 _C16 _T1s _E16 _T1s _T3 _d16 _RB _X2 _T1s _ba M.1 geno_s M.0',
+    'v': '_pw _J _EB _col0 _pw _ac _p8 _pG _ac _pw _col3 _P3 _pM _col2 _p8e _pw _c05 _col1 _col4 _p8e _col11 _col7 _Gmf _ne _col5 _col10 _EB _Gm4 _col6 _xi _eq _c05 _wE _xj _IB _col13 _Bt _col12 ui _col9 _p8f s _col8 _p8e _hb UVu _qlog _hb _qlog _col13 UV _p8e _T2 _qlog VV _qlog vl _C16 _col14 b0 _LR:10 boff _LR:5 b0 _FS:4 vh boff _FS:4 fl _FS:4 W _FS:4 _EW *:4 _col16 *:4 E _RB *:4 _lnO *:20 _blog:4 *:20 wl *:12 _lnq s12 qs s12 _lnq s12 _T3 s12 _T3',
+    's': '_wti _ones _X2:8 _I9 _Iq _X2:4 _GS _Gh _I16p sq _ptab:2 _psrc:2 _ptab _Gh _ptab _G64 _nI _X2:4 _G32 _I16 qg W:2 im1 _T2 W:4 _T1a _ba _T1b ptab _ba sk gt _ba ptab:2 _ba _GS ptab',
+    'p': 'P3J P3wE:16 P0I:5 P3LR:15 *f:8 P0I:4 P4fl:4 P2J _P7J _P7Iq P6I _P7J *f:16 _P5J *f:8 P3I P1I _P7Iq _P5Iq _P5J P6fl _P5Iq P2qg:2 *e:24 P1W:8 *e:16 *0:4 *e:6 P1fl P3J+ P1W:8 P6W:8 *0:4 _P7E16 _P5E16 *0:4 P6W:8 *0:4 P6W:8 P4I P4nI *1:4 P6W:8 *1:12 P4gt:4 P5Ia:2',
+    'g': '_pI _ic _XG _C17 _XG _lnO _I _XF _d16 _C16 _XG _E16 _XG _C17 _RB _cq _T1s _d16 _C17 _T1s:2 _send _d17 _T1s _d17 _T3 _bb Mx M _X2 M _ba Mx Mx+ geno_s _X2 M+ _pen M+ Mx+',
 }
 ORDER = {
-    'v': 'boff+ qlog ti TH mk E TH.l W.6+ C M.m0+*6 cl M.m0+*2 cx M.m1+*2 K M.m0+*2 M.m1+*2 M.m0+*4 mna M.m1+*6 M.m0+*2 M.m1+*2 mnb M.m1+*2 wl M.m2+*2 fl1 fl+ M.m2+*4 M.m1+*2 M.m2+*4 M.m3+*2 M.m2+*2 ilog M.m3+*2 M.m2+*2 M.m4+*6 M.m3+*2 M.m4+*2 M.m3+*2 M.m2+*2 qs+ s12.0+ s12.1+ s12.2+ s12.3+ HI+ HA+ kx+ KM+ sm+ ca+ sl+ KM3+ KM2+*2 ac+ ui+ Yc0+ s+ Yc0+ bs+ A+ bs+ UV.u+ UV+ VV+ vl+ ol+ vh+ ybk+ d12+ d122+ pl+ boff++ q1+',
-    's': 'SG2 SG3 W.0+ W.1+ W.2+ W.3+ qg+ W.4+ W.5+ ptab+ im1+ ptab+*3 gt+ ptab+ T2+ ptab+*7 Yc0+*2 ptab+ sq+ ptab+*2 psrc+ ptab+ G+ a2+ pen+ blog+*2 ad+ SG+',
-    'p': 'P0I+ P5RB*16 P4I.u P2EW*16 P7I P7nI P1I+ P3LR*5 P5I9.p P3LR*5 P0I+*2 P5I9.p P5EB*16 P3LR*5 P4I.u P2I.g P0I+ P2I.g P2I.l P2nI.l*3 P3I P3I16*5 P6I+ P4I.c*2 P4nI.c P4I.k*2 P4nI.k P3I16*10 P1W.c0+*4 P2J+ P1W.c0+*4 P4I+ P1M.m+*12 P2qg+*2 P1W.c0+*4 P1M.m+*4 P6W.c1+*16 P1W.c0+*4 P1fl+ P6W.c2+*12 P6M.m+*4 P6W.c2+*4 P6M.m+*4 P4nI+ P6fl+ P6M.m+*8 P5I+ P4gt+*2 P3J+ P4gt+*2 P3wE+*16 P7J+ P0I++',
-    'g': 'g M.0+ geno_s+ M.1+',
+    'v': 'ac HI HA kx *c ui+ sm Yca:2 s+ ca sl A UVu+ KM1 KM:2 UV+ Ycb VV+ ola Ycb vl+ d12 bs:2 olb vh+ ybk q1 pl+ boff+:2 ti TH mk qlog TH W+ *+:4 C *+:12 cl K E+ cx mna *+:4 mnb *+:4 fl+ fl1 *+:4 ilog *+:36 wl+ s12+ qs+ s12+:3',
+    's': 'psrc ptab Yca:2 ptab sq+ ptab Ycb:2 ptab a2 G+ SG pen SG blog:2 ad d12 W+:2 qg+ W+:4 im1+ gt+ ptab+ sk+ ptab+:2 T2 ptab+',
+    'p': 'P7Iz:2 P3wE+:16 P4ones P0I+:5 P5RBa:16 P5Ib P5RBb:16 P7I P7nI:2 P2EW+:16 *u:2 P4I9:2 P1I+ P4EB:16 P3LR+:15 *g:2 P0I+:4 *f+:16 *l:4 P6I+ *f+:16 P3I+ *c:3 *k:3 P2J+ *e+:8 P1W+:16 *e+:16 P1fl+ *e+:8 *0+:8 *e+:8 P4fl+:4 P4I+ P2qg+:2 P6W+:8 P6fl+ *e+:6 P6W+:8 *0+:4 P6W+:16 P5Ia+:2 *0+:4 P4nI+ *1+:16 P4gt+:4 P3J++',
+    'g': 'send M++:2 geno_s+',
 }
 FINAL = {
-    'v': 'boff+ qlog W.6+ ti E mk M.m0+*2 TH M.m0+*2 TH.l M.m0+*2 nb M.m1+*2 C M.m1+*2 C M.m1+*2 M.m0+*2 M.m1+*6 R M.m0+*2 M.m1+*2 M.m0+*2 K M.m0+*2 mna M.m0+*2 mnb M.m2+*2 M.m1+*2 fl1 M.m2+*4 ilog M.m2+*2 wl M.m3+*2 fl+ M.m3+*2 M.m2+*4 M.m4+*4 M.m3+*2 M.m2+*2 M.m4+*4 M.m3+*2 M.m2+*2 s12.0+ qs+ s12.1+ s12.2+ s12.3+ HI+ HA+ kx+ KM+ sm+ ca+ sl+ KM3+ KM2+*2 Yc0+*2 ol+ d12+ bs+ q1+ bs+ qlog+ plF+ ybk+ ti+ TH+ mk+ TH.l+ nb+ C+*2 R+ K+ mna+ ^yb2+ mnb+ fl1+ ^yb+ ilog+ ^yb3+ ^yb4+ ^yi+',
-    's': 'SG2 W.1+ W.0+ W.2+ qg+ W.3+ W.4+ W.5+ ptab+ im1+ ptab+*4 gt+ ptab+*9 Yc0+*2 ptab+*2 ptb+*2 a2+ ad+ pen+ SG+ SG2+ ^q42+ ^q4+ blog+*2 ^q43+ ^q44+ ^yi+*3 ^outso2+',
-    'p': 'P5RB*16 P7I.z P4I+ P1I+ P7I.z P2EW*16 P7I P7nI*2 P5I9.p P0I+ P3LR*5 P5I9.p P0I+ P5EB*4 P3LR*5 P5EB*8 P0I+ P5EB*4 P3LR*5 P0I+ P1M.m+*4 P2J+ P3I P7I.z+ P3I16*5 P1W.c0+*4 P3I16*5 P1W.c0+*4 P3I16*5 P6I+ P1M.m+*4 P5I+ P6W.c1+*12 P1M.m+*4 P1W.c0+*4 P1M.m+*4 P6fl+ P6W.c2+*8 P6W.c1+*4 P1W.c0+*4 P6W.c2+*4 P2qg+*2 P6M.m+*4 P4nI+ P6W.c2+*4 P1fl+ P6M.m+*12 P4gt+ P7I.z+ P4gt+*3 P5RB+*16 P7I+ P7nI+*2 P5I9.p+ P3EW.F+*8 P5I9.p+ P3EW.F+*8 P5EB+*16',
-    'g': 'M.0+ M.1+ ptb+*2 geno_s+',
+    'v': 'ac HI HA *c kx Yca ui+ Yca sm s+ ca sl A bs KM1 KM:2 UV+ ola bs VV+ Ycb:2 vl+ d12 olb vh+ ybk q1 pl+ boff+:2 qlog *+:4 E+ *+:4 ti TH *+:4 W+ mk *+:8 TH bs+ *+:8 C *+:4 wl+ bs+ fl+ K *+:4 mna *+:4 mnb *+:4 fl1 *+:4 ilog *+:16 s12+ qs+ s12+:3 HI+ HA+ *c+ kx+ Yca+ sm+ Yca+ ca+ sl+ KM1+ KM+:2 Ycb+ ola+ Ycb+ d12+ olb+ q1+ ybk+ qlog+ plF+ ti+ TH+ mk+ TH+ ^yb C+ ^yb K+ ^yb mna+ ^yb mnb+ fl1+ ilog+ ^yi:2',
+    's': 'ptab Yca:2 ptab sq+ ptab Ycb:2 ptab a2 G+ SG ad blog:2 SG W+ pen W+ qg+ W+:3 ptab+ W+ ptab+ im1+ ptab+ gt+ ptab+:4 Yca+:2 ptab+ ptb+ Ycb+:2 ptb+ a2+ SG+ pen+ SG+ blog+ ^q4 blog+ ad+ ^q4:3 ^yi:2 ^ou',
+    'p': 'P1I+ P3wE+:16 P7Iz:2 P4ones P6I+ P5RBa:16 P0I+:5 P5Ib P5RBb:16 P7I P7nI:2 P2EW+:16 P3LR+:15 P0I+:4 *f+:32 P4I9:2 P4EB:16 P3I+ *e+:24 P4I+ *e+:8 *g:2 *e+:14 *l:4 *k:3 P7Iz+:2 P1W+:8 P2J+ *0+:8 P1W+:8 P6W+:8 P5Ia+:2 P6fl+ P1fl+ P6W+:8 P2qg+:2 *0+:4 P6W+:16 *0+:4 P4nI+ *1+:16 P4gt+:4 P5RBa+:16 P5Ib+ P5RBb+:16 P7I+ P7nI+:2 P3EW+:16 P4I9+:2 P4EB+:16 *g+:2 *l+:4 *k+:3',
+    'g': 'geno_s+ ptb+:2',
 }
-PARTS = [[("s", 0, 32), ("s", 32, 64), ("s", 64, 128 - v), ("s", 128, 192), ("s", 192, 224), ("s", 224, 256), ("v", 128 - v, 128)] for v in (32, 20, 20, 20, 20, 40)]
-PARTS[0] = [("s", 0, 32), ("s", 32, 96), ("s", 128, 192), ("s", 192, 224), ("s", 224, 256), ("v", 96, 128)]
-OFFS = [(0, 64), (64, 256)]
-MAXIMA = [(0, 64), (64, 128), (128, 192), (192, 224), (224, 256)]
-SUMS = [(0, 128), (128, 224), (224, 256)]
-YI = "sssv"
-PB = 512
-EARLY = 3
-YV = 2
 
 
 def program(g, core, T, topo):
@@ -90,7 +100,6 @@ def program(g, core, T, topo):
     ops = []
     last = {}
     edges = []
-    part = {"name": "pre.", "runs": {}, "last": None, "step": 0, "of": ""}
 
     def t_(name, a=0, b=None, c=0, step=1, rows=(0, 128)):
         w, d, copies = TILES[name]
@@ -99,65 +108,69 @@ def program(g, core, T, topo):
         off, p = PLACE[name]
         off += p * (c + (c > 0) if name == "z" else c % copies)
         ap = T[BUF[d]][rows[0]:rows[1], off + a:off + b:step] if step != 1 else T[BUF[d]][rows[0]:rows[1], off + a:off + b]
-        return {"ap": ap, "rg": [(BUF[d], off + a, off + b)], "n": (b - a + step - 1) // step, "ind": False}
+        return {"ap": ap, "rg": [(BUF[d], off + a, off + b)], "n": (b - a + step - 1) // step, "w": BYTES[d], "ind": False}
 
     def p_(k, a, b, step=1, rows=(0, 128)):
         ap = T.P5[:, a // 8:b // 8, :] if k == 5 else T["P%d" % k][rows[0]:rows[1], a:b:step] if step != 1 else T["P%d" % k][rows[0]:rows[1], a:b]
-        return {"ap": ap, "rg": [("P%d" % k, 0, 512)], "ind": False}
+        return {"ap": ap, "rg": [("P%d" % k, a, b)], "n": (b - a + step - 1) // step, "w": 8, "ind": False}
 
-    def y_(t, a, b, step, rows=(0, 128)):
+    def y_(t, f0, f1, a, b, step, rows=(0, 128)):
         name = "Yc%d" % (t % 2)
-        return {"ap": T[name][rows[0]:rows[1], :, a:b:step], "rg": [(name, 0, 32)], "ind": False}
+        return {"ap": T[name][rows[0]:rows[1], 2 * f0:2 * f1, a:b:step], "rg": [(name, f0, f1)], "n": 2 * (f1 - f0) * ((b - a + step - 1) // step), "w": 2, "ind": False}
 
     def th_(a, b, step=1):
-        return {"ap": T.TH[:, a:b:step, :], "rg": [("TH", x, x + 1) for x in range(a, b, step)], "ind": False}
+        return {"ap": T.TH[:, a:b:step, :], "rg": [("TH", x, x + 1) for x in range(a, b, step)], "n": 16 * len(range(a, b, step)), "w": 2, "ind": False}
 
-    def m_(t, a, b, k=None):
-        x = t_("W", 4096 + 16 * a, 4096 + 16 * b, t) if k is None else t_("W", 4096 + 16 * a + k, 4096 + 16 * b, t, 16)
-        return dict(x, rg=[("M%d.%d" % (t % 2, r), a, b) for r in (range(16) if k is None else [k])])
+    def m_(t, a, b, k, two=False):
+        o = 2048 * (a // 128 + 1)
+        return dict(t_("W", o + 16 * a + k, o + 16 * b, t, 8 if two else 16), rg=[("M%d.%d" % (t % 2, r), a, b) for r in ((k, k + 8) if two else (k,))])
+
+    def c_(t, a, b, k=0, step=1):
+        o = 2048 * (a // 128)
+        return t_("W", o + 16 * a + k, o + 16 * b, t, step)
 
     def ind(win, off):
-        return {"ap": win["ap"].indirect(off["ap"]), "rg": win["rg"] + off["rg"], "win": win["rg"], "off": off["rg"], "ind": True}
+        return {"ap": win["ap"].indirect(off["ap"]), "rg": win["rg"] + off["rg"], "win": win["rg"], "off": off["rg"], "n": 16 * off["n"], "w": 4, "ind": True}
 
-    starts = {d: sorted((PLACE[x][0], x) for x in TILES if TILES[x][1] == d) for d in BUF}
-    dtype_of = {BUF[d]: d for d in BUF}
+    starts = {BUF[d]: sorted((PLACE[x][0], x) for x in TILES if TILES[x][1] == d) for d in BUF}
+    now = {"step": -1, "of": "", "last": {}}
 
     def name_of(region):
-        if region[0] not in dtype_of:
-            return "M" if region[0][0] == "M" else region[0]
-        return [x for o, x in starts[dtype_of[region[0]]] if o <= region[1]][-1]
+        if region[0] not in starts:
+            return "M" if region[0][0] == "M" else region[0][:2]
+        o, x = [(o, x) for o, x in starts[region[0]] if o <= region[1]][-1]
+        return x + "%d" % ((region[1] - o) // 16) if x == "col" else x
 
-    def add(q, emit, R, W, sem, inc, grp=None, role=None):
+    def add(q, emit, R, W, sem, inc, busy, grp=None, role=None, after=0.0):
         i = len(ops)
         ed = {}
+        banks = set()
         for (buf, a, b), wr in [(r, False) for r in R] + [(r, True) for r in W]:
             if buf[0] == "P":
-                runs = last.setdefault(buf, [("", []), ("", [])])
-                if runs[1][0] != q:
-                    runs[:] = [runs[1], (q, [])]
-                for j, grp2, role2 in runs[0][1]:
-                    ed[j] = 1
-                for j, grp2, role2 in runs[1][1]:
-                    if q == "p" and j != i and not (grp is not None and grp == grp2 and role == "mid" and role2 == "mid"):
-                        ed.setdefault(j, 0)
-                runs[1][1].append((i, grp, role))
-                continue
+                banks.add(buf)
+                if q == "p":
+                    row = last.setdefault("row" + buf, [])
+                    for j, grp2, role2 in row:
+                        if not (grp is not None and grp == grp2 and role == "mid" and role2 == "mid"):
+                            ed.setdefault(j, 0)
+                    if role != "mid":
+                        row[:] = []
+                    row.append((i, grp, role))
             lst = last.setdefault(buf, [])
             for (a2, b2, j, wr2, grp2) in lst:
                 if a2 < b and a < b2 and j != i and (wr or wr2) and not (wr and wr2 and grp is not None and grp == grp2):
-                    ed[j] = 1
+                    ed[j] = max(ed.get(j, 0), 0 if q == ops[j]["q"] == "p" else 1)
             if wr:
                 lst[:] = [x for x in lst if not (x[0] >= a and x[1] <= b and x[2] != i and not (grp is not None and x[4] == grp))]
             lst.append((a, b, i, wr, grp))
-        tag = name_of(W[0]) if W else q
-        if tag[0] == "P" and R:
-            tag += name_of(R[0])
-        k = q + tag.replace("Yc1", "Yc0") + part["of"]
-        if k != part["last"]:
-            part["runs"][k] = part["runs"].get(k, 0) + 1
-        part["last"] = k
-        run = 1 if part["of"] or k == "sptab" else part["runs"][k]
-        ops.append({"q": q, "emit": emit, "sem": sem, "inc": inc, "step": part["step"], "name": part["name"] + k + (str(run) if run > 1 else "")})
+        name = q + (name_of(W[0]) if W else "send")
+        if name[1:2] == "P" and R:
+            name += name_of(R[0])
+        name = q + now["of"] if now["of"][:1] == "*" else name + now["of"]
+        if now["last"].get(name, (0, None))[1] == now["step"] and q != "y":
+            ed.setdefault(now["last"][name][0], 0)
+        now["last"][name] = (i, now["step"])
+        ops.append({"q": q, "emit": emit, "sem": sem, "inc": inc, "busy": busy, "after": after, "banks": banks, "name": name, "step": now["step"]})
         edges.append(ed)
         return i
 
@@ -171,64 +184,77 @@ def program(g, core, T, topo):
     def raw(x):
         return x["ap"] if isinstance(x, dict) else x
 
+    def took(out, a, cycles, start=0.05):
+        if out["ind"] or a["ind"]:
+            return start + out["n"] * (SCATTER if out["ind"] else GATHER) * CYCLE
+        return max(64, a["n"] * cycles) * CYCLE
+
+    def narrow(*xs):
+        return 0.5 if all(x["w"] == 2 for x in xs) else 1
+
     def tt(out, a, b, op):
-        return add("v", lambda: g.vector.tensor_tensor(raw(out), raw(a), raw(b), op), rgs(a, b), out["rg"], "qv", 1)
+        return add("v", lambda: g.vector.tensor_tensor(raw(out), raw(a), raw(b), op), rgs(a, b), out["rg"], "qv", 1, took(out, a, 1 if 8 in (a["w"], b["w"]) else 2))
 
     def ts(out, a, s1, s2, o1, o2=None, grp=None):
         f = (lambda: g.vector.tensor_scalar(raw(out), raw(a), raw(s1), raw(s2), o1)) if o2 is None else (lambda: g.vector.tensor_scalar(raw(out), raw(a), raw(s1), raw(s2), o1, o2))
-        return add("v", f, rgs(a, s1, s2), out["rg"], "qv", 1, grp=grp)
+        return add("v", f, rgs(a, s1, s2), out["rg"], "qv", 1, took(out, a, narrow(out, a)), grp=grp)
 
     def cp(out, a):
-        return add("v", lambda: g.vector.tensor_copy(raw(out), raw(a)), rgs(a), out["rg"], "qv", 1)
+        return add("v", lambda: g.vector.tensor_copy(raw(out), raw(a)), rgs(a), out["rg"], "qv", 1, took(out, a, narrow(out, a)))
 
     def ms(out, val):
-        return add("v", lambda: g.vector.memset(raw(out), val), [], out["rg"], "qv", 1)
+        return add("v", lambda: g.vector.memset(raw(out), val), [], out["rg"], "qv", 1, took(out, out, narrow(out)))
 
     def red(out, a):
-        return add("v", lambda: g.vector.tensor_reduce(raw(out), raw(a), AxisListType.X, OP.add), rgs(a), out["rg"], "qv", 1)
+        return add("v", lambda: g.vector.tensor_reduce(raw(out), raw(a), AxisListType.X, OP.add), rgs(a), out["rg"], "qv", 1, took(out, a, 1))
 
     def scan(out, a, b, o0, o1):
-        return add("v", lambda: g.vector.tensor_tensor_scan(raw(out), raw(a), raw(b), 0.0, o0, o1), rgs(a, b), out["rg"], "qv", 1)
+        return add("v", lambda: g.vector.tensor_tensor_scan(raw(out), raw(a), raw(b), 0.0, o0, o1), rgs(a, b), out["rg"], "qv", 1, took(out, a, 1))
 
     def act(out, a, fn, bias=0.0, scale=1.0, grp=None):
         if out["ind"]:
-            return add("s", lambda: g.scalar.activation(raw(out), raw(a), fn), rgs(a) + out["off"], out["win"], "qs", 1)
+            return add("s", lambda: g.scalar.activation(raw(out), raw(a), fn), rgs(a) + out["off"], out["win"], "qs", 1, took(out, a, 1, 0.065))
         if isinstance(bias, float) and bias == 0.0:
             f = (lambda: g.scalar.activation(raw(out), raw(a), fn, scale=raw(scale))) if scale != 1.0 else (lambda: g.scalar.activation(raw(out), raw(a), fn))
         else:
             f = lambda: g.scalar.activation(raw(out), raw(a), fn, bias=raw(bias), scale=raw(scale))
-        return add("s", f, rgs(a, bias, scale), out["rg"], "qs", 1, grp=grp)
+        return add("s", f, rgs(a, bias, scale), out["rg"], "qs", 1, took(out, a, 1, 0.065), grp=grp)
 
     def mm(out, lhsT, rhs, start, stop, grp=None, role=None):
-        return add("p", lambda: g.tensor.matmul(raw(out), raw(lhsT), raw(rhs), start, stop), rgs(lhsT, rhs), out["rg"], "qp", 1, grp=grp, role=role)
+        return add("p", lambda: g.tensor.matmul(raw(out), raw(lhsT), raw(rhs), start, stop), rgs(lhsT, rhs), out["rg"], "qp", 1,
+                   max(min(64, lhsT["n"]), rhs["n"]) * CYCLE / 2, grp=grp, role=role)
 
     def iota(out, pattern, base=0, cm=0, whole=False):
         def f():
             if whole:
                 return g.iota(raw(out), pattern, base, cm)
             return g.iota(raw(out), pattern, base, cm, allow_small_or_imprecise_dtypes=True)
-        return add("g", f, [], out["rg"], "qg", 1)
+        return add("g", f, [], out["rg"], "qg", 1, 0.13 + 2 * out["n"] * CYCLE)
 
     def fill(out, val):
         return iota(out, [[0, out["n"]]], val)
 
     def select(out, a, pattern, op, other, base, cm):
-        return add("g", lambda: g.affine_select(raw(out), raw(a), pattern, op, other, base, cm), rgs(a), out["rg"], "qg", 1)
+        return add("g", lambda: g.affine_select(raw(out), raw(a), pattern, op, other, base, cm), rgs(a), out["rg"], "qg", 1, 0.17 + 2 * out["n"] * CYCLE)
 
     def keep(out, a):
         return select(out, a, [[0, out["n"]]], OP.is_ge, 0.0, 0, 0)
 
-    def load(name, out, q="y"):
+    def load(name, out, after, q="y"):
         eng = g.sync if q == "y" else g.scalar
-        return add(q, lambda: eng.dma_start(raw(out), T[name][:]), [], out["rg"], "ld_" + name, 16)
+        return add(q, lambda: eng.dma_start(raw(out), T[name][:]), [], out["rg"], "ld_" + name, 16, 0.1, after=after)
 
     def store(tag, dst, src, q="y"):
         eng = g.sync if q == "y" else g.scalar
-        return add(q, lambda: eng.dma_start(dst, raw(src)), src["rg"], [("out" + tag, 0, 1)], "st_" + tag, 16)
+        return add(q, lambda: eng.dma_start(dst, raw(src)), src["rg"], [("out" + tag, 0, 1)], "st_" + tag, 16, 0.1, after=1.0 + src["n"] * src["w"] / 2400)
 
-    load("wt", t_("wti"), "s")
-    for name, dst in (("bites", t_("z", 0, 512)), ("bank", t_("bk")), ("geno", t_("geno_s")), ("immun", t_("ilog", 0, 1024))):
-        load(name, dst)
+    load("wt", t_("wti"), 1.0, "s")
+    before = None
+    for name, dst, after in (("bites", t_("z", 0, 512), 1.5), ("bank", t_("bk"), 3.2), ("geno", t_("geno_s"), 6.6), ("immun", t_("ilog", 0, 1024), 7.4)):
+        i = load(name, dst, after)
+        if before is not None:
+            edges[i][before] = 0
+        before = i
 
     def send(srcs, t, dst_rank):
         dst = T.cores[dst_rank]
@@ -242,12 +268,12 @@ def program(g, core, T, topo):
                 return g.remote_dma(raw(out), raw(srcs[0]), sem, T.sem.rl, pid, rid, m)
             tr = RemoteDMATransfer(dst_ids=[DstId(rid=rid, pnc=pid)], dma_engine_mask=m, remote_sem=sem, srcs=[raw(x) for x in srcs], dsts=[raw(out)], alu_op=1)
             return g.remote_dma_fused([tr], local_sem=T.sem.rl)
-        i = add("g", f, rgs(*srcs), [], None, 0)
+        i = add("g", f, rgs(*srcs), [], None, 0, 2.3 if t == 1 else 0.3)
         ops[i]["remote"] = eng
-        j = add("n", None, [], out["rg"], "arr%d" % t, eng)
+        j = add("n", None, [], out["rg"], "arr%d" % t, eng, 0.0, after=LANDS)
         edges[j][i] = 0
 
-    P, PM, PG, P8, WF, WG, WS, CI, PK, PK0, PW, L1, L2, H1, W1 = [t_("col", c=k) for k in range(15)]
+    P, PM, PG, P8, WF, WG, WS, CI, PK, PK0, PW, L1, L2, H1, W1, CK, CS = [t_("col", c=k) for k in range(17)]
     ic = lambda n: t_("ic", 0, n)
     iota(t_("pI"), [[0, 1]], 0, 1, True)
     iota(t_("ic"), [[1, 256]])
@@ -255,11 +281,12 @@ def program(g, core, T, topo):
     ms(t_("c05", rows=(0, 64)), -2048.0)
     ms(t_("c05", rows=(64, 128)), 0.5)
     act(t_("ones"), t_("J"), AF.Sigmoid, scale=6400.0)
+    ops[-1]["busy"] += 1.3
     send([t_("z", 256, 512)], 1, (rank + 1) % n_ranks)
     iota(t_("C16"), [[0, 16], [-1, 16]], 16)
-    ms(t_("C16", rows=(64, 128)), 16 * Q0 + BIG)
+    ms(t_("C16", rows=(64, 128)), 16 * Q0 + BIG / 2)
     fill(t_("cq"), int(2048 * Q0))
-    iota(t_("C17"), [[0, 8], [-1, 17]], 17)
+    iota(t_("C17"), [[0, 8], [-2, 18]], 34)
     iota(t_("lnO"), [[16, 16]])
     ts(t_("pM"), t_("pI"), 15, None, OP.bitwise_and)
     ts(t_("pG"), t_("pI"), 4, None, OP.arith_shift_right)
@@ -281,27 +308,32 @@ def program(g, core, T, topo):
     act(t_("Iq"), t_("I"), AF.Copy, scale=-4096.0 * 256)
     for a, b in quarters:
         ts(t_("qlog", a, b), t_("bk", a, b), 1.0 / 4096 / 256, (Q0 - 0.5 + 1.0 / 8192) / 256, OP.mult, OP.add)
-
-    def numbers(k):
-        a, b = quarters[k]
-        mm(p_((5, 7, 1, 6)[k], 0, 256), t_("J"), t_("cq"), True, False)
-        mm(p_((5, 7, 1, 6)[k], 0, 256), t_("Iq"), t_("qlog", a, b), False, True)
-        tt(t_("blog", a, b), t_("bk", a, b), p_((5, 7, 1, 6)[k], 0, 256), OP.add)
-    numbers(0)
-    numbers(1)
-    for name, f in (("GS", BIG), ("G64", 64.0), ("G32", -32.0)):
-        act(t_(name), t_("Gmf"), AF.Copy, scale=f)
-    for name, f in (("nI", -1.0), ("I16", -4096.0), ("I9", 9.0)):
+    for k, (a, b) in enumerate(quarters):
+        bank = p_((5, 7)[k % 2], 256 * (k // 2), 256 * (k // 2) + 256)
+        mm(bank, t_("J"), t_("cq"), True, False)
+        mm(bank, t_("Iq"), t_("qlog", a, b), False, True)
+        tt(t_("blog", a, b), t_("bk", a, b), bank, OP.add)
+    for name, a, f in (("GS", 0, BIG), ("GS", 8, 2 * BIG), ("G64", 0, 128.0), ("G32", 0, -64.0), ("Gh", 0, 1.0), ("Gh", 8, 0.5)):
+        act(t_(name, a, a + 8), t_("Gmf"), AF.Copy, scale=f)
+    if "v" in OVER:
+        fill(t_("c8"), int(-BIG / 8))
+    for name, f in (("nI", -1.0), ("I16", -4096.0), ("I16p", 4096.0), ("I9", 9.0)):
         act(t_(name), t_("I"), AF.Copy, scale=f)
-    tt(CI, PG, P, OP.add)
-    ts(t_("IB"), ic(136), CI, BIG, OP.is_equal, OP.mult)
-    fill(t_("C17", 0, 136, step=17), 0)
+    ts(CI, PG, 2.0, P, OP.mult, OP.add)
+    ts(t_("IB"), ic(144), CI, BIG, OP.is_equal, OP.mult)
+    if any(AHEAD):
+        ts(t_("NB"), ic(144), CI, -BIG, OP.is_equal, OP.mult)
+        act(t_("NB", 17, 144, step=18), t_("Gmf"), AF.Copy, scale=BIG)
+        ts(CK, PM, -2.0, 32.0, OP.mult, OP.add)
+        act(t_("NC"), t_("Gmf"), AF.Copy, scale=CK)
+    fill(t_("C17", 0, 144, step=18), 0)
+    fill(t_("C17", 17, 144, step=18), 1)
     fill(t_("d16"), 0)
     fill(t_("d16", 0, 256, step=16), -4096)
     fill(t_("d17"), 0)
-    fill(t_("d17", 0, 136, step=17), int(-8 * BIG))
-    ms(t_("ac", 32, 33), 304.0 / 2)
-    ms(t_("ac", 33, 34), 7.59375 / 2)
+    fill(t_("d17", 0, 144, step=18), int(-8 * BIG))
+    ms(t_("ac", 32, 33), 304.0 / 128)
+    ms(t_("ac", 33, 34), 7.59375 / 128)
     ts(t_("eq"), ic(16), PM, None, OP.is_equal)
     ts(t_("ne"), ic(16), PM, 16384.0, OP.not_equal, OP.mult)
     tt(t_("Gm4"), t_("Gmf", 0, 4), t_("Gmf", 4, 8), OP.add)
@@ -310,18 +342,24 @@ def program(g, core, T, topo):
     ts(t_("RB", 112, 128), t_("eq"), -1.0, None, OP.mult)
     fill(t_("XG"), 1)
     select(t_("XG"), t_("XG"), [[-16, 8], [0, 16]], OP.is_ge, 0.0, 0, 1)
+    select(t_("XF"), t_("XG"), [[16, 8], [0, 16]], OP.is_ge, 0.0, 15, -1)
     select(t_("XG"), t_("XG"), [[1, 128]], OP.is_gt, 0.0, 0, -1)
     select(t_("XG"), t_("XG"), [[-1, 128]], OP.not_equal, -1.0, 0, 1)
+    for m in range(16):
+        ts(t_("FS", 128 * m, 128 * m + 128), t_("XF"), t_("eq", m, m + 1), None, OP.min)
+    ts(CS, PM, 1040.0, None, OP.add)
     for m in range(15):
         ts(t_("LR", 128 * m, 128 * m + 128), t_("XG"), t_("eq", m, m + 1), None, OP.min)
     ms(p_(3, 0, 256, 16), 0.0)
     ts(t_("lnO"), t_("lnO"), PM, 16.0, OP.add, OP.mult)
-    act(t_("lnq"), t_("lnO"), AF.Copy, scale=1.0 / 4096)
+    for h in range(2):
+        ts(t_("lnq", 8 * h, 8 * h + 8), t_("lnO", 8 * h, 8 * h + 8), 1.0 / 8192, (2056 + 2048 * h) / 8192 - 1, OP.mult, OP.add)
     for k in range(2):
         act(t_("ba", 16 * k, 16 * k + 16), t_("lnO"), AF.Identity, bias=16.0)
     for h in range(2):
         act(t_("ba", 32 + 8 * h, 40 + 8 * h), t_("lnO", 0, 8), AF.Identity, bias=16.0)
-    iota(t_("ba", 48, 80), [[4080, 2], [0, 16]], 16)
+    iota(t_("ba", 48, 80), [[2048, 2], [0, 16]], 16)
+    iota(t_("bb"), [[0, 2], [2048, 2], [0, 8]])
     fill(t_("X2", 0, 1), 0)
     fill(t_("X2", 2049, 2064), 0)
     for k in range(16):
@@ -330,14 +368,14 @@ def program(g, core, T, topo):
     tt(PK, PM, PK0, OP.add)
     ts(t_("T2", c=0), ic(32), PK, (Q0 + 8) / 256, OP.is_equal, OP.mult)
     seed = lambda a, b: t_("T1s", a, b, rows=(0, 16))
-    fill(seed(0, 544), 1)
-    select(seed(0, 272), seed(0, 272), [[1, 272]], OP.not_equal, Q0 / 256, -256, 16)
+    fill(seed(0, 560), 1)
+    select(seed(0, 272), seed(0, 272), [[1, 272]], OP.not_equal, Q0 / 256, -264, 16)
     for pattern in ([[-1, 16], [0, 16]], [[0, 16], [-1, 16]]):
-        select(seed(273, 529), seed(273, 529), pattern, OP.not_equal, Q0 / 256, 15, -1)
+        select(seed(289, 545), seed(289, 545), pattern, OP.not_equal, Q0 / 256, 15, -1)
     select(t_("E16", rows=(0, 16)), t_("ones", rows=(0, 16)), [[0, 8], [-1, 16]], OP.is_equal, 0.0, 0, 1)
     for k, name in enumerate(("T1a", "T1b")):
-        mm(p_(5, 0, 272), t_("E16", rows=(0, 16)), seed(272 * k, 272 * k + 272), True, True)
-        act(t_(name), p_(5, 0, 272), AF.Copy)
+        mm(p_((5, 7)[k], 0, 272 + 16 * k), t_("E16", rows=(0, 16)), seed(272 * k, 272 + 288 * k), True, True)
+        act(t_(name), p_((5, 7)[k], 0, 272 + 16 * k), AF.Copy)
     ms(t_("pw", 0, 1), 1.0)
     for k in (1, 2, 4):
         ts(t_("pw", k, 2 * k), t_("pw", 0, k), float(2 ** k), None, OP.mult)
@@ -358,9 +396,13 @@ def program(g, core, T, topo):
     hosts = lambda a=0, b=1024: t_("ptab", 16 + a, 16 + b)
     for k in range(4):
         act(hosts(256 * k, 256 * k + 256), t_("Bt"), AF.Identity, bias=t_("hb", k, k + 1), scale=L1)
-    places = lambda t: act(t_("psrc", c=t), t_("Bt"), AF.Identity, bias=t_("hb", 4 + t, 5 + t, 1), scale=L2)
-    for t in range(EARLY):
-        places(t)
+
+    def tables(t):
+        act(t_("psrc", c=t), t_("Bt"), AF.Identity, bias=t_("hb", 4 + t, 5 + t, 1), scale=L2)
+        if t:
+            act(t_("T2", c=t), t_("T2", c=0), AF.Copy, scale=(Q0 + 8 + t) / (Q0 + 8))
+    tables(0)
+    tables(1)
     ts(t_("p8e", c=1), ic(8), t_("p8f"), None, OP.is_equal)
     tt(t_("p8e", c=1), t_("p8e", c=1), t_("pw"), OP.mult)
     red(W1, t_("p8e", c=1))
@@ -372,165 +414,229 @@ def program(g, core, T, topo):
             mm(out, t_(wts, 15 - r, 143 - r), t_(src, a + r, b, 0, 16), first and r == 0, r == 15)
 
     def host(t):
+        now["step"] = t
         w = 32 if t + 2 < STEPS else 16
-        mm(p_(3, 256, 272), t_("J"), t_("c05"), True, False)
+        mm(p_(3, 384, 400), t_("J"), t_("c05"), True, False)
         for r in range(16):
-            mm(p_(3, 256, 272), t_("wE", 15 - r, 143 - r), t_("z", r, 256, t, 16), False, r == 15)
-        ts(t_("ui", c=t), p_(3, 256, 272), 1.5 * 2 ** 35, 1.5 * 2 ** 35, OP.add, OP.subtract)
-        tt(t_("s", c=t), p_(3, 256, 272), t_("ui", c=t), OP.subtract)
-        act(t_("sq", c=t), t_("s", c=t), AF.Square, bias=2047.5 + 592)
+            mm(p_(3, 384, 400), t_("wE", 15 - r, 143 - r), t_("z", r, 256, t, 16), False, r == 15)
+        ts(t_("ui", c=t), p_(3, 384, 400), 1.5 * 2 ** 35, 1.5 * 2 ** 35, OP.add, OP.subtract)
+        tt(t_("s", c=t), p_(3, 384, 400), t_("ui", c=t), OP.subtract)
+        if SQUARE[t] == "v":
+            ts(t_("s2"), t_("s", c=t), 2047.5 + 592, None, OP.add)
+            tt(t_("sq", c=t), t_("s2"), t_("s2"), OP.mult)
+        else:
+            act(t_("sq", c=t), t_("s", c=t), AF.Square, bias=2047.5 + 592)
         if w > 16:
-            part["of"] = ".u"
+            now["of"] = "u"
             ts(t_("UV", 16, 32, t), t_("s", c=t), 4.0, 8190.0, OP.mult, OP.add)
-            part["of"] = ""
+            now["of"] = ""
         ts(t_("UV", 0, 16, t), t_("sq", c=t), 1.0 / 32, t_("A", c=t - 1) if t else 311.59375, OP.mult, OP.add)
         ts(t_("VV", 0, w, t), t_("UV", 0, w, t), 1023, None, OP.bitwise_and)
         cp(t_("vl", c=t), t_("VV", 0, 16, t))
         if t:
-            act(t_("G"), ind(hosts(), t_("vl", c=t)), AF.Copy)
+            if PLACES[t] == "v":
+                cp(t_("G"), ind(hosts(), t_("vl", c=t)))
+            else:
+                act(t_("G"), ind(hosts(), t_("vl", c=t)), AF.Copy)
             to_list(p_(2, 256, 272), "G", 0, 256, "EW")
             cp(t_("pl", c=t), p_(2, 256, 272))
         ts(t_("vh", 0, w, t), t_("VV", 0, w, t), 16.0, None, OP.add)
         for m in range(15):
             mm(p_(3, m + 1, 256, 16), t_("LR", 128 * m, 128 * m + 128), t_("vh", 0, 16, t), True, True)
-        ts(t_("E"), p_(3, 0, 256), 0.0, None, OP.is_equal)
-        mm(p_(3, 272, 288), t_("I"), t_("vh", 0, 16, t), True, False)
+        now["of"] = "*f"
+        for m in range(16):
+            mm(p_(3, 256 + m, 384, 16), t_("FS", 128 * m, 128 * m + 128), t_("vh", 0, 16, t, 2), True, False)
+            mm(p_(3, 256 + m, 384, 16), t_("nI"), t_("vh", 1, 16, t, 2), False, True)
+        now["of"] = ""
+        ts(t_("E"), p_(3, 0, 384), 0.0, None, OP.is_equal)
+        mm(p_(3, 400, 416), t_("I"), t_("vh", 0, 16, t), True, False)
+        now["of"] = "*e"
         for m in range(15):
-            mm(p_(3, 272, 288), t_("I16"), t_("E", m + 1, 256, 0, 16), False, m == 14)
-        ts(t_("wl", 0, 32, t, 2), p_(3, 272, 288), PM, None, OP.max)
+            mm(p_(3, 400, 416, 2), t_("I16"), t_("E", m + 1, 256, 0, 32), False, False)
+            mm(p_(3, 401, 416, 2), t_("I16p"), t_("E", m + 17, 256, 0, 32), False, False)
+        for m in range(16):
+            mm(p_(3, 401, 416, 2), t_("I16p"), t_("E", 256 + m, 384, 0, 16), False, m == 15)
+        now["of"] = ""
+        ts(t_("wl", c=t), p_(3, 400, 416), PM, CS, OP.max, OP.min)
 
-    def step(t):
+    def gather(t):
         z = t_("z", c=t)
         n = 1024 + 256 * t
-        cross = t + 2 < STEPS
-        pl = t_("pl", c=t) if t else t_("vl", c=t)
-        W = lambda a, b, s=1: t_("W", a, b, t, s)
-        mm(p_(0, 0, 256), t_("I"), z, True, True)
-        twice = {x: 256 + 64 * k for k, x in enumerate(x for x in MAXIMA if x[1] - x[0] <= 32)}
-        for (a, b), o in twice.items():
-            for e in range(2):
-                mm(p_(0, o + e, o + 2 * (b - a), 2), t_("I"), t_("z", a, b, t), True, True)
+        now["step"] = t
         for a, b in OFFS:
             if t:
                 cp(t_("boff", a, b, t), ind(t_("blog", 0, n), t_("pl", a // 16, b // 16, t)))
             else:
                 ts(t_("b0", a, b), ind(t_("bk"), t_("vl", a // 16, b // 16)), 4095, None, OP.bitwise_and)
                 cp(t_("boff", a, b), t_("b0", a, b))
-                part["runs"].pop("vb0"), part["runs"].pop("vboff")
-        for k, (q, a, b) in enumerate(PARTS[t]):
-            part["of"] = ".%d" % k
+        for q, a, b in PARTS[t]:
             if q == "s":
-                act(W(16 * a, 16 * b), ind(t_("geno_s"), t_("boff", a, b, t)), AF.Copy)
+                act(c_(t, a, b), ind(t_("geno_s"), t_("boff", a, b, t)), AF.Copy)
             else:
-                cp(W(16 * a, 16 * b), ind(t_("geno_s"), t_("boff", a, b, t)))
-        part["of"] = ""
+                cp(c_(t, a, b), ind(t_("geno_s"), t_("boff", a, b, t)))
         keep(t_("geno_s", t, 4096, step=16), z)
         if t == STEPS - 1:
             store("sg", T.ygeno[:], t_("geno_s"))
-        qg, fl, gt, im1 = t_("qg", c=t), lambda h: t_("fl", 128 * h, 128 * h + 128, t), lambda h: t_("gt", 128 * h, 128 * h + 128, t), t_("im1", c=t)
         for h in range(2):
-            ts(t_("bs", 128 * h, 128 * h + 128, t), t_("boff", 128 * h, 128 * h + 128, t), float(t + 2048 * h), None, OP.add)
+            keep(m_(t, 128 * h, 128 * h + 128, 8), t_("z", 128 * h, 128 * h + 128, t))
+            now["of"] = "x"
+            if AHEAD[t]:
+                act(m_(t, 128 * h, 128 * h + 128, 0), ind(t_("z", 256 - n, 256, t - 1), t_("pl", 8 * h, 8 * h + 8, t)), AF.Copy)
+            elif t < 2:
+                keep(m_(t, 128 * h, 128 * h + 128, 0), t_("z", 128 * h, 128 * h + 128, t))
+            now["of"] = ""
+
+    def step(t):
+        z = t_("z", c=t)
+        n = 1024 + 256 * t
+        cross = t + 2 < STEPS
+        pl = t_("pl", c=t) if t else t_("vl", c=t)
+        qg, im1 = t_("qg", c=t), t_("im1", c=t)
+        fl, gt, nw = [lambda h, x=x: t_(x, 128 * h, 128 * h + 128, t) for x in ("fl", "gt", "nw")]
+        now["of"] = "u"
+        if AHEAD[t + 1] and AHEAD[t]:
+            act(t_("blog", n, n + 256), ind(t_("blog", 0, n), pl), AF.Copy)
+        elif AHEAD[t + 1]:
+            cp(t_("blog", n, n + 256), t_("boff", c=t))
+        now["of"] = ""
+        for h in range(2):
+            bs = t_("bs", 128 * h, 128 * h + 128, t)
+            if AHEAD[t] and not AHEAD[t + 1] or NUMBERS[t] == "s":
+                act(bs, ind(t_("blog", 0, n), t_("pl", 8 * h, 8 * h + 8, t)), AF.Identity, bias=float(t + 2048 * h))
+            else:
+                ts(bs, t_("blog", n + 128 * h, n + 128 * h + 128) if AHEAD[t] else t_("boff", 128 * h, 128 * h + 128, t), float(t + 2048 * h), None, OP.add)
         act(qg, ind(t_("qlog", 0, n), pl), AF.Copy)
         act(im1, ind(t_("ilog", 0, n), pl), AF.Identity, bias=-1.0)
         ts(t_("fl", c=t), qg, (Q0 + t + 0.5) / 256, None, OP.is_gt)
-        mm(p_(4, 256, 512), t_("I"), z, True, False)
-        mm(p_(4, 256, 512), t_("nI"), im1, False, True)
-        act(t_("gt", c=t), p_(4, 256, 512), AF.Sign, bias=-1.5)
+        if AHEAD[t]:
+            ts(t_("nw", c=t), qg, (Q0 + t + 6.5) / 256, None, OP.is_gt)
+        if t + 1 < STEPS:
+            for h in range(4):
+                mm(p_(4, 96 + 8 * h, 104 + 8 * h), fl(h % 2), t_("Gh", 8 * (h // 2), 8 * (h // 2) + 8), True, True)
+            act(t_("sk"), p_(4, 96, 128), AF.Relu, bias=0.75e9, scale=-1e9)
+        if OVER[t] == "v":
+            tt(t_("gt", c=t), ind(t_("ilog", 0, n), pl), z, OP.is_lt)
+        else:
+            mm(p_(4, 256, 512), t_("I"), z, True, False)
+            mm(p_(4, 256, 512), t_("nI"), im1, False, True)
+            act(t_("gt", c=t), p_(4, 256, 512), AF.Sign, bias=-1.5)
         mm(p_(2, 0, 256), t_("J"), t_("C16"), True, False)
         for h in range(2):
             mm(p_(2, 128 * h, 128 * h + 128), t_("qg", 128 * h, 128 * h + 128, t), t_("I16"), False, h == 1)
-        if t + 1 < STEPS:
-            act(t_("T2", c=t + 1), t_("T2", c=0), AF.Copy, scale=(Q0 + 9 + t) / (Q0 + 8))
-        if t and t + EARLY - 1 < STEPS:
-            places(t + EARLY - 1)
-        for j in range(15, -1, -1):
-            act(ind(t_("ptab"), t_("wl", 2 * j, 2 * j + 1, t)), t_("psrc", 16 * j, 16 * j + 16, t), AF.Sigmoid)
+        for j in range(7, -1, -1):
+            act(ind(t_("ptab"), t_("wl", 2 * j, 2 * j + 2, t)), t_("psrc", 32 * j, 32 * j + 32, t), AF.Sigmoid)
+        if t + 2 < STEPS:
+            tables(t + 2)
         if t + 1 == STEPS:
             for a, b in quarters:
                 if a < PB:
                     act(t_("ptb", a, b), hosts(a, b), AF.Copy)
                 else:
                     keep(t_("ptb", a, b), hosts(a, b))
-            part["of"] = ".F"
             to_list(p_(3, 64, 128), "ptb", 0, 1024, "EW")
-            part["of"] = ""
             cp(t_("plF"), p_(3, 64, 128))
+        if OVER[t] == "v":
+            now["of"] = "c"
+            mm(p_(4, 16, 48), t_("ones"), t_("c8"), True, False)
+            now["of"] = ""
         for h in range(4):
-            mm(p_(4, 16 + 8 * h, 24 + 8 * h), gt(h % 2), t_("GS"), True, True)
+            mm(p_(4, 16 + 8 * h, 24 + 8 * h), gt(h % 2), t_("GS", 8, 16) if OVER[t] == "v" else t_("GS", 0, 8), OVER[t] == "s", OVER[t] == "s" or h == 3)
+        if t + 1 < STEPS:
+            tt(t_("ac", 0, 32), p_(4, 16, 48), t_("sk"), OP.is_gt)
+            mm(p_(4, 48, 82), t_("ones"), t_("ac"), True, True)
+            red(t_("A", c=t), p_(4, 48, 82))
+            host(t + 1)
+            now["step"] = t
         scan(t_("qs", c=t), t_("d16"), p_(2, 0, 256), OP.add, OP.max)
-        for e, (a, b) in enumerate(MAXIMA):
-            part["of"] = ".m%d" % e
+        mm(p_(0, 0, 256), t_("I"), z, True, True)
+        twice = {x: 256 + 64 * k for k, x in enumerate(x for x in MAXIMA if x[1] - x[0] <= 32)}
+        for (a, b), o in twice.items():
+            for e in range(2):
+                mm(p_(0, o + e, o + 2 * (b - a), 2), t_("I"), t_("z", a, b, t), True, True)
+        top = lambda a, b, k: m_(t, a, b, k) if k % 8 else t_("MX", 2 * a + k // 8, 2 * b, 0, 2)
+        now["of"] = "*"
+        for a, b in MAXIMA:
             for k in range(16 if b - a > 32 else 0):
-                tt(m_(t, a, b, k), W(16 * a + k, 16 * b, 16), p_(0, a, b), OP.max)
+                tt(top(a, b, k), c_(t, a, b, k, 16), p_(0, a, b), OP.max)
             for k in range(8 if b - a <= 32 else 0):
-                two = dict(W(4096 + 16 * a + k, 4096 + 16 * b, 8), rg=m_(t, a, b, k)["rg"] + m_(t, a, b, k + 8)["rg"])
-                tt(two, W(16 * a + k, 16 * b, 8), p_(0, twice[a, b], twice[a, b] + 2 * (b - a)), OP.max)
-        part["of"] = ""
+                tt(m_(t, a, b, k, True) if k else t_("MX", 2 * a, 2 * b), c_(t, a, b, k, 8), p_(0, twice[a, b], twice[a, b] + 2 * (b - a)), OP.max)
+        now["of"] = ""
+        for h in range(2 if AHEAD[t] else 0):
+            tt(t_("m17", 128 * h, 128 * h + 128), m_(t, 128 * h, 128 * h + 128, 0), p_(0, 128 * h, 128 * h + 128), OP.max)
         for h in range(2):
             gk, kb = ("key", t, h), (1, 6)[h]
-            mm(p_(kb, 0, 136), t_("I"), t_("C17"), True, False, gk, "first")
-            if h:
-                mm(p_(kb, 0, 136), fl(h), t_("IB"), False, False, gk, "mid")
-            for c, (a, b) in enumerate(SUMS):
-                part["of"] = ".c%d" % c
+            mm(p_(kb, 0, 144), t_("I"), t_("C17"), True, False, gk, "first")
+            mm(p_(kb, 0, 144), fl(h), t_("IB"), False, False, gk, "mid")
+            if AHEAD[t]:
+                mm(p_(kb, 0, 144), nw(h), t_("NB"), False, False, gk, "mid")
+                mm(p_(kb, 17, 144, 18), nw(h), t_("NC"), False, False, gk, "mid")
+                mm(p_(kb, 17, 144, 18), m_(t, 128 * h, 128 * h + 128, 0), t_("G32"), False, False, gk, "mid")
+                mm(p_(kb, 17, 144, 18), t_("m17", 128 * h, 128 * h + 128), t_("G64"), False, False, gk, "mid")
+            for a, b in SUMS:
                 for k in range(16 if a // 128 == h else 0):
-                    mm(p_(kb, 1 + k, 136, 17, (a % 128, b - 128 * h)), W(16 * a + k, 16 * b, 16), t_("G32"), False, False, gk, "mid")
-            part["of"] = ".m"
+                    mm(p_(kb, 1 + k, 144, 18, (a % 128, b - 128 * h)), c_(t, a, b, k, 16), t_("G32"), False, False, gk, "mid")
+            now["of"] = "*%d" % h
             for k in sorted(range(16), key=lambda k: k % 8 if h else k):
-                end = h == 1 and k == 15
-                mm(p_(kb, 1 + k, 136, 17), m_(t, 128 * h, 128 * h + 128, k), t_("G64"), False, end, gk, "last" if end else "mid")
-            part["of"] = ""
-            if not h:
-                mm(p_(kb, 0, 136), fl(h), t_("IB"), False, True, gk, "last")
-            part["of"] = ".%d" % h
-            keep(m_(t, 128 * h, 128 * h + 128, 0), t_("z", 128 * h, 128 * h + 128, t))
-            o = 136 * h
-            scan(t_("s12", o, o + 136), t_("d17"), p_(kb, 0, 136), OP.add, OP.max)
-            part["of"] = ".%d" % (2 + h)
-            scan(t_("s12", 273 + o, 408 + o), p_(kb, 1, 136), t_("s12", o, o + 135), OP.max, OP.min)
-            part["of"] = ""
-        for k in range(2, 4 if t == 0 else 0):
-            numbers(k)
+                mm(p_(kb, 1 + k, 144, 18), top(128 * h, 128 * h + 128, k), t_("G64"), False, k == 15, gk, "last" if k == 15 else "mid")
+            now["of"] = ""
+            o = 144 * h
+            scan(t_("s12", o, o + 144), t_("d17"), p_(kb, 0, 144), OP.add, OP.max)
+            scan(t_("s12", 289 + o, 432 + o), p_(kb, 1, 144), t_("s12", o, o + 143), OP.max, OP.min)
+        if AHEAD[t + 1]:
+            gather(t + 1)
+            now["step"] = t
         KM = lambda a, b: t_("KM", a, b, t)
-        tt(t_("HI"), t_("s12", 16, 544, 0, 17), p_(4, 16, 48), OP.min)
-        ts(t_("HA"), t_("HI"), int(BIG) + 31, None, OP.bitwise_and)
-        ts(KM(0, 32), t_("HA"), -BIG, -4080.0, OP.add, OP.max)
-        if t + 1 < STEPS:
-            ts(t_("ac", 0, 32), t_("HA"), BIG, 64.0, OP.is_ge, OP.mult)
-            mm(p_(7, 0, 34), t_("J"), t_("ac"), True, True)
-            red(t_("A", c=t), p_(7, 0, 34))
-            host(t + 1)
+        tt(t_("HI"), t_("s12", 17, 576, 0, 18), p_(4, 16, 48), OP.min)
+        ts(t_("HA"), t_("HI"), 1, int(BIG / 2) + 31, OP.arith_shift_right, OP.bitwise_and)
+        KC = lambda a, b: t_("KC", a, b) if AHEAD[t] else KM(a, b)
+        now["of"] = "*c"
+        ts(KC(0, 32), t_("HA"), -BIG / 2, -2040.0, OP.add, OP.max)
+        now["of"] = ""
+        if AHEAD[t]:
+            ts(t_("HB"), t_("HI"), 1, None, OP.bitwise_and)
+            ts(t_("y"), t_("HB"), -2048.0, 16.0, OP.mult, OP.add)
+            now["of"] = "a"
+            tt(KM(0, 32), KC(0, 32), t_("y"), OP.min)
+            now["of"] = ""
         tt(t_("kx"), t_("HA", 0, 16), t_("HA", 16, 32), OP.max)
         tt(t_("sm"), t_("kx"), t_("qs", 15, 256, t, 16), OP.max)
         ts(t_("sl"), t_("sm"), 15, None, OP.bitwise_and)
         cp(KM(32, 48), t_("sl"))
         cp(KM(48, 64), t_("sl"))
-        ts(t_("ca"), KM(0, 16), -16.0, 16.0, OP.mult, OP.add)
-        tt(KM(64, 80), t_("ca"), KM(16, 32), OP.subtract)
-        for x in range(4):
-            if x < YV:
-                ts(y_(t, x, 32, 4), KM(0, 80), t_("Gm4", x, x + 1), None, OP.mult, grp=("Y", t))
-            else:
-                act(y_(t, x, 32, 4), KM(0, 80), AF.Copy, scale=t_("Gm4", x, x + 1), grp=("Y", t))
-        i = mm(p_(5, 16, 96), t_("I"), t_("ba"), True, False)
-        for e in range(2):
-            before = i
-            for k in range(8):
-                a, rows = 112 - 16 * (k % 2), (64 * e, 64 * e + 64)
-                out = dict(p_(5, 16, 56), ap=T.P5[32 * (k // 2):32 * (k // 2) + 32, 2:12, 4 * e:4 * e + 4])
-                i = mm(out, t_("RB", a, a + 32, rows=rows), y_(t, 4 * k, 4 * k + 4, 1, rows), False, e == 1 and k % 2 == 1)
-                edges[i][before] = 1
+        ts(t_("ca"), KC(0, 16), -16.0, 16.0, OP.mult, OP.add)
+        now["of"] = "1"
+        tt(KM(64, 80), t_("ca"), KC(16, 32), OP.subtract)
+        now["of"] = ""
         ol = lambda k, m=1: t_("ol", 16 * k, 16 * (k + m), t)
-        cp(ol(0, 5), p_(5, 16, 96))
-        act(t_("pen", 16, 32), p_(5, 32, 48), AF.Sigmoid, bias=-409550.0, scale=100.0)
-        act(t_("ad"), p_(5, 16, 48), AF.Copy, scale=1.0 / 4096)
+        for f0, f1 in ((0, 2), (2, 5)):
+            now["of"] = "ab"[f0 // 2]
+            for x in range(4):
+                if x < YV[f0 // 2]:
+                    ts(y_(t, f0, f1, x, 32, 4), KM(16 * f0, 16 * f1), t_("Gm4", x, x + 1), None, OP.mult, grp=("Y", t))
+                else:
+                    act(y_(t, f0, f1, x, 32, 4), KM(16 * f0, 16 * f1), AF.Copy, scale=t_("Gm4", x, x + 1), grp=("Y", t))
+            lists = p_(5, 16 + 16 * f0, 16 + 16 * f1)
+            i = mm(lists, t_("I"), t_("ba", 16 * f0, 16 * f1), True, False)
+            if not f0:
+                i = mm(lists, t_("I"), t_("bb"), False, False)
+            for e in range(2):
+                before = i
+                for k in range(8):
+                    a, rows = 112 - 16 * (k % 2), (64 * e, 64 * e + 64)
+                    out = dict(lists, ap=T.P5[32 * (k // 2):32 * (k // 2) + 32, 2 + 2 * f0:2 + 2 * f1, 4 * e:4 * e + 4])
+                    i = mm(out, t_("RB", a, a + 32, rows=rows), y_(t, f0, f1, 4 * k, 4 * k + 4, 1, rows), False, e == 1 and k % 2 == 1)
+                    edges[i][before] = 1
+            cp(ol(f0, f1 - f0), lists)
+        now["of"] = ""
+        act(t_("pen", 16, 32), p_(5, 80, 96), AF.Sigmoid, bias=1000.0, scale=-1.0)
+        act(t_("ad"), p_(5, 16, 48), AF.Copy, scale=1.0 / 8192)
         tt(t_("ybk"), ind(t_("X2", 0, 2049), ol(2)), t_("bs", c=t), OP.min)
         for h in range(2):
             act(t_("blog", n + 128 * h, n + 128 * h + 128), t_("ybk", 128 * h, 128 * h + 128), AF.Abs, bias=float(-t - 2048 * h))
-        tt(t_("q1"), ind(t_("T1a", 0, 4096 + 257), ol(4)), qg, OP.min)
+        tt(t_("q1"), ind(t_("T1a", 0, 2048 + 273), ol(4)), qg, OP.min)
         tt(t_("qlog", n, n + 256), ind(t_("T2", c=t), ol(3)), t_("q1"), OP.max)
-        win = dict(W(0, 8192), rg=W(0, 4096)["rg"] + m_(t, 0, 256)["rg"])
-        if cross:
+        win = dict(t_("W", c=t), rg=c_(t, 0, 128)["rg"] + c_(t, 128, 256)["rg"] + [("M%d.%d" % (t % 2, r), 0, 256) for r in range(16)])
+        if SECOND[t] == "v":
             for k in range(2):
                 d = t_("d12", 256 * k, 256 * k + 256)
                 tt(d, ind(win, ol(k)), z, OP.subtract)
@@ -539,10 +645,10 @@ def program(g, core, T, topo):
             act(t_("SG", 512, 768), p_(7, 0, 256), AF.Sigmoid, bias=-math.log(31.0), scale=40.0)
         else:
             d = t_("d12", 0, 256)
-            part["of"] = ".z"
+            now["of"] = "z"
             for k in range(2):
                 mm(p_(7, 256 * k, 256 * k + 256), t_("I"), z, k == 0, False)
-            part["of"] = ""
+            now["of"] = ""
             tt(d, ind(win, ol(0)), z, OP.subtract)
             act(t_("a2"), ind(win, ol(1)), AF.Copy)
             act(t_("SG", 0, 256), d, AF.Sigmoid, bias=-math.log(31.0), scale=-40.0)
@@ -550,48 +656,45 @@ def program(g, core, T, topo):
             for k in range(2):
                 mm(p_(7, 256 * k, 256 * k + 256), t_("nI"), t_("a2"), False, k == 1)
             act(t_("SG", 256, 768), p_(7, 0, 512), AF.Sigmoid, bias=-math.log(31.0), scale=40.0)
-        cnt = p_(5, 256, 304)
-        part["of"] = ".p"
-        mm(p_(5, 256, 288), t_("I9"), t_("pen"), True, False)
-        mm(p_(5, 288, 304), t_("I9"), t_("pen", 16, 32), False, False)
-        part["of"] = ""
+            if cross:
+                act(t_("d12", 256, 512), p_(7, 0, 256), AF.Copy, scale=-1.0)
+        cnt = p_(CB, 128, 176)
+        mm(p_(CB, 128, 160), t_("I9"), t_("pen"), True, False)
+        mm(p_(CB, 160, 176), t_("I9"), t_("pen", 16, 32), False, False)
         to_list(cnt, "SG", 0, 768, first=False)
         ts(t_("ti"), cnt, 1056.0, None, OP.mult)
         ts(th_(3, 6), cnt, 8.75, None, OP.is_gt)
         ts(t_("mk"), t_("ti"), 768, None, OP.bitwise_and)
-        part["of"] = ".l"
         ts(th_(0, 3), t_("mk"), 0.0, None, OP.is_equal)
-        part["of"] = ""
-        if cross:
+        if RANKS[t] == "p":
             D = lambda a, b: p_(2, 304 + 16 * a, 304 + 16 * b)
-            code = lambda a, b: p_(4, 64 + 16 * a, 64 + 16 * b)
-            part["of"] = ".u"
-            for k in range(2):
-                mm(code(k, k + 1), t_("I"), t_("vh", 16, 32, t), k == 0, False)
-            part["of"] = ".g"
+            code = lambda a, b: p_(5, 320 + 16 * a, 320 + 16 * b)
+            now["of"] = "*g"
             mm(D(0, 3), t_("I"), th_(3, 6), True, False)
             mm(D(2, 3), t_("I"), th_(4, 5), False, False)
-            part["of"] = ".l"
+            now["of"] = "*l"
             mm(D(0, 2), t_("I"), th_(2, 6, 3), False, False)
             mm(D(0, 3), t_("nI"), th_(0, 3), False, False)
             mm(D(0, 1), t_("nI"), th_(1, 2), False, False)
             mm(D(1, 3), t_("nI"), th_(0, 4, 3), False, True)
-            part["of"] = ""
+            now["of"] = "*u"
+            for k in range(2 if cross else 0):
+                mm(code(k, k + 1), t_("I"), t_("vh", 16, 32, t), k == 0, False)
+            now["of"] = ""
             ts(t_("C"), D(0, 3), -0.5, 0.5, OP.is_gt, OP.subtract)
 
             def ranks(o, first):
                 mm(code(o, o + 2), t_("I"), t_("C", 0, 32), first, False)
                 mm(code(o + 1, o + 2), t_("I"), t_("C", 32, 48), False, False)
                 mm(code(o, o + 1), t_("nI"), t_("C", 32, 48), False, True)
-            part["of"] = ".c"
-            ranks(0, False)
-            part["of"] = ""
-            cp(t_("cl", c=t), code(0, 2))
-            tt(t_("cx", c=t), ind(t_("T3"), t_("cl", c=t)), t_("d12"), OP.mult)
-            send([z, t_("cx", 0, 256, t), t_("cx", 256, 512, t)], t + 2, (rank + 2) % n_ranks)
-            part["of"] = ".k"
+            now["of"] = "*c"
+            if cross:
+                ranks(0, False)
+            now["of"] = "*k"
             ranks(2, True)
-            part["of"] = ""
+            now["of"] = ""
+            if cross:
+                cp(t_("cl", c=t), code(0, 2))
             less1 = code(2, 4)
         else:
             tt(t_("nb"), th_(0, 6, 2), th_(1, 6, 2), OP.add)
@@ -599,17 +702,26 @@ def program(g, core, T, topo):
             tt(t_("C", 32, 48), t_("nb", 32, 48), t_("nb", 0, 16), OP.is_lt)
             tt(t_("R"), t_("C", 0, 32), t_("C", 16, 48), OP.subtract)
             less1 = t_("R")
+            if cross:
+                for k in range(2):
+                    tt(t_("X", 16 * k, 16 * k + 16), t_("R", 16 * k, 16 * k + 16), t_("vh", 16, 32, t), OP.add)
+                cp(t_("cl", c=t), t_("X"))
+        if cross:
+            tt(t_("cx", c=t), ind(t_("T3"), t_("cl", c=t)), t_("d12"), OP.mult)
+            send([z, t_("cx", 0, 256, t), t_("cx", 256, 512, t)], t + 2, (rank + 2) % n_ranks)
         tt(t_("K"), t_("ad"), less1, OP.add)
         tt(t_("mna"), t_("lnq"), t_("K", 0, 16), OP.min)
         tt(t_("mnb"), t_("mna"), t_("K", 16, 32), OP.min)
-        ts(t_("fl1", c=t), t_("mnb"), 4096.0, 4096.0, OP.mult, OP.add)
+        ts(t_("fl1", c=t), t_("mnb"), 8192.0, 8192.0, OP.mult, OP.add)
         tt(t_("ilog", n, n + 256), ind(win, t_("fl1", c=t)), im1, OP.max)
 
     host(0)
     for t in range(STEPS):
-        part.update(name="", runs={}, last=None, step=t)
+        if not AHEAD[t]:
+            gather(t)
+        now["step"] = t
         step(t)
-    part.update(name="end.", runs={}, last=None)
+    now["step"] = STEPS
     for k, (a, b) in enumerate(quarters):
         lst = t_("plF", a // 16, b // 16)
         act(t_("q4", a, b), ind(t_("qlog"), lst), AF.Identity, bias=-4096.0 * Q0, scale=4096.0 * 256)
@@ -634,12 +746,37 @@ def queues(ops):
         row = rows[q] = []
         for t, words in [(0, FIRST[q])] + [(t, ORDER[q]) for t in range(STEPS - 2)] + [(STEPS - 2, FINAL[q])]:
             for word in words.split():
-                name, _, count = word.partition("*")
-                part = {"_": "pre.", "^": "end."}.get(name[0], "")
-                left = calls.get((t + name.count("+"), part + q + name.strip("_^+")), [])
+                name, _, count = word.partition(":")
+                step = {"_": -1, "^": STEPS}.get(name[0], t + name.count("+"))
+                left = calls.get((step, q + name.strip("_^+")), [])
                 row += [left.pop(0) for _ in range(min(int(count or 1), len(left)))]
         assert len(row) == sum(o["q"] == q for o in ops)
     return rows
+
+
+def banks(ops, edges, rows):
+    end = [None] * len(ops)
+    ahead = {q: 0 for q in rows}
+    free = {q: 0.0 for q in rows}
+    user = {}
+
+    def earliest(i):
+        o = ops[i]
+        t = free[o["q"]]
+        for j, w in edges[i].items():
+            if end[j] is None:
+                return None
+            t = max(t, end[j] + ((ops[j]["after"] + WAKE if ops[j]["after"] or ops[j]["q"] != o["q"] else OWN) if w else 0.0))
+        return max([t] + [end[j] + WAKE for bank in o["banks"] for q, j in user.get(bank, {}).items() if q != o["q"]])
+    for _ in ops:
+        t, q = min((earliest(row[ahead[q]]), q) for q, row in rows.items() if ahead[q] < len(row) and earliest(row[ahead[q]]) is not None)
+        i = rows[q][ahead[q]]
+        ahead[q] += 1
+        end[i] = t + ops[i]["busy"]
+        free[q] = end[i] if q != "n" else 0.0
+        for bank in ops[i]["banks"]:
+            edges[i].update({j: 1 for q2, j in user.setdefault(bank, {}).items() if q2 != q})
+            user[bank][q] = i
 
 
 def rank_program(g, core, T, topo):
@@ -647,6 +784,7 @@ def rank_program(g, core, T, topo):
         return
     ops, edges = program(g, core, T, topo)
     rows = queues(ops)
+    banks(ops, edges, rows)
     eng = {"v": g.vector, "s": g.scalar, "p": g.tensor, "g": g, "y": g.sync}
     total = {}
     at = [None] * len(ops)

@@ -9,33 +9,31 @@ Q0 = 192.0
 STEPS = 6
 LOG = 1024 + 256 * STEPS
 TILES = {
-    "LR": (1920, "bfloat16", 1), "z": (256, "bfloat16", 7), "bk": (1024, "int32", 1), "wti": (1, "int32", 1),
-    "T1a": (272, "bfloat16", 1), "T3": (1040, "bfloat16", 1), "Bt": (256, "bfloat16", 1), "RB": (240, "bfloat16", 1), "ba": (80, "bfloat16", 1),
-    "bb": (32, "bfloat16", 1), "nI": (128, "bfloat16", 1), "T1b": (288, "bfloat16", 1),
-    "C16": (256, "bfloat16", 1), "d16": (256, "bfloat16", 1), "c05": (16, "bfloat16", 1), "X2": (2064, "bfloat16", 1),
-    "MX": (512, "bfloat16", 1), "m17": (256, "bfloat16", 1), "nw": (256, "bfloat16", 2), "NB": (144, "bfloat16", 1), "NC": (8, "bfloat16", 1),
-    "HB": (32, "int32", 1), "y": (32, "bfloat16", 1), "KC": (32, "bfloat16", 1), "geno_s": (4096, "bfloat16", 1), "W": (8192, "bfloat16", 2),
+    "z": (256, "bfloat16", 7), "bk": (1024, "int32", 1), "wti": (1, "int32", 1),
+    "T1a": (272, "bfloat16", 1), "T3": (1040, "bfloat16", 1), "Bt": (256, "bfloat16", 1), "RB": (96, "bfloat16", 1), "ba": (80, "bfloat16", 1),
+    "bb": (32, "bfloat16", 1), "nI": (128, "bfloat16", 1), "I": (128, "bfloat16", 1), "Gh": (16, "bfloat16", 1), "T1b": (288, "bfloat16", 1),
+    "c05": (16, "bfloat16", 1), "KC": (32, "bfloat16", 1),
+    "geno_s": (4096, "bfloat16", 1), "W": (8192, "bfloat16", 2), "MX": (512, "bfloat16", 1),
     "blog": (LOG, "float32", 1), "qlog": (LOG, "bfloat16", 1), "ilog": (LOG, "bfloat16", 1), "ptab": (1056, "float32", 1), "psrc": (256, "float32", 6),
-    "EW": (144, "bfloat16", 1), "ptb": (1024, "bfloat16", 1), "hb": (16, "float32", 2),
-    "Iq": (128, "bfloat16", 1), "T2": (32, "bfloat16", 6), "cq": (256, "bfloat16", 1),
-    "q4": (1024, "float32", 1), "yb": (1024, "float32", 1), "yi": (1024, "bfloat16", 1), "plF": (64, "uint16", 1),
-    "pI": (1, "int32", 1), "pM": (1, "int32", 1), "pG": (1, "int32", 1), "p8": (1, "int32", 1), "col": (1, "float32", 17), "FS": (2048, "bfloat16", 1), "XF": (128, "bfloat16", 1), "I16p": (128, "bfloat16", 1),
-    "ic": (256, "float32", 1), "lnO": (16, "float32", 1), "lnq": (16, "float32", 1),
-    "I": (128, "bfloat16", 1), "I16": (128, "bfloat16", 1), "I9": (128, "bfloat16", 1), "J": (128, "bfloat16", 1),
-    "IB": (144, "bfloat16", 1), "XG": (128, "bfloat16", 1),
-    "Gmf": (8, "float32", 1), "Gm4": (4, "float32", 1), "GS": (16, "bfloat16", 1), "G64": (8, "bfloat16", 1), "G32": (8, "bfloat16", 1), "Gh": (16, "bfloat16", 1), "c8": (32, "bfloat16", 1),
-    "EB": (144, "bfloat16", 1), "wE": (144, "float16", 1), "eq": (16, "float32", 1), "ne": (16, "float32", 1),
-    "C17": (144, "bfloat16", 1), "d17": (144, "bfloat16", 1), "ones": (128, "bfloat16", 1),
-    "T1s": (560, "bfloat16", 1), "E16": (128, "bfloat16", 1), "b0": (256, "int32", 1), "pw": (8, "float32", 1), "p8e": (8, "float32", 2),
-    "p8f": (1, "float32", 1), "xi": (256, "int32", 1), "xj": (256, "int32", 1),
-    "ui": (16, "float32", 2), "UV": (32, "int32", 2), "s": (16, "float32", 2), "sq": (16, "float32", 2), "s2": (16, "float32", 1), "X": (32, "float32", 1), "VV": (32, "int32", 2), "vl": (16, "uint16", 3),
+    "ptb": (1024, "bfloat16", 1), "q4": (1024, "float32", 1), "yb": (1024, "float32", 1), "yi": (1024, "bfloat16", 1), "plF": (64, "uint16", 1),
+    "pI": (1, "int32", 1), "pM": (1, "int32", 1), "pG": (1, "int32", 1), "p8": (1, "int32", 1), "col": (1, "float32", 16),
+    "ic": (256, "float32", 1), "lnO": (16, "float32", 1), "lnq": (16, "float32", 1), "hb": (16, "float32", 2),
+    "I16": (128, "bfloat16", 1), "I16p": (128, "bfloat16", 1), "I9": (128, "bfloat16", 1), "Iq": (128, "bfloat16", 1), "J": (128, "bfloat16", 1),
+    "ones": (128, "bfloat16", 1), "IB": (136, "bfloat16", 1), "XG": (128, "bfloat16", 1), "XF": (128, "bfloat16", 1),
+    "LR": (1920, "bfloat16", 1), "FS": (2048, "bfloat16", 1), "X2": (1040, "bfloat16", 1), "T2": (32, "bfloat16", 6),
+    "Gmf": (8, "float32", 1), "Gm4": (4, "float32", 1), "GS": (8, "bfloat16", 1), "G64": (8, "bfloat16", 1), "G32": (8, "bfloat16", 1),
+    "EB": (144, "bfloat16", 1), "EW": (144, "bfloat16", 1), "wE": (144, "float16", 1), "eq": (16, "float32", 1), "ne": (16, "float32", 1),
+    "C16": (256, "bfloat16", 1), "d16": (256, "bfloat16", 1), "C17": (136, "bfloat16", 1), "d17": (136, "bfloat16", 1),
+    "cq": (256, "bfloat16", 1), "T1s": (560, "bfloat16", 1), "E16": (128, "bfloat16", 1), "b0": (256, "int32", 1),
+    "pw": (8, "float32", 1), "p8e": (8, "float32", 2), "p8f": (1, "float32", 1), "xi": (256, "int32", 1), "xj": (256, "int32", 1),
+    "ui": (16, "float32", 2), "UV": (32, "int32", 2), "s": (16, "float32", 2), "sq": (16, "float32", 2), "VV": (32, "int32", 2), "vl": (16, "uint16", 3),
     "vh": (32, "float16", 2), "G": (256, "bfloat16", 1), "pl": (16, "uint16", 2), "wl": (16, "uint16", 2), "E": (384, "bfloat16", 1),
     "boff": (256, "uint16", 2), "bs": (256, "float32", 2), "qg": (256, "bfloat16", 2), "im1": (256, "bfloat16", 2), "fl": (256, "bfloat16", 2), "gt": (256, "bfloat16", 2),
-    "qs": (256, "float32", 2), "sk": (32, "float32", 1), "ac": (34, "bfloat16", 1), "A": (1, "float32", 2), "s12": (576, "float32", 1), "HI": (32, "int32", 1), "HA": (32, "int32", 1),
-    "KM": (80, "bfloat16", 2), "kx": (16, "float32", 1), "sm": (16, "int32", 1), "sl": (16, "int32", 1), "ca": (16, "float32", 1),
-    "ol": (80, "uint16", 2), "pen": (32, "bfloat16", 1), "ybk": (256, "float32", 1), "q1": (256, "bfloat16", 1),
+    "qs": (256, "float32", 2), "sk": (32, "float32", 1), "ac": (34, "bfloat16", 1), "A": (1, "float32", 2), "s12": (576, "float32", 1),
+    "HI": (32, "int32", 1), "HA": (32, "int32", 1), "KM": (48, "bfloat16", 1), "ca": (16, "float32", 1), "kx": (16, "float32", 1), "sm": (16, "int32", 1), "sl": (16, "int32", 1),
+    "ol": (80, "uint16", 2), "pen": (16, "bfloat16", 1), "ybk": (256, "float32", 1), "q1": (256, "bfloat16", 1),
     "d12": (512, "bfloat16", 1), "a2": (256, "bfloat16", 1), "SG": (768, "bfloat16", 1), "ti": (48, "int32", 1), "mk": (48, "int32", 1),
-    "nb": (48, "bfloat16", 1), "C": (48, "bfloat16", 1), "R": (32, "float32", 1), "ad": (32, "float32", 1), "K": (32, "float32", 1),
+    "C": (48, "bfloat16", 1), "ad": (32, "float32", 1), "K": (32, "float32", 1),
     "mna": (16, "float32", 1), "mnb": (16, "float32", 1), "fl1": (16, "uint16", 2), "cl": (32, "uint16", 2), "cx": (512, "bfloat16", 4),
 }
 BYTES = {"float32": 4, "int32": 4, "bfloat16": 2, "uint16": 2, "float16": 2}
@@ -49,47 +47,39 @@ BUF = {"float32": "bigf", "int32": "bigi", "bfloat16": "bigb", "uint16": "bigu",
 SCRATCH = {BUF[_d]: ("sbuf", [128, _size[_d]], _d) for _d in BYTES}
 for _k in range(8):
     SCRATCH["P%d" % _k] = ("psum", [128, 64, 8] if _k == 5 else [128, 512], "float32")
-for _k in range(2):
-    SCRATCH["Yc%d" % _k] = ("sbuf", [128, 10, 32], "bfloat16")
+SCRATCH["Yc"] = ("sbuf", [128, 10, 32], "bfloat16")
 SCRATCH["TH"] = ("sbuf", [128, 6, 16], "bfloat16")
 LOADS = ["bites", "wt", "bank", "immun", "geno"]
 OUTS = [("yb", 0, 512, "y"), ("yb", 512, 1024, "y"), ("yi", 0, 512, "y"), ("yi", 512, 1024, "s")]
 STORES = ["sg"] + ["so%d" % k for k in range(len(OUTS))]
-SEMAPHORES = ["qv", "qs", "qp", "qg", "rl"] + ["arr%d" % t for t in range(1, STEPS)] + ["ld_" + n for n in LOADS] + ["st_" + n for n in STORES]
+SEMAPHORES = (["qv", "qs", "qp", "qg", "rl"] + ["arr%d" % t for t in range(1, STEPS)] + ["ld_" + n for n in LOADS] + ["st_" + n for n in STORES]
+              + ["cp%d" % k for k in range(18)])
 
-SHARE = (40, 16, 16, 16, 16, 32)
-PARTS = [[("s", 0, 32), ("s", 32, 64), ("s", 64, 128 - v), ("s", 128, 192), ("s", 192, 224), ("s", 224, 256)] + [("v", 128 - v, 128)] * (v > 0) for v in SHARE]
+SHARE = (48, 14, 14, 14, 14, 44)
+PARTS = [[("s", 0, 32), ("s", 32, 128 - v), ("s", 128, 192), ("s", 192, 224), ("s", 224, 256), ("v", 128 - v, 128)] for v in SHARE]
 OFFS = [(0, 64), (64, 256)]
 MAXIMA = [(0, 32), (32, 64), (64, 128), (128, 192), (192, 224), (224, 256)]
 SUMS = [(0, 128), (128, 224), (224, 256)]
 YI = "svvs"
 PB = 512
-AHEAD = [False, False, False, False, False, False, False]
-OVER = "ssssss"
-CB = 4
-SQUARE = "ssssss"
-PLACES = "ssssss"
-RANKS = "pppppp"
-SECOND = "ssssss"
-NUMBERS = "vvvvvv"
-YV = (2, 2)
-CYCLE, GATHER, SCATTER, WAKE, OWN, LANDS = 0.83e-3, 1.56, 3.8, 0.19, 0.19, 3.0
+CYCLE, GATHER, SCATTER, WAKE, OWN, LANDS = 0.83e-3, 1.56, 3.8, 0.19, 0.19, 4.0
+
 FIRST = {
-    'v': '_pw _J _EB _col0 _pw _ac _p8 _pG _ac _pw _col3 _P3 _pM _col2 _p8e _pw _c05 _col1 _col4 _p8e _col11 _col7 _Gmf _ne _col5 _col10 _EB _Gm4 _col6 _xi _eq _c05 _wE _xj _IB _col13 _Bt _col12 ui _col9 _p8f s _col8 _p8e _hb UVu _qlog _hb _qlog _col13 UV _p8e _T2 _qlog VV _qlog vl _C16 _col14 b0 _LR:10 boff _LR:5 b0 _FS:4 vh boff _FS:4 fl _FS:4 W _FS:4 _EW *:4 _col16 *:4 E _RB *:4 _lnO *:20 _blog:4 *:20 wl *:12 _lnq s12 qs s12 _lnq s12 _T3 s12 _T3',
-    's': '_wti _ones _X2:8 _I9 _Iq _X2:4 _GS _Gh _I16p sq _ptab:2 _psrc:2 _ptab _Gh _ptab _G64 _nI _X2:4 _G32 _I16 qg W:2 im1 _T2 W:4 _T1a _ba _T1b ptab _ba sk gt _ba ptab:2 _ba _GS ptab',
-    'p': 'P3J P3wE:16 P0I:5 P3LR:15 *f:8 P0I:4 P4fl:4 P2J _P7J _P7Iq P6I _P7J *f:16 _P5J *f:8 P3I P1I _P7Iq _P5Iq _P5J P6fl _P5Iq P2qg:2 *e:24 P1W:8 *e:16 *0:4 *e:6 P1fl P3J+ P1W:8 P6W:8 *0:4 _P7E16 _P5E16 *0:4 P6W:8 *0:4 P6W:8 P4I P4nI *1:4 P6W:8 *1:12 P4gt:4 P5Ia:2',
-    'g': '_pI _ic _XG _C17 _XG _lnO _I _XF _d16 _C16 _XG _E16 _XG _C17 _RB _cq _T1s _d16 _C17 _T1s:2 _send _d17 _T1s _d17 _T3 _bb Mx M _X2 M _ba Mx Mx+ geno_s _X2 M+ _pen M+ Mx+',
+    'v': '_J _pw _cq _ac _pw _col0 _pM _pG _col2 _p8 _EB _ac _col7 _col1 _col3 _pw _c05 _ne _col4 _pw _p8e _col5 _Gmf _col9 _p8f _col11 _p8e _col6 _EB _c05 _col10 _P3 _wE _eq _IB _xi _Gm4 _RB _col13 _col8 _xj _T2 ui _Bt _lnO s _qlog:2 UV UVu _hb _LR:5 _col12 _col13 _LR:10 VV _qlog vl _qlog vh b0:2 boff _col15 _C16 _p8e boff fl _blog _hb _blog W E *:2 _p8e *:8 _blog *:24 _col14 *:2 wl _blog *:8 bs *:4 s12 qs s12:2 _EW s12 bs:2',
+    's': '_wti _ones _Gh _X2:8 _FS:12 sq _GS _ba _G64 _X2:8 _Gh _ptab _RB _G32 _FS:4 _Iq _I16 _lnq _RB _nI _I16p _ba qg W:4 im1 W _ba _psrc _ba:2 ptab gt ptab _T1a _ba _T2 ptab sk _T1b ptab _I9 ptab _lnq',
+    'p': 'P3J _P5J _P7J P3wE:16 P6I _P5Iq P3LR:15 _P7Iq P1I *f:8 P6fl *f:24 P3I P2J P4fl:4 P0I:2 _P5J P4I _P5Iq *e:32 P1fl P1W:8 *e:8 P2qg:2 _P7J *0:4 P1W:8 *0:4 *e:6 _P5E16 _P7Iq P4nI *0:4 P6W:32 *0:4 *1:4 P3J+ *1:12 _P7E16 P4gt:4 P5Ia:2',
+    'g': '_pI _ic _XG:2 _lnO _XF _bb _XG _I _XG _C16 _d17 _C17 _E16 _C17 _X2 _send _T1s _d16 _T1s:2 _X2 _d16 _d17 M _ba _T1s Mx:2 M _T3',
 }
 ORDER = {
-    'v': 'ac HI HA kx *c ui+ sm Yca:2 s+ ca sl A UVu+ KM1 KM:2 UV+ Ycb VV+ ola Ycb vl+ d12 bs:2 olb vh+ ybk q1 pl+ boff+:2 ti TH mk qlog TH W+ *+:4 C *+:12 cl K E+ cx mna *+:4 mnb *+:4 fl+ fl1 *+:4 ilog *+:36 wl+ s12+ qs+ s12+:3',
-    's': 'psrc ptab Yca:2 ptab sq+ ptab Ycb:2 ptab a2 G+ SG pen SG blog:2 ad d12 W+:2 qg+ W+:4 im1+ gt+ ptab+ sk+ ptab+:2 T2 ptab+',
-    'p': 'P7Iz:2 P3wE+:16 P4ones P0I+:5 P5RBa:16 P5Ib P5RBb:16 P7I P7nI:2 P2EW+:16 *u:2 P4I9:2 P1I+ P4EB:16 P3LR+:15 *g:2 P0I+:4 *f+:16 *l:4 P6I+ *f+:16 P3I+ *c:3 *k:3 P2J+ *e+:8 P1W+:16 *e+:16 P1fl+ *e+:8 *0+:8 *e+:8 P4fl+:4 P4I+ P2qg+:2 P6W+:8 P6fl+ *e+:6 P6W+:8 *0+:4 P6W+:16 P5Ia+:2 *0+:4 P4nI+ *1+:16 P4gt+:4 P3J++',
-    'g': 'send M++:2 geno_s+',
+    'v': 'HI bs ac HA ui+ KC kx s+ A Yca sm Yca ca sl UV+ UVu+ KM1 KM:2 VV+ ola Ycb:2 vl+ d12 olb G+ ybk q1 pl+ vh+ boff+:2 ti TH mk TH qlog *+:2 C *+:4 W+ K cl *+:2 mna cx E+ *+:4 mnb fl+ *+:8 fl1 *+:4 ilog *+:4 wl+ *+:20 s12+ qs+ s12+:2 bs+ s12+ bs+:2',
+    's': 'Yca:2 sq+ ptab:2 Ycb:2 ptab a2 T3 SG T3 SG blog:4 pen d12 T2 ad W+:2 qg+ W+:3 im1+ ptab+:2 sk+ gt+ ptab+:3',
+    'p': 'P3wE+:16 P4ones P0I+:2 P1I+ P5RBa:16 P5Ib P7Iz:2 P5RBb:16 P7I P7nI:2 P2EW+:16 *u:2 P4EB:16 P4I9:2 P3LR+:15 *g:2 *f+:8 *l:4 *c:3 *k:3 P2J+ *f+:24 P3I+ P6I+ P1W+:16 *e+:32 *0+:4 P4fl+:4 *0+:4 P4I+ *e+:14 P3J++ *0+:4 P6W+:16 P1fl+ *0+:4 P6W+:8 P6fl+ P5Ia+:2 P2qg+:2 P6W+:8 P4nI+ *1+:16 P4gt+:4',
+    'g': 'M+ geno_s send geno_s+ Mx+ M++ Mx+ M+ M++',
 }
 FINAL = {
-    'v': 'ac HI HA *c kx Yca ui+ Yca sm s+ ca sl A bs KM1 KM:2 UV+ ola bs VV+ Ycb:2 vl+ d12 olb vh+ ybk q1 pl+ boff+:2 qlog *+:4 E+ *+:4 ti TH *+:4 W+ mk *+:8 TH bs+ *+:8 C *+:4 wl+ bs+ fl+ K *+:4 mna *+:4 mnb *+:4 fl1 *+:4 ilog *+:16 s12+ qs+ s12+:3 HI+ HA+ *c+ kx+ Yca+ sm+ Yca+ ca+ sl+ KM1+ KM+:2 Ycb+ ola+ Ycb+ d12+ olb+ q1+ ybk+ qlog+ plF+ ti+ TH+ mk+ TH+ ^yb C+ ^yb K+ ^yb mna+ ^yb mnb+ fl1+ ilog+ ^yi:2',
-    's': 'ptab Yca:2 ptab sq+ ptab Ycb:2 ptab a2 G+ SG ad blog:2 SG W+ pen W+ qg+ W+:3 ptab+ W+ ptab+ im1+ ptab+ gt+ ptab+:4 Yca+:2 ptab+ ptb+ Ycb+:2 ptb+ a2+ SG+ pen+ SG+ blog+ ^q4 blog+ ad+ ^q4:3 ^yi:2 ^ou',
-    'p': 'P1I+ P3wE+:16 P7Iz:2 P4ones P6I+ P5RBa:16 P0I+:5 P5Ib P5RBb:16 P7I P7nI:2 P2EW+:16 P3LR+:15 P0I+:4 *f+:32 P4I9:2 P4EB:16 P3I+ *e+:24 P4I+ *e+:8 *g:2 *e+:14 *l:4 *k:3 P7Iz+:2 P1W+:8 P2J+ *0+:8 P1W+:8 P6W+:8 P5Ia+:2 P6fl+ P1fl+ P6W+:8 P2qg+:2 *0+:4 P6W+:16 *0+:4 P4nI+ *1+:16 P4gt+:4 P5RBa+:16 P5Ib+ P5RBb+:16 P7I+ P7nI+:2 P3EW+:16 P4I9+:2 P4EB+:16 *g+:2 *l+:4 *k+:3',
+    'v': 'HI ac HA ui+ kx KC s+ sm Yca:2 A sl ca UV+ KM:2 KM1 VV+ ola Ycb:2 vl+ vh+ bs G+ olb d12 ybk pl+ q1 boff+:2 qlog W+ *+:2 ti *+:2 fl+ bs+ TH E+ mk *+:6 TH *+:8 C *+:6 K *+:2 mna *+:2 wl+ mnb *+:2 fl1 *+:2 ilog *+:14 s12+ *+:2 s12+ qs+ s12+:2 HI+ bs+ HA+ kx+ KC+ bs+ sm+ Yca+:2 ca+ sl+ KM1+ KM+:2 ola+ Ycb+:2 d12+ olb+ bs+ ybk+ q1+ qlog+ ti+ TH+ mk+ plF+ TH+ C+ ^yb K+ ^yb mna+ ^yb mnb+ ^yb fl1+ ilog+ ^yi:2',
+    's': 'ptab Yca:2 sq+ ptab:2 Ycb:2 a2 SG ad pen blog:4 SG W+ qg+ W+:4 ptab+ im1+ ptab+:2 gt+ ptab+:3 Yca+:2 ptab+:2 Ycb+:2 a2+ SG+ ptb+ pen+ SG+ blog+ ptb+ blog+:2 ad+ blog+ ^q4:4 ^yi:2 ^ou',
+    'p': 'P3wE+:16 P4ones P5RBa:16 P5Ib P7Iz:2 P5RBb:16 P0I+:2 P2EW+:16 P7I P7nI:2 P3LR+:15 *f+:8 P4EB:16 P4I9:2 *f+:24 P3I+ *g:2 P1I+ P6I+ P7Iz+:2 *e+:8 *l:4 *e+:16 P6fl+ *k:3 *e+:8 *0+:4 *e+:14 P1W+:8 *0+:4 P4I+ P1fl+ *0+:4 P6W+:8 P1W+:8 P2J+ P2qg+:2 *0+:4 P6W+:24 *1+:12 P4nI+ *1+:4 P4gt+:4 P5Ia+:2 P5RBa+:16 P5Ib+ P5RBb+:16 P7I+ P7nI+:2 P4EB+:16 P4I9+:2 P3EW+:16 *g+:2 *l+:4 *k+:3',
     'g': 'geno_s+ ptb+:2',
 }
 
@@ -107,27 +97,26 @@ def program(g, core, T, topo):
             b = w
         off, p = PLACE[name]
         off += p * (c + (c > 0) if name == "z" else c % copies)
-        ap = T[BUF[d]][rows[0]:rows[1], off + a:off + b:step] if step != 1 else T[BUF[d]][rows[0]:rows[1], off + a:off + b]
+        ap = T[BUF[d]][slice(*rows), off + a:off + b:step] if step != 1 else T[BUF[d]][slice(*rows), off + a:off + b]
         return {"ap": ap, "rg": [(BUF[d], off + a, off + b)], "n": (b - a + step - 1) // step, "w": BYTES[d], "ind": False}
 
     def p_(k, a, b, step=1, rows=(0, 128)):
         ap = T.P5[:, a // 8:b // 8, :] if k == 5 else T["P%d" % k][rows[0]:rows[1], a:b:step] if step != 1 else T["P%d" % k][rows[0]:rows[1], a:b]
         return {"ap": ap, "rg": [("P%d" % k, a, b)], "n": (b - a + step - 1) // step, "w": 8, "ind": False}
 
-    def y_(t, f0, f1, a, b, step, rows=(0, 128)):
-        name = "Yc%d" % (t % 2)
-        return {"ap": T[name][rows[0]:rows[1], 2 * f0:2 * f1, a:b:step], "rg": [(name, f0, f1)], "n": 2 * (f1 - f0) * ((b - a + step - 1) // step), "w": 2, "ind": False}
+    def y_(f0, f1, a, b, step, rows=(0, 128)):
+        return {"ap": T.Yc[rows[0]:rows[1], 2 * f0:2 * f1, a:b:step], "rg": [("Yc", f0, f1)], "n": 2 * (f1 - f0) * ((b - a + step - 1) // step), "w": 2, "ind": False}
 
     def th_(a, b, step=1):
         return {"ap": T.TH[:, a:b:step, :], "rg": [("TH", x, x + 1) for x in range(a, b, step)], "n": 16 * len(range(a, b, step)), "w": 2, "ind": False}
 
-    def m_(t, a, b, k, two=False):
-        o = 2048 * (a // 128 + 1)
-        return dict(t_("W", o + 16 * a + k, o + 16 * b, t, 8 if two else 16), rg=[("M%d.%d" % (t % 2, r), a, b) for r in ((k, k + 8) if two else (k,))])
-
     def c_(t, a, b, k=0, step=1):
         o = 2048 * (a // 128)
         return t_("W", o + 16 * a + k, o + 16 * b, t, step)
+
+    def m_(t, a, b, k, two=False):
+        o = 2048 * (a // 128 + 1)
+        return dict(t_("W", o + 16 * a + k, o + 16 * b, t, 8 if two else 16), rg=[("M%d.%d" % (t % 2, r), a, b) for r in ((k, k + 8) if two else (k,))])
 
     def ind(win, off):
         return {"ap": win["ap"].indirect(off["ap"]), "rg": win["rg"] + off["rg"], "win": win["rg"], "off": off["rg"], "n": 16 * off["n"], "w": 4, "ind": True}
@@ -244,17 +233,18 @@ def program(g, core, T, topo):
         eng = g.sync if q == "y" else g.scalar
         return add(q, lambda: eng.dma_start(raw(out), T[name][:]), [], out["rg"], "ld_" + name, 16, 0.1, after=after)
 
+    copies = []
+
+    def copy(out, src, grp=None):
+        copies.append(add("y", lambda: g.sync.dma_start(raw(out), raw(src)), src["rg"] + t_("ilog", 0, 16)["rg"], out["rg"], "cp%d" % len(copies), 16, 0.1, grp, after=1.5))
+
     def store(tag, dst, src, q="y"):
         eng = g.sync if q == "y" else g.scalar
         return add(q, lambda: eng.dma_start(dst, raw(src)), src["rg"], [("out" + tag, 0, 1)], "st_" + tag, 16, 0.1, after=1.0 + src["n"] * src["w"] / 2400)
 
     load("wt", t_("wti"), 1.0, "s")
-    before = None
-    for name, dst, after in (("bites", t_("z", 0, 512), 1.5), ("bank", t_("bk"), 3.2), ("geno", t_("geno_s"), 6.6), ("immun", t_("ilog", 0, 1024), 7.4)):
-        i = load(name, dst, after)
-        if before is not None:
-            edges[i][before] = 0
-        before = i
+    for name, dst, after in (("bites", t_("z", 0, 512), 1.5), ("bank", t_("bk"), 3.3), ("geno", t_("geno_s"), 6.6), ("immun", t_("ilog", 0, 1024), 7.4)):
+        load(name, dst, after)
 
     def send(srcs, t, dst_rank):
         dst = T.cores[dst_rank]
@@ -273,7 +263,7 @@ def program(g, core, T, topo):
         j = add("n", None, [], out["rg"], "arr%d" % t, eng, 0.0, after=LANDS)
         edges[j][i] = 0
 
-    P, PM, PG, P8, WF, WG, WS, CI, PK, PK0, PW, L1, L2, H1, W1, CK, CS = [t_("col", c=k) for k in range(17)]
+    P, PM, PG, P8, WF, WG, WS, CI, PK, PK0, PW, L1, L2, H1, W1, CS = [t_("col", c=k) for k in range(16)]
     ic = lambda n: t_("ic", 0, n)
     iota(t_("pI"), [[0, 1]], 0, 1, True)
     iota(t_("ic"), [[1, 256]])
@@ -284,9 +274,9 @@ def program(g, core, T, topo):
     ops[-1]["busy"] += 1.3
     send([t_("z", 256, 512)], 1, (rank + 1) % n_ranks)
     iota(t_("C16"), [[0, 16], [-1, 16]], 16)
-    ms(t_("C16", rows=(64, 128)), 16 * Q0 + BIG / 2)
-    fill(t_("cq"), int(2048 * Q0))
-    iota(t_("C17"), [[0, 8], [-2, 18]], 34)
+    ms(t_("C16", rows=(64, 128)), 16 * Q0 + BIG)
+    ms(t_("cq"), 2048 * Q0)
+    iota(t_("C17"), [[0, 8], [-1, 17]], 17)
     iota(t_("lnO"), [[16, 16]])
     ts(t_("pM"), t_("pI"), 15, None, OP.bitwise_and)
     ts(t_("pG"), t_("pI"), 4, None, OP.arith_shift_right)
@@ -309,64 +299,58 @@ def program(g, core, T, topo):
     for a, b in quarters:
         ts(t_("qlog", a, b), t_("bk", a, b), 1.0 / 4096 / 256, (Q0 - 0.5 + 1.0 / 8192) / 256, OP.mult, OP.add)
     for k, (a, b) in enumerate(quarters):
-        bank = p_((5, 7)[k % 2], 256 * (k // 2), 256 * (k // 2) + 256)
+        bank = p_((5, 7)[k % 2], 256, 512)
         mm(bank, t_("J"), t_("cq"), True, False)
         mm(bank, t_("Iq"), t_("qlog", a, b), False, True)
         tt(t_("blog", a, b), t_("bk", a, b), bank, OP.add)
-    for name, a, f in (("GS", 0, BIG), ("GS", 8, 2 * BIG), ("G64", 0, 128.0), ("G32", 0, -64.0), ("Gh", 0, 1.0), ("Gh", 8, 0.5)):
+    for name, a, f in (("GS", 0, BIG), ("G64", 0, 64.0), ("G32", 0, -32.0), ("Gh", 0, 1.0), ("Gh", 8, 0.5)):
         act(t_(name, a, a + 8), t_("Gmf"), AF.Copy, scale=f)
-    if "v" in OVER:
-        fill(t_("c8"), int(-BIG / 8))
     for name, f in (("nI", -1.0), ("I16", -4096.0), ("I16p", 4096.0), ("I9", 9.0)):
         act(t_(name), t_("I"), AF.Copy, scale=f)
-    ts(CI, PG, 2.0, P, OP.mult, OP.add)
-    ts(t_("IB"), ic(144), CI, BIG, OP.is_equal, OP.mult)
-    if any(AHEAD):
-        ts(t_("NB"), ic(144), CI, -BIG, OP.is_equal, OP.mult)
-        act(t_("NB", 17, 144, step=18), t_("Gmf"), AF.Copy, scale=BIG)
-        ts(CK, PM, -2.0, 32.0, OP.mult, OP.add)
-        act(t_("NC"), t_("Gmf"), AF.Copy, scale=CK)
-    fill(t_("C17", 0, 144, step=18), 0)
-    fill(t_("C17", 17, 144, step=18), 1)
+    tt(CI, PG, P, OP.add)
+    ts(t_("IB"), ic(136), CI, BIG, OP.is_equal, OP.mult)
+    fill(t_("C17", 0, 136, step=17), 0)
     fill(t_("d16"), 0)
     fill(t_("d16", 0, 256, step=16), -4096)
     fill(t_("d17"), 0)
-    fill(t_("d17", 0, 144, step=18), int(-8 * BIG))
+    fill(t_("d17", 0, 136, step=17), int(-8 * BIG))
     ms(t_("ac", 32, 33), 304.0 / 128)
     ms(t_("ac", 33, 34), 7.59375 / 128)
     ts(t_("eq"), ic(16), PM, None, OP.is_equal)
     ts(t_("ne"), ic(16), PM, 16384.0, OP.not_equal, OP.mult)
     tt(t_("Gm4"), t_("Gmf", 0, 4), t_("Gmf", 4, 8), OP.add)
-    fill(t_("pen", 0, 16), 0)
-    fill(t_("RB"), 0)
-    ts(t_("RB", 112, 128), t_("eq"), -1.0, None, OP.mult)
+    ms(t_("RB"), 0.0)
+    for e in range(2):
+        act(t_("RB", 16 + 48 * e, 32 + 48 * e, rows=(64 * e, 64 * e + 64)), t_("eq", rows=(64 * e, 64 * e + 64)), AF.Copy, scale=-1.0)
     fill(t_("XG"), 1)
     select(t_("XG"), t_("XG"), [[-16, 8], [0, 16]], OP.is_ge, 0.0, 0, 1)
     select(t_("XF"), t_("XG"), [[16, 8], [0, 16]], OP.is_ge, 0.0, 15, -1)
     select(t_("XG"), t_("XG"), [[1, 128]], OP.is_gt, 0.0, 0, -1)
     select(t_("XG"), t_("XG"), [[-1, 128]], OP.not_equal, -1.0, 0, 1)
     for m in range(16):
-        ts(t_("FS", 128 * m, 128 * m + 128), t_("XF"), t_("eq", m, m + 1), None, OP.min)
-    ts(CS, PM, 1040.0, None, OP.add)
+        act(t_("FS", 128 * m, 128 * m + 128), t_("XF"), AF.Copy, scale=t_("eq", m, m + 1))
     for m in range(15):
         ts(t_("LR", 128 * m, 128 * m + 128), t_("XG"), t_("eq", m, m + 1), None, OP.min)
+    ts(CS, PM, 1040.0, None, OP.add)
     ms(p_(3, 0, 256, 16), 0.0)
     ts(t_("lnO"), t_("lnO"), PM, 16.0, OP.add, OP.mult)
     for h in range(2):
-        ts(t_("lnq", 8 * h, 8 * h + 8), t_("lnO", 8 * h, 8 * h + 8), 1.0 / 8192, (2056 + 2048 * h) / 8192 - 1, OP.mult, OP.add)
+        act(t_("lnq", 8 * h, 8 * h + 8), t_("lnO", 8 * h, 8 * h + 8), AF.Identity, bias=(2056 + 2048 * h) / 8192 - 1, scale=1.0 / 8192)
     for k in range(2):
         act(t_("ba", 16 * k, 16 * k + 16), t_("lnO"), AF.Identity, bias=16.0)
-    for h in range(2):
-        act(t_("ba", 32 + 8 * h, 40 + 8 * h), t_("lnO", 0, 8), AF.Identity, bias=16.0)
-    iota(t_("ba", 48, 80), [[2048, 2], [0, 16]], 16)
+    for h in range(4):
+        act(t_("ba", 32 + 4 * h, 36 + 4 * h), t_("lnO", 0, 4), AF.Identity, bias=16.0)
+    iota(t_("ba", 48, 80), [[-2048, 2], [0, 16]], 2064)
     iota(t_("bb"), [[0, 2], [2048, 2], [0, 8]])
     fill(t_("X2", 0, 1), 0)
-    fill(t_("X2", 2049, 2064), 0)
+    fill(t_("X2", 1025, 1040), 0)
     for k in range(16):
-        act(t_("X2", k or 16, 2049, step=16), ic(128), AF.Identity, bias=t_("ne", k, k + 1), scale=-16.0, grp="X2")
+        act(t_("X2", k or 16, 1025, step=16), ic(64), AF.Identity, bias=t_("ne", k, k + 1), scale=-16.0, grp="X2")
     ts(PK0, PM, 0.0, 16.0, OP.is_equal, OP.mult)
     tt(PK, PM, PK0, OP.add)
     ts(t_("T2", c=0), ic(32), PK, (Q0 + 8) / 256, OP.is_equal, OP.mult)
+    stamps = lambda t: act(t_("T2", c=t), t_("T2", c=0), AF.Copy, scale=(Q0 + 8 + t) / (Q0 + 8))
+    stamps(1)
     seed = lambda a, b: t_("T1s", a, b, rows=(0, 16))
     fill(seed(0, 560), 1)
     select(seed(0, 272), seed(0, 272), [[1, 272]], OP.not_equal, Q0 / 256, -264, 16)
@@ -386,32 +370,40 @@ def program(g, core, T, topo):
     ts(t_("xj"), t_("xi"), 128, None, OP.bitwise_and)
     ts(t_("Bt"), t_("xj"), 0.5, None, OP.mult)
     fill(t_("T3"), 0)
-    ts(t_("T3", 15, 1039, step=4), t_("Bt"), 1.0 / 64, None, OP.mult)
-    ts(t_("T3", 16, 1040, step=4), t_("Bt"), -1.0 / 64, 1.0, OP.mult, OP.add)
+    now["step"] = 0
+    act(t_("T3", 15, 1039, step=4), t_("Bt"), AF.Copy, scale=1.0 / 64)
+    act(t_("T3", 16, 1040, step=4), t_("Bt"), AF.Identity, bias=1.0, scale=-1.0 / 64)
+    now["step"] = -1
     ts(L1, PM, 8.0, 1.0 / 64, OP.is_lt, OP.mult)
     ts(L2, L1, 200.0, None, OP.mult)
     ts(H1, L1, -1.0, 1.0 / 64, OP.mult, OP.add)
     ts(t_("hb"), t_("Bt", 0, 16), H1, None, OP.mult)
     ts(t_("hb", c=1), t_("hb"), 200.0, -100.0, OP.mult, OP.add)
-    hosts = lambda a=0, b=1024: t_("ptab", 16 + a, 16 + b)
-    for k in range(4):
-        act(hosts(256 * k, 256 * k + 256), t_("Bt"), AF.Identity, bias=t_("hb", k, k + 1), scale=L1)
-
-    def tables(t):
-        act(t_("psrc", c=t), t_("Bt"), AF.Identity, bias=t_("hb", 4 + t, 5 + t, 1), scale=L2)
-        if t:
-            act(t_("T2", c=t), t_("T2", c=0), AF.Copy, scale=(Q0 + 8 + t) / (Q0 + 8))
-    tables(0)
-    tables(1)
+    hosts = lambda a=0, b=1024, rows=(0, 128): t_("ptab", 16 + a, 16 + b, rows=rows)
+    act(hosts(768, 1024), t_("Bt"), AF.Identity, bias=t_("hb", 3, 4), scale=L1)
+    act(t_("psrc", c=0), t_("Bt"), AF.Identity, bias=t_("hb", 4, 5, 1), scale=L2)
+    bit_rows = lambda bit: (8 + bit, 128, 16)
+    for k in range(3):
+        copy(hosts(256 * k, 256 * k + 256), hosts(768, 1024))
+    for k in range(3):
+        for bit in range(2):
+            if not k >> bit & 1:
+                copy(hosts(256 * k, 256 * k + 256, bit_rows(bit)), hosts(768, 1024, bit_rows(2)), "rows")
+    for t in range(1, STEPS):
+        like = min(range(t), key=lambda x: bin((4 + x) ^ (4 + t)).count("1"))
+        copy(t_("psrc", c=t), t_("psrc", c=like))
+        for bit in range(4):
+            if ((4 + like) ^ (4 + t)) >> bit & 1:
+                copy(t_("psrc", c=t, rows=bit_rows(bit)), t_("psrc", c=0, rows=bit_rows(2 if (4 + t) >> bit & 1 else 0)), "rows")
     ts(t_("p8e", c=1), ic(8), t_("p8f"), None, OP.is_equal)
     tt(t_("p8e", c=1), t_("p8e", c=1), t_("pw"), OP.mult)
     red(W1, t_("p8e", c=1))
     ts(H1, H1, 255.0 * 64, 1.0, OP.mult, OP.add)
     ts(t_("EW"), t_("EB"), W1, H1, OP.mult, OP.mult)
 
-    def to_list(out, src, a, b, wts="EB", first=True):
+    def to_list(out, src, a, b, wts="EB", stop=True):
         for r in range(16):
-            mm(out, t_(wts, 15 - r, 143 - r), t_(src, a + r, b, 0, 16), first and r == 0, r == 15)
+            mm(out, t_(wts, 15 - r, 143 - r), t_(src, a + r, b, 0, 16), r == 0, stop and r == 15)
 
     def host(t):
         now["step"] = t
@@ -421,11 +413,7 @@ def program(g, core, T, topo):
             mm(p_(3, 384, 400), t_("wE", 15 - r, 143 - r), t_("z", r, 256, t, 16), False, r == 15)
         ts(t_("ui", c=t), p_(3, 384, 400), 1.5 * 2 ** 35, 1.5 * 2 ** 35, OP.add, OP.subtract)
         tt(t_("s", c=t), p_(3, 384, 400), t_("ui", c=t), OP.subtract)
-        if SQUARE[t] == "v":
-            ts(t_("s2"), t_("s", c=t), 2047.5 + 592, None, OP.add)
-            tt(t_("sq", c=t), t_("s2"), t_("s2"), OP.mult)
-        else:
-            act(t_("sq", c=t), t_("s", c=t), AF.Square, bias=2047.5 + 592)
+        act(t_("sq", c=t), t_("s", c=t), AF.Square, bias=2047.5 + 592)
         if w > 16:
             now["of"] = "u"
             ts(t_("UV", 16, 32, t), t_("s", c=t), 4.0, 8190.0, OP.mult, OP.add)
@@ -434,10 +422,7 @@ def program(g, core, T, topo):
         ts(t_("VV", 0, w, t), t_("UV", 0, w, t), 1023, None, OP.bitwise_and)
         cp(t_("vl", c=t), t_("VV", 0, 16, t))
         if t:
-            if PLACES[t] == "v":
-                cp(t_("G"), ind(hosts(), t_("vl", c=t)))
-            else:
-                act(t_("G"), ind(hosts(), t_("vl", c=t)), AF.Copy)
+            cp(t_("G"), ind(hosts(), t_("vl", c=t)))
             to_list(p_(2, 256, 272), "G", 0, 256, "EW")
             cp(t_("pl", c=t), p_(2, 256, 272))
         ts(t_("vh", 0, w, t), t_("VV", 0, w, t), 16.0, None, OP.add)
@@ -459,9 +444,11 @@ def program(g, core, T, topo):
         now["of"] = ""
         ts(t_("wl", c=t), p_(3, 400, 416), PM, CS, OP.max, OP.min)
 
-    def gather(t):
+    def step(t):
         z = t_("z", c=t)
         n = 1024 + 256 * t
+        cross = t + 2 < STEPS
+        pl = t_("pl", c=t) if t else t_("vl", c=t)
         now["step"] = t
         for a, b in OFFS:
             if t:
@@ -480,53 +467,30 @@ def program(g, core, T, topo):
         for h in range(2):
             keep(m_(t, 128 * h, 128 * h + 128, 8), t_("z", 128 * h, 128 * h + 128, t))
             now["of"] = "x"
-            if AHEAD[t]:
-                act(m_(t, 128 * h, 128 * h + 128, 0), ind(t_("z", 256 - n, 256, t - 1), t_("pl", 8 * h, 8 * h + 8, t)), AF.Copy)
-            elif t < 2:
+            if t < 2:
                 keep(m_(t, 128 * h, 128 * h + 128, 0), t_("z", 128 * h, 128 * h + 128, t))
             now["of"] = ""
-
-    def step(t):
-        z = t_("z", c=t)
-        n = 1024 + 256 * t
-        cross = t + 2 < STEPS
-        pl = t_("pl", c=t) if t else t_("vl", c=t)
         qg, im1 = t_("qg", c=t), t_("im1", c=t)
-        fl, gt, nw = [lambda h, x=x: t_(x, 128 * h, 128 * h + 128, t) for x in ("fl", "gt", "nw")]
-        now["of"] = "u"
-        if AHEAD[t + 1] and AHEAD[t]:
-            act(t_("blog", n, n + 256), ind(t_("blog", 0, n), pl), AF.Copy)
-        elif AHEAD[t + 1]:
-            cp(t_("blog", n, n + 256), t_("boff", c=t))
-        now["of"] = ""
-        for h in range(2):
-            bs = t_("bs", 128 * h, 128 * h + 128, t)
-            if AHEAD[t] and not AHEAD[t + 1] or NUMBERS[t] == "s":
-                act(bs, ind(t_("blog", 0, n), t_("pl", 8 * h, 8 * h + 8, t)), AF.Identity, bias=float(t + 2048 * h))
-            else:
-                ts(bs, t_("blog", n + 128 * h, n + 128 * h + 128) if AHEAD[t] else t_("boff", 128 * h, 128 * h + 128, t), float(t + 2048 * h), None, OP.add)
+        fl, gt = [lambda h, x=x: t_(x, 128 * h, 128 * h + 128, t) for x in ("fl", "gt")]
+        for h in range(4):
+            ts(t_("bs", 64 * h, 64 * h + 64, t), t_("boff", 64 * h, 64 * h + 64, t), float(t + 1024 * h), None, OP.add)
         act(qg, ind(t_("qlog", 0, n), pl), AF.Copy)
         act(im1, ind(t_("ilog", 0, n), pl), AF.Identity, bias=-1.0)
         ts(t_("fl", c=t), qg, (Q0 + t + 0.5) / 256, None, OP.is_gt)
-        if AHEAD[t]:
-            ts(t_("nw", c=t), qg, (Q0 + t + 6.5) / 256, None, OP.is_gt)
         if t + 1 < STEPS:
             for h in range(4):
                 mm(p_(4, 96 + 8 * h, 104 + 8 * h), fl(h % 2), t_("Gh", 8 * (h // 2), 8 * (h // 2) + 8), True, True)
             act(t_("sk"), p_(4, 96, 128), AF.Relu, bias=0.75e9, scale=-1e9)
-        if OVER[t] == "v":
-            tt(t_("gt", c=t), ind(t_("ilog", 0, n), pl), z, OP.is_lt)
-        else:
-            mm(p_(4, 256, 512), t_("I"), z, True, False)
-            mm(p_(4, 256, 512), t_("nI"), im1, False, True)
-            act(t_("gt", c=t), p_(4, 256, 512), AF.Sign, bias=-1.5)
+        mm(p_(4, 256, 512), t_("I"), z, True, False)
+        mm(p_(4, 256, 512), t_("nI"), im1, False, True)
+        act(t_("gt", c=t), p_(4, 256, 512), AF.Sign, bias=-1.5)
         mm(p_(2, 0, 256), t_("J"), t_("C16"), True, False)
         for h in range(2):
             mm(p_(2, 128 * h, 128 * h + 128), t_("qg", 128 * h, 128 * h + 128, t), t_("I16"), False, h == 1)
         for j in range(7, -1, -1):
             act(ind(t_("ptab"), t_("wl", 2 * j, 2 * j + 2, t)), t_("psrc", 32 * j, 32 * j + 32, t), AF.Sigmoid)
-        if t + 2 < STEPS:
-            tables(t + 2)
+        if cross:
+            stamps(t + 2)
         if t + 1 == STEPS:
             for a, b in quarters:
                 if a < PB:
@@ -535,12 +499,8 @@ def program(g, core, T, topo):
                     keep(t_("ptb", a, b), hosts(a, b))
             to_list(p_(3, 64, 128), "ptb", 0, 1024, "EW")
             cp(t_("plF"), p_(3, 64, 128))
-        if OVER[t] == "v":
-            now["of"] = "c"
-            mm(p_(4, 16, 48), t_("ones"), t_("c8"), True, False)
-            now["of"] = ""
         for h in range(4):
-            mm(p_(4, 16 + 8 * h, 24 + 8 * h), gt(h % 2), t_("GS", 8, 16) if OVER[t] == "v" else t_("GS", 0, 8), OVER[t] == "s", OVER[t] == "s" or h == 3)
+            mm(p_(4, 16 + 8 * h, 24 + 8 * h), gt(h % 2), t_("GS"), True, True)
         if t + 1 < STEPS:
             tt(t_("ac", 0, 32), p_(4, 16, 48), t_("sk"), OP.is_gt)
             mm(p_(4, 48, 82), t_("ones"), t_("ac"), True, True)
@@ -548,168 +508,120 @@ def program(g, core, T, topo):
             host(t + 1)
             now["step"] = t
         scan(t_("qs", c=t), t_("d16"), p_(2, 0, 256), OP.add, OP.max)
-        mm(p_(0, 0, 256), t_("I"), z, True, True)
-        twice = {x: 256 + 64 * k for k, x in enumerate(x for x in MAXIMA if x[1] - x[0] <= 32)}
-        for (a, b), o in twice.items():
-            for e in range(2):
-                mm(p_(0, o + e, o + 2 * (b - a), 2), t_("I"), t_("z", a, b, t), True, True)
+        for e in range(2):
+            mm(p_(0, e, 512, 2), t_("I"), z, True, True)
         top = lambda a, b, k: m_(t, a, b, k) if k % 8 else t_("MX", 2 * a + k // 8, 2 * b, 0, 2)
         now["of"] = "*"
         for a, b in MAXIMA:
-            for k in range(16 if b - a > 32 else 0):
-                tt(top(a, b, k), c_(t, a, b, k, 16), p_(0, a, b), OP.max)
-            for k in range(8 if b - a <= 32 else 0):
-                tt(m_(t, a, b, k, True) if k else t_("MX", 2 * a, 2 * b), c_(t, a, b, k, 8), p_(0, twice[a, b], twice[a, b] + 2 * (b - a)), OP.max)
+            for k in range(8):
+                tt(m_(t, a, b, k, True) if k else t_("MX", 2 * a, 2 * b), c_(t, a, b, k, 8), p_(0, 2 * a, 2 * b), OP.max)
         now["of"] = ""
-        for h in range(2 if AHEAD[t] else 0):
-            tt(t_("m17", 128 * h, 128 * h + 128), m_(t, 128 * h, 128 * h + 128, 0), p_(0, 128 * h, 128 * h + 128), OP.max)
         for h in range(2):
             gk, kb = ("key", t, h), (1, 6)[h]
-            mm(p_(kb, 0, 144), t_("I"), t_("C17"), True, False, gk, "first")
-            mm(p_(kb, 0, 144), fl(h), t_("IB"), False, False, gk, "mid")
-            if AHEAD[t]:
-                mm(p_(kb, 0, 144), nw(h), t_("NB"), False, False, gk, "mid")
-                mm(p_(kb, 17, 144, 18), nw(h), t_("NC"), False, False, gk, "mid")
-                mm(p_(kb, 17, 144, 18), m_(t, 128 * h, 128 * h + 128, 0), t_("G32"), False, False, gk, "mid")
-                mm(p_(kb, 17, 144, 18), t_("m17", 128 * h, 128 * h + 128), t_("G64"), False, False, gk, "mid")
+            mm(p_(kb, 0, 136), t_("I"), t_("C17"), True, False, gk, "first")
+            mm(p_(kb, 0, 136), fl(h), t_("IB"), False, False, gk, "mid")
             for a, b in SUMS:
                 for k in range(16 if a // 128 == h else 0):
-                    mm(p_(kb, 1 + k, 144, 18, (a % 128, b - 128 * h)), c_(t, a, b, k, 16), t_("G32"), False, False, gk, "mid")
+                    mm(p_(kb, 1 + k, 136, 17, (a % 128, b - 128 * h)), c_(t, a, b, k, 16), t_("G32"), False, False, gk, "mid")
             now["of"] = "*%d" % h
-            for k in sorted(range(16), key=lambda k: k % 8 if h else k):
-                mm(p_(kb, 1 + k, 144, 18), top(128 * h, 128 * h + 128, k), t_("G64"), False, k == 15, gk, "last" if k == 15 else "mid")
+            for k in sorted(range(16), key=lambda k: k % 8):
+                mm(p_(kb, 1 + k, 136, 17), top(128 * h, 128 * h + 128, k), t_("G64"), False, k == 15, gk, "last" if k == 15 else "mid")
             now["of"] = ""
-            o = 144 * h
-            scan(t_("s12", o, o + 144), t_("d17"), p_(kb, 0, 144), OP.add, OP.max)
-            scan(t_("s12", 289 + o, 432 + o), p_(kb, 1, 144), t_("s12", o, o + 143), OP.max, OP.min)
-        if AHEAD[t + 1]:
-            gather(t + 1)
-            now["step"] = t
-        KM = lambda a, b: t_("KM", a, b, t)
-        tt(t_("HI"), t_("s12", 17, 576, 0, 18), p_(4, 16, 48), OP.min)
-        ts(t_("HA"), t_("HI"), 1, int(BIG / 2) + 31, OP.arith_shift_right, OP.bitwise_and)
-        KC = lambda a, b: t_("KC", a, b) if AHEAD[t] else KM(a, b)
-        now["of"] = "*c"
-        ts(KC(0, 32), t_("HA"), -BIG / 2, -2040.0, OP.add, OP.max)
-        now["of"] = ""
-        if AHEAD[t]:
-            ts(t_("HB"), t_("HI"), 1, None, OP.bitwise_and)
-            ts(t_("y"), t_("HB"), -2048.0, 16.0, OP.mult, OP.add)
-            now["of"] = "a"
-            tt(KM(0, 32), KC(0, 32), t_("y"), OP.min)
-            now["of"] = ""
+            o = 136 * h
+            scan(t_("s12", o, o + 136), t_("d17"), p_(kb, 0, 136), OP.add, OP.max)
+            scan(t_("s12", 273 + o, 408 + o), p_(kb, 1, 136), t_("s12", o, o + 135), OP.max, OP.min)
+        tt(t_("HI"), t_("s12", 16, 544, 0, 17), p_(4, 16, 48), OP.min)
+        ts(t_("HA"), t_("HI"), int(BIG) + 31, None, OP.bitwise_and)
+        ts(t_("KC"), t_("HA"), -BIG, -2040.0, OP.add, OP.max)
         tt(t_("kx"), t_("HA", 0, 16), t_("HA", 16, 32), OP.max)
         tt(t_("sm"), t_("kx"), t_("qs", 15, 256, t, 16), OP.max)
         ts(t_("sl"), t_("sm"), 15, None, OP.bitwise_and)
-        cp(KM(32, 48), t_("sl"))
-        cp(KM(48, 64), t_("sl"))
-        ts(t_("ca"), KC(0, 16), -16.0, 16.0, OP.mult, OP.add)
+        cp(t_("KM", 0, 16), t_("sl"))
+        cp(t_("KM", 32, 48), t_("sl"))
+        ts(t_("ca"), t_("KC", 0, 16), -16.0, 16.0, OP.mult, OP.add)
         now["of"] = "1"
-        tt(KM(64, 80), t_("ca"), KC(16, 32), OP.subtract)
+        tt(t_("KM", 16, 32), t_("ca"), t_("KC", 16, 32), OP.subtract)
         now["of"] = ""
         ol = lambda k, m=1: t_("ol", 16 * k, 16 * (k + m), t)
-        for f0, f1 in ((0, 2), (2, 5)):
+
+        for f0, f1, codes in ((0, 2, t_("KC")), (2, 5, t_("KM"))):
             now["of"] = "ab"[f0 // 2]
             for x in range(4):
-                if x < YV[f0 // 2]:
-                    ts(y_(t, f0, f1, x, 32, 4), KM(16 * f0, 16 * f1), t_("Gm4", x, x + 1), None, OP.mult, grp=("Y", t))
+                if x < 2:
+                    ts(y_(f0, f1, x, 32, 4), codes, t_("Gm4", x, x + 1), None, OP.mult, grp="Y")
                 else:
-                    act(y_(t, f0, f1, x, 32, 4), KM(16 * f0, 16 * f1), AF.Copy, scale=t_("Gm4", x, x + 1), grp=("Y", t))
+                    act(y_(f0, f1, x, 32, 4), codes, AF.Copy, scale=t_("Gm4", x, x + 1), grp="Y")
             lists = p_(5, 16 + 16 * f0, 16 + 16 * f1)
-            i = mm(lists, t_("I"), t_("ba", 16 * f0, 16 * f1), True, False)
+            mm(lists, t_("I"), t_("ba", 16 * f0, 16 * f1), True, False)
             if not f0:
-                i = mm(lists, t_("I"), t_("bb"), False, False)
+                mm(lists, t_("I"), t_("bb"), False, False)
             for e in range(2):
-                before = i
                 for k in range(8):
-                    a, rows = 112 - 16 * (k % 2), (64 * e, 64 * e + 64)
+                    a = 48 * e + 16 - 16 * (k % 2)
                     out = dict(lists, ap=T.P5[32 * (k // 2):32 * (k // 2) + 32, 2 + 2 * f0:2 + 2 * f1, 4 * e:4 * e + 4])
-                    i = mm(out, t_("RB", a, a + 32, rows=rows), y_(t, f0, f1, 4 * k, 4 * k + 4, 1, rows), False, e == 1 and k % 2 == 1)
-                    edges[i][before] = 1
+                    mm(out, t_("RB", a, a + 32), y_(f0, f1, 4 * k, 4 * k + 4, 1), False, e == 1 and k % 2 == 1)
             cp(ol(f0, f1 - f0), lists)
         now["of"] = ""
-        act(t_("pen", 16, 32), p_(5, 80, 96), AF.Sigmoid, bias=1000.0, scale=-1.0)
+        act(t_("pen"), p_(5, 64, 80), AF.Sigmoid, bias=1000.0, scale=-1.0)
         act(t_("ad"), p_(5, 16, 48), AF.Copy, scale=1.0 / 8192)
-        tt(t_("ybk"), ind(t_("X2", 0, 2049), ol(2)), t_("bs", c=t), OP.min)
-        for h in range(2):
-            act(t_("blog", n + 128 * h, n + 128 * h + 128), t_("ybk", 128 * h, 128 * h + 128), AF.Abs, bias=float(-t - 2048 * h))
-        tt(t_("q1"), ind(t_("T1a", 0, 2048 + 273), ol(4)), qg, OP.min)
-        tt(t_("qlog", n, n + 256), ind(t_("T2", c=t), ol(3)), t_("q1"), OP.max)
+        tt(t_("ybk"), ind(t_("X2", 0, 1025), ol(2)), t_("bs", c=t), OP.min)
+        for h in range(4):
+            act(t_("blog", n + 64 * h, n + 64 * h + 64), t_("ybk", 64 * h, 64 * h + 64), AF.Abs, bias=float(-t - 1024 * h))
+        tt(t_("q1"), ind(t_("T1a", 0, 2048 + 273), ol(3)), qg, OP.min)
+        tt(t_("qlog", n, n + 256), ind(t_("T2", c=t), ol(4)), t_("q1"), OP.max)
         win = dict(t_("W", c=t), rg=c_(t, 0, 128)["rg"] + c_(t, 128, 256)["rg"] + [("M%d.%d" % (t % 2, r), 0, 256) for r in range(16)])
-        if SECOND[t] == "v":
-            for k in range(2):
-                d = t_("d12", 256 * k, 256 * k + 256)
-                tt(d, ind(win, ol(k)), z, OP.subtract)
-                act(t_("SG", 256 * k, 256 * k + 256), d, AF.Sigmoid, bias=-math.log(31.0), scale=-40.0)
-                mm(p_(7, 0, 256), t_(("I", "nI")[k]), d, k == 0, k == 1)
-            act(t_("SG", 512, 768), p_(7, 0, 256), AF.Sigmoid, bias=-math.log(31.0), scale=40.0)
-        else:
-            d = t_("d12", 0, 256)
-            now["of"] = "z"
-            for k in range(2):
-                mm(p_(7, 256 * k, 256 * k + 256), t_("I"), z, k == 0, False)
-            now["of"] = ""
-            tt(d, ind(win, ol(0)), z, OP.subtract)
-            act(t_("a2"), ind(win, ol(1)), AF.Copy)
-            act(t_("SG", 0, 256), d, AF.Sigmoid, bias=-math.log(31.0), scale=-40.0)
-            mm(p_(7, 256, 512), t_("I"), d, False, False)
-            for k in range(2):
-                mm(p_(7, 256 * k, 256 * k + 256), t_("nI"), t_("a2"), False, k == 1)
-            act(t_("SG", 256, 768), p_(7, 0, 512), AF.Sigmoid, bias=-math.log(31.0), scale=40.0)
-            if cross:
-                act(t_("d12", 256, 512), p_(7, 0, 256), AF.Copy, scale=-1.0)
-        cnt = p_(CB, 128, 176)
-        mm(p_(CB, 128, 160), t_("I9"), t_("pen"), True, False)
-        mm(p_(CB, 160, 176), t_("I9"), t_("pen", 16, 32), False, False)
-        to_list(cnt, "SG", 0, 768, first=False)
+        d = t_("d12", 0, 256)
+        now["of"] = "z"
+        for k in range(2):
+            mm(p_(7, 256 * k, 256 * k + 256), t_("I"), z, k == 0, False)
+        now["of"] = ""
+        tt(d, ind(win, ol(0)), z, OP.subtract)
+        act(t_("a2"), ind(win, ol(1)), AF.Copy)
+        act(t_("SG", 0, 256), d, AF.Sigmoid, bias=-math.log(31.0), scale=-40.0)
+        mm(p_(7, 256, 512), t_("I"), d, False, False)
+        for k in range(2):
+            mm(p_(7, 256 * k, 256 * k + 256), t_("nI"), t_("a2"), False, k == 1)
+        act(t_("SG", 256, 768), p_(7, 0, 512), AF.Sigmoid, bias=-math.log(31.0), scale=40.0)
+        if cross:
+            act(t_("d12", 256, 512), p_(7, 0, 256), AF.Copy, scale=-1.0)
+        cnt = p_(4, 128, 176)
+        to_list(cnt, "SG", 0, 768, stop=False)
+        for k in range(2):
+            mm(p_(4, 144 + 16 * k, 160 + 16 * k), t_("I9"), t_("pen"), False, k == 1)
         ts(t_("ti"), cnt, 1056.0, None, OP.mult)
         ts(th_(3, 6), cnt, 8.75, None, OP.is_gt)
         ts(t_("mk"), t_("ti"), 768, None, OP.bitwise_and)
         ts(th_(0, 3), t_("mk"), 0.0, None, OP.is_equal)
-        if RANKS[t] == "p":
-            D = lambda a, b: p_(2, 304 + 16 * a, 304 + 16 * b)
-            code = lambda a, b: p_(5, 320 + 16 * a, 320 + 16 * b)
-            now["of"] = "*g"
-            mm(D(0, 3), t_("I"), th_(3, 6), True, False)
-            mm(D(2, 3), t_("I"), th_(4, 5), False, False)
-            now["of"] = "*l"
-            mm(D(0, 2), t_("I"), th_(2, 6, 3), False, False)
-            mm(D(0, 3), t_("nI"), th_(0, 3), False, False)
-            mm(D(0, 1), t_("nI"), th_(1, 2), False, False)
-            mm(D(1, 3), t_("nI"), th_(0, 4, 3), False, True)
-            now["of"] = "*u"
-            for k in range(2 if cross else 0):
-                mm(code(k, k + 1), t_("I"), t_("vh", 16, 32, t), k == 0, False)
-            now["of"] = ""
-            ts(t_("C"), D(0, 3), -0.5, 0.5, OP.is_gt, OP.subtract)
+        D = lambda a, b: p_(2, 304 + 16 * a, 304 + 16 * b)
+        code = lambda a, b: p_(5, 320 + 16 * a, 320 + 16 * b)
+        now["of"] = "*g"
+        mm(D(0, 3), t_("I"), th_(3, 6), True, False)
+        mm(D(2, 3), t_("I"), th_(4, 5), False, False)
+        now["of"] = "*l"
+        mm(D(0, 2), t_("I"), th_(2, 6, 3), False, False)
+        mm(D(0, 3), t_("nI"), th_(0, 3), False, False)
+        mm(D(0, 1), t_("nI"), th_(1, 2), False, False)
+        mm(D(1, 3), t_("nI"), th_(0, 4, 3), False, True)
+        now["of"] = "*u"
+        for k in range(2 if cross else 0):
+            mm(code(k, k + 1), t_("I"), t_("vh", 16, 32, t), k == 0, False)
+        now["of"] = ""
+        ts(t_("C"), D(0, 3), -0.5, 0.5, OP.is_gt, OP.subtract)
 
-            def ranks(o, first):
-                mm(code(o, o + 2), t_("I"), t_("C", 0, 32), first, False)
-                mm(code(o + 1, o + 2), t_("I"), t_("C", 32, 48), False, False)
-                mm(code(o, o + 1), t_("nI"), t_("C", 32, 48), False, True)
-            now["of"] = "*c"
-            if cross:
-                ranks(0, False)
-            now["of"] = "*k"
-            ranks(2, True)
+        def ranks(name, o, first):
+            now["of"] = name
+            mm(code(o, o + 2), t_("I"), t_("C", 0, 32), first, False)
+            mm(code(o + 1, o + 2), t_("I"), t_("C", 32, 48), False, False)
+            mm(code(o, o + 1), t_("nI"), t_("C", 32, 48), False, True)
             now["of"] = ""
-            if cross:
-                cp(t_("cl", c=t), code(0, 2))
-            less1 = code(2, 4)
-        else:
-            tt(t_("nb"), th_(0, 6, 2), th_(1, 6, 2), OP.add)
-            tt(t_("C", 0, 32), t_("nb", 0, 32), t_("nb", 16, 48), OP.is_le)
-            tt(t_("C", 32, 48), t_("nb", 32, 48), t_("nb", 0, 16), OP.is_lt)
-            tt(t_("R"), t_("C", 0, 32), t_("C", 16, 48), OP.subtract)
-            less1 = t_("R")
-            if cross:
-                for k in range(2):
-                    tt(t_("X", 16 * k, 16 * k + 16), t_("R", 16 * k, 16 * k + 16), t_("vh", 16, 32, t), OP.add)
-                cp(t_("cl", c=t), t_("X"))
         if cross:
+            ranks("*c", 0, False)
+        ranks("*k", 2, True)
+        if cross:
+            cp(t_("cl", c=t), code(0, 2))
             tt(t_("cx", c=t), ind(t_("T3"), t_("cl", c=t)), t_("d12"), OP.mult)
             send([z, t_("cx", 0, 256, t), t_("cx", 256, 512, t)], t + 2, (rank + 2) % n_ranks)
-        tt(t_("K"), t_("ad"), less1, OP.add)
+        tt(t_("K"), t_("ad"), code(2, 4), OP.add)
         tt(t_("mna"), t_("lnq"), t_("K", 0, 16), OP.min)
         tt(t_("mnb"), t_("mna"), t_("K", 16, 32), OP.min)
         ts(t_("fl1", c=t), t_("mnb"), 8192.0, 8192.0, OP.mult, OP.add)
@@ -717,9 +629,6 @@ def program(g, core, T, topo):
 
     host(0)
     for t in range(STEPS):
-        if not AHEAD[t]:
-            gather(t)
-        now["step"] = t
         step(t)
     now["step"] = STEPS
     for k, (a, b) in enumerate(quarters):

import math
from concourse.mybir import dt, AluOpType, AxisListType, ActivationFunctionType
from concourse.bass import DstId, RemoteDMATransfer

OP = AluOpType
AF = ActivationFunctionType
BIG = 131072.0
Q0 = 192.0
STEPS = 6
LOG = 1024 + 256 * STEPS
TILES = {
    "z": (256, "bfloat16", 7), "bk": (1024, "int32", 1), "wti": (1, "int32", 1),
    "T1a": (272, "bfloat16", 1), "T3": (1040, "bfloat16", 1), "Bt": (256, "bfloat16", 1), "RB": (96, "bfloat16", 1), "ba": (80, "bfloat16", 1),
    "bb": (32, "bfloat16", 1), "nI": (128, "bfloat16", 1), "I": (128, "bfloat16", 1), "Gh": (16, "bfloat16", 1), "T1b": (288, "bfloat16", 1),
    "c05": (16, "bfloat16", 1), "KC": (32, "bfloat16", 1),
    "geno_s": (4096, "bfloat16", 1), "W": (8192, "bfloat16", 2), "MX": (512, "bfloat16", 1),
    "blog": (LOG, "float32", 1), "qlog": (LOG, "bfloat16", 1), "ilog": (LOG, "bfloat16", 1), "ptab": (1056, "float32", 1), "psrc": (256, "float32", 6),
    "ptb": (1024, "bfloat16", 1), "q4": (1024, "float32", 1), "yb": (1024, "float32", 1), "yi": (1024, "bfloat16", 1), "plF": (64, "uint16", 1),
    "pI": (1, "int32", 1), "pM": (1, "int32", 1), "pG": (1, "int32", 1), "p8": (1, "int32", 1), "col": (1, "float32", 16),
    "ic": (256, "float32", 1), "lnO": (16, "float32", 1), "lnq": (16, "float32", 1), "hb": (16, "float32", 2),
    "I16": (128, "bfloat16", 1), "I16p": (128, "bfloat16", 1), "I9": (128, "bfloat16", 1), "Iq": (128, "bfloat16", 1), "J": (128, "bfloat16", 1),
    "ones": (128, "bfloat16", 1), "IB": (136, "bfloat16", 1), "XG": (128, "bfloat16", 1), "XF": (128, "bfloat16", 1),
    "LR": (1920, "bfloat16", 1), "FS": (2048, "bfloat16", 1), "X2": (1040, "bfloat16", 1), "T2": (32, "bfloat16", 6),
    "Gmf": (8, "float32", 1), "Gm4": (4, "float32", 1), "GS": (8, "bfloat16", 1), "G64": (8, "bfloat16", 1), "G32": (8, "bfloat16", 1),
    "EB": (144, "bfloat16", 1), "EW": (144, "bfloat16", 1), "wE": (144, "float16", 1), "eq": (16, "float32", 1), "ne": (16, "float32", 1),
    "C16": (256, "bfloat16", 1), "d16": (256, "bfloat16", 1), "C17": (136, "bfloat16", 1), "d17": (136, "bfloat16", 1),
    "cq": (256, "bfloat16", 1), "T1s": (560, "bfloat16", 1), "E16": (128, "bfloat16", 1), "b0": (256, "int32", 1),
    "pw": (8, "float32", 1), "p8e": (8, "float32", 2), "p8f": (1, "float32", 1), "xi": (256, "int32", 1), "xj": (256, "int32", 1),
    "ui": (16, "float32", 2), "UV": (32, "int32", 2), "s": (16, "float32", 2), "sq": (16, "float32", 2), "VV": (32, "int32", 2), "vl": (16, "uint16", 3),
    "vh": (32, "float16", 2), "G": (256, "bfloat16", 1), "pl": (16, "uint16", 2), "wl": (16, "uint16", 2), "E": (384, "bfloat16", 1),
    "boff": (256, "uint16", 2), "bs": (256, "float32", 2), "qg": (256, "bfloat16", 2), "im1": (256, "bfloat16", 2), "fl": (256, "bfloat16", 2), "gt": (256, "bfloat16", 2),
    "qs": (256, "float32", 2), "sk": (32, "float32", 1), "ac": (34, "bfloat16", 1), "A": (1, "float32", 2), "s12": (576, "float32", 1),
    "HI": (32, "int32", 1), "HA": (32, "int32", 1), "KM": (48, "bfloat16", 1), "ca": (16, "float32", 1), "kx": (16, "float32", 1), "sm": (16, "int32", 1), "sl": (16, "int32", 1),
    "ol": (80, "uint16", 2), "pen": (16, "bfloat16", 1), "ybk": (256, "float32", 1), "q1": (256, "bfloat16", 1),
    "d12": (512, "bfloat16", 1), "a2": (256, "bfloat16", 1), "SG": (768, "bfloat16", 1), "ti": (48, "int32", 1), "mk": (48, "int32", 1),
    "C": (48, "bfloat16", 1), "ad": (32, "float32", 1), "K": (32, "float32", 1),
    "mna": (16, "float32", 1), "mnb": (16, "float32", 1), "fl1": (16, "uint16", 2), "cl": (32, "uint16", 2), "cx": (512, "bfloat16", 4),
}
BYTES = {"float32": 4, "int32": 4, "bfloat16": 2, "uint16": 2, "float16": 2}
PLACE = {}
_size = {d: 0 for d in BYTES}
for _n, (_w, _d, _c) in TILES.items():
    _p = (_w + 15) // 16 * 16
    PLACE[_n] = (_size[_d], _p)
    _size[_d] += _p * _c
BUF = {"float32": "bigf", "int32": "bigi", "bfloat16": "bigb", "uint16": "bigu", "float16": "bigh"}
SCRATCH = {BUF[_d]: ("sbuf", [128, _size[_d]], _d) for _d in BYTES}
for _k in range(8):
    SCRATCH["P%d" % _k] = ("psum", [128, 64, 8] if _k == 5 else [128, 512], "float32")
SCRATCH["Yc"] = ("sbuf", [128, 10, 32], "bfloat16")
SCRATCH["TH"] = ("sbuf", [128, 6, 16], "bfloat16")
LOADS = ["bites", "wt", "bank", "immun", "geno"]
OUTS = [("yb", 0, 512, "y"), ("yb", 512, 1024, "y"), ("yi", 0, 512, "y"), ("yi", 512, 1024, "s")]
STORES = ["sg"] + ["so%d" % k for k in range(len(OUTS))]
SEMAPHORES = (["qv", "qs", "qp", "qg", "rl"] + ["arr%d" % t for t in range(1, STEPS)] + ["ld_" + n for n in LOADS] + ["st_" + n for n in STORES]
              + ["cp%d" % k for k in range(18)])

SHARE = (48, 14, 14, 14, 14, 44)
PARTS = [[("s", 0, 32), ("s", 32, 128 - v), ("s", 128, 192), ("s", 192, 224), ("s", 224, 256), ("v", 128 - v, 128)] for v in SHARE]
OFFS = [(0, 64), (64, 256)]
MAXIMA = [(0, 32), (32, 64), (64, 128), (128, 192), (192, 224), (224, 256)]
SUMS = [(0, 128), (128, 224), (224, 256)]
YI = "svvs"
PB = 512
CYCLE, GATHER, SCATTER, WAKE, OWN, LANDS = 0.83e-3, 1.56, 3.8, 0.19, 0.19, 4.0

FIRST = {
    'v': '_J _pw _cq _ac _pw _col0 _pM _pG _col2 _p8 _EB _ac _col7 _col1 _col3 _pw _c05 _ne _col4 _pw _p8e _col5 _Gmf _col9 _p8f _col11 _p8e _col6 _EB _c05 _col10 _P3 _wE _eq _IB _xi _Gm4 _RB _col13 _col8 _xj _T2 ui _Bt _lnO s _qlog:2 UV UVu _hb _LR:5 _col12 _col13 _LR:10 VV _qlog vl _qlog vh b0:2 boff _col15 _C16 _p8e boff fl _blog _hb _blog W E *:2 _p8e *:8 _blog *:24 _col14 *:2 wl _blog *:8 bs *:4 s12 qs s12:2 _EW s12 bs:2',
    's': '_wti _ones _Gh _X2:8 _FS:12 sq _GS _ba _G64 _X2:8 _Gh _ptab _RB _G32 _FS:4 _Iq _I16 _lnq _RB _nI _I16p _ba qg W:4 im1 W _ba _psrc _ba:2 ptab gt ptab _T1a _ba _T2 ptab sk _T1b ptab _I9 ptab _lnq',
    'p': 'P3J _P5J _P7J P3wE:16 P6I _P5Iq P3LR:15 _P7Iq P1I *f:8 P6fl *f:24 P3I P2J P4fl:4 P0I:2 _P5J P4I _P5Iq *e:32 P1fl P1W:8 *e:8 P2qg:2 _P7J *0:4 P1W:8 *0:4 *e:6 _P5E16 _P7Iq P4nI *0:4 P6W:32 *0:4 *1:4 P3J+ *1:12 _P7E16 P4gt:4 P5Ia:2',
    'g': '_pI _ic _XG:2 _lnO _XF _bb _XG _I _XG _C16 _d17 _C17 _E16 _C17 _X2 _send _T1s _d16 _T1s:2 _X2 _d16 _d17 M _ba _T1s Mx:2 M _T3',
}
ORDER = {
    'v': 'HI bs ac HA ui+ KC kx s+ A Yca sm Yca ca sl UV+ UVu+ KM1 KM:2 VV+ ola Ycb:2 vl+ d12 olb G+ ybk q1 pl+ vh+ boff+:2 ti TH mk TH qlog *+:2 C *+:4 W+ K cl *+:2 mna cx E+ *+:4 mnb fl+ *+:8 fl1 *+:4 ilog *+:4 wl+ *+:20 s12+ qs+ s12+:2 bs+ s12+ bs+:2',
    's': 'Yca:2 sq+ ptab:2 Ycb:2 ptab a2 T3 SG T3 SG blog:4 pen d12 T2 ad W+:2 qg+ W+:3 im1+ ptab+:2 sk+ gt+ ptab+:3',
    'p': 'P3wE+:16 P4ones P0I+:2 P1I+ P5RBa:16 P5Ib P7Iz:2 P5RBb:16 P7I P7nI:2 P2EW+:16 *u:2 P4EB:16 P4I9:2 P3LR+:15 *g:2 *f+:8 *l:4 *c:3 *k:3 P2J+ *f+:24 P3I+ P6I+ P1W+:16 *e+:32 *0+:4 P4fl+:4 *0+:4 P4I+ *e+:14 P3J++ *0+:4 P6W+:16 P1fl+ *0+:4 P6W+:8 P6fl+ P5Ia+:2 P2qg+:2 P6W+:8 P4nI+ *1+:16 P4gt+:4',
    'g': 'M+ geno_s send geno_s+ Mx+ M++ Mx+ M+ M++',
}
FINAL = {
    'v': 'HI ac HA ui+ kx KC s+ sm Yca:2 A sl ca UV+ KM:2 KM1 VV+ ola Ycb:2 vl+ vh+ bs G+ olb d12 ybk pl+ q1 boff+:2 qlog W+ *+:2 ti *+:2 fl+ bs+ TH E+ mk *+:6 TH *+:8 C *+:6 K *+:2 mna *+:2 wl+ mnb *+:2 fl1 *+:2 ilog *+:14 s12+ *+:2 s12+ qs+ s12+:2 HI+ bs+ HA+ kx+ KC+ bs+ sm+ Yca+:2 ca+ sl+ KM1+ KM+:2 ola+ Ycb+:2 d12+ olb+ bs+ ybk+ q1+ qlog+ ti+ TH+ mk+ plF+ TH+ C+ ^yb K+ ^yb mna+ ^yb mnb+ ^yb fl1+ ilog+ ^yi:2',
    's': 'ptab Yca:2 sq+ ptab:2 Ycb:2 a2 SG ad pen blog:4 SG W+ qg+ W+:4 ptab+ im1+ ptab+:2 gt+ ptab+:3 Yca+:2 ptab+:2 Ycb+:2 a2+ SG+ ptb+ pen+ SG+ blog+ ptb+ blog+:2 ad+ blog+ ^q4:4 ^yi:2 ^ou',
    'p': 'P3wE+:16 P4ones P5RBa:16 P5Ib P7Iz:2 P5RBb:16 P0I+:2 P2EW+:16 P7I P7nI:2 P3LR+:15 *f+:8 P4EB:16 P4I9:2 *f+:24 P3I+ *g:2 P1I+ P6I+ P7Iz+:2 *e+:8 *l:4 *e+:16 P6fl+ *k:3 *e+:8 *0+:4 *e+:14 P1W+:8 *0+:4 P4I+ P1fl+ *0+:4 P6W+:8 P1W+:8 P2J+ P2qg+:2 *0+:4 P6W+:24 *1+:12 P4nI+ *1+:4 P4gt+:4 P5Ia+:2 P5RBa+:16 P5Ib+ P5RBb+:16 P7I+ P7nI+:2 P4EB+:16 P4I9+:2 P3EW+:16 *g+:2 *l+:4 *k+:3',
    'g': 'geno_s+ ptb+:2',
}


def program(g, core, T, topo):
    rank = T.rank_of(core)
    n_ranks = len(T.cores)
    ops = []
    last = {}
    edges = []

    def t_(name, a=0, b=None, c=0, step=1, rows=(0, 128)):
        w, d, copies = TILES[name]
        if b is None:
            b = w
        off, p = PLACE[name]
        off += p * (c + (c > 0) if name == "z" else c % copies)
        ap = T[BUF[d]][slice(*rows), off + a:off + b:step] if step != 1 else T[BUF[d]][slice(*rows), off + a:off + b]
        return {"ap": ap, "rg": [(BUF[d], off + a, off + b)], "n": (b - a + step - 1) // step, "w": BYTES[d], "ind": False}

    def p_(k, a, b, step=1, rows=(0, 128)):
        ap = T.P5[:, a // 8:b // 8, :] if k == 5 else T["P%d" % k][rows[0]:rows[1], a:b:step] if step != 1 else T["P%d" % k][rows[0]:rows[1], a:b]
        return {"ap": ap, "rg": [("P%d" % k, a, b)], "n": (b - a + step - 1) // step, "w": 8, "ind": False}

    def y_(f0, f1, a, b, step, rows=(0, 128)):
        return {"ap": T.Yc[rows[0]:rows[1], 2 * f0:2 * f1, a:b:step], "rg": [("Yc", f0, f1)], "n": 2 * (f1 - f0) * ((b - a + step - 1) // step), "w": 2, "ind": False}

    def th_(a, b, step=1):
        return {"ap": T.TH[:, a:b:step, :], "rg": [("TH", x, x + 1) for x in range(a, b, step)], "n": 16 * len(range(a, b, step)), "w": 2, "ind": False}

    def c_(t, a, b, k=0, step=1):
        o = 2048 * (a // 128)
        return t_("W", o + 16 * a + k, o + 16 * b, t, step)

    def m_(t, a, b, k, two=False):
        o = 2048 * (a // 128 + 1)
        return dict(t_("W", o + 16 * a + k, o + 16 * b, t, 8 if two else 16), rg=[("M%d.%d" % (t % 2, r), a, b) for r in ((k, k + 8) if two else (k,))])

    def ind(win, off):
        return {"ap": win["ap"].indirect(off["ap"]), "rg": win["rg"] + off["rg"], "win": win["rg"], "off": off["rg"], "n": 16 * off["n"], "w": 4, "ind": True}

    starts = {BUF[d]: sorted((PLACE[x][0], x) for x in TILES if TILES[x][1] == d) for d in BUF}
    now = {"step": -1, "of": "", "last": {}}

    def name_of(region):
        if region[0] not in starts:
            return "M" if region[0][0] == "M" else region[0][:2]
        o, x = [(o, x) for o, x in starts[region[0]] if o <= region[1]][-1]
        return x + "%d" % ((region[1] - o) // 16) if x == "col" else x

    def add(q, emit, R, W, sem, inc, busy, grp=None, role=None, after=0.0):
        i = len(ops)
        ed = {}
        banks = set()
        for (buf, a, b), wr in [(r, False) for r in R] + [(r, True) for r in W]:
            if buf[0] == "P":
                banks.add(buf)
                if q == "p":
                    row = last.setdefault("row" + buf, [])
                    for j, grp2, role2 in row:
                        if not (grp is not None and grp == grp2 and role == "mid" and role2 == "mid"):
                            ed.setdefault(j, 0)
                    if role != "mid":
                        row[:] = []
                    row.append((i, grp, role))
            lst = last.setdefault(buf, [])
            for (a2, b2, j, wr2, grp2) in lst:
                if a2 < b and a < b2 and j != i and (wr or wr2) and not (wr and wr2 and grp is not None and grp == grp2):
                    ed[j] = max(ed.get(j, 0), 0 if q == ops[j]["q"] == "p" else 1)
            if wr:
                lst[:] = [x for x in lst if not (x[0] >= a and x[1] <= b and x[2] != i and not (grp is not None and x[4] == grp))]
            lst.append((a, b, i, wr, grp))
        name = q + (name_of(W[0]) if W else "send")
        if name[1:2] == "P" and R:
            name += name_of(R[0])
        name = q + now["of"] if now["of"][:1] == "*" else name + now["of"]
        if now["last"].get(name, (0, None))[1] == now["step"] and q != "y":
            ed.setdefault(now["last"][name][0], 0)
        now["last"][name] = (i, now["step"])
        ops.append({"q": q, "emit": emit, "sem": sem, "inc": inc, "busy": busy, "after": after, "banks": banks, "name": name, "step": now["step"]})
        edges.append(ed)
        return i

    def rgs(*xs):
        out = []
        for x in xs:
            if isinstance(x, dict):
                out += x["rg"]
        return out

    def raw(x):
        return x["ap"] if isinstance(x, dict) else x

    def took(out, a, cycles, start=0.05):
        if out["ind"] or a["ind"]:
            return start + out["n"] * (SCATTER if out["ind"] else GATHER) * CYCLE
        return max(64, a["n"] * cycles) * CYCLE

    def narrow(*xs):
        return 0.5 if all(x["w"] == 2 for x in xs) else 1

    def tt(out, a, b, op):
        return add("v", lambda: g.vector.tensor_tensor(raw(out), raw(a), raw(b), op), rgs(a, b), out["rg"], "qv", 1, took(out, a, 1 if 8 in (a["w"], b["w"]) else 2))

    def ts(out, a, s1, s2, o1, o2=None, grp=None):
        f = (lambda: g.vector.tensor_scalar(raw(out), raw(a), raw(s1), raw(s2), o1)) if o2 is None else (lambda: g.vector.tensor_scalar(raw(out), raw(a), raw(s1), raw(s2), o1, o2))
        return add("v", f, rgs(a, s1, s2), out["rg"], "qv", 1, took(out, a, narrow(out, a)), grp=grp)

    def cp(out, a):
        return add("v", lambda: g.vector.tensor_copy(raw(out), raw(a)), rgs(a), out["rg"], "qv", 1, took(out, a, narrow(out, a)))

    def ms(out, val):
        return add("v", lambda: g.vector.memset(raw(out), val), [], out["rg"], "qv", 1, took(out, out, narrow(out)))

    def red(out, a):
        return add("v", lambda: g.vector.tensor_reduce(raw(out), raw(a), AxisListType.X, OP.add), rgs(a), out["rg"], "qv", 1, took(out, a, 1))

    def scan(out, a, b, o0, o1):
        return add("v", lambda: g.vector.tensor_tensor_scan(raw(out), raw(a), raw(b), 0.0, o0, o1), rgs(a, b), out["rg"], "qv", 1, took(out, a, 1))

    def act(out, a, fn, bias=0.0, scale=1.0, grp=None):
        if out["ind"]:
            return add("s", lambda: g.scalar.activation(raw(out), raw(a), fn), rgs(a) + out["off"], out["win"], "qs", 1, took(out, a, 1, 0.065))
        if isinstance(bias, float) and bias == 0.0:
            f = (lambda: g.scalar.activation(raw(out), raw(a), fn, scale=raw(scale))) if scale != 1.0 else (lambda: g.scalar.activation(raw(out), raw(a), fn))
        else:
            f = lambda: g.scalar.activation(raw(out), raw(a), fn, bias=raw(bias), scale=raw(scale))
        return add("s", f, rgs(a, bias, scale), out["rg"], "qs", 1, took(out, a, 1, 0.065), grp=grp)

    def mm(out, lhsT, rhs, start, stop, grp=None, role=None):
        return add("p", lambda: g.tensor.matmul(raw(out), raw(lhsT), raw(rhs), start, stop), rgs(lhsT, rhs), out["rg"], "qp", 1,
                   max(min(64, lhsT["n"]), rhs["n"]) * CYCLE / 2, grp=grp, role=role)

    def iota(out, pattern, base=0, cm=0, whole=False):
        def f():
            if whole:
                return g.iota(raw(out), pattern, base, cm)
            return g.iota(raw(out), pattern, base, cm, allow_small_or_imprecise_dtypes=True)
        return add("g", f, [], out["rg"], "qg", 1, 0.13 + 2 * out["n"] * CYCLE)

    def fill(out, val):
        return iota(out, [[0, out["n"]]], val)

    def select(out, a, pattern, op, other, base, cm):
        return add("g", lambda: g.affine_select(raw(out), raw(a), pattern, op, other, base, cm), rgs(a), out["rg"], "qg", 1, 0.17 + 2 * out["n"] * CYCLE)

    def keep(out, a):
        return select(out, a, [[0, out["n"]]], OP.is_ge, 0.0, 0, 0)

    def load(name, out, after, q="y"):
        eng = g.sync if q == "y" else g.scalar
        return add(q, lambda: eng.dma_start(raw(out), T[name][:]), [], out["rg"], "ld_" + name, 16, 0.1, after=after)

    copies = []

    def copy(out, src, grp=None):
        copies.append(add("y", lambda: g.sync.dma_start(raw(out), raw(src)), src["rg"] + t_("ilog", 0, 16)["rg"], out["rg"], "cp%d" % len(copies), 16, 0.1, grp, after=1.5))

    def store(tag, dst, src, q="y"):
        eng = g.sync if q == "y" else g.scalar
        return add(q, lambda: eng.dma_start(dst, raw(src)), src["rg"], [("out" + tag, 0, 1)], "st_" + tag, 16, 0.1, after=1.0 + src["n"] * src["w"] / 2400)

    load("wt", t_("wti"), 1.0, "s")
    for name, dst, after in (("bites", t_("z", 0, 512), 1.5), ("bank", t_("bk"), 3.3), ("geno", t_("geno_s"), 6.6), ("immun", t_("ilog", 0, 1024), 7.4)):
        load(name, dst, after)

    def send(srcs, t, dst_rank):
        dst = T.cores[dst_rank]
        rid, pid, _se = topo.addr(dst)
        m = topo.mask(core, dst)
        eng = len(topo.engines(core, dst))
        out = t_("z", c=t)
        sem = T.sem["arr%d" % t]
        def f():
            if len(srcs) == 1:
                return g.remote_dma(raw(out), raw(srcs[0]), sem, T.sem.rl, pid, rid, m)
            tr = RemoteDMATransfer(dst_ids=[DstId(rid=rid, pnc=pid)], dma_engine_mask=m, remote_sem=sem, srcs=[raw(x) for x in srcs], dsts=[raw(out)], alu_op=1)
            return g.remote_dma_fused([tr], local_sem=T.sem.rl)
        i = add("g", f, rgs(*srcs), [], None, 0, 2.3 if t == 1 else 0.3)
        ops[i]["remote"] = eng
        j = add("n", None, [], out["rg"], "arr%d" % t, eng, 0.0, after=LANDS)
        edges[j][i] = 0

    P, PM, PG, P8, WF, WG, WS, CI, PK, PK0, PW, L1, L2, H1, W1, CS = [t_("col", c=k) for k in range(16)]
    ic = lambda n: t_("ic", 0, n)
    iota(t_("pI"), [[0, 1]], 0, 1, True)
    iota(t_("ic"), [[1, 256]])
    ms(t_("J"), 1.0 / 64)
    ms(t_("c05", rows=(0, 64)), -2048.0)
    ms(t_("c05", rows=(64, 128)), 0.5)
    act(t_("ones"), t_("J"), AF.Sigmoid, scale=6400.0)
    ops[-1]["busy"] += 1.3
    send([t_("z", 256, 512)], 1, (rank + 1) % n_ranks)
    iota(t_("C16"), [[0, 16], [-1, 16]], 16)
    ms(t_("C16", rows=(64, 128)), 16 * Q0 + BIG)
    ms(t_("cq"), 2048 * Q0)
    iota(t_("C17"), [[0, 8], [-1, 17]], 17)
    iota(t_("lnO"), [[16, 16]])
    ts(t_("pM"), t_("pI"), 15, None, OP.bitwise_and)
    ts(t_("pG"), t_("pI"), 4, None, OP.arith_shift_right)
    ts(t_("p8"), t_("pI"), 7, None, OP.bitwise_and)
    ts(P, t_("pI"), 1.0, None, OP.add)
    cp(PM, t_("pM"))
    cp(PG, t_("pG"))
    ts(P8, t_("p8"), -1.0, 7.0, OP.mult, OP.add)
    cp(t_("p8f"), t_("p8"))
    ts(t_("Gmf"), ic(8), PG, None, OP.is_equal)
    ms(t_("EB"), 0.0)
    cp(t_("EB", 15, 128, step=16), t_("Gmf"))
    cp(WF, t_("wti"))
    ts(WG, WF, 2047.5, -4096.0, OP.is_gt, OP.mult)
    tt(WS, WF, WG, OP.add)
    ts(t_("wE"), t_("EB"), WS, None, OP.mult)
    select(t_("I"), t_("ones"), [[-1, 128]], OP.is_equal, 0.0, 0, 1)
    quarters = [(a, a + 256) for a in range(0, 1024, 256)]
    act(t_("Iq"), t_("I"), AF.Copy, scale=-4096.0 * 256)
    for a, b in quarters:
        ts(t_("qlog", a, b), t_("bk", a, b), 1.0 / 4096 / 256, (Q0 - 0.5 + 1.0 / 8192) / 256, OP.mult, OP.add)
    for k, (a, b) in enumerate(quarters):
        bank = p_((5, 7)[k % 2], 256, 512)
        mm(bank, t_("J"), t_("cq"), True, False)
        mm(bank, t_("Iq"), t_("qlog", a, b), False, True)
        tt(t_("blog", a, b), t_("bk", a, b), bank, OP.add)
    for name, a, f in (("GS", 0, BIG), ("G64", 0, 64.0), ("G32", 0, -32.0), ("Gh", 0, 1.0), ("Gh", 8, 0.5)):
        act(t_(name, a, a + 8), t_("Gmf"), AF.Copy, scale=f)
    for name, f in (("nI", -1.0), ("I16", -4096.0), ("I16p", 4096.0), ("I9", 9.0)):
        act(t_(name), t_("I"), AF.Copy, scale=f)
    tt(CI, PG, P, OP.add)
    ts(t_("IB"), ic(136), CI, BIG, OP.is_equal, OP.mult)
    fill(t_("C17", 0, 136, step=17), 0)
    fill(t_("d16"), 0)
    fill(t_("d16", 0, 256, step=16), -4096)
    fill(t_("d17"), 0)
    fill(t_("d17", 0, 136, step=17), int(-8 * BIG))
    ms(t_("ac", 32, 33), 304.0 / 128)
    ms(t_("ac", 33, 34), 7.59375 / 128)
    ts(t_("eq"), ic(16), PM, None, OP.is_equal)
    ts(t_("ne"), ic(16), PM, 16384.0, OP.not_equal, OP.mult)
    tt(t_("Gm4"), t_("Gmf", 0, 4), t_("Gmf", 4, 8), OP.add)
    ms(t_("RB"), 0.0)
    for e in range(2):
        act(t_("RB", 16 + 48 * e, 32 + 48 * e, rows=(64 * e, 64 * e + 64)), t_("eq", rows=(64 * e, 64 * e + 64)), AF.Copy, scale=-1.0)
    fill(t_("XG"), 1)
    select(t_("XG"), t_("XG"), [[-16, 8], [0, 16]], OP.is_ge, 0.0, 0, 1)
    select(t_("XF"), t_("XG"), [[16, 8], [0, 16]], OP.is_ge, 0.0, 15, -1)
    select(t_("XG"), t_("XG"), [[1, 128]], OP.is_gt, 0.0, 0, -1)
    select(t_("XG"), t_("XG"), [[-1, 128]], OP.not_equal, -1.0, 0, 1)
    for m in range(16):
        act(t_("FS", 128 * m, 128 * m + 128), t_("XF"), AF.Copy, scale=t_("eq", m, m + 1))
    for m in range(15):
        ts(t_("LR", 128 * m, 128 * m + 128), t_("XG"), t_("eq", m, m + 1), None, OP.min)
    ts(CS, PM, 1040.0, None, OP.add)
    ms(p_(3, 0, 256, 16), 0.0)
    ts(t_("lnO"), t_("lnO"), PM, 16.0, OP.add, OP.mult)
    for h in range(2):
        act(t_("lnq", 8 * h, 8 * h + 8), t_("lnO", 8 * h, 8 * h + 8), AF.Identity, bias=(2056 + 2048 * h) / 8192 - 1, scale=1.0 / 8192)
    for k in range(2):
        act(t_("ba", 16 * k, 16 * k + 16), t_("lnO"), AF.Identity, bias=16.0)
    for h in range(4):
        act(t_("ba", 32 + 4 * h, 36 + 4 * h), t_("lnO", 0, 4), AF.Identity, bias=16.0)
    iota(t_("ba", 48, 80), [[-2048, 2], [0, 16]], 2064)
    iota(t_("bb"), [[0, 2], [2048, 2], [0, 8]])
    fill(t_("X2", 0, 1), 0)
    fill(t_("X2", 1025, 1040), 0)
    for k in range(16):
        act(t_("X2", k or 16, 1025, step=16), ic(64), AF.Identity, bias=t_("ne", k, k + 1), scale=-16.0, grp="X2")
    ts(PK0, PM, 0.0, 16.0, OP.is_equal, OP.mult)
    tt(PK, PM, PK0, OP.add)
    ts(t_("T2", c=0), ic(32), PK, (Q0 + 8) / 256, OP.is_equal, OP.mult)
    stamps = lambda t: act(t_("T2", c=t), t_("T2", c=0), AF.Copy, scale=(Q0 + 8 + t) / (Q0 + 8))
    stamps(1)
    seed = lambda a, b: t_("T1s", a, b, rows=(0, 16))
    fill(seed(0, 560), 1)
    select(seed(0, 272), seed(0, 272), [[1, 272]], OP.not_equal, Q0 / 256, -264, 16)
    for pattern in ([[-1, 16], [0, 16]], [[0, 16], [-1, 16]]):
        select(seed(289, 545), seed(289, 545), pattern, OP.not_equal, Q0 / 256, 15, -1)
    select(t_("E16", rows=(0, 16)), t_("ones", rows=(0, 16)), [[0, 8], [-1, 16]], OP.is_equal, 0.0, 0, 1)
    for k, name in enumerate(("T1a", "T1b")):
        mm(p_((5, 7)[k], 0, 272 + 16 * k), t_("E16", rows=(0, 16)), seed(272 * k, 272 + 288 * k), True, True)
        act(t_(name), p_((5, 7)[k], 0, 272 + 16 * k), AF.Copy)
    ms(t_("pw", 0, 1), 1.0)
    for k in (1, 2, 4):
        ts(t_("pw", k, 2 * k), t_("pw", 0, k), float(2 ** k), None, OP.mult)
    ts(t_("p8e"), ic(8), P8, None, OP.is_equal)
    tt(t_("p8e"), t_("p8e"), t_("pw"), OP.mult)
    red(PW, t_("p8e"))
    ts(t_("xi"), ic(256), PW, None, OP.mult)
    ts(t_("xj"), t_("xi"), 128, None, OP.bitwise_and)
    ts(t_("Bt"), t_("xj"), 0.5, None, OP.mult)
    fill(t_("T3"), 0)
    now["step"] = 0
    act(t_("T3", 15, 1039, step=4), t_("Bt"), AF.Copy, scale=1.0 / 64)
    act(t_("T3", 16, 1040, step=4), t_("Bt"), AF.Identity, bias=1.0, scale=-1.0 / 64)
    now["step"] = -1
    ts(L1, PM, 8.0, 1.0 / 64, OP.is_lt, OP.mult)
    ts(L2, L1, 200.0, None, OP.mult)
    ts(H1, L1, -1.0, 1.0 / 64, OP.mult, OP.add)
    ts(t_("hb"), t_("Bt", 0, 16), H1, None, OP.mult)
    ts(t_("hb", c=1), t_("hb"), 200.0, -100.0, OP.mult, OP.add)
    hosts = lambda a=0, b=1024, rows=(0, 128): t_("ptab", 16 + a, 16 + b, rows=rows)
    act(hosts(768, 1024), t_("Bt"), AF.Identity, bias=t_("hb", 3, 4), scale=L1)
    act(t_("psrc", c=0), t_("Bt"), AF.Identity, bias=t_("hb", 4, 5, 1), scale=L2)
    bit_rows = lambda bit: (8 + bit, 128, 16)
    for k in range(3):
        copy(hosts(256 * k, 256 * k + 256), hosts(768, 1024))
    for k in range(3):
        for bit in range(2):
            if not k >> bit & 1:
                copy(hosts(256 * k, 256 * k + 256, bit_rows(bit)), hosts(768, 1024, bit_rows(2)), "rows")
    for t in range(1, STEPS):
        like = min(range(t), key=lambda x: bin((4 + x) ^ (4 + t)).count("1"))
        copy(t_("psrc", c=t), t_("psrc", c=like))
        for bit in range(4):
            if ((4 + like) ^ (4 + t)) >> bit & 1:
                copy(t_("psrc", c=t, rows=bit_rows(bit)), t_("psrc", c=0, rows=bit_rows(2 if (4 + t) >> bit & 1 else 0)), "rows")
    ts(t_("p8e", c=1), ic(8), t_("p8f"), None, OP.is_equal)
    tt(t_("p8e", c=1), t_("p8e", c=1), t_("pw"), OP.mult)
    red(W1, t_("p8e", c=1))
    ts(H1, H1, 255.0 * 64, 1.0, OP.mult, OP.add)
    ts(t_("EW"), t_("EB"), W1, H1, OP.mult, OP.mult)

    def to_list(out, src, a, b, wts="EB", stop=True):
        for r in range(16):
            mm(out, t_(wts, 15 - r, 143 - r), t_(src, a + r, b, 0, 16), r == 0, stop and r == 15)

    def host(t):
        now["step"] = t
        w = 32 if t + 2 < STEPS else 16
        mm(p_(3, 384, 400), t_("J"), t_("c05"), True, False)
        for r in range(16):
            mm(p_(3, 384, 400), t_("wE", 15 - r, 143 - r), t_("z", r, 256, t, 16), False, r == 15)
        ts(t_("ui", c=t), p_(3, 384, 400), 1.5 * 2 ** 35, 1.5 * 2 ** 35, OP.add, OP.subtract)
        tt(t_("s", c=t), p_(3, 384, 400), t_("ui", c=t), OP.subtract)
        act(t_("sq", c=t), t_("s", c=t), AF.Square, bias=2047.5 + 592)
        if w > 16:
            now["of"] = "u"
            ts(t_("UV", 16, 32, t), t_("s", c=t), 4.0, 8190.0, OP.mult, OP.add)
            now["of"] = ""
        ts(t_("UV", 0, 16, t), t_("sq", c=t), 1.0 / 32, t_("A", c=t - 1) if t else 311.59375, OP.mult, OP.add)
        ts(t_("VV", 0, w, t), t_("UV", 0, w, t), 1023, None, OP.bitwise_and)
        cp(t_("vl", c=t), t_("VV", 0, 16, t))
        if t:
            cp(t_("G"), ind(hosts(), t_("vl", c=t)))
            to_list(p_(2, 256, 272), "G", 0, 256, "EW")
            cp(t_("pl", c=t), p_(2, 256, 272))
        ts(t_("vh", 0, w, t), t_("VV", 0, w, t), 16.0, None, OP.add)
        for m in range(15):
            mm(p_(3, m + 1, 256, 16), t_("LR", 128 * m, 128 * m + 128), t_("vh", 0, 16, t), True, True)
        now["of"] = "*f"
        for m in range(16):
            mm(p_(3, 256 + m, 384, 16), t_("FS", 128 * m, 128 * m + 128), t_("vh", 0, 16, t, 2), True, False)
            mm(p_(3, 256 + m, 384, 16), t_("nI"), t_("vh", 1, 16, t, 2), False, True)
        now["of"] = ""
        ts(t_("E"), p_(3, 0, 384), 0.0, None, OP.is_equal)
        mm(p_(3, 400, 416), t_("I"), t_("vh", 0, 16, t), True, False)
        now["of"] = "*e"
        for m in range(15):
            mm(p_(3, 400, 416, 2), t_("I16"), t_("E", m + 1, 256, 0, 32), False, False)
            mm(p_(3, 401, 416, 2), t_("I16p"), t_("E", m + 17, 256, 0, 32), False, False)
        for m in range(16):
            mm(p_(3, 401, 416, 2), t_("I16p"), t_("E", 256 + m, 384, 0, 16), False, m == 15)
        now["of"] = ""
        ts(t_("wl", c=t), p_(3, 400, 416), PM, CS, OP.max, OP.min)

    def step(t):
        z = t_("z", c=t)
        n = 1024 + 256 * t
        cross = t + 2 < STEPS
        pl = t_("pl", c=t) if t else t_("vl", c=t)
        now["step"] = t
        for a, b in OFFS:
            if t:
                cp(t_("boff", a, b, t), ind(t_("blog", 0, n), t_("pl", a // 16, b // 16, t)))
            else:
                ts(t_("b0", a, b), ind(t_("bk"), t_("vl", a // 16, b // 16)), 4095, None, OP.bitwise_and)
                cp(t_("boff", a, b), t_("b0", a, b))
        for q, a, b in PARTS[t]:
            if q == "s":
                act(c_(t, a, b), ind(t_("geno_s"), t_("boff", a, b, t)), AF.Copy)
            else:
                cp(c_(t, a, b), ind(t_("geno_s"), t_("boff", a, b, t)))
        keep(t_("geno_s", t, 4096, step=16), z)
        if t == STEPS - 1:
            store("sg", T.ygeno[:], t_("geno_s"))
        for h in range(2):
            keep(m_(t, 128 * h, 128 * h + 128, 8), t_("z", 128 * h, 128 * h + 128, t))
            now["of"] = "x"
            if t < 2:
                keep(m_(t, 128 * h, 128 * h + 128, 0), t_("z", 128 * h, 128 * h + 128, t))
            now["of"] = ""
        qg, im1 = t_("qg", c=t), t_("im1", c=t)
        fl, gt = [lambda h, x=x: t_(x, 128 * h, 128 * h + 128, t) for x in ("fl", "gt")]
        for h in range(4):
            ts(t_("bs", 64 * h, 64 * h + 64, t), t_("boff", 64 * h, 64 * h + 64, t), float(t + 1024 * h), None, OP.add)
        act(qg, ind(t_("qlog", 0, n), pl), AF.Copy)
        act(im1, ind(t_("ilog", 0, n), pl), AF.Identity, bias=-1.0)
        ts(t_("fl", c=t), qg, (Q0 + t + 0.5) / 256, None, OP.is_gt)
        if t + 1 < STEPS:
            for h in range(4):
                mm(p_(4, 96 + 8 * h, 104 + 8 * h), fl(h % 2), t_("Gh", 8 * (h // 2), 8 * (h // 2) + 8), True, True)
            act(t_("sk"), p_(4, 96, 128), AF.Relu, bias=0.75e9, scale=-1e9)
        mm(p_(4, 256, 512), t_("I"), z, True, False)
        mm(p_(4, 256, 512), t_("nI"), im1, False, True)
        act(t_("gt", c=t), p_(4, 256, 512), AF.Sign, bias=-1.5)
        mm(p_(2, 0, 256), t_("J"), t_("C16"), True, False)
        for h in range(2):
            mm(p_(2, 128 * h, 128 * h + 128), t_("qg", 128 * h, 128 * h + 128, t), t_("I16"), False, h == 1)
        for j in range(7, -1, -1):
            act(ind(t_("ptab"), t_("wl", 2 * j, 2 * j + 2, t)), t_("psrc", 32 * j, 32 * j + 32, t), AF.Sigmoid)
        if cross:
            stamps(t + 2)
        if t + 1 == STEPS:
            for a, b in quarters:
                if a < PB:
                    act(t_("ptb", a, b), hosts(a, b), AF.Copy)
                else:
                    keep(t_("ptb", a, b), hosts(a, b))
            to_list(p_(3, 64, 128), "ptb", 0, 1024, "EW")
            cp(t_("plF"), p_(3, 64, 128))
        for h in range(4):
            mm(p_(4, 16 + 8 * h, 24 + 8 * h), gt(h % 2), t_("GS"), True, True)
        if t + 1 < STEPS:
            tt(t_("ac", 0, 32), p_(4, 16, 48), t_("sk"), OP.is_gt)
            mm(p_(4, 48, 82), t_("ones"), t_("ac"), True, True)
            red(t_("A", c=t), p_(4, 48, 82))
            host(t + 1)
            now["step"] = t
        scan(t_("qs", c=t), t_("d16"), p_(2, 0, 256), OP.add, OP.max)
        for e in range(2):
            mm(p_(0, e, 512, 2), t_("I"), z, True, True)
        top = lambda a, b, k: m_(t, a, b, k) if k % 8 else t_("MX", 2 * a + k // 8, 2 * b, 0, 2)
        now["of"] = "*"
        for a, b in MAXIMA:
            for k in range(8):
                tt(m_(t, a, b, k, True) if k else t_("MX", 2 * a, 2 * b), c_(t, a, b, k, 8), p_(0, 2 * a, 2 * b), OP.max)
        now["of"] = ""
        for h in range(2):
            gk, kb = ("key", t, h), (1, 6)[h]
            mm(p_(kb, 0, 136), t_("I"), t_("C17"), True, False, gk, "first")
            mm(p_(kb, 0, 136), fl(h), t_("IB"), False, False, gk, "mid")
            for a, b in SUMS:
                for k in range(16 if a // 128 == h else 0):
                    mm(p_(kb, 1 + k, 136, 17, (a % 128, b - 128 * h)), c_(t, a, b, k, 16), t_("G32"), False, False, gk, "mid")
            now["of"] = "*%d" % h
            for k in sorted(range(16), key=lambda k: k % 8):
                mm(p_(kb, 1 + k, 136, 17), top(128 * h, 128 * h + 128, k), t_("G64"), False, k == 15, gk, "last" if k == 15 else "mid")
            now["of"] = ""
            o = 136 * h
            scan(t_("s12", o, o + 136), t_("d17"), p_(kb, 0, 136), OP.add, OP.max)
            scan(t_("s12", 273 + o, 408 + o), p_(kb, 1, 136), t_("s12", o, o + 135), OP.max, OP.min)
        tt(t_("HI"), t_("s12", 16, 544, 0, 17), p_(4, 16, 48), OP.min)
        ts(t_("HA"), t_("HI"), int(BIG) + 31, None, OP.bitwise_and)
        ts(t_("KC"), t_("HA"), -BIG, -2040.0, OP.add, OP.max)
        tt(t_("kx"), t_("HA", 0, 16), t_("HA", 16, 32), OP.max)
        tt(t_("sm"), t_("kx"), t_("qs", 15, 256, t, 16), OP.max)
        ts(t_("sl"), t_("sm"), 15, None, OP.bitwise_and)
        cp(t_("KM", 0, 16), t_("sl"))
        cp(t_("KM", 32, 48), t_("sl"))
        ts(t_("ca"), t_("KC", 0, 16), -16.0, 16.0, OP.mult, OP.add)
        now["of"] = "1"
        tt(t_("KM", 16, 32), t_("ca"), t_("KC", 16, 32), OP.subtract)
        now["of"] = ""
        ol = lambda k, m=1: t_("ol", 16 * k, 16 * (k + m), t)

        for f0, f1, codes in ((0, 2, t_("KC")), (2, 5, t_("KM"))):
            now["of"] = "ab"[f0 // 2]
            for x in range(4):
                if x < 2:
                    ts(y_(f0, f1, x, 32, 4), codes, t_("Gm4", x, x + 1), None, OP.mult, grp="Y")
                else:
                    act(y_(f0, f1, x, 32, 4), codes, AF.Copy, scale=t_("Gm4", x, x + 1), grp="Y")
            lists = p_(5, 16 + 16 * f0, 16 + 16 * f1)
            mm(lists, t_("I"), t_("ba", 16 * f0, 16 * f1), True, False)
            if not f0:
                mm(lists, t_("I"), t_("bb"), False, False)
            for e in range(2):
                for k in range(8):
                    a = 48 * e + 16 - 16 * (k % 2)
                    out = dict(lists, ap=T.P5[32 * (k // 2):32 * (k // 2) + 32, 2 + 2 * f0:2 + 2 * f1, 4 * e:4 * e + 4])
                    mm(out, t_("RB", a, a + 32), y_(f0, f1, 4 * k, 4 * k + 4, 1), False, e == 1 and k % 2 == 1)
            cp(ol(f0, f1 - f0), lists)
        now["of"] = ""
        act(t_("pen"), p_(5, 64, 80), AF.Sigmoid, bias=1000.0, scale=-1.0)
        act(t_("ad"), p_(5, 16, 48), AF.Copy, scale=1.0 / 8192)
        tt(t_("ybk"), ind(t_("X2", 0, 1025), ol(2)), t_("bs", c=t), OP.min)
        for h in range(4):
            act(t_("blog", n + 64 * h, n + 64 * h + 64), t_("ybk", 64 * h, 64 * h + 64), AF.Abs, bias=float(-t - 1024 * h))
        tt(t_("q1"), ind(t_("T1a", 0, 2048 + 273), ol(3)), qg, OP.min)
        tt(t_("qlog", n, n + 256), ind(t_("T2", c=t), ol(4)), t_("q1"), OP.max)
        win = dict(t_("W", c=t), rg=c_(t, 0, 128)["rg"] + c_(t, 128, 256)["rg"] + [("M%d.%d" % (t % 2, r), 0, 256) for r in range(16)])
        d = t_("d12", 0, 256)
        now["of"] = "z"
        for k in range(2):
            mm(p_(7, 256 * k, 256 * k + 256), t_("I"), z, k == 0, False)
        now["of"] = ""
        tt(d, ind(win, ol(0)), z, OP.subtract)
        act(t_("a2"), ind(win, ol(1)), AF.Copy)
        act(t_("SG", 0, 256), d, AF.Sigmoid, bias=-math.log(31.0), scale=-40.0)
        mm(p_(7, 256, 512), t_("I"), d, False, False)
        for k in range(2):
            mm(p_(7, 256 * k, 256 * k + 256), t_("nI"), t_("a2"), False, k == 1)
        act(t_("SG", 256, 768), p_(7, 0, 512), AF.Sigmoid, bias=-math.log(31.0), scale=40.0)
        if cross:
            act(t_("d12", 256, 512), p_(7, 0, 256), AF.Copy, scale=-1.0)
        cnt = p_(4, 128, 176)
        to_list(cnt, "SG", 0, 768, stop=False)
        for k in range(2):
            mm(p_(4, 144 + 16 * k, 160 + 16 * k), t_("I9"), t_("pen"), False, k == 1)
        ts(t_("ti"), cnt, 1056.0, None, OP.mult)
        ts(th_(3, 6), cnt, 8.75, None, OP.is_gt)
        ts(t_("mk"), t_("ti"), 768, None, OP.bitwise_and)
        ts(th_(0, 3), t_("mk"), 0.0, None, OP.is_equal)
        D = lambda a, b: p_(2, 304 + 16 * a, 304 + 16 * b)
        code = lambda a, b: p_(5, 320 + 16 * a, 320 + 16 * b)
        now["of"] = "*g"
        mm(D(0, 3), t_("I"), th_(3, 6), True, False)
        mm(D(2, 3), t_("I"), th_(4, 5), False, False)
        now["of"] = "*l"
        mm(D(0, 2), t_("I"), th_(2, 6, 3), False, False)
        mm(D(0, 3), t_("nI"), th_(0, 3), False, False)
        mm(D(0, 1), t_("nI"), th_(1, 2), False, False)
        mm(D(1, 3), t_("nI"), th_(0, 4, 3), False, True)
        now["of"] = "*u"
        for k in range(2 if cross else 0):
            mm(code(k, k + 1), t_("I"), t_("vh", 16, 32, t), k == 0, False)
        now["of"] = ""
        ts(t_("C"), D(0, 3), -0.5, 0.5, OP.is_gt, OP.subtract)

        def ranks(name, o, first):
            now["of"] = name
            mm(code(o, o + 2), t_("I"), t_("C", 0, 32), first, False)
            mm(code(o + 1, o + 2), t_("I"), t_("C", 32, 48), False, False)
            mm(code(o, o + 1), t_("nI"), t_("C", 32, 48), False, True)
            now["of"] = ""
        if cross:
            ranks("*c", 0, False)
        ranks("*k", 2, True)
        if cross:
            cp(t_("cl", c=t), code(0, 2))
            tt(t_("cx", c=t), ind(t_("T3"), t_("cl", c=t)), t_("d12"), OP.mult)
            send([z, t_("cx", 0, 256, t), t_("cx", 256, 512, t)], t + 2, (rank + 2) % n_ranks)
        tt(t_("K"), t_("ad"), code(2, 4), OP.add)
        tt(t_("mna"), t_("lnq"), t_("K", 0, 16), OP.min)
        tt(t_("mnb"), t_("mna"), t_("K", 16, 32), OP.min)
        ts(t_("fl1", c=t), t_("mnb"), 8192.0, 8192.0, OP.mult, OP.add)
        tt(t_("ilog", n, n + 256), ind(win, t_("fl1", c=t)), im1, OP.max)

    host(0)
    for t in range(STEPS):
        step(t)
    now["step"] = STEPS
    for k, (a, b) in enumerate(quarters):
        lst = t_("plF", a // 16, b // 16)
        act(t_("q4", a, b), ind(t_("qlog"), lst), AF.Identity, bias=-4096.0 * Q0, scale=4096.0 * 256)
        tt(t_("yb", a, b), ind(t_("blog"), lst), t_("q4", a, b), OP.add)
    for k, (a, b) in enumerate(quarters):
        lst = t_("plF", a // 16, b // 16)
        if YI[k] == "v":
            cp(t_("yi", a, b), ind(t_("ilog"), lst))
        else:
            act(t_("yi", a, b), ind(t_("ilog"), lst), AF.Copy)
    for k, (name, a, b, q) in enumerate(OUTS):
        store("so%d" % k, {"yb": T.ybank, "yi": T.yimm}[name][:, a:b], t_(name, a, b), q)
    return ops, edges


def queues(ops):
    calls = {}
    for i, o in enumerate(ops):
        calls.setdefault((o["step"], o["name"]), []).append(i)
    rows = {q: [i for i, o in enumerate(ops) if o["q"] == q] for q in "yn"}
    for q in "vspg":
        row = rows[q] = []
        for t, words in [(0, FIRST[q])] + [(t, ORDER[q]) for t in range(STEPS - 2)] + [(STEPS - 2, FINAL[q])]:
            for word in words.split():
                name, _, count = word.partition(":")
                step = {"_": -1, "^": STEPS}.get(name[0], t + name.count("+"))
                left = calls.get((step, q + name.strip("_^+")), [])
                row += [left.pop(0) for _ in range(min(int(count or 1), len(left)))]
        assert len(row) == sum(o["q"] == q for o in ops)
    return rows


def banks(ops, edges, rows):
    end = [None] * len(ops)
    ahead = {q: 0 for q in rows}
    free = {q: 0.0 for q in rows}
    user = {}

    def earliest(i):
        o = ops[i]
        t = free[o["q"]]
        for j, w in edges[i].items():
            if end[j] is None:
                return None
            t = max(t, end[j] + ((ops[j]["after"] + WAKE if ops[j]["after"] or ops[j]["q"] != o["q"] else OWN) if w else 0.0))
        return max([t] + [end[j] + WAKE for bank in o["banks"] for q, j in user.get(bank, {}).items() if q != o["q"]])
    for _ in ops:
        t, q = min((earliest(row[ahead[q]]), q) for q, row in rows.items() if ahead[q] < len(row) and earliest(row[ahead[q]]) is not None)
        i = rows[q][ahead[q]]
        ahead[q] += 1
        end[i] = t + ops[i]["busy"]
        free[q] = end[i] if q != "n" else 0.0
        for bank in ops[i]["banks"]:
            edges[i].update({j: 1 for q2, j in user.setdefault(bank, {}).items() if q2 != q})
            user[bank][q] = i


def rank_program(g, core, T, topo):
    if T.rank_of(core) is None:
        return
    ops, edges = program(g, core, T, topo)
    rows = queues(ops)
    banks(ops, edges, rows)
    eng = {"v": g.vector, "s": g.scalar, "p": g.tensor, "g": g, "y": g.sync}
    total = {}
    at = [None] * len(ops)
    know = {q: {} for q in eng}
    snap = [None] * len(ops)

    def issue(i):
        o = ops[i]
        q = o["q"]
        if q == "n":
            at[i] = (o["sem"], o["inc"])
            snap[i] = {o["sem"]: o["inc"]}
            total[o["sem"]] = o["inc"]
            return
        k = know[q]
        want = {}
        for j, w in edges[i].items():
            if w:
                s, v = at[j]
                if k.get(s, 0) < v and want.get(s, (0, 0))[0] < v:
                    want[s] = (v, j)
        for s in list(want):
            v, j = want[s]
            if any(s2 != s and snap[j2].get(s, 0) >= v for s2, (v2, j2) in want.items()):
                del want[s]
        for s, (v, j) in want.items():
            eng[q].wait_ge(T.sem[s], v)
            for s2, v2 in snap[j].items():
                if k.get(s2, 0) < v2:
                    k[s2] = v2
        ins = o["emit"]()
        snap[i] = dict(k)
        if o["sem"] is not None:
            total[o["sem"]] = total.get(o["sem"], 0) + o["inc"]
            ins.then_inc(T.sem[o["sem"]], o["inc"])
            at[i] = (o["sem"], total[o["sem"]])
            snap[i][o["sem"]] = total[o["sem"]]
        if "remote" in o:
            total["rl"] = total.get("rl", 0) + o["remote"]

    ahead = {q: 0 for q in rows}
    left = len(ops)
    while left:
        before = left
        for q, row in rows.items():
            while ahead[q] < len(row) and all(snap[j] is not None for j in edges[row[ahead[q]]]):
                issue(row[ahead[q]])
                ahead[q] += 1
                left -= 1
        assert left < before
    for s in sorted(total):
        if know["g"].get(s, 0) < total[s]:
            g.wait_ge(T.sem[s], total[s])
